import numpy as np, ml_dtypes
CORES = [6,15,38,47]
N = 4
BF = ml_dtypes.bfloat16
def gentries(a):
    return np.ascontiguousarray(a.reshape(8, 16, -1).transpose(0, 2, 1)).reshape(8, -1)
def gtable(e):
    e = np.asarray(e); return np.ascontiguousarray(e.reshape(8, -1, 16).transpose(0, 2, 1)).reshape(128, -1).astype(np.int32)
V, VM, RO = 4096, 100, 3
H = V // 2
def toward(rng, share):
    c = int(share * H); a, b = 2 * rng.permutation(H), 2 * rng.permutation(H) + 1; e, o = 2 * rng.permutation(H), 2 * rng.permutation(H) + 1
    t = np.zeros(V, np.int64); t[a[:c]] = o[:c]; t[a[c:]] = e[c:]; t[b[:c]] = e[:c]; t[b[c:]] = o[c:]
    return t
def lean(rng, s):
    t = np.zeros(V, np.int64); k = 2 * np.arange(H // 2); e = 2 * rng.permutation(H)
    t[s * H + k] = (1 - s) * H + 1 + rng.permutation(k); t[(1 - s) * H + k] = e[:H // 2]
    t[1::2] = rng.permutation(np.concatenate([e[H // 2:], s * H + 1 + k]))
    return t
def put(u, a, b):
    i = int(np.argmax(u == b)); u[i] = u[a]; u[a] = b
def targets(rng):
    return np.stack([toward(rng, s) for s in rng.permutation(np.array([0.4, 0.5, 0.5, 0.6, 0.7, 0.8, 0.9, 1.0]))])
def points(rng):
    return np.floor((rng.integers(VM // 4, VM + 1, (N, 8, 16, 1)) + 1) * rng.random((N, 8, 16, V))).astype(np.int64)
def nudge(rng, x):
    for g in range(8):
        j = rng.permutation(V)[:V // 16]; r = rng.integers(0, N, V // 16); i = rng.integers(0, 16, V // 16)
        v = x[r, g, i, j]; x[r, g, i, j] = np.where(v < VM, v + 1, v - 1)
    return x
def pack(rng, x, t):
    d = {"z": np.ascontiguousarray(x.reshape(N, 128, V)).astype(np.float32).astype(BF)}
    d["q"] = np.stack([gtable(t)] * N)
    return d
def setup_inputs(rng):
    return pack(rng, points(rng), targets(rng))
def setup_inputs_ties(rng):
    s = rng.integers(0, VM + 1, (N, 8, 16, 6)); k = rng.permutation(np.array([2, 2, 3, 3, 4, 4, 6, 6]))
    ix = rng.integers(0, k[:, None], (8, V))
    return pack(rng, nudge(rng, np.take_along_axis(s, ix[None, :, None, :], 3)), targets(rng))
def setup_inputs_corners(rng):
    x = np.repeat(VM * rng.integers(0, 2, (N, 8, 1, V)), 16, axis=2)
    return pack(rng, nudge(rng, x), targets(rng))
def setup_inputs_ends(rng):
    j = np.arange(V); x = points(rng); x[..., 0] = 0; x[..., 1] = VM; x[..., V - 1] = VM
    t = np.zeros((8, V), np.int64); o = rng.permutation(8)
    t[o[0]] = (j + 1) % V; t[o[1]] = (j - 1) % V; t[o[2]] = j ^ 1; t[o[3]] = np.where(j % 2 == 0, V - 1 - j, (j + H + 1) % V)
    u = j.copy(); s = rng.random(V) < 0.5
    for p in range(2):
        i = np.flatnonzero(s & (j % 2 == p)); u[i] = rng.permutation(i)
    t[o[4]] = u
    y = x[:, o[5]]; y[:] = y[:, :, 2:3].copy()
    a = 2 * int(rng.integers(0, H)); b = (a + 2 * int(rng.integers(2, H - 3)) + 1) % V
    y[:, :, a] = VM - y[:, :, a]; y[:, :, b] = y[:, :, a]
    u = toward(rng, 0.7); put(u, a, b); t[o[5]] = u
    y = x[:, o[6]]; u = toward(rng, 0.5); put(u, V - 1, 0); put(u, 0, V - 2)
    y[:, :, [0, V - 2]] = y[:, :, [V - 3]]; y[:, :, [1, V - 1]] = VM - y[:, :, [V - 3]]
    e = 2 * np.arange(H); e = e[u[e] % 2 == 1]; y[:, :, e] = y[:, :, e - 1]; t[o[6]] = u
    y = x[:, o[7]]; y[:] = y[:, :, 2:3].copy(); t[o[7]] = rng.permutation(V)
    return pack(rng, x, t)
def setup_inputs_crowd(rng):
    x = points(rng); t = np.zeros((8, V), np.int64); o = rng.permutation(8); ev = 2 * np.arange(H)
    for i in range(5): t[o[i]] = toward(rng, (1.0, 1.0, 0.95, 0.9, 0.9)[i])
    t[o[5], ev] = (ev + 2 * rng.integers(1, H - 2) + 1) % V; t[o[5], ev + 1] = 2 * rng.permutation(H)
    t[o[6]] = lean(rng, 0); t[o[7]] = lean(rng, 1)
    for g in range(8):
        m = ev[t[g, ev] % 2 == 1]; y = x[:, g]; y[:, :, m] = y[:, :, t[g, m]]
    return pack(rng, x, t)
def setup_inputs_spread(rng):
    x = (VM + 1) * np.exp2(-rng.integers(0, 6, (N, 8, 1, V)).astype(np.float64)) * rng.random((N, 8, 16, V))
    x = np.floor(x * (rng.random((N, 8, 16, 1)) > 0.0625)).astype(np.int64)
    return pack(rng, np.minimum(x, VM), np.stack([toward(rng, s) for s in 0.1 + 0.9 * rng.random(8)]))
def check_inputs(d):
    bad = []
    v = np.asarray(d["z"]).astype(np.float32)
    if not np.all((v >= 0) & (v <= VM) & (v == np.floor(v))): bad.append("z holds whole numbers of its range")
    if np.any(d["q"] != d["q"][:1]): bad.append("q alike on all ranks")
    if any(np.any(np.sort(gentries(a), axis=1) != np.arange(V)) for a in d["q"]): bad.append("q is a permutation in each group")
    return bad
def dist(c):
    return np.add.reduce(np.abs(c), axis=(0, 2))
def reference(z, q):
    x = z.astype(np.float32).astype(np.int32).reshape(N, 8, 16, V); t = gentries(q[0]).astype(np.int64); j = np.arange(V)
    for rnd in range(RO):
        left, right = np.roll(x, 1, axis=3), np.roll(x, -1, axis=3); ix = t[None, :, None, :]
        a = np.take_along_axis(x, ix, 3); b = np.take_along_axis(right, ix, 3)
        gain = dist(left - x) + dist(x - right) - dist(left - right) - dist(a - x) - dist(x - b) + dist(a - b)
        moves = ((gain > 0) & (j % 2 == rnd % 2) & (t % 2 != j % 2)).astype(np.int64)
        guest = np.zeros((8, V), np.int64); np.put_along_axis(guest, t, moves, 1)
        w = 1 - moves + guest; base = np.add.accumulate(w, axis=1) - w
        new = np.where(moves == 1, np.take_along_axis(base, t, 1) + 1, base)
        old = np.argsort(new, axis=1)
        x = np.take_along_axis(x, old[None, :, None, :], 3)
        t = np.take_along_axis(np.take_along_axis(new, t, 1), old, 1)
    return {"yz": x.reshape(N, 128, V).astype(np.float32).astype(BF), "yq": np.stack([t] * N).astype(np.float32)}

@@ -1,0 +1,632 @@
+import numpy as np
+from concourse.mybir import AluOpType as A, ActivationFunctionType as F
+from concourse.bass import DstId, RemoteDMATransfer
+
+C_ACT = False
+PSUM_OPS = True
+OV = ()
+XV = ()
+PE_NS = 0.5
+HOP = 2600.0
+LAT = 90.0
+TT_SB = 2.0
+B1 = 10000.0
+SEED = 0
+NOISE = 0.0
+
+H, Q, WD, CW, LW = 2, 4, 512, 32, 128
+BF, HF, FP, I32, U16 = "bfloat16", "float16", "float32", "int32", "uint16"
+BUF = {
+    "zt": (4112, BF), "yt": (4096, BF), "Et": (2112, BF), "Ot": (2112, BF), "Xt": (2048, BF),
+    "tA": (2048, BF), "tB": (2048, BF), "tC": (2048, BF), "tD": (2048, BF), "tF": (2048, BF), "tG": (2048, BF),
+    "LE": (130, U16), "LO": (130, U16), "LX": (128, U16), "LY": (256, U16),
+    "win1": (4608, BF), "win20": (4096, BF), "win21": (4096, BF), "win22": (4096, BF), "win3": (4096, BF), "rowsE": (512, BF), "rowsO": (512, BF),
+    "sP0": (128, HF), "sP1": (256, HF), "sP2": (256, HF), "rP0": (128, HF), "rP1": (256, HF), "rP2": (256, HF),
+    "rE0": (256, HF), "rE1": (256, HF), "rE2": (256, HF), "rX0": (128, HF), "rX1": (128, HF), "rX2": (256, HF),
+    "hX0": (32, HF), "hX1": (32, HF), "hX2": (64, HF), "qf": (256, FP),
+    "wI": (256, FP), "wP": (256, FP), "wM": (256, BF), "wV": (256, BF), "wL": (768, FP), "wQ": (512, FP), "wN": (256, FP),
+    "gI": (512, FP), "gP": (512, HF), "gQ": (1024, HF), "maskE": (512, HF), "mask1": (1024, HF),
+    "mv": (32, HF), "nv": (32, HF), "d1": (32, FP), "d2": (32, FP), "ud": (32, U16), "cum": (40, HF), "mvL": (32, FP), "vL": (32, FP),
+    "pe": (32, FP), "s1": (32, FP), "s2": (32, FP), "s3": (32, FP), "uO": (32, U16), "uE": (32, U16), "ntab": (64, HF),
+    "l1": (192, HF), "qo": (64, I32), "qn": (64, I32), "q1": (32, I32), "n1": (64, I32), "n2": (64, I32), "n3": (64, I32),
+    "n4": (64, I32), "n5": (64, I32), "offN": (64, U16), "lo1": (64, BF), "offO": (32, U16), "loE": (32, BF),
+    "qhi": (64, BF), "qlo": (64, BF), "m1": (32, I32), "m2": (32, I32), "m3": (32, I32), "m8": (32, I32), "m4": (64, I32),
+    "m5": (64, I32), "m6": (32, I32), "m7": (32, I32), "pen": (32, FP), "md": (32, FP),
+    "qi": (256, I32), "qh": (256, HF), "qt1": (128, I32), "qt2": (128, I32), "QE": (128, HF), "q0": (64, I32), "uq0": (64, U16), "q0h": (64, HF),
+    "ones": (512, BF), "irows": (1024, BF), "ia": (1024, BF), "ib": (1024, BF),
+    "X": (384, FP), "val": (1024, BF), "pi": (16, I32), "pf": (32, FP), "Mi": (16, FP), "Mq": (8, FP), "Y": (32, FP), "X2": (128, FP),
+    "X3": (128, FP), "idb": (128, BF), "nidb": (128, BF), "nidh": (128, HF), "nsh": (128, HF), "ncar": (128, HF), "sh2": (128, BF), "dg": (256, BF),
+    "W": (144, HF), "base3": (384, BF), "c3": (6144, BF), "blkb": (16, BF), "blkh": (8, HF), "blkf": (8, FP), "e0": (8, BF), "LT": (1024, HF),
+    "GE": (1024, HF), "Rh": (1024, HF), "RQ": (512, HF), "Sel": (512, BF), "sel": (16, BF), "WG": (480, HF), "RS": (896, HF), "sq": (512, HF),
+    "v2": (128, FP), "cl": (16, U16), "cPO": (256, FP), "dump": (32, FP), "cmd": (32, FP),
+}
+AL, SB = {}, {}
+for _k, (_w, _d) in BUF.items():
+    _o = SB.get("pool" + _d, (0, _d))[0]
+    AL[_k] = ("pool" + _d, _o, _w); SB["pool" + _d] = (_o + (_w + 15) // 16 * 16, _d)
+SCRATCH = {k: ("sbuf", [128, w], d) for k, (w, d) in SB.items()}
+for _b in range(8):
+    SCRATCH["p%d" % _b] = ("psum", [128, 512], "float32")
+SEMAPHORES = ["v", "t", "s", "gp", "loc"] + ["d%d" % k for k in range(24)] + [k + str(t) for k in ("rs", "ag", "hx", "hi") for t in range(3)]
+
+
+def V(n, lo=0, hi=None, st=1):
+    b, o, w = AL[n]
+    return ("V", b, o + lo, o + (w if hi is None else hi), st)
+
+
+def IND(w, o):
+    return ("I", w, o)
+
+
+def nel(v):
+    return 16 * nel(v[2]) if v[0] == "I" else len(range(v[2], v[3], v[4]))
+
+
+def two(v):
+    return v[0] == "V" and v[1] in SB and SB[v[1]][1] in (BF, HF, U16)
+
+
+def isv(a):
+    return isinstance(a, tuple) and len(a) > 0 and a[0] in ("V", "I")
+
+
+def cost(eng, ins):
+    m, a = ins[0], ins[1]
+    if eng == "t":
+        return PE_NS * max(64, nel(a[0])) * (1 if two(a[1]) else 4)
+    vs = [x for x in a if isv(x)]
+    n = max(nel(x) for x in vs if x[0] == "I") if any(x[0] == "I" for x in vs) else nel(a[0])
+    if eng == "gp":
+        return 150 + 2.0 * n
+    if a[0][0] == "I":
+        return 60 + 3.9 * n
+    if any(x[0] == "I" for x in vs):
+        return 60 + 1.62 * n
+    if eng == "s":
+        return 70 + 1.04 * n
+    big = [x for x in vs if nel(x) == n]
+    c = 0.5 if all(two(x) for x in big) else 1.0
+    if m == "tensor_tensor" and a[1][1] in SB and a[2][1] in SB:
+        c = TT_SB if c == 0.5 else 2.0
+    return 1.04 * max(64, c * n)
+
+
+def plan(r):
+    ops = []; boost = [0.0]
+
+    def spans(x):
+        return spans(x[1]) + spans(x[2]) if x[0] == "I" else [(x[1], x[2], x[3])]
+
+    def op(eng, *ins):
+        rd, wr = [], []
+        for m, a, kw in ins:
+            if a[0][0] == "I":
+                wr += spans(a[0][1]); rd += spans(a[0][2])
+            else:
+                wr += spans(a[0])
+            for x in list(a[1:]) + list(kw.values()):
+                if isv(x):
+                    rd += spans(x)
+        ops.append((eng, "c", ins, sorted(set(rd)), sorted(set(wr)), sum(cost(eng, i) for i in ins), boost[0]))
+
+    def ts(o, i, s1, s2, o0, o1=None):
+        op("v", ("tensor_scalar", (o, i, s1, s2, o0) if o1 is None else (o, i, s1, s2, o0, o1), {}))
+
+    def tt(o, a, b, f):
+        op("v", ("tensor_tensor", (o, a, b, f), {}))
+
+    def cp(o, i):
+        op("v", ("tensor_copy", (o, i), {}))
+
+    def ms(o, c):
+        op("v", ("memset", (o, c), {}))
+
+    def act(o, i, f=None, **kw):
+        op("s", ("activation", (o, i, f if f is not None else (F.Identity if kw else F.Copy)), kw))
+
+    def iota(o, pat, base, cm):
+        op("gp", ("iota", (o, pat, base, cm), {} if SB[o[1]][1] == I32 else {"allow_small_or_imprecise_dtypes": True}))
+
+    def mm(groups, first=True, last=True):
+        ins = []
+        for gr in groups:
+            for k, (o, l, x) in enumerate(gr):
+                ins.append(("matmul", (o, l, x, first and k == 0, last and k == len(gr) - 1), {}))
+        op("t", *ins)
+
+    def dma(eng, items, load, ns):
+        sp = sorted(set(s for x in items for s in spans(x[0])))
+        rd = sorted(set(s for x in items if isv(x[3]) for s in spans(x[3])))
+        ops.append((eng, "d", (load, items), rd if load else sp, sp if load else [], ns, 0.0))
+
+    def remote(kind, t, n, w, ns, src=None):
+        sl = lambda b, x: V(b, w * x, w * x + w)
+        srcs = [sl(src, x) for x in others] if src else [sl(n, r)]
+        ops.append(("gp", "r", (kind, t, srcs, sl(n, r)), [s for x in srcs for s in spans(x)], [s for x in others for s in spans(sl(n, x))], ns, 0.0))
+
+    P = lambda b, lo=0, hi=512, st=1: ("V", "p%d" % b, lo, hi, st)
+    col = lambda n, j: V(n, j, j + 1)
+    ZW = V("zt", 16)
+    SHR, AND = A.arith_shift_right, A.bitwise_and
+    EQ, MUL, ADD = A.is_equal, A.mult, A.add
+    others = [x for x in range(4) if x != r]
+
+    dma("sy", [(V("qi"), 0, 128, "q", 0, 128, 0, 256), (V("zt", 0, 16), 0, 128, "z", 0, 128, 4080, 16)], True, 2200)
+    for c in range(4):
+        dma("sy" if c % 2 else "s", [(V("zt", 16 + 1024 * c, 1040 + 1024 * c), 0, 128, "z", 0, 128, 1024 * c, 1024)], True, 2600 + 700 * c)
+    dma("s", [(V("q0"), 16 * u, 16, "q", 16 * (2 * r + u // 4), 16, 64 * (u % 4), 64) for u in range(8)], True, 2500)
+
+    iota(V("X"), [[1, 384]], -128, 0)
+    X = lambda lo, hi, st=1: V("X", 128 + lo, 128 + hi, st)
+    iota(col("pi", 0), [[0, 1]], 0, 1)
+    iota(V("X3"), [[1, 8], [0, 16]], 0, 0)
+    iota(V("v2"), [[16, 8], [2, 16]], 0, -1)
+    for j, (sh, an) in enumerate([(0, 15), (4, 7), (6, 1), (4, 3), (0, 7), (3, 1), (1, 7), (0, 1)]):
+        ts(col("pi", j + 1), col("pi", 0), sh, an, SHR, AND)
+    cp(V("pf", 0, 9), V("pi", 0, 9))
+    pf = lambda j: col("pf", j)
+    lin = lambda o, a, c, b: ts(pf(o), pf(a), float(c), b, MUL, ADD)
+    blk = lambda n, a: V(n, 128 * a, 128 * a + 128)
+    ts(V("idb"), X(0, 128), pf(0), None, EQ)
+    ts(V("blkb", 0, 8), X(0, 8), pf(2), None, EQ)
+    ts(V("blkb", 8, 16), X(0, 8), pf(2), -1.0, EQ, MUL)
+    ts(V("nidb"), X(0, 128), pf(0), -1.0, EQ, MUL)
+    ts(V("base3", 256, 384), V("X3"), pf(2), None, EQ)
+    for k in range(4):
+        ts(blk("sq", k), V("v2"), float(16 * (k % 2) - k // 2), None, EQ)
+    for k in range(4):
+        tt(blk("sq", k), blk("sq", k), V("base3", 256, 384), MUL)
+    ts(V("nidh"), X(0, 128), pf(0), -1.0, EQ, MUL)
+    ts(V("nsh"), X(-1, 127), pf(0), -1.0, EQ, MUL)
+    ts(V("ncar"), X(127, 255), pf(0), -1.0, EQ, MUL)
+    ts(V("sh2"), X(2, 130), pf(0), None, EQ)
+    ts(V("blkh"), X(0, 8), pf(2), None, EQ)
+    ts(V("blkf"), X(0, 8), pf(2), None, EQ)
+    ts(V("Mi"), X(0, 16), pf(1), None, EQ)
+    ts(V("Mq"), X(0, 8), pf(4), None, EQ)
+    ts(col("e0", 0), pf(1), 0.0, None, EQ)
+    lin(12, 2, 16, 0.0); lin(13, 3, 16, pf(1)); lin(14, 3, 64, pf(1))
+    ts(pf(15), pf(1), 3.5, None, A.is_lt)
+    lin(16, 2, 4, pf(6)); lin(17, 5, 32, pf(16)); lin(18, 5, 96, pf(16)); lin(19, 5, 64, pf(16)); lin(20, 2, 4, pf(19))
+    lin(21, 2, 4, 0.0); lin(22, 8, 32, pf(21)); lin(23, 7, 96, pf(22))
+    lin(24, 3, 16, 0.0); ts(pf(25), pf(4), 16.0, col("Mi", 2), MUL, MUL); lin(26, 1, 2, -2047.0); lin(27, 1, 1, 112.0)
+    ts(V("W", 0, 143), X(-15, 128), pf(12), None, EQ)
+    ts(V("base3", 0, 128), X(-4, 124), pf(12), None, EQ)
+    ts(V("base3", 128, 256), X(-5, 123), pf(12), None, EQ)
+    for i in range(16):
+        boost[0] = B1 - 300.0 * i
+        act(V("c3", 384 * i, 384 * i + 384), V("base3"), scale=col("Mi", i))
+    boost[0] = 0.0
+    RowH = lambda i: V("c3", 384 * i, 384 * i + 128)
+    RowL = lambda i: V("c3", 384 * i + 128, 384 * i + 256)
+    Brd = lambda i: V("c3", 384 * i + 256, 384 * i + 384)
+    Col = lambda i: V("W", 15 - i, 143 - i)
+    iota(V("ia"), [[1, 16], [0, 64]], 0, 0)
+    iota(V("ib"), [[0, 16], [1, 64]], 0, 0)
+    iota(V("val"), [[16, 8], [0, 8], [1, 16]], 0, -1)
+    iota(V("X2"), [[16, 2], [0, 4], [1, 16]], 0, 0)
+    iota(V("Y", 0, 6), [[-2, 3], [16, 2]], 4, 0)
+    iota(V("Y", 6, 10), [[2, 2], [16, 2]], 2, 0)
+    iota(V("dump"), [[16, 32]], 4096, 0)
+    iota(V("cmd"), [[2048 - 256, 2], [-16, 16]], -4096, 0)
+    iota(V("cPO"), [[32, 8], [0, 2], [256, 16]], 0, 0)
+    ts(V("Rh"), V("val"), 0.0, None, EQ)
+    ts(V("LT"), V("val"), 0.0, None, A.is_gt)
+    ts(V("GE"), V("val"), 0.0, None, A.is_le)
+    for qt in range(4):
+        ts(blk("RQ", qt), V("X2"), pf(13), col("Mq", qt), EQ, MUL)
+        ts(blk("Sel", qt), X(-16 * qt, 128 - 16 * qt), pf(14), pf(15), EQ, MUL)
+        ts(V("RS", 224 * qt, 224 * qt + 224), X(-96, 128), pf(13), col("Mq", qt), EQ, MUL)
+    RS = lambda v, s: V("RS", 224 * v + 96 - 32 * s, 224 * v + 224 - 32 * s)
+    ts(V("Y", 10, 20), V("Y", 0, 10), pf(13), 64.0, EQ, MUL)
+    ts(V("Y", 20, 30), V("Y", 0, 10), 1.0, pf(13), ADD, EQ)
+    tt(V("sel", 0, 10), V("Y", 10, 20), V("Y", 20, 30), ADD)
+    for e in range(2):
+        ts(V("WG", 240 * e, 240 * e + 240), X(0, 240), pf(27), col("blkf", 2 * r + e), EQ, MUL)
+    ts(V("cl", 0, 2), X(0, 4, 2), pf(17), None, ADD)
+    ts(V("cl", 2, 4), X(64, 68, 2), pf(18), None, ADD)
+    ts(V("cl", 4, 8), X(0, 4), pf(23), None, ADD)
+    ts(V("cl", 8, 10), X(0, 4, 2), pf(19), None, ADD)
+    ts(V("cl", 10, 12), X(32, 36, 2), pf(19), None, ADD)
+    ts(V("cl", 12, 16), X(0, 8, 2), pf(20), None, ADD)
+    cL2, cX, cEO, cQ, cF = V("cl", 0, 2), V("cl", 2, 4), V("cl", 4, 8), V("cl", 8, 12), V("cl", 12, 16)
+    ts(V("dump"), V("dump"), pf(1), None, ADD)
+    ts(V("cmd"), V("cmd"), pf(1), None, A.subtract)
+    ts(V("cPO"), V("cPO"), pf(26), None, ADD)
+    for k in range(2):
+        ts(blk("dg", k), X(0, 128), pf(0), col("Mi", 2 + k), EQ, MUL)
+    for k in range(2):
+        mm([[(P(7), blk("dg", 0), V("ia", 512 * k, 512 * k + 512)), (P(7), blk("dg", 1), V("ib", 512 * k, 512 * k + 512))]])
+        act(V("irows", 512 * k, 512 * k + 512), P(7), bias=pf(25))
+    ms(V("ones"), 1.0)
+
+    def masks(bank, lo, out):
+        mm([[(P(bank, i, 512, 16), Brd(i), lo)] for i in range(16)])
+        ts(out, P(bank), pf(1), None, EQ)
+
+    def prep(p, win):
+        e = V("qn", 0, 32)
+        ts(V("m1"), e, 0xE0, None, AND)
+        ts(V("m2"), e, 8, None, SHR)
+        tt(V("m3"), V("m1"), V("m2"), ADD)
+        ts(V("offO"), V("m3"), pf(24), None, ADD)
+        ts(V("m8"), e, 1, 15, SHR, AND)
+        cp(V("loE"), V("m8"))
+        masks(6, V("loE"), V("maskE"))
+        ts(V("m4"), V("qn"), 6, None, SHR); cp(V("qhi"), V("m4"))
+        ts(V("m5"), V("qn"), 63, None, AND); cp(V("qlo"), V("m5"))
+        ts(V("m6"), V("q1"), 1, None, SHR); tt(V("md"), V("m6"), V("cmd"), ADD)
+        ts(V("m7"), V("q1"), 1, None, AND)
+        ts(V("pen"), V("m7"), float(p), -100000.0, EQ, MUL)
+        for k, (rows, pp) in enumerate((("rowsE", p), ("rowsO", 1 - p))):
+            b = 7 - k
+            gr = [(P(b), blk("Sel", qt), V(win, 1024 * qt + pp, 1024 * qt + 1024, 2)) for qt in range(4)]
+            if win == "win3":
+                gr.append((P(b), V("sh2"), V("irows", pp, 1024, 2)))
+            for i in range(16):
+                gr.append((P(b, i, 512, 16), RowH(i), V("qhi", 32 * k, 32 * k + 32)))
+                gr.append((P(b, i, 512, 16), RowL(i), V("qlo", 32 * k, 32 * k + 32)))
+            cuts = [0, 1, 2, 3, 4] + list(range(8, len(gr), 4)) + [len(gr)]
+            for a, z_ in zip(cuts[:-1], cuts[1:]):
+                mm([gr[a:z_]], a == 0, z_ == len(gr))
+            act(V(rows), P(b))
+
+    ms(V("cum", 0, 8), 0.0)
+    for c in range(8):
+        ms(V("win3", 512 * c, 512 * c + 512), 0.0)
+    for n in ("win1", "win20", "win21", "win22"):
+        for c in range(8):
+            iota(V(n, 512 * c, 512 * c + 512), [[0, 512]], 0, 0)
+    ts(V("qh"), V("qi"), -2048.0, None, ADD)
+    o = P(5, 0, 128)
+    mm([[(o, blk("sq", 0), V("qh", 0, 256, 2)), (o, blk("sq", 1), V("qh", 1, 256, 2))]])
+    ts(V("LX"), o, 2048.0, None, ADD)
+    ts(V("qt1"), o, 2049.0, None, ADD)
+    cp(V("QE"), o)
+    ts(V("qt2"), V("qt1"), 4095, None, AND)
+    cp(V("LE", 0, 128), V("qt2"))
+    cp(V("uq0"), V("q0"))
+    ts(V("q0h"), V("q0"), -2048.0, None, ADD)
+    for k in range(2):
+        cp(IND(V("win3"), V("uq0", 32 * k, 32 * k + 32)), V("irows", 512 * k, 512 * k + 512))
+    mm([[(P(6, 32 * k, 32 * k + 32), blk("sq", 2 * k + e), V("q0h", e, 64, 2)) for e in range(2)] for k in range(2)]
+       + [[(P(6, 64 + 16 * e, 80 + 16 * e), V("WG", 240 * e + 112 - 16 * a, 240 * e + 240 - 16 * a), V("QE", a, 128, 8)) for a in range(8)] for e in range(2)])
+    ts(V("qn"), P(6, 0, 64), 2048.0, None, ADD)
+    ts(V("q1"), P(6, 64, 96), 2048.0, None, ADD)
+    prep(0, "win3")
+
+    PLUS, MINUS = V("blkb", 0, 8), V("blkb", 8, 16)
+
+    def mx(o, sb, bank, alt):
+        tt(o, sb, P(bank) if PSUM_OPS else alt, A.max)
+
+    def stage(bank, x):
+        if PSUM_OPS:
+            mm([[(P(bank), V("idb"), x)]])
+
+    def coords0():
+        ze = lambda s, d=0: V("zt", 16 + 2 * s + d, 16 + 2 * s + d + 1023, 2)
+        for c in range(4):
+            s = 512 * c; t_ = lambda n: V(n, s, s + 512)
+            stage(c % 2, ze(s))
+            mx(t_("tA"), ze(s, -1), c % 2, ze(s)); mx(t_("tB"), ze(s, 1), c % 2, ze(s))
+            mm([[(P(4), V("idb"), ze(s, -1)), (P(4), V("nidb"), ze(s, 1))]])
+            act(t_("tC"), P(4), F.Relu)
+        for c in range(4):
+            s = 512 * c; t_ = lambda n: V(n, s, s + 512)
+            act(t_("Xt"), IND(ZW, V("LX", 32 * c, 32 * c + 32)))
+            act(t_("Et"), IND(ZW, V("LE", 32 * c, 32 * c + 32)))
+            stage(c % 2, ze(s)); stage(2 + c % 2, t_("Et"))
+            mx(t_("tD"), t_("Xt"), c % 2, ze(s)); mx(t_("tF"), t_("Et"), c % 2, ze(s)); mx(t_("tG"), t_("Xt"), 2 + c % 2, t_("Et"))
+            mm([[(P(5, x, 128, 16), l, sg) for l, sg in ((blk("tA", x), PLUS), (blk("tB", x), PLUS), (blk("tC", x), MINUS),
+                 (V("zt", 17 + 256 * x, 272 + 256 * x, 2), MINUS), (blk("tD", x), MINUS), (blk("tF", x), MINUS), (blk("tG", x), PLUS))]
+                for x in range(4 * c, 4 * c + 4)])
+        act(V("sP0"), P(5, 0, 128))
+
+    def shuffle(bank, n, w, halo):
+        mm([[(P(bank, w * v, w * v + w), RS(v, s), V(n, w * s, w * s + w)) for s in range(4)] for v in range(4)]
+           + ([[(P(bank, 4 * w, 4 * w + 2), RS(0, s), V(n, w * s, w * s + 2)) for s in range(4)]] if halo else []))
+
+    def coords(t):
+        es = 1 - t % 2
+        shuffle(0, "rE%d" % (t - 1), 64, True)
+        ts(V("LO", 0, 129), P(0, 1, 258, 2), 2048.0, None, ADD)
+        ts(V("LE", 0, 129), P(0, 0, 258, 2), 2048.0, None, ADD)
+        shuffle(5, "rX%d" % (t - 1), 32, False)
+        ts(V("LX"), P(5, 0, 128), 2048.0, None, ADD)
+        for c in range(4):
+            s = 512 * c; y = 528 * c; t_ = lambda n: V(n, s, s + 512); be, bo = c % 2, 2 + c % 2
+            (cp if c in OV else act)(V("Ot", y, y + 528), IND(ZW, V("LO", 32 * c, 32 * c + 33)))
+            act(V("Et", y, y + 512 + 16 * es), IND(ZW, V("LE", 32 * c, 32 * c + 32 + es)))
+            o0, o1, e = V("Ot", y, y + 512), V("Ot", y + 1, y + 513), V("Et", y + es, y + es + 512)
+            stage(be, e); stage(bo, o0)
+            mx(t_("tA"), o0, be, e); mx(t_("tB"), o1, be, e)
+            if C_ACT:
+                mm([[(P(4), V("idb"), o1), (P(4), V("nidb"), o0)]])
+                act(t_("tC"), P(4), F.Relu)
+            else:
+                mx(t_("tC"), o1, bo, o0)
+            (cp if c in XV else act)(t_("Xt"), IND(ZW, V("LX", 32 * c, 32 * c + 32)))
+            mx(t_("tD"), t_("Xt"), bo, o0); mx(t_("tF"), t_("Xt"), be, e)
+            xs = range(4 * c, 4 * c + 4)
+            mm([[(P(5, 2 * x, 256, 32), l, sg) for l, sg in [(blk("tA", x), PLUS), (blk("tB", x), PLUS), (blk("tC", x), MINUS)]
+                 + ([(V("Ot", y + 128 * (x % 4), y + 128 * (x % 4) + 128), MINUS)] if C_ACT else [])] for x in xs])
+            mm([[(P(5, 2 * x + 1, 256, 32), l, sg) for l, sg in ((blk("tD", x), PLUS), (blk("tF", x), PLUS), (blk("tA", x), MINUS))] for x in xs])
+        act(V("sP%d" % t), P(5, 0, 256), bias=-1600.0)
+
+    def rep(bank, lo, n, rhs, aa=range(8)):
+        return [[(P(bank, lo + n * k, lo + n * k + nel(rhs)), blk("Rh", a), rhs)] for k, a in enumerate(aa)]
+
+    def index(t):
+        p = t % 2; c0 = 2048.0 - p; w = 32 if t == 0 else 64
+        sP, rP, W2 = "sP%d" % t, "rP%d" % t, "win2%d" % t
+        remote("rs", t, rP, w, HOP, sP)
+        part = lambda x, lo, st, hi=w: V(sP if x == r else rP, w * x + lo, w * x + hi, st)
+        order = [r] + others; L = P(1, 0, 32)
+        if t == 0:
+            mm([[(L, V("nidh"), part(x, 0, 1)) for x in order]])
+        else:
+            mm([[(P(0, 32 * a, 32 * a + 32), blk("Rh", a), part(x, 1, 2)) for x in order] for a in range(8)])
+            act(V("wI"), P(0, 0, 256))
+            tt(V("gI"), IND(V("wI"), V("offO")), V("maskE"), MUL)
+            gr = [(L, V("nidh" if p else "nsh"), part(x, 0, 2)) for x in order]
+            if p == 0:
+                for x in order:
+                    for h in range(2):
+                        gr += [(P(1, 16 * h + 1, 16 * h + 16), V("ncar"), part(x, 32 * h, 2, 32 * h + 30)),
+                               (P(1, 16 * h, 16 * h + 1), V("ncar"), part(x, 32 * h + 30, 1, 32 * h + 31))]
+            mm([gr], last=False)
+            mm([[(P(1, b, 32, 4), blk("gI", b), V("blkf")) for b in range(4)]], first=False)
+        tt(V("mv"), L, V("pen"), A.is_lt)
+        tt(V("d1"), V("mv"), V("md"), MUL)
+        tt(V("d2"), V("d1"), V("dump"), ADD)
+        cp(V("ud"), V("d2"))
+        cp(IND(V("win1"), V("ud")), V("ones"))
+        mm(rep(2, 0, 32, V("mv")))
+        act(V("wM"), P(2, 0, 256))
+        act(V("mvL"), IND(V("wM"), cL2))
+        mm([[(P(3, j, j + 1), blk("win1", j), col("e0", 0))] for j in range(32)])
+        if t < 2:
+            dma("sy", [(V("win1", 0, 4096), 16 * u, 1, V("win3"), 16 * u + 8, 1, 0, 0) for u in range(8)], True, 2500)
+        c1, cb = V("cum", 1, 33), V("cum", 0, 32)
+        op("v", ("tensor_tensor_scan", (c1, P(3, 0, 32), V("mv"), 0.0, ADD, A.subtract), {}))
+        if p == 0:
+            act(V("nv"), V("mv"), scale=-1.0)
+        mm([[(P(0, 32 * a, 32 * a + 32), blk(n, a), x) for n, x in [("LT", c1), ("GE", cb)] + ([("Rh", V("nv"))] if p == 0 else [])] for a in range(8)])
+        tt(V("wP"), P(0, 0, 256), V("cPO"), ADD)
+        tt(V("gP"), IND(V("wP"), V("offO")), V("maskE"), MUL)
+        ts(V("uO"), IND(V("wP"), cL2), c0, None, ADD)
+        cp(IND(V(W2), V("uO")), V("rowsO"))
+        if p == 0:
+            act(V("pe"), IND(V("wP"), cL2), bias=-2.0)
+        else:
+            tt(V("nv"), c1, cb, A.subtract)
+            mm(rep(2, 0, 32, V("nv")))
+            act(V("wV"), P(2, 0, 256))
+            act(V("vL"), IND(V("wV"), cL2))
+            tt(V("pe"), IND(V("wP"), cL2), V("vL"), ADD)
+        mm([[(L, Col(i), V("gP", i, 512, 16)) for i in range(16)]])
+        tt(V("s1"), L, V("pe"), A.subtract)
+        tt(V("s2"), V("s1"), V("mvL"), MUL)
+        tt(V("s3"), V("s2"), V("pe"), ADD)
+        ts(V("uE"), V("s3"), c0 + 1, None, ADD)
+        cp(IND(V(W2), V("uE")), V("rowsE"))
+        act(V("ntab", 0, 32), V("s3"), bias=c0 - 2047.0)
+        act(V("ntab", 32, 64), IND(V("wP"), cL2), bias=c0 - 2048.0)
+        E, Xr = "rE%d" % t, "rX%d" % t; w = 64
+        if t < 2:
+            pn = 1 - p
+            mm([[(P(3, 96 * k + cc, 96 * k + 96, 16), V(W2, 256 * cc + pp, 256 * cc + 256, 2), V("sel", 4 * k, 4 * k + 6))]
+                for k, pp in ((0, pn), (1, 1 - pn)) for cc in range(16)])
+            act(V("l1"), P(3, 0, 192), bias=-2048.0)
+            for b in range(2):
+                mm(rep(b, 0, 96, V("l1", 64, 160), range(4 * b, 4 * b + 4)))
+                (cp if b else act)(V("wL", 384 * b, 384 * b + 384), P(b, 0, 384))
+            cp(V(E, w * r, w * r + w), IND(V("wL"), cEO))
+            act(V(Xr, 32 * r, 32 * r + 32), IND(V("wL"), cX))
+            remote("ag", t, E, w, HOP)
+            remote("hx", t, Xr, 32, 1.7 * HOP)
+            mm(rep(7, 0, w, V("l1", 0, 32)) + rep(7, 32, w, V("l1", 160, 192)))
+        else:
+            mm([[(P(3, cc, w, 32), blk(W2, cc), V("sel", 4, 6))] for cc in range(32)])
+            act(V("l1", 0, w), P(3, 0, w), bias=-2048.0)
+            mm(rep(0, 0, w, V("l1", 0, w)))
+            act(V("wL", 0, 512), P(0))
+            cp(V(E, w * r, w * r + w), IND(V("wL", 0, 512), cF))
+            remote("ag", t, E, w, HOP)
+            mm([[(P(2, y, w, 32), V(W2, y, 4096, 32), V("sel", 0, 2))] for y in range(32)])
+            act(V("l1", w, 2 * w), P(2, 0, w), bias=-2048.0)
+            mm(rep(7, 0, w, V("l1", w, 2 * w)))
+        act(V("wQ"), P(7))
+        ts(V("qo"), IND(V("wQ"), cQ if t < 2 else cF), 2048.0, None, ADD)
+        mm([[(P(6, w * qt, w * qt + w), blk("RQ", qt), V("ntab"))] for qt in range(4)])
+        act(V("wN"), P(6, 0, 256))
+        ts(V("n1"), V("qo"), 1, 15, SHR, AND); cp(V("lo1"), V("n1"))
+        ts(V("n2"), V("qo"), 4, 0xC0, SHR, AND)
+        ts(V("n3"), V("qo"), 5, 31, SHR, AND)
+        ts(V("n4"), V("qo"), 1, None, AND)
+        ts(V("n5"), V("n4"), float(p), 32.0, A.not_equal, MUL)
+        tt(V("n2"), V("n2"), V("n3"), ADD); tt(V("n2"), V("n2"), V("n5"), ADD); cp(V("offN"), V("n2"))
+        for k in range(2):
+            m_ = V("mask1", 512 * k, 512 * k + 512)
+            masks(7 - k, V("lo1", 32 * k, 32 * k + 32), m_)
+            tt(V("gQ", 512 * k, 512 * k + 512), IND(V("wN"), V("offN", 32 * k, 32 * k + 32)), m_, MUL)
+        if t < 2:
+            mm([[(P(6, 0, w), Col(i), V("gQ", i, 1024, 16)) for i in range(16)]] + [[(P(6, 64 + j, 96, 4), blk("gQ", j), V("blkh"))] for j in range(4)])
+            ts(V("qn"), P(6, 0, w), 2048.0, None, ADD)
+            ts(V("q1"), P(6, 64, 96), 2048.0, None, ADD)
+            prep(1 - p, W2)
+        else:
+            mm([[(P(6, j, w, 8), blk("gQ", j), V("blkh"))] for j in range(8)])
+            cp(V(Xr, w * r, w * r + w), P(6, 0, w))
+            remote("hx", t, Xr, w, 1.7 * HOP)
+            ts(V("qf"), V(Xr), 2048.0, None, ADD)
+            for e, q in enumerate(("sy", "s")):
+                dma(q, [(V("qf", 32 * j, 32 * j + 32), 0, 128, "yq", j, 1, 0, 4096) for j in range(e, 8, 2)], False, 2500)
+
+    coords0(); index(0); coords(1); index(1); coords(2); index(2)
+    shuffle(0, "rE2", 64, False)
+    ts(V("LY"), P(0, 0, 256), 2048.0, None, ADD)
+    for c in range(8):
+        (cp if c % 2 else act)(V("yt", 512 * c, 512 * c + 512), IND(ZW, V("LY", 32 * c, 32 * c + 32)))
+        if c % 2:
+            dma("sy", [(V("yt", 512 * c - 512, 512 * c + 512), 0, 128, "yz", 0, 128, 512 * c - 512, 1024)], False, 2800)
+    return ops
+
+
+def schedule(ops):
+    n = len(ops); deps = [set() for _ in range(n)]; acc = {}; bank = {}
+    home = {(b, c): o for (b, o, w) in AL.values() for c in range(o // 16, (o + w + 15) // 16)}
+    for j, (eng, kind, _, rd, wr) in enumerate(o[:5] for o in ops):
+        for nm in set(x[0] for x in rd + wr if x[0] not in SB):
+            before, now = bank.get(nm, ([], []))
+            if now and ops[now[0]][0] == eng:
+                deps[j].update(before + (now[-1:] if eng == "t" else [])); bank[nm] = (before, now + [j])
+            else:
+                deps[j].update(now); bank[nm] = (now, [j])
+        for lst, isw in ((rd, False), (wr, True)):
+            for (nm, lo, hi) in lst:
+                if nm in SB:
+                    key = (nm, home[(nm, lo // 16)]); old = acc.get(key, [])
+                    deps[j].update(i for (i, l2, h2, w2) in old if (isw or w2) and lo < h2 and l2 < hi and i != j)
+                    acc[key] = [x for x in old if not (isw and lo <= x[1] and x[2] <= hi)] + [(j, lo, hi, isw)]
+    succ = [[] for _ in range(n)]
+    for j in range(n):
+        for i in deps[j]:
+            succ[i].append(j)
+    hold = lambda j: ops[j][5] if ops[j][1] == "c" else (100.0 * len(ops[j][2][1]) if ops[j][1] == "d" else 300.0)
+    rank = [0.0] * n; key = [0.0] * n; u = np.random.default_rng(SEED).random(n)
+    for j in range(n - 1, -1, -1):
+        rank[j] = ops[j][5] + max([rank[k] + LAT for k in succ[j]] + [0.0])
+        key[j] = max([rank[j] + ops[j][6] + NOISE * float(u[j])] + [key[k] + 1.0 for k in succ[j]])
+    start = [0.0] * n; fin = [0.0] * n; busy = {}
+    for j in sorted(range(n), key=lambda j: (-key[j], j)):
+        t0 = max([fin[i] + (0.0 if ops[i][0] == "t" and ops[j][0] == "t" else LAT) for i in deps[j]] + [0.0])
+        b = busy.setdefault(ops[j][0], [])
+        for (s, e) in b:
+            if t0 + hold(j) <= s:
+                break
+            t0 = max(t0, e)
+        start[j] = t0; fin[j] = t0 + ops[j][5]
+        b.append((t0, t0 + hold(j))); b.sort()
+    return deps, sorted(range(n), key=lambda j: (start[j], j)), start, fin
+
+
+def helper_of(T, topo, c):
+    ok = [x for x in topo.cores_of(c) if T.rank_of(x) is None and all(topo.may_write(x, d) for d in T.cores if d != c)]
+    return sorted(ok, key=lambda x: topo.die(x) != topo.die(c))[0]
+
+
+def dst_id(topo, c):
+    rid, pid, _ = topo.addr(c)
+    return DstId(rid=rid, pnc=pid)
+
+
+def mask_to_others(T, topo, src, r):
+    m = -1
+    for x in range(4):
+        if x != r:
+            m &= topo.mask(src, T.cores[x])
+    return m
+
+
+def bits(m):
+    return bin(m).count("1")
+
+
+def rs_masks(T, topo, r):
+    c = T.cores[r]; oth = [x for x in range(4) if x != r]
+    m = mask_to_others(T, topo, c, r); e = [k for k in topo.engines(c, T.cores[oth[0]]) if m >> k & 1]
+    direct = lambda x: topo.mates(topo.chip(c), topo.chip(T.cores[x])) or topo.same_plane(topo.chip(c), topo.chip(T.cores[x]))
+    q = len(e) // 4
+    return {x: sum(1 << k for k in part) for x, part in zip(sorted(oth, key=direct), (e[:2 * q], e[2 * q:3 * q], e[3 * q:]))}
+
+
+def rank_program(g, core, T, topo):
+    S = T.sem
+
+    def ap(x):
+        if not isv(x):
+            return x
+        if x[0] == "I":
+            return ap(x[1]).indirect(ap(x[2]))
+        return T[x[1]][:, x[2]:x[3]] if x[4] == 1 else T[x[1]][:, x[2]:x[3]:x[4]]
+
+    def spread(src, dst, r, m, sem):
+        oth = [x for x in range(4) if x != r]
+        g.remote_dma_fused([RemoteDMATransfer(dst_ids=[dst_id(topo, T.cores[x]) for x in oth], dma_engine_mask=m, remote_sem=sem,
+                                              srcs=[ap(src)], dsts=[ap(dst) for x in oth])], local_sem=S.loc)
+
+    for r in range(4):
+        if core == helper_of(T, topo, T.cores[r]):
+            m = mask_to_others(T, topo, core, r)
+            for t in range(3):
+                w = AL["hX%d" % t][2]
+                g.wait_ge(S["hi%d" % t], bits(topo.mask(T.cores[r], core)))
+                spread(V("hX%d" % t), V("rX%d" % t, w * r, w * r + w), r, m, S["hx%d" % t])
+            g.wait_ge(S.loc, 3 * bits(m))
+            return
+    r = T.rank_of(core)
+    if r is None:
+        return
+    ops = plan(r)
+    deps, order = schedule(ops)[:2]
+    oth = [x for x in range(4) if x != r]
+    QU = {"v": g.vector, "t": g.tensor, "s": g.scalar, "gp": g, "sy": g.sync}
+    needed = set(i for j in range(len(ops)) for i in deps[j] if not (ops[i][0] == "t" and ops[j][0] == "t"))
+    sig = {}; cnt = {"v": 0, "t": 0, "s": 0, "gp": 0}; nd = 0
+    for j in order:
+        eng, kind, pay = ops[j][:3]
+        if kind == "c":
+            if j in needed:
+                cnt[eng] += 1; sig[j] = (eng, cnt[eng])
+        elif kind == "d":
+            sig[j] = ("d%d" % nd, 16 * len(pay[1])); nd += 1
+        else:
+            snd = lambda x: T.cores[x] if pay[0] == "ag" else helper_of(T, topo, T.cores[x])
+            sig[j] = ("%s%d" % pay[:2], sum(bits(rs_masks(T, topo, x)[r] if pay[0] == "rs" else mask_to_others(T, topo, snd(x), x)) for x in oth))
+
+    def call(q, m, a, kw):
+        f = {"matmul": lambda: q.matmul, "tensor_scalar": lambda: q.tensor_scalar, "tensor_tensor": lambda: q.tensor_tensor,
+             "tensor_copy": lambda: q.tensor_copy, "memset": lambda: q.memset, "activation": lambda: q.activation,
+             "iota": lambda: q.iota, "tensor_tensor_scan": lambda: q.tensor_tensor_scan}[m]()
+        return f(*[ap(x) for x in a], **{k: ap(x) for k, x in kw.items()})
+
+    waited = {}; loc = 0
+    for j in order:
+        eng, kind, pay = ops[j][:3]; q = QU[eng]; want = {}
+        for i in deps[j]:
+            if not (ops[i][0] == "t" and eng == "t"):
+                nm, c = sig[i]; want[nm] = max(want.get(nm, 0), c)
+        for nm, c in sorted(want.items()):
+            if waited.get((eng, nm), 0) < c:
+                q.wait_ge(S[nm], c); waited[(eng, nm)] = c
+        if kind == "c":
+            for m, a, kw in pay:
+                ins = call(q, m, a, kw)
+            if j in sig:
+                ins.then_inc(S[eng], 1)
+        elif kind == "d":
+            for v, p0, pn, tn, r0, rn, c0, cn in pay[1]:
+                sb, hb = T[v[1]][p0:p0 + pn, v[2]:v[3]], (T[tn[1]][r0:r0 + rn, tn[2]:tn[3]] if isv(tn) else T[tn][r0:r0 + rn, c0:c0 + cn])
+                (q.dma_start(sb, hb) if pay[0] else q.dma_start(hb, sb)).then_inc(S[sig[j][0]], 16)
+        else:
+            k, t, srcs, dst = pay; sem = S[sig[j][0]]
+            if k == "rs":
+                mk = rs_masks(T, topo, r)
+                g.remote_dma_fused([RemoteDMATransfer(dst_ids=[dst_id(topo, T.cores[x])], dma_engine_mask=mk[x], remote_sem=sem, src=ap(a), dst=ap(dst))
+                                    for x, a in zip(oth, srcs)], local_sem=S.loc)
+                loc += sum(bits(v) for v in mk.values())
+            elif k == "ag":
+                m = mask_to_others(T, topo, core, r); spread(srcs[0], dst, r, m, sem); loc += bits(m)
+            else:
+                hc = helper_of(T, topo, core); rid, pid, _ = topo.addr(hc); m = topo.mask(core, hc)
+                g.remote_dma(ap(V("hX%d" % t)), ap(srcs[0]), S["hi%d" % t], S.loc, pid, rid, m)
+                loc += bits(m)
+    done = {}
+    for nm, c in sig.values():
+        done[nm] = max(done.get(nm, 0), c)
+    for nm, c in sorted(done.items()):
+        g.wait_ge(S[nm], c)
+    g.wait_ge(S.loc, loc)

@@ -1,27 +1,25 @@
-import numpy as np
 from concourse.mybir import AluOpType as A, ActivationFunctionType as F
 from concourse.bass import DstId, RemoteDMATransfer
 
-C_ACT = False
-PSUM_OPS = True
-OV = ()
-XV = ()
+PSUM_OPS = False
+OV = (2,)
+XV = (0, 2)
+BV = (0, 1, 3)
+W3 = 2
 PE_NS = 0.5
-HOP = 2600.0
-LAT = 90.0
-TT_SB = 2.0
+HOP = 3000.0
+LAT = 100.0
+TT_SB = 1.0
 B1 = 10000.0
-SEED = 0
-NOISE = 0.0
 
-H, Q, WD, CW, LW = 2, 4, 512, 32, 128
 BF, HF, FP, I32, U16 = "bfloat16", "float16", "float32", "int32", "uint16"
 BUF = {
-    "zt": (4112, BF), "yt": (4096, BF), "Et": (2112, BF), "Ot": (2112, BF), "Xt": (2048, BF),
+    "zt": (4112, BF), "yt": (4096, BF), "Et": (2176, BF), "Ot": (2176, BF), "zero": (256, HF), "Xt": (2048, BF),
     "tA": (2048, BF), "tB": (2048, BF), "tC": (2048, BF), "tD": (2048, BF), "tF": (2048, BF), "tG": (2048, BF),
     "LE": (130, U16), "LO": (130, U16), "LX": (128, U16), "LY": (256, U16),
     "win1": (4608, BF), "win20": (4096, BF), "win21": (4096, BF), "win22": (4096, BF), "win3": (4096, BF), "rowsE": (512, BF), "rowsO": (512, BF),
-    "sP0": (128, HF), "sP1": (256, HF), "sP2": (256, HF), "rP0": (128, HF), "rP1": (256, HF), "rP2": (256, HF),
+    "sP0": (128, HF), "sP1": (128, HF), "sP2": (128, HF), "rP0": (128, HF), "rP1": (128, HF), "rP2": (128, HF),
+    "sR1": (128, HF), "sR2": (128, HF), "rR1": (128, HF), "rR2": (128, HF),
     "rE0": (256, HF), "rE1": (256, HF), "rE2": (256, HF), "rX0": (128, HF), "rX1": (128, HF), "rX2": (256, HF),
     "hX0": (32, HF), "hX1": (32, HF), "hX2": (64, HF), "qf": (256, FP),
     "wI": (256, FP), "wP": (256, FP), "wM": (256, BF), "wV": (256, BF), "wL": (768, FP), "wQ": (512, FP), "wN": (256, FP),
@@ -47,7 +45,7 @@ for _k, (_w, _d) in BUF.items():
 SCRATCH = {k: ("sbuf", [128, w], d) for k, (w, d) in SB.items()}
 for _b in range(8):
     SCRATCH["p%d" % _b] = ("psum", [128, 512], "float32")
-SEMAPHORES = ["v", "t", "s", "gp", "loc"] + ["d%d" % k for k in range(24)] + [k + str(t) for k in ("rs", "ag", "hx", "hi") for t in range(3)]
+SEMAPHORES = ["v", "t", "s", "gp", "loc"] + ["d%d" % k for k in range(24)] + [k + str(t) for k in ("rs", "rr", "ag", "hx", "hi") for t in range(3)]
 
 
 def V(n, lo=0, hi=None, st=1):
@@ -240,6 +238,7 @@ def plan(r):
         mm([[(P(7), blk("dg", 0), V("ia", 512 * k, 512 * k + 512)), (P(7), blk("dg", 1), V("ib", 512 * k, 512 * k + 512))]])
         act(V("irows", 512 * k, 512 * k + 512), P(7), bias=pf(25))
     ms(V("ones"), 1.0)
+    ms(V("zero"), 0.0)
 
     def masks(bank, lo, out):
         mm([[(P(bank, i, 512, 16), Brd(i), lo)] for i in range(16)])
@@ -274,7 +273,10 @@ def plan(r):
 
     ms(V("cum", 0, 8), 0.0)
     for c in range(8):
-        ms(V("win3", 512 * c, 512 * c + 512), 0.0)
+        if c < W3:
+            act(V("win3", 512 * c, 512 * c + 512), V("ones"), scale=0.0)
+        else:
+            ms(V("win3", 512 * c, 512 * c + 512), 0.0)
     for n in ("win1", "win20", "win21", "win22"):
         for c in range(8):
             iota(V(n, 512 * c, 512 * c + 512), [[0, 512]], 0, 0)
@@ -323,6 +325,7 @@ def plan(r):
                  (V("zt", 17 + 256 * x, 272 + 256 * x, 2), MINUS), (blk("tD", x), MINUS), (blk("tF", x), MINUS), (blk("tG", x), PLUS))]
                 for x in range(4 * c, 4 * c + 4)])
         act(V("sP0"), P(5, 0, 128))
+        remote("rs", 0, "rP0", 32, HOP, "sP0")
 
     def shuffle(bank, n, w, halo):
         mm([[(P(bank, w * v, w * v + w), RS(v, s), V(n, w * s, w * s + w)) for s in range(4)] for v in range(4)]
@@ -341,43 +344,54 @@ def plan(r):
             act(V("Et", y, y + 512 + 16 * es), IND(ZW, V("LE", 32 * c, 32 * c + 32 + es)))
             o0, o1, e = V("Ot", y, y + 512), V("Ot", y + 1, y + 513), V("Et", y + es, y + es + 512)
             stage(be, e); stage(bo, o0)
-            mx(t_("tA"), o0, be, e); mx(t_("tB"), o1, be, e)
-            if C_ACT:
-                mm([[(P(4), V("idb"), o1), (P(4), V("nidb"), o0)]])
-                act(t_("tC"), P(4), F.Relu)
-            else:
-                mx(t_("tC"), o1, bo, o0)
+            mx(t_("tA"), o0, be, e)
+            if c in BV:
+                mx(t_("tB"), o1, be, e)
             (cp if c in XV else act)(t_("Xt"), IND(ZW, V("LX", 32 * c, 32 * c + 32)))
             mx(t_("tD"), t_("Xt"), bo, o0); mx(t_("tF"), t_("Xt"), be, e)
-            xs = range(4 * c, 4 * c + 4)
-            mm([[(P(5, 2 * x, 256, 32), l, sg) for l, sg in [(blk("tA", x), PLUS), (blk("tB", x), PLUS), (blk("tC", x), MINUS)]
-                 + ([(V("Ot", y + 128 * (x % 4), y + 128 * (x % 4) + 128), MINUS)] if C_ACT else [])] for x in xs])
-            mm([[(P(5, 2 * x + 1, 256, 32), l, sg) for l, sg in ((blk("tD", x), PLUS), (blk("tF", x), PLUS), (blk("tA", x), MINUS))] for x in xs])
-        act(V("sP%d" % t), P(5, 0, 256), bias=-1600.0)
+            mm([[(P(5, x, 128, 16), l, sg) for l, sg in ((blk("tD", x), PLUS), (blk("tF", x), PLUS), (blk("tA", x), MINUS))] for x in range(4 * c, 4 * c + 4)])
+        act(V("sP%d" % t), P(5, 0, 128), bias=-1600.0)
+        remote("rs", t, "rP%d" % t, 32, HOP, "sP%d" % t)
+        for c in range(4):
+            s = 512 * c; y = 528 * c; t_ = lambda n: V(n, s, s + 512); bd = 2 + c % 2
+            o0, o1, e = V("Ot", y, y + 512), V("Ot", y + 1, y + 513), V("Et", y + es, y + es + 512)
+            if c not in BV:
+                stage(c % 2, e); mx(t_("tB"), o1, c % 2, e)
+            mm([[(P(bd), V("idb"), o1), (P(bd), V("nidb"), o0)]])
+            act(t_("tC"), P(bd), F.Relu)
+            mm([[(P(4, x, 128, 16), l, sg) for l, sg in ((blk("tA", x), PLUS), (blk("tB", x), PLUS), (blk("tC", x), MINUS),
+                 (V("Ot", 128 * x + 16 * c, 128 * x + 16 * c + 128), MINUS))] for x in range(4 * c, 4 * c + 4)])
+        act(V("sR%d" % t), P(4, 0, 128), bias=-1600.0)
+        remote("rr", t, "rR%d" % t, 32, HOP, "sR%d" % t)
 
     def rep(bank, lo, n, rhs, aa=range(8)):
         return [[(P(bank, lo + n * k, lo + n * k + nel(rhs)), blk("Rh", a), rhs)] for k, a in enumerate(aa)]
 
     def index(t):
-        p = t % 2; c0 = 2048.0 - p; w = 32 if t == 0 else 64
+        p = t % 2; c0 = 2048.0 - p
         sP, rP, W2 = "sP%d" % t, "rP%d" % t, "win2%d" % t
-        remote("rs", t, rP, w, HOP, sP)
-        part = lambda x, lo, st, hi=w: V(sP if x == r else rP, w * x + lo, w * x + hi, st)
+        part = lambda x: V(sP if x == r else rP, 32 * x, 32 * x + 32)
+        rem = lambda x, lo=0, hi=32: V(("sR%d" if x == r else "rR%d") % t, 32 * x + lo, 32 * x + hi)
         order = [r] + others; L = P(1, 0, 32)
         if t == 0:
-            mm([[(L, V("nidh"), part(x, 0, 1)) for x in order]])
+            mm([[(L, V("nidh"), part(x)) for x in order]])
         else:
-            mm([[(P(0, 32 * a, 32 * a + 32), blk("Rh", a), part(x, 1, 2)) for x in order] for a in range(8)])
-            act(V("wI"), P(0, 0, 256))
+            for b in range(2):
+                wa = lambda a: P(2 * b, 32 * (a % 4), 32 * (a % 4) + 32)
+                mm([[(P(2 * b, 0, 128), V("nidh"), V("zero", 0, 128))] + [(wa(a), blk("Rh", a), part(r)) for a in range(4 * b, 4 * b + 4)]], last=False)
+            for b in range(2):
+                wa = lambda a: P(2 * b, 32 * (a % 4), 32 * (a % 4) + 32)
+                mm([[(wa(a), blk("Rh", a), part(x)) for a in range(4 * b, 4 * b + 4) for x in others]], first=False)
+                (cp if b else act)(V("wI", 128 * b, 128 * b + 128), P(2 * b, 0, 128))
             tt(V("gI"), IND(V("wI"), V("offO")), V("maskE"), MUL)
-            gr = [(L, V("nidh" if p else "nsh"), part(x, 0, 2)) for x in order]
+            gr = [(L, V("nidh" if p else "nsh"), rem(x)) for x in order]
             if p == 0:
                 for x in order:
                     for h in range(2):
-                        gr += [(P(1, 16 * h + 1, 16 * h + 16), V("ncar"), part(x, 32 * h, 2, 32 * h + 30)),
-                               (P(1, 16 * h, 16 * h + 1), V("ncar"), part(x, 32 * h + 30, 1, 32 * h + 31))]
-            mm([gr], last=False)
-            mm([[(P(1, b, 32, 4), blk("gI", b), V("blkf")) for b in range(4)]], first=False)
+                        gr += [(P(1, 16 * h + 1, 16 * h + 16), V("ncar"), rem(x, 16 * h, 16 * h + 15)),
+                               (P(1, 16 * h, 16 * h + 1), V("ncar"), rem(x, 16 * h + 15, 16 * h + 16))]
+            mm([[(L, V("nidh"), V("zero", 0, 32))] + [(P(1, b, 32, 4), blk("gI", b), V("blkf")) for b in range(4)]], last=False)
+            mm([gr], first=False)
         tt(V("mv"), L, V("pen"), A.is_lt)
         tt(V("d1"), V("mv"), V("md"), MUL)
         tt(V("d2"), V("d1"), V("dump"), ADD)
@@ -393,7 +407,10 @@ def plan(r):
         op("v", ("tensor_tensor_scan", (c1, P(3, 0, 32), V("mv"), 0.0, ADD, A.subtract), {}))
         if p == 0:
             act(V("nv"), V("mv"), scale=-1.0)
-        mm([[(P(0, 32 * a, 32 * a + 32), blk(n, a), x) for n, x in [("LT", c1), ("GE", cb)] + ([("Rh", V("nv"))] if p == 0 else [])] for a in range(8)])
+            mm([[(P(0, 0, 256), V("nidh"), V("zero"))] + [(P(0, 32 * a, 32 * a + 32), blk("Rh", a), V("nv")) for a in range(8)]], last=False)
+            mm([[(P(0, 32 * a, 32 * a + 32), blk(n, a), x) for a in range(8) for n, x in (("LT", c1), ("GE", cb))]], first=False)
+        else:
+            mm([[(P(0, 32 * a, 32 * a + 32), blk(n, a), x) for n, x in (("LT", c1), ("GE", cb))] for a in range(8)])
         tt(V("wP"), P(0, 0, 256), V("cPO"), ADD)
         tt(V("gP"), IND(V("wP"), V("offO")), V("maskE"), MUL)
         ts(V("uO"), IND(V("wP"), cL2), c0, None, ADD)
@@ -470,8 +487,10 @@ def plan(r):
     ts(V("LY"), P(0, 0, 256), 2048.0, None, ADD)
     for c in range(8):
         (cp if c % 2 else act)(V("yt", 512 * c, 512 * c + 512), IND(ZW, V("LY", 32 * c, 32 * c + 32)))
-        if c % 2:
-            dma("sy", [(V("yt", 512 * c - 512, 512 * c + 512), 0, 128, "yz", 0, 128, 512 * c - 512, 1024)], False, 2800)
+        if c % 2 and c < 6:
+            dma("sy", [(V("yt", 512 * c - 512, 512 * c + 512), 0, 128, "yz", 0, 128, 512 * c - 512, 1024)], False, 3200)
+        elif c >= 6:
+            dma("sy", [(V("yt", 512 * c, 512 * c + 512), 0, 128, "yz", 0, 128, 512 * c, 512)], False, 2900)
     return ops
 
 
@@ -496,10 +515,10 @@ def schedule(ops):
         for i in deps[j]:
             succ[i].append(j)
     hold = lambda j: ops[j][5] if ops[j][1] == "c" else (100.0 * len(ops[j][2][1]) if ops[j][1] == "d" else 300.0)
-    rank = [0.0] * n; key = [0.0] * n; u = np.random.default_rng(SEED).random(n)
+    rank = [0.0] * n; key = [0.0] * n
     for j in range(n - 1, -1, -1):
         rank[j] = ops[j][5] + max([rank[k] + LAT for k in succ[j]] + [0.0])
-        key[j] = max([rank[j] + ops[j][6] + NOISE * float(u[j])] + [key[k] + 1.0 for k in succ[j]])
+        key[j] = max([rank[j] + ops[j][6]] + [key[k] + 1.0 for k in succ[j]])
     start = [0.0] * n; fin = [0.0] * n; busy = {}
     for j in sorted(range(n), key=lambda j: (-key[j], j)):
         t0 = max([fin[i] + (0.0 if ops[i][0] == "t" and ops[j][0] == "t" else LAT) for i in deps[j]] + [0.0])
@@ -585,7 +604,7 @@ def rank_program(g, core, T, topo):
             sig[j] = ("d%d" % nd, 16 * len(pay[1])); nd += 1
         else:
             snd = lambda x: T.cores[x] if pay[0] == "ag" else helper_of(T, topo, T.cores[x])
-            sig[j] = ("%s%d" % pay[:2], sum(bits(rs_masks(T, topo, x)[r] if pay[0] == "rs" else mask_to_others(T, topo, snd(x), x)) for x in oth))
+            sig[j] = ("%s%d" % pay[:2], sum(bits(rs_masks(T, topo, x)[r] if pay[0] in ("rs", "rr") else mask_to_others(T, topo, snd(x), x)) for x in oth))
 
     def call(q, m, a, kw):
         f = {"matmul": lambda: q.matmul, "tensor_scalar": lambda: q.tensor_scalar, "tensor_tensor": lambda: q.tensor_tensor,
@@ -613,7 +632,7 @@ def rank_program(g, core, T, topo):
                 (q.dma_start(sb, hb) if pay[0] else q.dma_start(hb, sb)).then_inc(S[sig[j][0]], 16)
         else:
             k, t, srcs, dst = pay; sem = S[sig[j][0]]
-            if k == "rs":
+            if k in ("rs", "rr"):
                 mk = rs_masks(T, topo, r)
                 g.remote_dma_fused([RemoteDMATransfer(dst_ids=[dst_id(topo, T.cores[x])], dma_engine_mask=mk[x], remote_sem=sem, src=ap(a), dst=ap(dst))
                                     for x, a in zip(oth, srcs)], local_sem=S.loc)

@@ -1,21 +1,20 @@
 from concourse.mybir import AluOpType as A, ActivationFunctionType as F
 from concourse.bass import DstId, RemoteDMATransfer
 
-PSUM_OPS = False
 OV = (2,)
-XV = (0, 2)
-BV = (0, 1, 3)
-W3 = 2
+XV = (0,)
+BV = (0, 3)
+B0 = (1, 2, 3)
+G0 = (3,)
 PE_NS = 0.5
-HOP = 3000.0
+HOP = 3200.0
 LAT = 100.0
-TT_SB = 1.0
-B1 = 10000.0
 
 BF, HF, FP, I32, U16 = "bfloat16", "float16", "float32", "int32", "uint16"
 BUF = {
-    "zt": (4112, BF), "yt": (4096, BF), "Et": (2176, BF), "Ot": (2176, BF), "zero": (256, HF), "Xt": (2048, BF),
-    "tA": (2048, BF), "tB": (2048, BF), "tC": (2048, BF), "tD": (2048, BF), "tF": (2048, BF), "tG": (2048, BF),
+    "zt": (4112, BF), "yt": (4096, BF), "Et": (2176, BF), "Ot": (2176, BF), "zero": (256, HF), "zb": (1024, BF), "Xt": (2048, BF),
+    "hA": (16, BF), "tA": (2048, BF), "hB": (16, BF), "tB": (2048, BF), "hC": (16, BF), "tC": (2048, BF),
+    "tD": (2048, BF), "tF": (2048, BF), "tG": (2048, BF),
     "LE": (130, U16), "LO": (130, U16), "LX": (128, U16), "LY": (256, U16),
     "win1": (4608, BF), "win20": (4096, BF), "win21": (4096, BF), "win22": (4096, BF), "win3": (4096, BF), "rowsE": (512, BF), "rowsO": (512, BF),
     "sP0": (128, HF), "sP1": (128, HF), "sP2": (128, HF), "rP0": (128, HF), "rP1": (128, HF), "rP2": (128, HF),
@@ -33,7 +32,7 @@ BUF = {
     "qi": (256, I32), "qh": (256, HF), "qt1": (128, I32), "qt2": (128, I32), "QE": (128, HF), "q0": (64, I32), "uq0": (64, U16), "q0h": (64, HF),
     "ones": (512, BF), "irows": (1024, BF), "ia": (1024, BF), "ib": (1024, BF),
     "X": (384, FP), "val": (1024, BF), "pi": (16, I32), "pf": (32, FP), "Mi": (16, FP), "Mq": (8, FP), "Y": (32, FP), "X2": (128, FP),
-    "X3": (128, FP), "idb": (128, BF), "nidb": (128, BF), "nidh": (128, HF), "nsh": (128, HF), "ncar": (128, HF), "sh2": (128, BF), "dg": (256, BF),
+    "X3": (128, FP), "idb": (128, BF), "nidb": (128, BF), "nidh": (128, HF), "sh2": (128, BF), "dg": (256, BF),
     "W": (144, HF), "base3": (384, BF), "c3": (6144, BF), "blkb": (16, BF), "blkh": (8, HF), "blkf": (8, FP), "e0": (8, BF), "LT": (1024, HF),
     "GE": (1024, HF), "Rh": (1024, HF), "RQ": (512, HF), "Sel": (512, BF), "sel": (16, BF), "WG": (480, HF), "RS": (896, HF), "sq": (512, HF),
     "v2": (128, FP), "cl": (16, U16), "cPO": (256, FP), "dump": (32, FP), "cmd": (32, FP),
@@ -42,6 +41,7 @@ AL, SB = {}, {}
 for _k, (_w, _d) in BUF.items():
     _o = SB.get("pool" + _d, (0, _d))[0]
     AL[_k] = ("pool" + _d, _o, _w); SB["pool" + _d] = (_o + (_w + 15) // 16 * 16, _d)
+STARTS = set(AL[n][:2] for n in ("tA", "tB", "tC"))
 SCRATCH = {k: ("sbuf", [128, w], d) for k, (w, d) in SB.items()}
 for _b in range(8):
     SCRATCH["p%d" % _b] = ("psum", [128, 512], "float32")
@@ -86,7 +86,7 @@ def cost(eng, ins):
     big = [x for x in vs if nel(x) == n]
     c = 0.5 if all(two(x) for x in big) else 1.0
     if m == "tensor_tensor" and a[1][1] in SB and a[2][1] in SB:
-        c = TT_SB if c == 0.5 else 2.0
+        c = 2 * c
     return 1.04 * max(64, c * n)
 
 
@@ -94,6 +94,8 @@ def plan(r):
     ops = []; boost = [0.0]
 
     def spans(x):
+        if x[0] == "V" and (x[1], x[2] + 1) in STARTS:
+            return [(x[1], x[2], x[2] + 1), (x[1], x[2] + 1, x[3])] if x[3] > x[2] + 1 else [(x[1], x[2], x[3])]
         return spans(x[1]) + spans(x[2]) if x[0] == "I" else [(x[1], x[2], x[3])]
 
     def op(eng, *ins):
@@ -133,15 +135,16 @@ def plan(r):
                 ins.append(("matmul", (o, l, x, first and k == 0, last and k == len(gr) - 1), {}))
         op("t", *ins)
 
-    def dma(eng, items, load, ns):
+    def dma(eng, items, load, ns, after=None):
         sp = sorted(set(s for x in items for s in spans(x[0])))
-        rd = sorted(set(s for x in items if isv(x[3]) for s in spans(x[3])))
+        rd = sorted(set(s for x in items if isv(x[3]) for s in spans(x[3]))) + (spans(after) if after else [])
         ops.append((eng, "d", (load, items), rd if load else sp, sp if load else [], ns, 0.0))
 
     def remote(kind, t, n, w, ns, src=None):
         sl = lambda b, x: V(b, w * x, w * x + w)
         srcs = [sl(src, x) for x in others] if src else [sl(n, r)]
-        ops.append(("gp", "r", (kind, t, srcs, sl(n, r)), [s for x in srcs for s in spans(x)], [s for x in others for s in spans(sl(n, x))], ns, 0.0))
+        ops.append(("gp", "r", (kind, t, srcs, sl(n, r)), [s for x in srcs for s in spans(x)], [s for x in others for s in spans(sl(n, x))], ns,
+                    4000.0 if kind == "ag" and t < 2 else 0.0))
 
     P = lambda b, lo=0, hi=512, st=1: ("V", "p%d" % b, lo, hi, st)
     col = lambda n, j: V(n, j, j + 1)
@@ -176,8 +179,6 @@ def plan(r):
     for k in range(4):
         tt(blk("sq", k), blk("sq", k), V("base3", 256, 384), MUL)
     ts(V("nidh"), X(0, 128), pf(0), -1.0, EQ, MUL)
-    ts(V("nsh"), X(-1, 127), pf(0), -1.0, EQ, MUL)
-    ts(V("ncar"), X(127, 255), pf(0), -1.0, EQ, MUL)
     ts(V("sh2"), X(2, 130), pf(0), None, EQ)
     ts(V("blkh"), X(0, 8), pf(2), None, EQ)
     ts(V("blkf"), X(0, 8), pf(2), None, EQ)
@@ -190,15 +191,14 @@ def plan(r):
     lin(21, 2, 4, 0.0); lin(22, 8, 32, pf(21)); lin(23, 7, 96, pf(22))
     lin(24, 3, 16, 0.0); ts(pf(25), pf(4), 16.0, col("Mi", 2), MUL, MUL); lin(26, 1, 2, -2047.0); lin(27, 1, 1, 112.0)
     ts(V("W", 0, 143), X(-15, 128), pf(12), None, EQ)
-    ts(V("base3", 0, 128), X(-4, 124), pf(12), None, EQ)
-    ts(V("base3", 128, 256), X(-5, 123), pf(12), None, EQ)
-    for i in range(16):
-        boost[0] = B1 - 300.0 * i
-        act(V("c3", 384 * i, 384 * i + 384), V("base3"), scale=col("Mi", i))
+    ms(V("ones"), 1.0)
+    for k, (step, row) in enumerate(((0, 0), (1000, 4), (1000, 5))):
+        for c in range(4):
+            boost[0] = -1200.0 * (4 * k + c)
+            op("gp", ("affine_select", (V("c3", 2048 * k + 512 * c, 2048 * k + 512 * c + 512), V("ones"), [[-1, 4], [-16, 8], [step, 16]],
+                                        EQ, 0.0, -4 * c - step * row, 1), {}))
     boost[0] = 0.0
-    RowH = lambda i: V("c3", 384 * i, 384 * i + 128)
-    RowL = lambda i: V("c3", 384 * i + 128, 384 * i + 256)
-    Brd = lambda i: V("c3", 384 * i + 256, 384 * i + 384)
+    Brd, RowH, RowL = [lambda i, k=k: blk("c3", 16 * k + i) for k in range(3)]
     Col = lambda i: V("W", 15 - i, 143 - i)
     iota(V("ia"), [[1, 16], [0, 64]], 0, 0)
     iota(V("ib"), [[0, 16], [1, 64]], 0, 0)
@@ -237,8 +237,8 @@ def plan(r):
     for k in range(2):
         mm([[(P(7), blk("dg", 0), V("ia", 512 * k, 512 * k + 512)), (P(7), blk("dg", 1), V("ib", 512 * k, 512 * k + 512))]])
         act(V("irows", 512 * k, 512 * k + 512), P(7), bias=pf(25))
-    ms(V("ones"), 1.0)
     ms(V("zero"), 0.0)
+    ms(V("zb"), 0.0)
 
     def masks(bank, lo, out):
         mm([[(P(bank, i, 512, 16), Brd(i), lo)] for i in range(16)])
@@ -272,12 +272,9 @@ def plan(r):
             act(V(rows), P(b))
 
     ms(V("cum", 0, 8), 0.0)
-    for c in range(8):
-        if c < W3:
-            act(V("win3", 512 * c, 512 * c + 512), V("ones"), scale=0.0)
-        else:
-            ms(V("win3", 512 * c, 512 * c + 512), 0.0)
-    for n in ("win1", "win20", "win21", "win22"):
+    for k, n in enumerate(("win3", "win1", "win20")):
+        dma("sy", [(V(n, 1024 * c, 1024 * c + 1024), 0, 128, V("zb"), 0, 128, 0, 0) for c in range(4)], True, 4000 + 3500 * k, ZW)
+    for n in ("win21", "win22"):
         for c in range(8):
             iota(V(n, 512 * c, 512 * c + 512), [[0, 512]], 0, 0)
     ts(V("qh"), V("qi"), -2048.0, None, ADD)
@@ -300,29 +297,35 @@ def plan(r):
 
     PLUS, MINUS = V("blkb", 0, 8), V("blkb", 8, 16)
 
-    def mx(o, sb, bank, alt):
-        tt(o, sb, P(bank) if PSUM_OPS else alt, A.max)
+    def mx(o, a, b):
+        tt(o, a, b, A.max)
 
-    def stage(bank, x):
-        if PSUM_OPS:
-            mm([[(P(bank), V("idb"), x)]])
+    def relu(o, bank, a, b):
+        mm([[(P(bank), V("idb"), a), (P(bank), V("nidb"), b)]])
+        act(o, P(bank), F.Relu)
 
     def coords0():
         ze = lambda s, d=0: V("zt", 16 + 2 * s + d, 16 + 2 * s + d + 1023, 2)
         for c in range(4):
             s = 512 * c; t_ = lambda n: V(n, s, s + 512)
-            stage(c % 2, ze(s))
-            mx(t_("tA"), ze(s, -1), c % 2, ze(s)); mx(t_("tB"), ze(s, 1), c % 2, ze(s))
-            mm([[(P(4), V("idb"), ze(s, -1)), (P(4), V("nidb"), ze(s, 1))]])
-            act(t_("tC"), P(4), F.Relu)
+            mx(t_("tA"), ze(s, -1), ze(s))
+            if c in B0:
+                relu(t_("tB"), c % 2, ze(s, 1), ze(s))
+            else:
+                mx(t_("tB"), ze(s, 1), ze(s))
+            relu(t_("tC"), 4, ze(s, -1), ze(s, 1))
         for c in range(4):
             s = 512 * c; t_ = lambda n: V(n, s, s + 512)
             act(t_("Xt"), IND(ZW, V("LX", 32 * c, 32 * c + 32)))
             act(t_("Et"), IND(ZW, V("LE", 32 * c, 32 * c + 32)))
-            stage(c % 2, ze(s)); stage(2 + c % 2, t_("Et"))
-            mx(t_("tD"), t_("Xt"), c % 2, ze(s)); mx(t_("tF"), t_("Et"), c % 2, ze(s)); mx(t_("tG"), t_("Xt"), 2 + c % 2, t_("Et"))
+            mx(t_("tD"), t_("Xt"), ze(s)); mx(t_("tF"), t_("Et"), ze(s))
+            if c in G0:
+                relu(t_("tG"), 2 + c % 2, t_("Et"), t_("Xt"))
+            else:
+                mx(t_("tG"), t_("Xt"), t_("Et"))
             mm([[(P(5, x, 128, 16), l, sg) for l, sg in ((blk("tA", x), PLUS), (blk("tB", x), PLUS), (blk("tC", x), MINUS),
-                 (V("zt", 17 + 256 * x, 272 + 256 * x, 2), MINUS), (blk("tD", x), MINUS), (blk("tF", x), MINUS), (blk("tG", x), PLUS))]
+                 (V("zt", 17 + 256 * x, 272 + 256 * x, 2), MINUS), (blk("tD", x), MINUS), (blk("tF", x), MINUS), (blk("tG", x), PLUS))
+                 + (((V("zt", 16 + 256 * x, 271 + 256 * x, 2), PLUS),) if c in B0 else ()) + (((blk("Xt", x), PLUS),) if c in G0 else ())]
                 for x in range(4 * c, 4 * c + 4)])
         act(V("sP0"), P(5, 0, 128))
         remote("rs", 0, "rP0", 32, HOP, "sP0")
@@ -339,28 +342,31 @@ def plan(r):
         shuffle(5, "rX%d" % (t - 1), 32, False)
         ts(V("LX"), P(5, 0, 128), 2048.0, None, ADD)
         for c in range(4):
-            s = 512 * c; y = 528 * c; t_ = lambda n: V(n, s, s + 512); be, bo = c % 2, 2 + c % 2
+            s = 512 * c; y = 528 * c; t_ = lambda n: V(n, s, s + 512)
             (cp if c in OV else act)(V("Ot", y, y + 528), IND(ZW, V("LO", 32 * c, 32 * c + 33)))
             act(V("Et", y, y + 512 + 16 * es), IND(ZW, V("LE", 32 * c, 32 * c + 32 + es)))
             o0, o1, e = V("Ot", y, y + 512), V("Ot", y + 1, y + 513), V("Et", y + es, y + es + 512)
-            stage(be, e); stage(bo, o0)
-            mx(t_("tA"), o0, be, e)
+            mx(t_("tA"), o0, e)
             if c in BV:
-                mx(t_("tB"), o1, be, e)
+                mx(t_("tB"), o1, e)
             (cp if c in XV else act)(t_("Xt"), IND(ZW, V("LX", 32 * c, 32 * c + 32)))
-            mx(t_("tD"), t_("Xt"), bo, o0); mx(t_("tF"), t_("Xt"), be, e)
+            mx(t_("tD"), t_("Xt"), o0); mx(t_("tF"), t_("Xt"), e)
             mm([[(P(5, x, 128, 16), l, sg) for l, sg in ((blk("tD", x), PLUS), (blk("tF", x), PLUS), (blk("tA", x), MINUS))] for x in range(4 * c, 4 * c + 4)])
         act(V("sP%d" % t), P(5, 0, 128), bias=-1600.0)
         remote("rs", t, "rP%d" % t, 32, HOP, "sP%d" % t)
-        for c in range(4):
-            s = 512 * c; y = 528 * c; t_ = lambda n: V(n, s, s + 512); bd = 2 + c % 2
+        sh = lambda n, x: V(n, 128 * x - es, 128 * x + 128 - es)
+        for c in ((3, 0, 1, 2) if es else range(4)):
+            s = 512 * c; y = 528 * c; t_ = lambda n: V(n, s, s + 512)
             o0, o1, e = V("Ot", y, y + 512), V("Ot", y + 1, y + 513), V("Et", y + es, y + es + 512)
             if c not in BV:
-                stage(c % 2, e); mx(t_("tB"), o1, c % 2, e)
-            mm([[(P(bd), V("idb"), o1), (P(bd), V("nidb"), o0)]])
-            act(t_("tC"), P(bd), F.Relu)
-            mm([[(P(4, x, 128, 16), l, sg) for l, sg in ((blk("tA", x), PLUS), (blk("tB", x), PLUS), (blk("tC", x), MINUS),
-                 (V("Ot", 128 * x + 16 * c, 128 * x + 16 * c + 128), MINUS))] for x in range(4 * c, 4 * c + 4)])
+                mx(t_("tB"), o1, e)
+            relu(t_("tC"), 2 + c % 2, o0 if es else o1, o1 if es else o0)
+            if es and c == 3:
+                for n in "ABC":
+                    cp(col("h" + n, 15), col("t" + n, 2047))
+            xs = [x for x in range(4 * c, 4 * c + 4) if not (es and x == 12)] + ([12] if es and c == 2 else [])
+            mm([[(P(4, x, 128, 16), l, sg) for l, sg in ((sh("tA", x), PLUS), (sh("tB", x), PLUS), (sh("tC", x), MINUS),
+                 (V("Ot", 128 * x + 16 * (x // 4), 128 * x + 16 * (x // 4) + 128), MINUS))] for x in xs])
         act(V("sR%d" % t), P(4, 0, 128), bias=-1600.0)
         remote("rr", t, "rR%d" % t, 32, HOP, "sR%d" % t)
 
@@ -371,7 +377,7 @@ def plan(r):
         p = t % 2; c0 = 2048.0 - p
         sP, rP, W2 = "sP%d" % t, "rP%d" % t, "win2%d" % t
         part = lambda x: V(sP if x == r else rP, 32 * x, 32 * x + 32)
-        rem = lambda x, lo=0, hi=32: V(("sR%d" if x == r else "rR%d") % t, 32 * x + lo, 32 * x + hi)
+        rem = lambda x: V(("sR%d" if x == r else "rR%d") % t, 32 * x, 32 * x + 32)
         order = [r] + others; L = P(1, 0, 32)
         if t == 0:
             mm([[(L, V("nidh"), part(x)) for x in order]])
@@ -384,14 +390,8 @@ def plan(r):
                 mm([[(wa(a), blk("Rh", a), part(x)) for a in range(4 * b, 4 * b + 4) for x in others]], first=False)
                 (cp if b else act)(V("wI", 128 * b, 128 * b + 128), P(2 * b, 0, 128))
             tt(V("gI"), IND(V("wI"), V("offO")), V("maskE"), MUL)
-            gr = [(L, V("nidh" if p else "nsh"), rem(x)) for x in order]
-            if p == 0:
-                for x in order:
-                    for h in range(2):
-                        gr += [(P(1, 16 * h + 1, 16 * h + 16), V("ncar"), rem(x, 16 * h, 16 * h + 15)),
-                               (P(1, 16 * h, 16 * h + 1), V("ncar"), rem(x, 16 * h + 15, 16 * h + 16))]
             mm([[(L, V("nidh"), V("zero", 0, 32))] + [(P(1, b, 32, 4), blk("gI", b), V("blkf")) for b in range(4)]], last=False)
-            mm([gr], first=False)
+            mm([[(L, V("nidh"), rem(x)) for x in order]], first=False)
         tt(V("mv"), L, V("pen"), A.is_lt)
         tt(V("d1"), V("mv"), V("md"), MUL)
         tt(V("d2"), V("d1"), V("dump"), ADD)
@@ -450,7 +450,7 @@ def plan(r):
             act(V("l1", 0, w), P(3, 0, w), bias=-2048.0)
             mm(rep(0, 0, w, V("l1", 0, w)))
             act(V("wL", 0, 512), P(0))
-            cp(V(E, w * r, w * r + w), IND(V("wL", 0, 512), cF))
+            act(V(E, w * r, w * r + w), IND(V("wL", 0, 512), cF))
             remote("ag", t, E, w, HOP)
             mm([[(P(2, y, w, 32), V(W2, y, 4096, 32), V("sel", 0, 2))] for y in range(32)])
             act(V("l1", w, 2 * w), P(2, 0, w), bias=-2048.0)
@@ -609,7 +609,7 @@ def rank_program(g, core, T, topo):
     def call(q, m, a, kw):
         f = {"matmul": lambda: q.matmul, "tensor_scalar": lambda: q.tensor_scalar, "tensor_tensor": lambda: q.tensor_tensor,
              "tensor_copy": lambda: q.tensor_copy, "memset": lambda: q.memset, "activation": lambda: q.activation,
-             "iota": lambda: q.iota, "tensor_tensor_scan": lambda: q.tensor_tensor_scan}[m]()
+             "iota": lambda: q.iota, "affine_select": lambda: q.affine_select, "tensor_tensor_scan": lambda: q.tensor_tensor_scan}[m]()
         return f(*[ap(x) for x in a], **{k: ap(x) for k, x in kw.items()})
 
     waited = {}; loc = 0

@@ -1,51 +1,44 @@
 from concourse.mybir import AluOpType as A, ActivationFunctionType as F
 from concourse.bass import DstId, RemoteDMATransfer
 
-OV = (2,)
-XV = (0,)
-BV = (0, 3)
-B0 = (1, 2, 3)
-G0 = (3,)
-PE_NS = 0.5
-HOP = 3200.0
-LAT = 100.0
+PAR = {
+    "S": ("BC", "BC", "BC", "BC"),
+    "X": "ffff",
+    "S0": ("BCD", "BCD"), "X0": "ss",
+    "fin": "svsv", "onv": ("rE",),
+}
+ORDER = "000c0s0Z01021x0d2S1t0e070m0l0p060z0q0j0n080k0o0t0r0B0Q0A0H0u0E0S0Y0V0U1A0W0R0X0T1r0x0y180J1n041O1p1B190I1F1Q1N1P2V1G1R1H1I1U1z1a1b1o1c2W1h1d1V1e05030w1T1W2X1Z0g2Y1f1y1g1i1q223q1j201k1l0v1J1C2j3t282k1u242Z1K2m301X310a330f341M0O353u0C0K290D230N2b0L1S0M0b2U1L1Y090P1m3v1D2T1s1v3w3x321w212Q2d1E372a2c2R2526273z383y2e2p2P2f2g36392l0h0i3A2h3a3F2n2i2q3G2s0F3V3b2v0G3C3B3r3D2H3s3W3H2o3o2t3n3X3I2r3c2y123d3Y2I2w113Z2E3J102A142z402F132x412u3p3e2B152C3f2D2J2G433g2K16443h423E452L3i2M3j463k2N4O493K2O173l4a474c4d3L3m4b4P3M4e483N3O3P4Q4f4g4h4j4i4k4R3Q4S4l3R4T3S4U3T4m4V4o4n4w4q4y4W4x4p4z3U4r4X4s4Y4Z4t50524u515556534A545H4v575I5J585M595a5c5b5L4B5e5S5K635N5f5d5P5O5R5g5h5Q655U5T4C5Z615j5W5i5Y5V5k675X5l5m604D4E5n4G4H4F4I624K5p644J665q5r685s4L6b695o5t6a6F6d6e4M6c6g5u6f6x5v6G6n6v6j6h6H6l6m6J6I6i6s6K6k6L6z6M6o6N6P6q6p6O6t6r6B4N6Q6u6R5w6S5A6w5z6y6T5B6A6C6U6W6V6D6Z706X6E7B5C6Y5x715y725D7374757C7F7D5E787E7G795F7H7j7I7k7b7l7J7m7a7d7L767K7c5G7n7e7M7f7N777O7P7g7Q7S7h7R7V7W7T8x7U8y8A7X8z8B7Y7Z8082818C8D8R848I8T8J8F7o858E87868H898K888f8G7p8h8g8a8i8V8b8L8M8P8N8O838X8Q8j8S8U7q8W8Y7t8c917u8Z7v7r7i7w909v927s8k9594938l9c979l9w969p9z98999b9d9n9e9a9i9x8m9g8n7x9y9f9j7y8q9h8p9A8r7z9B8d9r8o9C9k9D7A9m9E9o9q9s9F9t8s9uaj8e9G8t8u8v9H9I9J9K9M9L9P9Q9Nak8wan9Oalam9R9Sao9T9U9Wap9Vaqatar9Xasa4aua5a6avaw9Yaxa7ayazaA9ZaDaEaBa0aCa1a2aFa8a3aGaHaIaKaJaLa9aaaSabacaMaTadaUaNaVaOaeb7aPaWaXafaYaZagaQb8b0aRb9b1bab2b3bfbcb4bbbgbdahbkaiblbhbibebmbjb5b6"
 
 BF, HF, FP, I32, U16 = "bfloat16", "float16", "float32", "int32", "uint16"
-BUF = {
-    "zt": (4112, BF), "yt": (4096, BF), "Et": (2176, BF), "Ot": (2176, BF), "zero": (256, HF), "zb": (1024, BF), "Xt": (2048, BF),
-    "hA": (16, BF), "tA": (2048, BF), "hB": (16, BF), "tB": (2048, BF), "hC": (16, BF), "tC": (2048, BF),
-    "tD": (2048, BF), "tF": (2048, BF), "tG": (2048, BF),
-    "LE": (130, U16), "LO": (130, U16), "LX": (128, U16), "LY": (256, U16),
-    "win1": (4608, BF), "win20": (4096, BF), "win21": (4096, BF), "win22": (4096, BF), "win3": (4096, BF), "rowsE": (512, BF), "rowsO": (512, BF),
-    "sP0": (128, HF), "sP1": (128, HF), "sP2": (128, HF), "rP0": (128, HF), "rP1": (128, HF), "rP2": (128, HF),
-    "sR1": (128, HF), "sR2": (128, HF), "rR1": (128, HF), "rR2": (128, HF),
-    "rE0": (256, HF), "rE1": (256, HF), "rE2": (256, HF), "rX0": (128, HF), "rX1": (128, HF), "rX2": (256, HF),
-    "hX0": (32, HF), "hX1": (32, HF), "hX2": (64, HF), "qf": (256, FP),
-    "wI": (256, FP), "wP": (256, FP), "wM": (256, BF), "wV": (256, BF), "wL": (768, FP), "wQ": (512, FP), "wN": (256, FP),
-    "gI": (512, FP), "gP": (512, HF), "gQ": (1024, HF), "maskE": (512, HF), "mask1": (1024, HF),
-    "mv": (32, HF), "nv": (32, HF), "d1": (32, FP), "d2": (32, FP), "ud": (32, U16), "cum": (40, HF), "mvL": (32, FP), "vL": (32, FP),
-    "pe": (32, FP), "s1": (32, FP), "s2": (32, FP), "s3": (32, FP), "uO": (32, U16), "uE": (32, U16), "ntab": (64, HF),
-    "l1": (192, HF), "qo": (64, I32), "qn": (64, I32), "q1": (32, I32), "n1": (64, I32), "n2": (64, I32), "n3": (64, I32),
-    "n4": (64, I32), "n5": (64, I32), "offN": (64, U16), "lo1": (64, BF), "offO": (32, U16), "loE": (32, BF),
-    "qhi": (64, BF), "qlo": (64, BF), "m1": (32, I32), "m2": (32, I32), "m3": (32, I32), "m8": (32, I32), "m4": (64, I32),
-    "m5": (64, I32), "m6": (32, I32), "m7": (32, I32), "pen": (32, FP), "md": (32, FP),
-    "qi": (256, I32), "qh": (256, HF), "qt1": (128, I32), "qt2": (128, I32), "QE": (128, HF), "q0": (64, I32), "uq0": (64, U16), "q0h": (64, HF),
-    "ones": (512, BF), "irows": (1024, BF), "ia": (1024, BF), "ib": (1024, BF),
-    "X": (384, FP), "val": (1024, BF), "pi": (16, I32), "pf": (32, FP), "Mi": (16, FP), "Mq": (8, FP), "Y": (32, FP), "X2": (128, FP),
-    "X3": (128, FP), "idb": (128, BF), "nidb": (128, BF), "nidh": (128, HF), "sh2": (128, BF), "dg": (256, BF),
-    "W": (144, HF), "base3": (384, BF), "c3": (6144, BF), "blkb": (16, BF), "blkh": (8, HF), "blkf": (8, FP), "e0": (8, BF), "LT": (1024, HF),
-    "GE": (1024, HF), "Rh": (1024, HF), "RQ": (512, HF), "Sel": (512, BF), "sel": (16, BF), "WG": (480, HF), "RS": (896, HF), "sq": (512, HF),
-    "v2": (128, FP), "cl": (16, U16), "cPO": (256, FP), "dump": (32, FP), "cmd": (32, FP),
+PER = {
+    "zt": (6160, BF), "yt": (2048, BF), "Et": (1056, BF), "Ot": (1056, BF), "Xt": (1024, BF),
+    "tA": (1040, BF), "tB": (1024, BF), "tC": (1024, BF), "tD": (1024, BF), "tF": (1024, BF), "tG": (1024, BF),
+    "LE": (66, U16), "LO": (66, U16), "LX": (64, U16), "LY": (128, U16), "W2": (4096, BF), "rows": (512, BF), "rowsM": (256, BF), "rowsI": (512, BF),
+    "TP": (512, BF), "TM": (256, BF), "VP": (96, FP),
+    "sP0": (64, HF), "rP0": (64, HF), "sP1": (128, HF), "rP1": (128, HF), "sP2": (128, HF), "rP2": (128, HF),
+    "rE0": (192, HF), "rE1": (192, HF), "rE2": (128, HF), "rX2": (128, HF), "qf": (128, FP),
+    "wI": (384, FP), "wN": (256, FP), "wL": (512, FP), "gI": (256, FP), "gP": (256, HF), "gQ": (512, HF), "maskE": (256, HF), "mask1": (512, HF),
+    "cum": (32, HF), "s1": (16, FP), "nt": (32, HF), "uO": (16, U16), "uE": (16, U16), "uq": (16, U16),
+    "l1": (96, HF), "qa": (32, I32), "qb": (64, I32), "uN": (64, U16), "qc": (16, I32), "qd": (32, I32), "uP": (32, U16),
+    "qi": (128, I32), "qh": (128, HF), "q0h": (32, HF), "uq0": (32, U16),
 }
+BUF = {
+    "WG": (4096, BF), "zb": (2048, BF), "TI": (544, BF), "vI": (32, FP), "X": (272, FP), "pi": (16, I32), "pf": (32, FP), "X2": (128, FP),
+    "Y": (8, FP), "idb": (128, BF), "nidb": (128, BF), "idh": (128, HF), "nidh": (128, HF), "LT": (128, HF), "GE": (128, HF),
+    "Mr": (128, HF), "Rh": (1024, HF), "RS": (1056, HF), "sq": (512, HF), "grp": (128, HF), "pm": (16, BF), "blkf": (8, FP), "blkh": (8, HF),
+    "Mi": (16, BF), "sel": (10, BF), "Y2": (10, FP), "c2": (32, HF), "c2f": (16, FP), "two": (16, HF), "idc": (32, FP), "ci": (8, I32), "cf": (16, FP),
+    "cl": (24, U16), "hX4": (32, HF), "hX5": (32, HF), "hX6": (32, HF),
+}
+for _k, _v in PER.items():
+    BUF[_k + "_0"] = _v; BUF[_k + "_1"] = _v
 AL, SB = {}, {}
 for _k, (_w, _d) in BUF.items():
     _o = SB.get("pool" + _d, (0, _d))[0]
     AL[_k] = ("pool" + _d, _o, _w); SB["pool" + _d] = (_o + (_w + 15) // 16 * 16, _d)
-STARTS = set(AL[n][:2] for n in ("tA", "tB", "tC"))
 SCRATCH = {k: ("sbuf", [128, w], d) for k, (w, d) in SB.items()}
 for _b in range(8):
     SCRATCH["p%d" % _b] = ("psum", [128, 512], "float32")
-SEMAPHORES = ["v", "t", "s", "gp", "loc"] + ["d%d" % k for k in range(24)] + [k + str(t) for k in ("rs", "rr", "ag", "hx", "hi") for t in range(3)]
+SEMAPHORES = ["v", "t", "s", "gp", "loc"] + ["d%d" % k for k in range(20)] + [k + str(t) for k in ("rs", "ag", "hx", "hi") for t in range(7)]
 
 
 def V(n, lo=0, hi=None, st=1):
@@ -61,41 +54,14 @@ def nel(v):
     return 16 * nel(v[2]) if v[0] == "I" else len(range(v[2], v[3], v[4]))
 
 
-def two(v):
-    return v[0] == "V" and v[1] in SB and SB[v[1]][1] in (BF, HF, U16)
-
-
 def isv(a):
     return isinstance(a, tuple) and len(a) > 0 and a[0] in ("V", "I")
 
 
-def cost(eng, ins):
-    m, a = ins[0], ins[1]
-    if eng == "t":
-        return PE_NS * max(64, nel(a[0])) * (1 if two(a[1]) else 4)
-    vs = [x for x in a if isv(x)]
-    n = max(nel(x) for x in vs if x[0] == "I") if any(x[0] == "I" for x in vs) else nel(a[0])
-    if eng == "gp":
-        return 150 + 2.0 * n
-    if a[0][0] == "I":
-        return 60 + 3.9 * n
-    if any(x[0] == "I" for x in vs):
-        return 60 + 1.62 * n
-    if eng == "s":
-        return 70 + 1.04 * n
-    big = [x for x in vs if nel(x) == n]
-    c = 0.5 if all(two(x) for x in big) else 1.0
-    if m == "tensor_tensor" and a[1][1] in SB and a[2][1] in SB:
-        c = 2 * c
-    return 1.04 * max(64, c * n)
-
-
 def plan(r):
-    ops = []; boost = [0.0]
+    ops = []; mark = [0]
 
     def spans(x):
-        if x[0] == "V" and (x[1], x[2] + 1) in STARTS:
-            return [(x[1], x[2], x[2] + 1), (x[1], x[2] + 1, x[3])] if x[3] > x[2] + 1 else [(x[1], x[2], x[3])]
         return spans(x[1]) + spans(x[2]) if x[0] == "I" else [(x[1], x[2], x[3])]
 
     def op(eng, *ins):
@@ -108,7 +74,7 @@ def plan(r):
             for x in list(a[1:]) + list(kw.values()):
                 if isv(x):
                     rd += spans(x)
-        ops.append((eng, "c", ins, sorted(set(rd)), sorted(set(wr)), sum(cost(eng, i) for i in ins), boost[0]))
+        ops.append((eng, "c", ins, sorted(set(rd)), sorted(set(wr)), 0.0, mark[0]))
 
     def ts(o, i, s1, s2, o0, o1=None):
         op("v", ("tensor_scalar", (o, i, s1, s2, o0) if o1 is None else (o, i, s1, s2, o0, o1), {}))
@@ -125,6 +91,14 @@ def plan(r):
     def act(o, i, f=None, **kw):
         op("s", ("activation", (o, i, f if f is not None else (F.Identity if kw else F.Copy)), kw))
 
+    def mov(key, o, i, bias=None):
+        if key in PAR["onv"]:
+            cp(o, i) if bias is None else ts(o, i, bias, None, A.add)
+        elif bias is None:
+            act(o, i)
+        else:
+            act(o, i, bias=bias)
+
     def iota(o, pat, base, cm):
         op("gp", ("iota", (o, pat, base, cm), {} if SB[o[1]][1] == I32 else {"allow_small_or_imprecise_dtypes": True}))
 
@@ -135,366 +109,372 @@ def plan(r):
                 ins.append(("matmul", (o, l, x, first and k == 0, last and k == len(gr) - 1), {}))
         op("t", *ins)
 
-    def dma(eng, items, load, ns, after=None):
+    def dma(items, load, ns, split, after=None):
         sp = sorted(set(s for x in items for s in spans(x[0])))
-        rd = sorted(set(s for x in items if isv(x[3]) for s in spans(x[3]))) + (spans(after) if after else [])
-        ops.append((eng, "d", (load, items), rd if load else sp, sp if load else [], ns, 0.0))
+        rd = spans(items[0][3]) + spans(after) if after else []
+        ops.append(("sy", "d", (load, items, split), rd if load else sp, sp if load else [], ns, mark[0]))
 
-    def remote(kind, t, n, w, ns, src=None):
+    def remote(kind, t, n, w, src=None):
         sl = lambda b, x: V(b, w * x, w * x + w)
         srcs = [sl(src, x) for x in others] if src else [sl(n, r)]
-        ops.append(("gp", "r", (kind, t, srcs, sl(n, r)), [s for x in srcs for s in spans(x)], [s for x in others for s in spans(sl(n, x))], ns,
-                    4000.0 if kind == "ag" and t < 2 else 0.0))
+        ops.append(("gp", "r", (kind, t, srcs, sl(n, r)), [s for x in srcs for s in spans(x)], [s for x in others for s in spans(sl(n, x))], 0.0, mark[0]))
 
-    P = lambda b, lo=0, hi=512, st=1: ("V", "p%d" % b, lo, hi, st)
     col = lambda n, j: V(n, j, j + 1)
-    ZW = V("zt", 16)
+    blk = lambda n, a: V(n, 128 * a, 128 * a + 128)
     SHR, AND = A.arith_shift_right, A.bitwise_and
-    EQ, MUL, ADD = A.is_equal, A.mult, A.add
+    EQ, MUL, ADD, SUB = A.is_equal, A.mult, A.add, A.subtract
     others = [x for x in range(4) if x != r]
 
-    dma("sy", [(V("qi"), 0, 128, "q", 0, 128, 0, 256), (V("zt", 0, 16), 0, 128, "z", 0, 128, 4080, 16)], True, 2200)
-    for c in range(4):
-        dma("sy" if c % 2 else "s", [(V("zt", 16 + 1024 * c, 1040 + 1024 * c), 0, 128, "z", 0, 128, 1024 * c, 1024)], True, 2600 + 700 * c)
-    dma("s", [(V("q0"), 16 * u, 16, "q", 16 * (2 * r + u // 4), 16, 64 * (u % 4), 64) for u in range(8)], True, 2500)
+    def loads(b):
+        n = "zt_%d" % b; z = lambda lo, hi, hf, c0: (V(n, lo, hi), 64 * hf, 64, "z", 64 * b, 64, c0, hi - lo)
+        t0 = 3400 + 2900 * b
+        dma([z(2048, 4096, 0, 0), z(2048, 4096, 1, 2048)], True, t0, True)
+        dma([(V("qi_%d" % b), 64 * hf, 64, "q", 64 * b, 64, 128 * hf, 128) for hf in range(2)], True, t0 + 100, True)
+        dma([z(4096, 6144, 0, 2048), z(0, 2048, 1, 0)], True, t0 + 1500, True)
+        h = lambda c, hf: V(n, c, c + 1) + (64 * hf,)
+        cp(h(2047, 0), h(6143, 0)); cp(h(6144, 0), h(2048, 0)); cp(h(4096, 1), h(0, 1))
 
-    iota(V("X"), [[1, 384]], -128, 0)
-    X = lambda lo, hi, st=1: V("X", 128 + lo, 128 + hi, st)
+    mark[0] = 1; loads(0); mark[0] = 0; loads(1)
+
+    iota(V("X"), [[1, 272]], -64, 0)
+    X = lambda lo, hi, st=1: V("X", 64 + lo, 64 + hi, st)
     iota(col("pi", 0), [[0, 1]], 0, 1)
-    iota(V("X3"), [[1, 8], [0, 16]], 0, 0)
-    iota(V("v2"), [[16, 8], [2, 16]], 0, -1)
+    iota(V("X2"), [[0, 8], [1, 16]], 0, 0)
+    iota(V("Y"), [[1, 4], [4, 2]], 0, 0)
+    iota(V("vI"), [[2048, 2], [128, 2], [256, 8]], 8192, 1)
+    iota(V("c2f"), [[256, 16]], -2047, 2)
+    iota(V("idc"), [[1, 2], [2048, 2], [32, 8]], 8192, 0)
     for j, (sh, an) in enumerate([(0, 15), (4, 7), (6, 1), (4, 3), (0, 7), (3, 1), (1, 7), (0, 1)]):
         ts(col("pi", j + 1), col("pi", 0), sh, an, SHR, AND)
     cp(V("pf", 0, 9), V("pi", 0, 9))
     pf = lambda j: col("pf", j)
     lin = lambda o, a, c, b: ts(pf(o), pf(a), float(c), b, MUL, ADD)
-    blk = lambda n, a: V(n, 128 * a, 128 * a + 128)
-    ts(V("idb"), X(0, 128), pf(0), None, EQ)
-    ts(V("blkb", 0, 8), X(0, 8), pf(2), None, EQ)
-    ts(V("blkb", 8, 16), X(0, 8), pf(2), -1.0, EQ, MUL)
-    ts(V("nidb"), X(0, 128), pf(0), -1.0, EQ, MUL)
-    ts(V("base3", 256, 384), V("X3"), pf(2), None, EQ)
+    ms(V("grp"), 1.0)
+    sel = lambda o, pat, f, base, cm: op("gp", ("affine_select", (o, V("grp"), pat, f, 0.0, base, cm), {}))
     for k in range(4):
-        ts(blk("sq", k), V("v2"), float(16 * (k % 2) - k // 2), None, EQ)
-    for k in range(4):
-        tt(blk("sq", k), blk("sq", k), V("base3", 256, 384), MUL)
-    ts(V("nidh"), X(0, 128), pf(0), -1.0, EQ, MUL)
-    ts(V("sh2"), X(2, 130), pf(0), None, EQ)
-    ts(V("blkh"), X(0, 8), pf(2), None, EQ)
+        sel(blk("sq", k), [[-16, 8], [1000, 2], [-2, 8]], EQ, -(k // 2) - 1000 * (k % 2), 1)
+    lin(9, 3, -2048, 4096.0); lin(10, 3, -2048, 4097.0)
+    zc, zc1 = pf(9), pf(10)
+    sel(V("idh"), [[-1, 128]], EQ, 0, 1)
+    act(V("idb"), V("idh"))
+    act(V("nidb"), V("idh"), scale=-1.0)
+    ts(V("pm", 0, 8), V("Y"), pf(2), None, EQ)
+    ts(V("pm", 8, 16), V("Y"), pf(2), -1.0, EQ, MUL)
+    act(V("nidh"), V("idh"), scale=-1.0)
+    sel(V("LT"), [[1, 128]], A.is_gt, 0, -1)
+    sel(V("GE"), [[-1, 128]], A.is_ge, 0, 1)
     ts(V("blkf"), X(0, 8), pf(2), None, EQ)
+    ts(V("blkh"), X(0, 8), pf(2), None, EQ)
     ts(V("Mi"), X(0, 16), pf(1), None, EQ)
-    ts(V("Mq"), X(0, 8), pf(4), None, EQ)
-    ts(col("e0", 0), pf(1), 0.0, None, EQ)
-    lin(12, 2, 16, 0.0); lin(13, 3, 16, pf(1)); lin(14, 3, 64, pf(1))
-    ts(pf(15), pf(1), 3.5, None, A.is_lt)
-    lin(16, 2, 4, pf(6)); lin(17, 5, 32, pf(16)); lin(18, 5, 96, pf(16)); lin(19, 5, 64, pf(16)); lin(20, 2, 4, pf(19))
-    lin(21, 2, 4, 0.0); lin(22, 8, 32, pf(21)); lin(23, 7, 96, pf(22))
-    lin(24, 3, 16, 0.0); ts(pf(25), pf(4), 16.0, col("Mi", 2), MUL, MUL); lin(26, 1, 2, -2047.0); lin(27, 1, 1, 112.0)
-    ts(V("W", 0, 143), X(-15, 128), pf(12), None, EQ)
-    ms(V("ones"), 1.0)
-    for k, (step, row) in enumerate(((0, 0), (1000, 4), (1000, 5))):
-        for c in range(4):
-            boost[0] = -1200.0 * (4 * k + c)
-            op("gp", ("affine_select", (V("c3", 2048 * k + 512 * c, 2048 * k + 512 * c + 512), V("ones"), [[-1, 4], [-16, 8], [step, 16]],
-                                        EQ, 0.0, -4 * c - step * row, 1), {}))
-    boost[0] = 0.0
-    Brd, RowH, RowL = [lambda i, k=k: blk("c3", 16 * k + i) for k in range(3)]
-    Col = lambda i: V("W", 15 - i, 143 - i)
-    iota(V("ia"), [[1, 16], [0, 64]], 0, 0)
-    iota(V("ib"), [[0, 16], [1, 64]], 0, 0)
-    iota(V("val"), [[16, 8], [0, 8], [1, 16]], 0, -1)
-    iota(V("X2"), [[16, 2], [0, 4], [1, 16]], 0, 0)
-    iota(V("Y", 0, 6), [[-2, 3], [16, 2]], 4, 0)
-    iota(V("Y", 6, 10), [[2, 2], [16, 2]], 2, 0)
-    iota(V("dump"), [[16, 32]], 4096, 0)
-    iota(V("cmd"), [[2048 - 256, 2], [-16, 16]], -4096, 0)
-    iota(V("cPO"), [[32, 8], [0, 2], [256, 16]], 0, 0)
-    ts(V("Rh"), V("val"), 0.0, None, EQ)
-    ts(V("LT"), V("val"), 0.0, None, A.is_gt)
-    ts(V("GE"), V("val"), 0.0, None, A.is_le)
-    for qt in range(4):
-        ts(blk("RQ", qt), V("X2"), pf(13), col("Mq", qt), EQ, MUL)
-        ts(blk("Sel", qt), X(-16 * qt, 128 - 16 * qt), pf(14), pf(15), EQ, MUL)
-        ts(V("RS", 224 * qt, 224 * qt + 224), X(-96, 128), pf(13), col("Mq", qt), EQ, MUL)
-    RS = lambda v, s: V("RS", 224 * v + 96 - 32 * s, 224 * v + 224 - 32 * s)
-    ts(V("Y", 10, 20), V("Y", 0, 10), pf(13), 64.0, EQ, MUL)
-    ts(V("Y", 20, 30), V("Y", 0, 10), 1.0, pf(13), ADD, EQ)
-    tt(V("sel", 0, 10), V("Y", 10, 20), V("Y", 20, 30), ADD)
-    for e in range(2):
-        ts(V("WG", 240 * e, 240 * e + 240), X(0, 240), pf(27), col("blkf", 2 * r + e), EQ, MUL)
-    ts(V("cl", 0, 2), X(0, 4, 2), pf(17), None, ADD)
-    ts(V("cl", 2, 4), X(64, 68, 2), pf(18), None, ADD)
-    ts(V("cl", 4, 8), X(0, 4), pf(23), None, ADD)
-    ts(V("cl", 8, 10), X(0, 4, 2), pf(19), None, ADD)
-    ts(V("cl", 10, 12), X(32, 36, 2), pf(19), None, ADD)
-    ts(V("cl", 12, 16), X(0, 8, 2), pf(20), None, ADD)
-    cL2, cX, cEO, cQ, cF = V("cl", 0, 2), V("cl", 2, 4), V("cl", 4, 8), V("cl", 8, 12), V("cl", 12, 16)
-    ts(V("dump"), V("dump"), pf(1), None, ADD)
-    ts(V("cmd"), V("cmd"), pf(1), None, A.subtract)
-    ts(V("cPO"), V("cPO"), pf(26), None, ADD)
-    for k in range(2):
-        ts(blk("dg", k), X(0, 128), pf(0), col("Mi", 2 + k), EQ, MUL)
-    for k in range(2):
-        mm([[(P(7), blk("dg", 0), V("ia", 512 * k, 512 * k + 512)), (P(7), blk("dg", 1), V("ib", 512 * k, 512 * k + 512))]])
-        act(V("irows", 512 * k, 512 * k + 512), P(7), bias=pf(25))
-    ms(V("zero"), 0.0)
-    ms(V("zb"), 0.0)
+    for y in range(3):
+        iota(V("Y2", y, 6, 3), [[2, 2]], (0, 4, 1)[y], 0)
+    iota(V("Y2", 6, 8), [[2, 2]], 5, 0); iota(V("Y2", 8, 10), [[1, 2]], 0, 0)
+    ts(V("sel"), V("Y2"), pf(7), None, EQ)
+    ts(V("Mr"), V("X2"), pf(1), None, EQ)
+    for a in range(8):
+        ts(blk("Rh", a), V("Mr"), col("blkf", a), None, MUL)
+    ms(V("RS"), 0.0)
+    for v in range(6):
+        sel(V("RS", 176 * v + 48, 176 * v + 176), [[-64 if v < 4 else 64, 2], [1000, 4], [-1, 16]], EQ, -16 * v if v < 4 else 128 - 48 * v, 1)
+    RS = lambda v, x: V("RS", 176 * v + 48 - 16 * x, 176 * v + 176 - 16 * x)
+    act(V("c2", 0, 16), V("c2f"), bias=1.0)
+    act(V("c2", 16, 32), V("c2f"))
+    lin(12, 2, 256, 0.0); lin(13, 1, 2, pf(12))
+    ts(V("cf", 0, 3), X(0, 33, 16), pf(1), None, ADD)
+    ts(V("ci", 0, 3), V("cf", 0, 3), 1.0 / 3, -0.3, MUL, ADD)
+    ts(V("cf", 3, 6), V("ci", 0, 3), -3.0, None, MUL)
+    tt(V("cf", 6, 9), V("cf", 0, 3), V("cf", 3, 6), ADD)
+    ts(V("cf", 9, 12), V("cf", 6, 9), 64.0, 64.0, MUL, ADD)
+    tt(V("cf", 0, 3), V("cf", 9, 12), V("cf", 6, 9), MUL)
+    tt(V("cf", 3, 6), V("cf", 0, 3), V("ci", 0, 3), ADD)
+    lin(14, 2, 16, 0.0)
+    ts(V("cl", 0, 3), V("cf", 3, 6), pf(14), None, ADD)
+    lin(16, 2, 8, pf(5)); lin(17, 6, 64, pf(16)); lin(18, 2, 32, pf(1))
+    ts(V("cl", 4, 6), X(0, 129, 128), pf(17), None, ADD)
+    lin(19, 2, 8, pf(7)); lin(20, 8, 256, pf(19))
+    ts(V("cl", 16, 20), X(0, 193, 64), pf(19), None, ADD)
+    ts(V("cl", 20, 24), X(0, 193, 64), pf(20), None, ADD)
+    ts(V("cl", 10, 12), X(0, 129, 128), pf(0), None, ADD)
+    ts(V("cl", 12, 14), X(0, 17, 16), pf(18), None, ADD)
+    cS, cP, cP2, cP0, cQ0, cF = V("cl", 0, 3), V("cl", 16, 20), V("cl", 20, 24), V("cl", 4, 6), V("cl", 10, 12), V("cl", 12, 14)
+    ms(V("two"), 2.0)
+    iota(V("TI"), [[0, 544]], 0, 0)
+    act(V("TI", 16, 528, 16), V("vI"))
+    tt(V("TI", 17, 529, 16), V("vI"), V("TI", 16, 528, 16), SUB)
+    ms(V("zb", 0, 128), 0.0)
+    for c in range(4):
+        iota(V("zb", max(128, 512 * c), 512 * c + 512), [[0, 512 - 128 * (c == 0)]], 0, 0)
+    for k, n in enumerate(("WG", "W2_0", "W2_1")):
+        dma([(V(n, 2048 * c, 2048 * c + 2048), 0, 128, V("zb"), 0, 128, 0, 0) for c in range(2)], True, 4500 + 2700 * k, False, V("zt_%d" % min(k, 1)))
+    PLUS, MINUS = V("pm", 0, 8), V("pm", 8, 16)
+    Rh = lambda a: blk("Rh", a)
 
-    def masks(bank, lo, out):
-        mm([[(P(bank, i, 512, 16), Brd(i), lo)] for i in range(16)])
-        ts(out, P(bank), pf(1), None, EQ)
+    def batch(b):
+        N = lambda n: "%s_%d" % (n, b)
+        W = lambda n, lo=0, hi=None, st=1: V(N(n), lo, hi, st)
+        P = lambda k, lo=0, hi=512, st=1: ("V", "p%d" % (4 * b + k), lo, hi, st)
+        ZW = W("zt"); flip = [0]
 
-    def prep(p, win):
-        e = V("qn", 0, 32)
-        ts(V("m1"), e, 0xE0, None, AND)
-        ts(V("m2"), e, 8, None, SHR)
-        tt(V("m3"), V("m1"), V("m2"), ADD)
-        ts(V("offO"), V("m3"), pf(24), None, ADD)
-        ts(V("m8"), e, 1, 15, SHR, AND)
-        cp(V("loE"), V("m8"))
-        masks(6, V("loE"), V("maskE"))
-        ts(V("m4"), V("qn"), 6, None, SHR); cp(V("qhi"), V("m4"))
-        ts(V("m5"), V("qn"), 63, None, AND); cp(V("qlo"), V("m5"))
-        ts(V("m6"), V("q1"), 1, None, SHR); tt(V("md"), V("m6"), V("cmd"), ADD)
-        ts(V("m7"), V("q1"), 1, None, AND)
-        ts(V("pen"), V("m7"), float(p), -100000.0, EQ, MUL)
-        for k, (rows, pp) in enumerate((("rowsE", p), ("rowsO", 1 - p))):
-            b = 7 - k
-            gr = [(P(b), blk("Sel", qt), V(win, 1024 * qt + pp, 1024 * qt + 1024, 2)) for qt in range(4)]
-            if win == "win3":
-                gr.append((P(b), V("sh2"), V("irows", pp, 1024, 2)))
-            for i in range(16):
-                gr.append((P(b, i, 512, 16), RowH(i), V("qhi", 32 * k, 32 * k + 32)))
-                gr.append((P(b, i, 512, 16), RowL(i), V("qlo", 32 * k, 32 * k + 32)))
-            cuts = [0, 1, 2, 3, 4] + list(range(8, len(gr), 4)) + [len(gr)]
-            for a, z_ in zip(cuts[:-1], cuts[1:]):
-                mm([gr[a:z_]], a == 0, z_ == len(gr))
-            act(V(rows), P(b))
-
-    ms(V("cum", 0, 8), 0.0)
-    for k, n in enumerate(("win3", "win1", "win20")):
-        dma("sy", [(V(n, 1024 * c, 1024 * c + 1024), 0, 128, V("zb"), 0, 128, 0, 0) for c in range(4)], True, 4000 + 3500 * k, ZW)
-    for n in ("win21", "win22"):
-        for c in range(8):
-            iota(V(n, 512 * c, 512 * c + 512), [[0, 512]], 0, 0)
-    ts(V("qh"), V("qi"), -2048.0, None, ADD)
-    o = P(5, 0, 128)
-    mm([[(o, blk("sq", 0), V("qh", 0, 256, 2)), (o, blk("sq", 1), V("qh", 1, 256, 2))]])
-    ts(V("LX"), o, 2048.0, None, ADD)
-    ts(V("qt1"), o, 2049.0, None, ADD)
-    cp(V("QE"), o)
-    ts(V("qt2"), V("qt1"), 4095, None, AND)
-    cp(V("LE", 0, 128), V("qt2"))
-    cp(V("uq0"), V("q0"))
-    ts(V("q0h"), V("q0"), -2048.0, None, ADD)
-    for k in range(2):
-        cp(IND(V("win3"), V("uq0", 32 * k, 32 * k + 32)), V("irows", 512 * k, 512 * k + 512))
-    mm([[(P(6, 32 * k, 32 * k + 32), blk("sq", 2 * k + e), V("q0h", e, 64, 2)) for e in range(2)] for k in range(2)]
-       + [[(P(6, 64 + 16 * e, 80 + 16 * e), V("WG", 240 * e + 112 - 16 * a, 240 * e + 240 - 16 * a), V("QE", a, 128, 8)) for a in range(8)] for e in range(2)])
-    ts(V("qn"), P(6, 0, 64), 2048.0, None, ADD)
-    ts(V("q1"), P(6, 64, 96), 2048.0, None, ADD)
-    prep(0, "win3")
-
-    PLUS, MINUS = V("blkb", 0, 8), V("blkb", 8, 16)
-
-    def mx(o, a, b):
-        tt(o, a, b, A.max)
-
-    def relu(o, bank, a, b):
-        mm([[(P(bank), V("idb"), a), (P(bank), V("nidb"), b)]])
-        act(o, P(bank), F.Relu)
-
-    def coords0():
-        ze = lambda s, d=0: V("zt", 16 + 2 * s + d, 16 + 2 * s + d + 1023, 2)
-        for c in range(4):
-            s = 512 * c; t_ = lambda n: V(n, s, s + 512)
-            mx(t_("tA"), ze(s, -1), ze(s))
-            if c in B0:
-                relu(t_("tB"), c % 2, ze(s, 1), ze(s))
+        def term(o, a, x, on_s):
+            if on_s:
+                k = flip[0]; flip[0] = 1 - k; ps = P(k, 0, nel(o))
+                mm([[(ps, V("idb"), a), (ps, V("nidb"), x)]])
+                act(o, ps, F.Relu)
             else:
-                mx(t_("tB"), ze(s, 1), ze(s))
-            relu(t_("tC"), 4, ze(s, -1), ze(s, 1))
-        for c in range(4):
-            s = 512 * c; t_ = lambda n: V(n, s, s + 512)
-            act(t_("Xt"), IND(ZW, V("LX", 32 * c, 32 * c + 32)))
-            act(t_("Et"), IND(ZW, V("LE", 32 * c, 32 * c + 32)))
-            mx(t_("tD"), t_("Xt"), ze(s)); mx(t_("tF"), t_("Et"), ze(s))
-            if c in G0:
-                relu(t_("tG"), 2 + c % 2, t_("Et"), t_("Xt"))
+                tt(o, a, x, A.max)
+
+        def reduce(out, items):
+            d = {}
+            for v, s in items:
+                d[v] = d.get(v, 0) + s
+            return [(out, v, PLUS if s > 0 else MINUS) for v, s in d.items() for _ in range(abs(s))]
+
+        def rep(k, lo, rhs):
+            n = nel(rhs)
+            return [[(P(k, lo + a, lo + 8 * n, 8), Rh(a), rhs)] for a in range(8)]
+
+        def split(v, row):
+            st = 512 // nel(v); hi = W("TP", row, 512, st)
+            mov("hi", hi, v)
+            tt(W("TP", row + 1, 512, st), v, hi, SUB)
+
+        def fields(q, w, ints, offs):
+            ts(W(ints, 0, w), q, 5, 255, SHR, AND)
+            ts(W(ints, w, 2 * w), q, 1, 15, SHR, AND)
+            cp(W(offs), W(ints))
+
+        def prep(t, q, c):
+            e = ("V", q[1], q[2], q[2] + 16, 1)
+            ts(W("qc"), e, c, 4097.0, ADD, MUL)
+            ts(W("uq"), e, c, None, ADD)
+            mov("VPq", W("VP", 64, 96), q, c + 8192.0)
+            fields(W("qc"), 16, "qd", "uP")
+            mov("maskE", W("maskE"), IND(V("Mi"), W("uP", 16, 32)))
+            if t:
+                rows(t)
+
+        def rows(t):
+            split(W("VP", 64, 96), 4 * t + 2 if t < 2 else 14)
+            mm([[(P(3, 128 * k, 128 * k + 128), blk(N("TP"), k), V("idb"))] for k in range(4)])
+            mov("rows", W("rows"), P(3))
+
+        def start():
+            ts(W("qh"), W("qi"), -2048.0, None, ADD)
+            o = P(2, 0, 64)
+            mm([[(o, blk("sq", 0), W("qh", 0, 128, 2)), (o, blk("sq", 1), W("qh", 1, 128, 2))]])
+            ts(W("LX"), o, zc, None, ADD)
+            ts(W("LE", 0, 64), o, zc1, None, ADD)
+
+        def prep0():
+            for n in ("TP", "TM", "wN"):
+                iota(W(n), [[0, AL[N(n)][2]]], 0, 0)
+            ms(W("cum", 0, 8), 0.0)
+            iota(W("wI", 128, 256), [[0, 128]], 100000, 0); iota(W("wI", 256, 384), [[0, 128]], 0, 0)
+            mm([[(P(3, 128 * hf, 128 * hf + 128), Rh(4 * hf + r), W("qh"))] for hf in range(2)])
+            act(W("wL", 0, 256), P(3, 0, 256))
+            act(W("q0h"), IND(W("wL", 0, 256), cQ0))
+            ts(W("uq0"), W("q0h"), 2048.0, None, ADD)
+            mm([[(P(3, 16 * pp, 16 * pp + 16), blk("sq", 2 * pp + e), W("q0h", e, 32, 2)) for e in range(2)] for pp in range(2)])
+            prep(0, P(3, 0, 32), 2048.0)
+            mm([[(P(3, 128 * k, 128 * k + 128), V("TI", 16 - 2 * b + 128 * k, 144 - 2 * b + 128 * k), V("idb"))] for k in range(4)])
+            act(W("rowsI"), P(3))
+            for k in range(2):
+                cp(IND(V("WG"), W("uq0", 16 * k, 16 * k + 16)), W("rowsI", 256 * k, 256 * k + 256))
+            mm([[(P(3, 16 * pp + cc, 16 * pp + cc + 1), V("WG", 256 * cc + pp, 256 * cc + 256, 2), col("sel", 8 + b))] for pp in range(2) for cc in range(16)])
+            act(W("l1", 32, 64), P(3, 0, 32), bias=-10240.0)
+            mm(rep(3, 256, W("l1", 32, 64)))
+            act(W("wL", 256, 512), P(3, 256, 512))
+            act(W("VP", 0, 64), IND(W("wL", 256, 512), cP), bias=10240.0)
+            act(W("VP", 0, 64, 2), V("idc"), bias=pf(13))
+            split(W("VP", 0, 64), 0)
+            rows(0)
+
+        def coords0():
+            ze = lambda s, n, d=0: W("zt", 2048 + 2 * s + d, 2048 + 2 * s + d + 2 * n - 1, 2)
+            t_ = lambda n, s, w: W(n, s, s + w)
+            for c in (1, 0):
+                s = 512 * c; S = PAR["S0"][c]
+                term(t_("tA", s, 512), ze(s, 512), ze(s, 512, -1), "A" in S)
+                term(t_("tB", s, 512), ze(s, 512), ze(s, 512, 1), "B" in S)
+                term(t_("tC", s, 512), ze(s, 512, -1), ze(s, 512, 1), "C" in S)
+                gr = [(P(2, 256, 320), V("idb"), V("zb", 0, 64))] if c == 1 else []
+                for x in range(4 * c, 4 * c + 4):
+                    k = 128 * x
+                    it = [(t_("tA", k, 128), 1), (t_("tB", k, 128), 1), (t_("tC", k, 128), -1)]
+                    it += [(ze(k, 128, -1), 1)] * ("A" in S) + [(ze(k, 128, 1), 1)] * ("B" in S) + [(ze(k, 128, 1), -1)] * ("C" in S)
+                    gr += reduce(P(2, 256 + x, 320, 8), it)
+                mm([gr], c == 1, False)
+            for c in range(2):
+                s = 512 * c; S = PAR["S0"][c]
+                act(t_("Xt", s, 512), IND(ZW, W("LX", 32 * c, 32 * c + 32)))
+                term(t_("tD", s, 512), t_("Xt", s, 512), ze(s, 512), "D" in S)
+                i1 = IND(ZW, W("LE", 32 * c, 32 * c + 32))
+                e = ze(s, 512)
+                if PAR["X0"][c] == "s":
+                    act(t_("Et", s, 512), i1); i1 = t_("Et", s, 512)
+                else:
+                    e = t_("Et", s, 512); mov("E0", e, ze(s, 512))
+                tt(t_("tF", s, 512), i1, e, A.max)
+                tt(t_("tG", s, 512), i1, t_("Xt", s, 512), A.max)
+                for n, sg in (("tD", -1), ("tF", -1), ("tG", 1)):
+                    gr = []
+                    for x in range(4 * c, 4 * c + 4):
+                        k = 128 * x
+                        gr += reduce(P(2, 256 + x, 320, 8), [(t_(n, k, 128), sg)] + [(ze(k, 128), -1)] * ("D" in S and n == "tD"))
+                    mm([gr], False, c == 1 and n == "tG")
+            mov("sP", W("sP0"), P(2, 256, 320))
+            remote("rs", b, N("rP0"), 16, N("sP0"))
+
+        def coords(t):
+            es = 1 - t % 2; E = N("rE%d" % (t - 1))
+            rng = [(v, 0, 48, 3 + 48 * v) for v in range(4)] + [(4, 0, 2, 195)] + [(5, 46, 47, 1)] * es
+            mm([[(P(2, o, o + hi - lo), RS(v, x), V(E, 48 * x + lo, 48 * x + hi)) for x in [r] + others] for v, lo, hi, o in rng])
+            ts(W("LO", 0, 65), P(2, 4 - 3 * es, 197 - 3 * es, 3), zc, None, ADD)
+            ts(W("LE", 0, 64 + es), P(2, 3, 193 + 3 * es, 3), zc, None, ADD)
+            ts(W("LX"), P(2, 5, 195, 3), zc, None, ADD)
+            t_ = lambda n, s, w: W(n, s, s + w)
+            left = lambda k, n: t_("Ot", k + 15 * es, n)
+            right = lambda k, n: t_("Ot", k + 15 * es + 1, n)
+            SS = PAR["S"][2 * t - 2:2 * t]
+            for c in range(2):
+                s = 512 * c; S = SS[c]
+                for L, G, hi in (("LO", "Ot", 65), ("LE", "Et", 64 + es)):
+                    lo, hi = (0, 34) if c == 0 else (34, hi)
+                    act(W(G, 16 * lo, 16 * hi), IND(ZW, W(L, lo, hi)))
+                term(t_("tC", s, 512), left(s, 512), right(s, 512), "C" in S)
+                term(t_("tB", s, 512), t_("Et", s, 512), right(s, 512), "B" in S)
+                lo, n = (0, 512 + es) if c == 0 else (512 + es, 512)
+                term(t_("tA", lo, n), t_("Et", lo, n), left(lo, n), False)
+            for c in range(2):
+                S = SS[c]; gr = [(P(2, 256, 384), V("idb"), V("zb", 0, 128))] if c == 0 else []
+                for x in range(4 * c, 4 * c + 4):
+                    k = 128 * x
+                    it = [(t_("tA", k, 128), 1), (t_("tB", k, 128), 1), (t_("tC", k, 128), -1)]
+                    it += [(right(k, 128), 1)] * ("B" in S) + [(right(k, 128), -1)] * ("C" in S)
+                    gr += reduce(P(2, 257 + 2 * x, 384, 16), it)
+                    gr += reduce(P(2, 256 + 2 * x, 384, 16), [(t_("tA", k + es, 128), -1)])
+                mm([gr], c == 0, False)
+            for c in range(2):
+                s = 512 * c; S = SS[c]
+                ix = IND(ZW, W("LX", 32 * c, 32 * c + 32))
+                if PAR["X"][2 * t - 2 + c] == "s":
+                    act(t_("Xt", s, 512), ix); ix = t_("Xt", s, 512)
+                for n, o in (("D", lambda k, w: left(k + es, w)), ("F", lambda k, w: t_("Et", k + es, w))):
+                    term(t_("t" + n, s, 512), ix, o(s, 512), n in S)
+                    gr = []
+                    for x in range(4 * c, 4 * c + 4):
+                        gr += reduce(P(2, 256 + 2 * x, 384, 16), [(t_("t" + n, 128 * x, 128), 1)] + [(o(128 * x, 128), 1)] * (n in S))
+                    mm([gr], False, c == 1 and n == "F")
+            mov("sP", W("sP%d" % t), P(2, 256, 384), -1600.0)
+            remote("rs", 2 * t + b, N("rP%d" % t), 32, N("sP%d" % t))
+
+        def index(t):
+            p = t % 2; row = 4 + 3 * b + t
+            w = 32 if t else 16; st = 2 if t else 1
+            part = lambda x, k: W(("sP%d" if x == r else "rP%d") % t, w * x + k, w * x + w, st)
+            L = P(1, 0, 16)
+            if t:
+                o = 256 * (1 - p)
+                mm([[(P(0, 0, 128), V("idb"), V("zb", 0, 128))] + [(P(0, a, 128, 8), Rh(a), part(r, 0)) for a in range(8)]], last=False)
+                mm([[(P(0, a, 128, 8), Rh(a), part(x, 0)) for x in others for a in range(8)]], first=False)
+                mov("wI", W("wI", o, o + 128), P(0, 0, 128))
+            tt(W("gI"), IND(W("wI", 128 * (1 - p), 128 * (1 - p) + 256), W("uP", 0, 16)), W("maskE"), MUL)
+            if t:
+                mm([[(L, V("nidh"), part(x, 1)) for x in [r] + others]], last=False)
+                mm([[(P(1, 8 * R, 8 * R + 8), blk(N("gI"), R), V("blkf")) for R in range(2)]], first=False)
             else:
-                mx(t_("tG"), t_("Xt"), t_("Et"))
-            mm([[(P(5, x, 128, 16), l, sg) for l, sg in ((blk("tA", x), PLUS), (blk("tB", x), PLUS), (blk("tC", x), MINUS),
-                 (V("zt", 17 + 256 * x, 272 + 256 * x, 2), MINUS), (blk("tD", x), MINUS), (blk("tF", x), MINUS), (blk("tG", x), PLUS))
-                 + (((V("zt", 16 + 256 * x, 271 + 256 * x, 2), PLUS),) if c in B0 else ()) + (((blk("Xt", x), PLUS),) if c in G0 else ())]
-                for x in range(4 * c, 4 * c + 4)])
-        act(V("sP0"), P(5, 0, 128))
-        remote("rs", 0, "rP0", 32, HOP, "sP0")
+                mm([[(L, V("nidh"), part(r, 0))] + [(P(1, 8 * R, 8 * R + 8), blk(N("gI"), R), V("blkf")) for R in range(2)]], last=False)
+                mm([[(L, V("nidh"), part(x, 0)) for x in others]], first=False)
+            mv = W("TM", row, 256, 16)
+            ts(mv, L, 0.0, None, A.is_lt)
+            mm([[(P(0, 128 + 128 * R, 256 + 128 * R), blk(N("TM"), R), V("idb"))] for R in range(2)])
+            mov("rowsM", W("rowsM"), P(0, 128, 384))
+            cp(IND(V("WG"), W("uq")), W("rowsM"))
+            PO = P(1, 16, 32)
+            mm([[(PO, V("idh"), V("c2", 16 * p, 16 * p + 16))] + ([(PO, V("nidb"), mv)] if p == 0 else [])], last=False)
+            mm([[(P(2, cc, cc + 1), V("WG", 256 * cc + 1 - p, 256 * cc + 256, 2), col("Mi", row))] for cc in range(16)])
+            c1, cb = W("cum", 8, 24), W("cum", 7, 23)
+            op("v", ("tensor_tensor_scan", (c1, P(2, 0, 16), mv, 0.0, ADD, SUB), {}))
+            mm([[(PO, V("LT"), c1), (PO, V("GE"), cb)]], first=False)
+            nE, nO = W("nt", 0, 16), W("nt", 16, 32)
+            mov("nO", nO, PO)
+            ts(W("uO"), nO, 2047.0, None, ADD)
+            cp(IND(W("W2"), W("uO")), W("rows", 256, 512))
+            mm(rep(0, 0, nO))
+            mov("wNo", W("wN", 128 * (1 - p), 128 * (1 - p) + 128), P(0, 0, 128))
+            tt(W("gP"), IND(W("wN"), W("uP", 0, 16)), W("maskE"), MUL)
+            stay = lambda o, u, d: [(o, u, nO)] + ([(o, u, c1), (o, d, cb)] if p else [(o, d, V("two"))])
+            mm([stay(P(1, 48, 64), V("idh"), V("nidh"))])
+            mm([stay(P(1, 32, 48), V("nidh"), V("idh"))], last=False)
+            mm([[(P(1, 32 + 8 * R, 40 + 8 * R), blk(N("gP"), R), V("blkh")) for R in range(2)]], first=False)
+            tt(W("s1"), P(1, 32, 48), mv, MUL)
+            tt(nE, P(1, 48, 64), W("s1"), ADD)
+            ts(W("uE"), nE, 2048.0, None, ADD)
+            cp(IND(W("W2"), W("uE")), W("rows", 0, 256))
+            mm(rep(3, 0, nE))
+            mov("wNe", W("wN", 128 * p, 128 * p + 128), P(3, 0, 128), 1.0)
+            E = N("rE%d" % t)
+            if t < 2:
+                pn = 1 - p
+                mm([[(P(2, 32 + 16 * k + cc, 128, 32), W("W2", 256 * cc + pp, 256 * cc + 256, 2), V("sel", 3 * t, 3 * t + 3))]
+                    for k, pp in ((0, pn), (1, 1 - pn)) for cc in range(16)])
+                mov("l1", W("l1"), P(2, 32, 128), -10240.0)
+                mm(rep(1, 256, W("l1", 48 - 16 * (1 - t), 64)))
+                mm(rep(0, 0, W("l1", 0, 32)))
+                mov("wL2", W("wL", 256 + 128 * t, 512), P(1, 256, 512 - 128 * t))
+                mov("wL1", W("wL", 0, 256), P(0, 0, 256))
+                mov("rE", V(E, 48 * r, 48 * r + 48), IND(W("wL"), cS))
+                remote("ag", 2 * t + b, E, 48)
+                if t == 0:
+                    mov("VP", W("VP", 0, 64), IND(W("wL"), cP2), 10240.0)
+                    split(W("VP", 0, 64), 4)
+                else:
+                    mov("VP", W("VP", 0, 32), IND(W("wL", 0, 256), cP0), 10240.0)
+                    split(W("VP", 0, 32), 10)
+                ts(W("qa"), W("l1", 64, 96), 2048.0, 4097.0, ADD, MUL)
+            else:
+                mm([[(P(2, 32 + cc, 33 + cc), blk(N("W2"), cc), col("sel", 6))] for cc in range(32)])
+                mov("l1", W("l1", 0, 32), P(2, 32, 64), -10240.0)
+                mm(rep(0, 0, W("l1", 0, 32)))
+                mov("wL1", W("wL", 0, 256), P(0, 0, 256))
+                mov("rE", V(E, 32 * r, 32 * r + 32), IND(W("wL", 0, 256), cF))
+                remote("ag" if b else "hx", 6 - b, E, 32)
+                mm([[(P(1, 64 + y, 65 + y), W("W2", y, 4096, 32), col("sel", 7))] for y in range(32)])
+                mov("l1q", W("l1", 32, 64), P(1, 64, 96), -10240.0)
+                mm(rep(3, 256, W("l1", 32, 64)))
+                mov("wL2", W("wL", 256, 512), P(3, 256, 512))
+                ts(W("qa"), IND(W("wL", 256, 512), cP0), 2048.0, 4097.0, ADD, MUL)
+            fields(W("qa"), 32, "qb", "uN")
+            mov("mask1", W("mask1"), IND(V("Mi"), W("uN", 32, 64)))
+            tt(W("gQ"), IND(W("wN"), W("uN", 0, 32)), W("mask1"), MUL)
+            mm([[(P(3, 8 * k, 8 * k + 8), blk(N("gQ"), k), V("blkh"))] for k in range(4)])
+            if t < 2:
+                prep(t + 1, P(3, 0, 32), 2047.0)
+            else:
+                mov("rX", W("rX2", 32 * r, 32 * r + 32), P(3, 0, 32))
+                remote("hx", 4 + b, N("rX2"), 32)
+                mov("qf", W("qf"), W("rX2"), 2047.0)
+                dma([(W("qf", 32 * x, 32 * x + 32), 0, 128, "yq", 4 * b + x, 1, 0, 4096) for x in range(4)], False, 2500, b == 1)
 
-    def shuffle(bank, n, w, halo):
-        mm([[(P(bank, w * v, w * v + w), RS(v, s), V(n, w * s, w * s + w)) for s in range(4)] for v in range(4)]
-           + ([[(P(bank, 4 * w, 4 * w + 2), RS(0, s), V(n, w * s, w * s + 2)) for s in range(4)]] if halo else []))
+        def final():
+            E = N("rE2")
+            mm([[(P(2, 32 * v, 32 * v + 32), RS(v, x), V(E, 32 * x, 32 * x + 32)) for x in [r] + others] for v in range(4)])
+            ts(W("LY"), P(2, 0, 128), zc, None, ADD)
+            for c in range(4):
+                (cp if PAR["fin"][c] == "v" else act)(W("yt", 512 * c, 512 * c + 512), IND(ZW, W("LY", 32 * c, 32 * c + 32)))
+                if c % 2:
+                    dma([(W("yt", 512 * c - 512, 512 * c + 512), 64 * hf, 64, "yz", 64 * b, 64, 2048 * hf + 512 * c - 512, 1024) for hf in range(2)], False, 3000, b + c == 4)
 
-    def coords(t):
-        es = 1 - t % 2
-        shuffle(0, "rE%d" % (t - 1), 64, True)
-        ts(V("LO", 0, 129), P(0, 1, 258, 2), 2048.0, None, ADD)
-        ts(V("LE", 0, 129), P(0, 0, 258, 2), 2048.0, None, ADD)
-        shuffle(5, "rX%d" % (t - 1), 32, False)
-        ts(V("LX"), P(5, 0, 128), 2048.0, None, ADD)
-        for c in range(4):
-            s = 512 * c; y = 528 * c; t_ = lambda n: V(n, s, s + 512)
-            (cp if c in OV else act)(V("Ot", y, y + 528), IND(ZW, V("LO", 32 * c, 32 * c + 33)))
-            act(V("Et", y, y + 512 + 16 * es), IND(ZW, V("LE", 32 * c, 32 * c + 32 + es)))
-            o0, o1, e = V("Ot", y, y + 512), V("Ot", y + 1, y + 513), V("Et", y + es, y + es + 512)
-            mx(t_("tA"), o0, e)
-            if c in BV:
-                mx(t_("tB"), o1, e)
-            (cp if c in XV else act)(t_("Xt"), IND(ZW, V("LX", 32 * c, 32 * c + 32)))
-            mx(t_("tD"), t_("Xt"), o0); mx(t_("tF"), t_("Xt"), e)
-            mm([[(P(5, x, 128, 16), l, sg) for l, sg in ((blk("tD", x), PLUS), (blk("tF", x), PLUS), (blk("tA", x), MINUS))] for x in range(4 * c, 4 * c + 4)])
-        act(V("sP%d" % t), P(5, 0, 128), bias=-1600.0)
-        remote("rs", t, "rP%d" % t, 32, HOP, "sP%d" % t)
-        sh = lambda n, x: V(n, 128 * x - es, 128 * x + 128 - es)
-        for c in ((3, 0, 1, 2) if es else range(4)):
-            s = 512 * c; y = 528 * c; t_ = lambda n: V(n, s, s + 512)
-            o0, o1, e = V("Ot", y, y + 512), V("Ot", y + 1, y + 513), V("Et", y + es, y + es + 512)
-            if c not in BV:
-                mx(t_("tB"), o1, e)
-            relu(t_("tC"), 2 + c % 2, o0 if es else o1, o1 if es else o0)
-            if es and c == 3:
-                for n in "ABC":
-                    cp(col("h" + n, 15), col("t" + n, 2047))
-            xs = [x for x in range(4 * c, 4 * c + 4) if not (es and x == 12)] + ([12] if es and c == 2 else [])
-            mm([[(P(4, x, 128, 16), l, sg) for l, sg in ((sh("tA", x), PLUS), (sh("tB", x), PLUS), (sh("tC", x), MINUS),
-                 (V("Ot", 128 * x + 16 * (x // 4), 128 * x + 16 * (x // 4) + 128), MINUS))] for x in xs])
-        act(V("sR%d" % t), P(4, 0, 128), bias=-1600.0)
-        remote("rr", t, "rR%d" % t, 32, HOP, "sR%d" % t)
+        return [start, coords0, prep0, lambda: index(0), lambda: coords(1), lambda: index(1), lambda: coords(2), lambda: index(2), final]
 
-    def rep(bank, lo, n, rhs, aa=range(8)):
-        return [[(P(bank, lo + n * k, lo + n * k + nel(rhs)), blk("Rh", a), rhs)] for k, a in enumerate(aa)]
-
-    def index(t):
-        p = t % 2; c0 = 2048.0 - p
-        sP, rP, W2 = "sP%d" % t, "rP%d" % t, "win2%d" % t
-        part = lambda x: V(sP if x == r else rP, 32 * x, 32 * x + 32)
-        rem = lambda x: V(("sR%d" if x == r else "rR%d") % t, 32 * x, 32 * x + 32)
-        order = [r] + others; L = P(1, 0, 32)
-        if t == 0:
-            mm([[(L, V("nidh"), part(x)) for x in order]])
-        else:
-            for b in range(2):
-                wa = lambda a: P(2 * b, 32 * (a % 4), 32 * (a % 4) + 32)
-                mm([[(P(2 * b, 0, 128), V("nidh"), V("zero", 0, 128))] + [(wa(a), blk("Rh", a), part(r)) for a in range(4 * b, 4 * b + 4)]], last=False)
-            for b in range(2):
-                wa = lambda a: P(2 * b, 32 * (a % 4), 32 * (a % 4) + 32)
-                mm([[(wa(a), blk("Rh", a), part(x)) for a in range(4 * b, 4 * b + 4) for x in others]], first=False)
-                (cp if b else act)(V("wI", 128 * b, 128 * b + 128), P(2 * b, 0, 128))
-            tt(V("gI"), IND(V("wI"), V("offO")), V("maskE"), MUL)
-            mm([[(L, V("nidh"), V("zero", 0, 32))] + [(P(1, b, 32, 4), blk("gI", b), V("blkf")) for b in range(4)]], last=False)
-            mm([[(L, V("nidh"), rem(x)) for x in order]], first=False)
-        tt(V("mv"), L, V("pen"), A.is_lt)
-        tt(V("d1"), V("mv"), V("md"), MUL)
-        tt(V("d2"), V("d1"), V("dump"), ADD)
-        cp(V("ud"), V("d2"))
-        cp(IND(V("win1"), V("ud")), V("ones"))
-        mm(rep(2, 0, 32, V("mv")))
-        act(V("wM"), P(2, 0, 256))
-        act(V("mvL"), IND(V("wM"), cL2))
-        mm([[(P(3, j, j + 1), blk("win1", j), col("e0", 0))] for j in range(32)])
-        if t < 2:
-            dma("sy", [(V("win1", 0, 4096), 16 * u, 1, V("win3"), 16 * u + 8, 1, 0, 0) for u in range(8)], True, 2500)
-        c1, cb = V("cum", 1, 33), V("cum", 0, 32)
-        op("v", ("tensor_tensor_scan", (c1, P(3, 0, 32), V("mv"), 0.0, ADD, A.subtract), {}))
-        if p == 0:
-            act(V("nv"), V("mv"), scale=-1.0)
-            mm([[(P(0, 0, 256), V("nidh"), V("zero"))] + [(P(0, 32 * a, 32 * a + 32), blk("Rh", a), V("nv")) for a in range(8)]], last=False)
-            mm([[(P(0, 32 * a, 32 * a + 32), blk(n, a), x) for a in range(8) for n, x in (("LT", c1), ("GE", cb))]], first=False)
-        else:
-            mm([[(P(0, 32 * a, 32 * a + 32), blk(n, a), x) for n, x in (("LT", c1), ("GE", cb))] for a in range(8)])
-        tt(V("wP"), P(0, 0, 256), V("cPO"), ADD)
-        tt(V("gP"), IND(V("wP"), V("offO")), V("maskE"), MUL)
-        ts(V("uO"), IND(V("wP"), cL2), c0, None, ADD)
-        cp(IND(V(W2), V("uO")), V("rowsO"))
-        if p == 0:
-            act(V("pe"), IND(V("wP"), cL2), bias=-2.0)
-        else:
-            tt(V("nv"), c1, cb, A.subtract)
-            mm(rep(2, 0, 32, V("nv")))
-            act(V("wV"), P(2, 0, 256))
-            act(V("vL"), IND(V("wV"), cL2))
-            tt(V("pe"), IND(V("wP"), cL2), V("vL"), ADD)
-        mm([[(L, Col(i), V("gP", i, 512, 16)) for i in range(16)]])
-        tt(V("s1"), L, V("pe"), A.subtract)
-        tt(V("s2"), V("s1"), V("mvL"), MUL)
-        tt(V("s3"), V("s2"), V("pe"), ADD)
-        ts(V("uE"), V("s3"), c0 + 1, None, ADD)
-        cp(IND(V(W2), V("uE")), V("rowsE"))
-        act(V("ntab", 0, 32), V("s3"), bias=c0 - 2047.0)
-        act(V("ntab", 32, 64), IND(V("wP"), cL2), bias=c0 - 2048.0)
-        E, Xr = "rE%d" % t, "rX%d" % t; w = 64
-        if t < 2:
-            pn = 1 - p
-            mm([[(P(3, 96 * k + cc, 96 * k + 96, 16), V(W2, 256 * cc + pp, 256 * cc + 256, 2), V("sel", 4 * k, 4 * k + 6))]
-                for k, pp in ((0, pn), (1, 1 - pn)) for cc in range(16)])
-            act(V("l1"), P(3, 0, 192), bias=-2048.0)
-            for b in range(2):
-                mm(rep(b, 0, 96, V("l1", 64, 160), range(4 * b, 4 * b + 4)))
-                (cp if b else act)(V("wL", 384 * b, 384 * b + 384), P(b, 0, 384))
-            cp(V(E, w * r, w * r + w), IND(V("wL"), cEO))
-            act(V(Xr, 32 * r, 32 * r + 32), IND(V("wL"), cX))
-            remote("ag", t, E, w, HOP)
-            remote("hx", t, Xr, 32, 1.7 * HOP)
-            mm(rep(7, 0, w, V("l1", 0, 32)) + rep(7, 32, w, V("l1", 160, 192)))
-        else:
-            mm([[(P(3, cc, w, 32), blk(W2, cc), V("sel", 4, 6))] for cc in range(32)])
-            act(V("l1", 0, w), P(3, 0, w), bias=-2048.0)
-            mm(rep(0, 0, w, V("l1", 0, w)))
-            act(V("wL", 0, 512), P(0))
-            act(V(E, w * r, w * r + w), IND(V("wL", 0, 512), cF))
-            remote("ag", t, E, w, HOP)
-            mm([[(P(2, y, w, 32), V(W2, y, 4096, 32), V("sel", 0, 2))] for y in range(32)])
-            act(V("l1", w, 2 * w), P(2, 0, w), bias=-2048.0)
-            mm(rep(7, 0, w, V("l1", w, 2 * w)))
-        act(V("wQ"), P(7))
-        ts(V("qo"), IND(V("wQ"), cQ if t < 2 else cF), 2048.0, None, ADD)
-        mm([[(P(6, w * qt, w * qt + w), blk("RQ", qt), V("ntab"))] for qt in range(4)])
-        act(V("wN"), P(6, 0, 256))
-        ts(V("n1"), V("qo"), 1, 15, SHR, AND); cp(V("lo1"), V("n1"))
-        ts(V("n2"), V("qo"), 4, 0xC0, SHR, AND)
-        ts(V("n3"), V("qo"), 5, 31, SHR, AND)
-        ts(V("n4"), V("qo"), 1, None, AND)
-        ts(V("n5"), V("n4"), float(p), 32.0, A.not_equal, MUL)
-        tt(V("n2"), V("n2"), V("n3"), ADD); tt(V("n2"), V("n2"), V("n5"), ADD); cp(V("offN"), V("n2"))
-        for k in range(2):
-            m_ = V("mask1", 512 * k, 512 * k + 512)
-            masks(7 - k, V("lo1", 32 * k, 32 * k + 32), m_)
-            tt(V("gQ", 512 * k, 512 * k + 512), IND(V("wN"), V("offN", 32 * k, 32 * k + 32)), m_, MUL)
-        if t < 2:
-            mm([[(P(6, 0, w), Col(i), V("gQ", i, 1024, 16)) for i in range(16)]] + [[(P(6, 64 + j, 96, 4), blk("gQ", j), V("blkh"))] for j in range(4)])
-            ts(V("qn"), P(6, 0, w), 2048.0, None, ADD)
-            ts(V("q1"), P(6, 64, 96), 2048.0, None, ADD)
-            prep(1 - p, W2)
-        else:
-            mm([[(P(6, j, w, 8), blk("gQ", j), V("blkh"))] for j in range(8)])
-            cp(V(Xr, w * r, w * r + w), P(6, 0, w))
-            remote("hx", t, Xr, w, 1.7 * HOP)
-            ts(V("qf"), V(Xr), 2048.0, None, ADD)
-            for e, q in enumerate(("sy", "s")):
-                dma(q, [(V("qf", 32 * j, 32 * j + 32), 0, 128, "yq", j, 1, 0, 4096) for j in range(e, 8, 2)], False, 2500)
-
-    coords0(); index(0); coords(1); index(1); coords(2); index(2)
-    shuffle(0, "rE2", 64, False)
-    ts(V("LY"), P(0, 0, 256), 2048.0, None, ADD)
-    for c in range(8):
-        (cp if c % 2 else act)(V("yt", 512 * c, 512 * c + 512), IND(ZW, V("LY", 32 * c, 32 * c + 32)))
-        if c % 2 and c < 6:
-            dma("sy", [(V("yt", 512 * c - 512, 512 * c + 512), 0, 128, "yz", 0, 128, 512 * c - 512, 1024)], False, 3200)
-        elif c >= 6:
-            dma("sy", [(V("yt", 512 * c, 512 * c + 512), 0, 128, "yz", 0, 128, 512 * c, 512)], False, 2900)
+    for steps in zip(batch(0), batch(1)):
+        for b in range(2):
+            mark[0] = 1 - b
+            steps[b]()
     return ops
 
 
-def schedule(ops):
+def depend(ops):
     n = len(ops); deps = [set() for _ in range(n)]; acc = {}; bank = {}
     home = {(b, c): o for (b, o, w) in AL.values() for c in range(o // 16, (o + w + 15) // 16)}
     for j, (eng, kind, _, rd, wr) in enumerate(o[:5] for o in ops):
@@ -510,26 +490,14 @@ def schedule(ops):
                     key = (nm, home[(nm, lo // 16)]); old = acc.get(key, [])
                     deps[j].update(i for (i, l2, h2, w2) in old if (isw or w2) and lo < h2 and l2 < hi and i != j)
                     acc[key] = [x for x in old if not (isw and lo <= x[1] and x[2] <= hi)] + [(j, lo, hi, isw)]
-    succ = [[] for _ in range(n)]
-    for j in range(n):
-        for i in deps[j]:
-            succ[i].append(j)
-    hold = lambda j: ops[j][5] if ops[j][1] == "c" else (100.0 * len(ops[j][2][1]) if ops[j][1] == "d" else 300.0)
-    rank = [0.0] * n; key = [0.0] * n
-    for j in range(n - 1, -1, -1):
-        rank[j] = ops[j][5] + max([rank[k] + LAT for k in succ[j]] + [0.0])
-        key[j] = max([rank[j] + ops[j][6]] + [key[k] + 1.0 for k in succ[j]])
-    start = [0.0] * n; fin = [0.0] * n; busy = {}
-    for j in sorted(range(n), key=lambda j: (-key[j], j)):
-        t0 = max([fin[i] + (0.0 if ops[i][0] == "t" and ops[j][0] == "t" else LAT) for i in deps[j]] + [0.0])
-        b = busy.setdefault(ops[j][0], [])
-        for (s, e) in b:
-            if t0 + hold(j) <= s:
-                break
-            t0 = max(t0, e)
-        start[j] = t0; fin[j] = t0 + ops[j][5]
-        b.append((t0, t0 + hold(j))); b.sort()
-    return deps, sorted(range(n), key=lambda j: (start[j], j)), start, fin
+    return deps
+
+
+def common_order(ops):
+    al = "0123456789abcdefghijklmnopqrstuvwxyzABCDEFGHIJKLMNOPQRSTUVWXYZ"
+    o = [62 * al.index(ORDER[k]) + al.index(ORDER[k + 1]) for k in range(0, len(ORDER), 2)]
+    first = [j for j in range(len(ops)) if ops[j][1] == "d" and ops[j][2][0] and not ops[j][3]]
+    return first + [j for j in o if j not in first]
 
 
 def helper_of(T, topo, c):
@@ -548,6 +516,11 @@ def mask_to_others(T, topo, src, r):
         if x != r:
             m &= topo.mask(src, T.cores[x])
     return m
+
+
+def mask_to_helper(T, topo, r):
+    c = T.cores[r]
+    return topo.mask(c, helper_of(T, topo, c)) & ~mask_to_others(T, topo, c, r)
 
 
 def bits(m):
@@ -570,6 +543,8 @@ def rank_program(g, core, T, topo):
             return x
         if x[0] == "I":
             return ap(x[1]).indirect(ap(x[2]))
+        if len(x) > 5:
+            return T[x[1]][x[5]:x[5] + 64, x[2]:x[3]]
         return T[x[1]][:, x[2]:x[3]] if x[4] == 1 else T[x[1]][:, x[2]:x[3]:x[4]]
 
     def spread(src, dst, r, m, sem):
@@ -577,20 +552,23 @@ def rank_program(g, core, T, topo):
         g.remote_dma_fused([RemoteDMATransfer(dst_ids=[dst_id(topo, T.cores[x]) for x in oth], dma_engine_mask=m, remote_sem=sem,
                                               srcs=[ap(src)], dsts=[ap(dst) for x in oth])], local_sem=S.loc)
 
+    hbuf = lambda t: V("hX%d" % t)
     for r in range(4):
         if core == helper_of(T, topo, T.cores[r]):
-            m = mask_to_others(T, topo, core, r)
-            for t in range(3):
-                w = AL["hX%d" % t][2]
-                g.wait_ge(S["hi%d" % t], bits(topo.mask(T.cores[r], core)))
-                spread(V("hX%d" % t), V("rX%d" % t, w * r, w * r + w), r, m, S["hx%d" % t])
-            g.wait_ge(S.loc, 3 * bits(m))
+            m = mask_to_others(T, topo, core, r); ops = plan(r); n = 0
+            for j in common_order(ops):
+                if ops[j][1] == "r" and ops[j][2][0] == "hx":
+                    t = ops[j][2][1]
+                    g.wait_ge(S["hi%d" % t], bits(mask_to_helper(T, topo, r)))
+                    spread(hbuf(t), ops[j][2][3], r, m, S["hx%d" % t]); n += 1
+            g.wait_ge(S.loc, n * bits(m))
             return
     r = T.rank_of(core)
     if r is None:
         return
-    ops = plan(r)
-    deps, order = schedule(ops)[:2]
+    ops = plan(r); deps = depend(ops); order = common_order(ops)
+    pos = {j: k for k, j in enumerate(order)}
+    assert len(pos) == len(ops) and all(pos[i] < pos[j] for j in range(len(ops)) for i in deps[j])
     oth = [x for x in range(4) if x != r]
     QU = {"v": g.vector, "t": g.tensor, "s": g.scalar, "gp": g, "sy": g.sync}
     needed = set(i for j in range(len(ops)) for i in deps[j] if not (ops[i][0] == "t" and ops[j][0] == "t"))
@@ -604,7 +582,7 @@ def rank_program(g, core, T, topo):
             sig[j] = ("d%d" % nd, 16 * len(pay[1])); nd += 1
         else:
             snd = lambda x: T.cores[x] if pay[0] == "ag" else helper_of(T, topo, T.cores[x])
-            sig[j] = ("%s%d" % pay[:2], sum(bits(rs_masks(T, topo, x)[r] if pay[0] in ("rs", "rr") else mask_to_others(T, topo, snd(x), x)) for x in oth))
+            sig[j] = ("%s%d" % pay[:2], sum(bits(rs_masks(T, topo, x)[r] if pay[0] == "rs" else mask_to_others(T, topo, snd(x), x)) for x in oth))
 
     def call(q, m, a, kw):
         f = {"matmul": lambda: q.matmul, "tensor_scalar": lambda: q.tensor_scalar, "tensor_tensor": lambda: q.tensor_tensor,
@@ -618,21 +596,23 @@ def rank_program(g, core, T, topo):
         for i in deps[j]:
             if not (ops[i][0] == "t" and eng == "t"):
                 nm, c = sig[i]; want[nm] = max(want.get(nm, 0), c)
-        for nm, c in sorted(want.items()):
-            if waited.get((eng, nm), 0) < c:
-                q.wait_ge(S[nm], c); waited[(eng, nm)] = c
+        for e in [eng] + (["s"] if kind == "d" and pay[2] else []):
+            for nm, c in sorted(want.items()):
+                if waited.get((e, nm), 0) < c:
+                    QU[e].wait_ge(S[nm], c); waited[(e, nm)] = c
         if kind == "c":
             for m, a, kw in pay:
                 ins = call(q, m, a, kw)
             if j in sig:
                 ins.then_inc(S[eng], 1)
         elif kind == "d":
-            for v, p0, pn, tn, r0, rn, c0, cn in pay[1]:
-                sb, hb = T[v[1]][p0:p0 + pn, v[2]:v[3]], (T[tn[1]][r0:r0 + rn, tn[2]:tn[3]] if isv(tn) else T[tn][r0:r0 + rn, c0:c0 + cn])
+            for k, (v, p0, pn, tn, r0, rn, c0, cn) in enumerate(pay[1]):
+                sb, hb = T[v[1]][p0:p0 + pn, v[2]:v[3]], (ap(tn) if isv(tn) else T[tn][r0:r0 + rn, c0:c0 + cn])
+                q = g.scalar if pay[2] and k % 2 else g.sync
                 (q.dma_start(sb, hb) if pay[0] else q.dma_start(hb, sb)).then_inc(S[sig[j][0]], 16)
         else:
             k, t, srcs, dst = pay; sem = S[sig[j][0]]
-            if k in ("rs", "rr"):
+            if k == "rs":
                 mk = rs_masks(T, topo, r)
                 g.remote_dma_fused([RemoteDMATransfer(dst_ids=[dst_id(topo, T.cores[x])], dma_engine_mask=mk[x], remote_sem=sem, src=ap(a), dst=ap(dst))
                                     for x, a in zip(oth, srcs)], local_sem=S.loc)
@@ -640,8 +620,8 @@ def rank_program(g, core, T, topo):
             elif k == "ag":
                 m = mask_to_others(T, topo, core, r); spread(srcs[0], dst, r, m, sem); loc += bits(m)
             else:
-                hc = helper_of(T, topo, core); rid, pid, _ = topo.addr(hc); m = topo.mask(core, hc)
-                g.remote_dma(ap(V("hX%d" % t)), ap(srcs[0]), S["hi%d" % t], S.loc, pid, rid, m)
+                hc = helper_of(T, topo, core); rid, pid, _ = topo.addr(hc); m = mask_to_helper(T, topo, r)
+                g.remote_dma(ap(hbuf(t)), ap(srcs[0]), S["hi%d" % t], S.loc, pid, rid, m)
                 loc += bits(m)
     done = {}
     for nm, c in sig.values():

@@ -1,32 +1,29 @@
 from concourse.mybir import AluOpType as A, ActivationFunctionType as F
 from concourse.bass import DstId, RemoteDMATransfer
 
-PAR = {
-    "S": ("BC", "BC", "BC", "BC"),
-    "X": "ffff",
-    "S0": ("BCD", "BCD"), "X0": "ss",
-    "fin": "svsv", "onv": ("rE",),
-}
-ORDER = "000c0s0Z01021x0d2S1t0e070m0l0p060z0q0j0n080k0o0t0r0B0Q0A0H0u0E0S0Y0V0U1A0W0R0X0T1r0x0y180J1n041O1p1B190I1F1Q1N1P2V1G1R1H1I1U1z1a1b1o1c2W1h1d1V1e05030w1T1W2X1Z0g2Y1f1y1g1i1q223q1j201k1l0v1J1C2j3t282k1u242Z1K2m301X310a330f341M0O353u0C0K290D230N2b0L1S0M0b2U1L1Y090P1m3v1D2T1s1v3w3x321w212Q2d1E372a2c2R2526273z383y2e2p2P2f2g36392l0h0i3A2h3a3F2n2i2q3G2s0F3V3b2v0G3C3B3r3D2H3s3W3H2o3o2t3n3X3I2r3c2y123d3Y2I2w113Z2E3J102A142z402F132x412u3p3e2B152C3f2D2J2G433g2K16443h423E452L3i2M3j463k2N4O493K2O173l4a474c4d3L3m4b4P3M4e483N3O3P4Q4f4g4h4j4i4k4R3Q4S4l3R4T3S4U3T4m4V4o4n4w4q4y4W4x4p4z3U4r4X4s4Y4Z4t50524u515556534A545H4v575I5J585M595a5c5b5L4B5e5S5K635N5f5d5P5O5R5g5h5Q655U5T4C5Z615j5W5i5Y5V5k675X5l5m604D4E5n4G4H4F4I624K5p644J665q5r685s4L6b695o5t6a6F6d6e4M6c6g5u6f6x5v6G6n6v6j6h6H6l6m6J6I6i6s6K6k6L6z6M6o6N6P6q6p6O6t6r6B4N6Q6u6R5w6S5A6w5z6y6T5B6A6C6U6W6V6D6Z706X6E7B5C6Y5x715y725D7374757C7F7D5E787E7G795F7H7j7I7k7b7l7J7m7a7d7L767K7c5G7n7e7M7f7N777O7P7g7Q7S7h7R7V7W7T8x7U8y8A7X8z8B7Y7Z8082818C8D8R848I8T8J8F7o858E87868H898K888f8G7p8h8g8a8i8V8b8L8M8P8N8O838X8Q8j8S8U7q8W8Y7t8c917u8Z7v7r7i7w909v927s8k9594938l9c979l9w969p9z98999b9d9n9e9a9i9x8m9g8n7x9y9f9j7y8q9h8p9A8r7z9B8d9r8o9C9k9D7A9m9E9o9q9s9F9t8s9uaj8e9G8t8u8v9H9I9J9K9M9L9P9Q9Nak8wan9Oalam9R9Sao9T9U9Wap9Vaqatar9Xasa4aua5a6avaw9Yaxa7ayazaA9ZaDaEaBa0aCa1a2aFa8a3aGaHaIaKaJaLa9aaaSabacaMaTadaUaNaVaOaeb7aPaWaXafaYaZagaQb8b0aRb9b1bab2b3bfbcb4bbbgbdahbkaiblbhbibebmbjb5b6"
+PAR = {"S": ("BCX",) * 8, "S0": ("BCD", "BC")}
+ONV = "10101100100000001100100001011110000001111001000101100000101000111100101010101111010101111000011001110011001010001111011100010000100010001100100101100011110101100001101000110"
+ORDER = "000102030405060708090a0i0j0l0k0x0s0o0E0t0q0r0p0v0u1D2R0h0w0G3p0Z0F1E0C0D0I0H0B1F0Q181Q140X161S0A1P1012110y1B0Y151G0W0S1R1j0z1H0R1k171l0U131I1m0T1J1T1n2W2S1K1W1o2X0c0V1p1X2Y302Z1U310b320d3334212a381Y1V242U22392c2b2m251Z2o26232T202e0N272d2n28292f1L2p2g2l3q1M2h2s3r2i1x351N3s0e0g370f0P3u1O3t2u1z3v3a3w0n3T2x0O3C2q0m2r1a2A3b1c3D2j2B2t3c2C2G2y193E3d1b2I3e2V363y3F1h2v2k3U3f2K3G1i3g2H2z3V2J1d3h3W1f2w3X3i0J2D3x3A3j0K2E3Y3H2F2L1q2M1y2N1g3Z3I2O3J2P3k403z1s1r3l3B1A0L3m410M3K423n1t434P1u3L461e443o494a473N48452Q4Q4b4c4R3M4d4S3O4g4e4T3P4V4f4h4u4U4i3Q4j4W1v1C1w4t4k4X4v4l4m4Y3R4n4Z4w52503S4o55564q4p5L534r545157584s595a5M5c5N5b5Q5O5X5d5S5R5e5T5P5Y5U665Z6b5V5f60695h5g5j67615i634x5k4y5W5l6i626c4A644z4B5p654C6e686a6d4D4E5m6f5r5q4I4F6g4H4J6h6j4G4K6P5s6k4L5n6S6u6n6Z6l4M6p6v6m6o4N6Q6I5o6A6T6r6R6q6W4O6w6U6D6L6V6X6t6x6Y706J6s716G72756E6y766B736z777879747a6C5v6F6H6K6M7b7c6N5t7d6O7P7e7f7Z5u7h7g7t5w7i5x7k7s5y7j7u5A7m5z7Q7v7l5B7n5C5E7o7R8P5F7p5D7U5G7S7W7T7V5H7q7X5I7r7Y5J805K8Q818R828U8S918588898692838W8T87848V8a8b9a8Y8c8d8f8e8X9f908h978Z938i9i8j948k9b958m988l968g8n9d8o9m7w999g7x9c9e7y9h9j7z9k8t7A8s9la37B8u7H7C7D8v7E7I9n7F7G9T9o7J7K9W9r9p7L9q7M9H7N9s9U8p9I9t9M9V9X9v8qa09y9Y9x9Z9ua19z9w9Aa28r9Ba4a59Ka69Ca79E9Daa9F9N7O9G9P9Jab9L9Oa8adac9Qae9R8xa99SafaE8waO8yag8z8Aah8Bakai8C8HajaF8D8I8E8J8K8G8FasaG8LaJamataLaH8MalanaIaKaMaoaN8NaQaPap8OaRauaSaqaVaTaraYaZbraUaWavaXawb0axb1b2b5b3b4b6bdaybeazaAbfaBb7bgbsbhb8bib9btbabkbbbxbjbcbAblbybmbnbvbobubzaCbBbwbCbHbGaDbEbDbFbIbpbq"
 
 BF, HF, FP, I32, U16 = "bfloat16", "float16", "float32", "int32", "uint16"
 PER = {
     "zt": (6160, BF), "yt": (2048, BF), "Et": (1056, BF), "Ot": (1056, BF), "Xt": (1024, BF),
     "tA": (1040, BF), "tB": (1024, BF), "tC": (1024, BF), "tD": (1024, BF), "tF": (1024, BF), "tG": (1024, BF),
     "LE": (66, U16), "LO": (66, U16), "LX": (64, U16), "LY": (128, U16), "W2": (4096, BF), "rows": (512, BF), "rowsM": (256, BF), "rowsI": (512, BF),
-    "TP": (512, BF), "TM": (256, BF), "VP": (96, FP),
+    "TP": (512, BF), "TM": (256, BF), "VP": (128, FP), "TQ": (512, BF), "fl": (32, HF),
     "sP0": (64, HF), "rP0": (64, HF), "sP1": (128, HF), "rP1": (128, HF), "sP2": (128, HF), "rP2": (128, HF),
     "rE0": (192, HF), "rE1": (192, HF), "rE2": (128, HF), "rX2": (128, HF), "qf": (128, FP),
-    "wI": (384, FP), "wN": (256, FP), "wL": (512, FP), "gI": (256, FP), "gP": (256, HF), "gQ": (512, HF), "maskE": (256, HF), "mask1": (512, HF),
-    "cum": (32, HF), "s1": (16, FP), "nt": (32, HF), "uO": (16, U16), "uE": (16, U16), "uq": (16, U16),
-    "l1": (96, HF), "qa": (32, I32), "qb": (64, I32), "uN": (64, U16), "qc": (16, I32), "qd": (32, I32), "uP": (32, U16),
+    "wI": (256, FP), "wN": (256, FP), "wL": (512, FP), "gI": (512, FP), "gP": (256, HF), "gQ": (1024, HF), "maskE": (256, HF), "maskO": (256, HF),
+    "mask1": (512, HF), "cum": (32, HF), "s1": (16, FP), "nt": (32, HF), "uO": (16, U16), "uE": (16, U16), "uq": (16, U16),
+    "l1": (128, HF), "qa": (64, I32), "qb": (128, I32), "uN": (128, U16), "qd": (192, I32), "uP": (128, U16),
     "qi": (128, I32), "qh": (128, HF), "q0h": (32, HF), "uq0": (32, U16),
 }
 BUF = {
     "WG": (4096, BF), "zb": (2048, BF), "TI": (544, BF), "vI": (32, FP), "X": (272, FP), "pi": (16, I32), "pf": (32, FP), "X2": (128, FP),
     "Y": (8, FP), "idb": (128, BF), "nidb": (128, BF), "idh": (128, HF), "nidh": (128, HF), "LT": (128, HF), "GE": (128, HF),
-    "Mr": (128, HF), "Rh": (1024, HF), "RS": (1056, HF), "sq": (512, HF), "grp": (128, HF), "pm": (16, BF), "blkf": (8, FP), "blkh": (8, HF),
-    "Mi": (16, BF), "sel": (10, BF), "Y2": (10, FP), "c2": (32, HF), "c2f": (16, FP), "two": (16, HF), "idc": (32, FP), "ci": (8, I32), "cf": (16, FP),
+    "Mr": (128, HF), "Rh": (1024, HF), "RS": (1056, HF), "sq": (512, HF), "grp": (128, HF), "pm": (48, BF), "Y4": (16, FP), "cb": (128, BF),
+    "blkf": (8, FP), "blkh": (8, HF), "Mi": (16, BF), "Mp": (64, BF), "Y3": (64, FP), "pen": (8, HF), "sel": (8, BF), "Y2": (8, FP), "c2": (32, HF),
+    "c2f": (16, FP), "wD": (4096, FP), "two": (16, HF), "idc": (32, FP), "ci": (8, I32), "cf": (16, FP),
     "cl": (24, U16), "hX4": (32, HF), "hX5": (32, HF), "hX6": (32, HF),
 }
 for _k, _v in PER.items():
@@ -38,7 +35,7 @@ for _k, (_w, _d) in BUF.items():
 SCRATCH = {k: ("sbuf", [128, w], d) for k, (w, d) in SB.items()}
 for _b in range(8):
     SCRATCH["p%d" % _b] = ("psum", [128, 512], "float32")
-SEMAPHORES = ["v", "t", "s", "gp", "loc"] + ["d%d" % k for k in range(20)] + [k + str(t) for k in ("rs", "ag", "hx", "hi") for t in range(7)]
+SEMAPHORES = ["v", "t", "s", "gp", "loc"] + ["d%d" % k for k in range(26)] + [k + str(t) for k in ("rs", "ag", "hx", "hi") for t in range(7)]
 
 
 def V(n, lo=0, hi=None, st=1):
@@ -59,7 +56,7 @@ def isv(a):
 
 
 def plan(r):
-    ops = []; mark = [0]
+    ops = []; mark = [0]; nm = [0]
 
     def spans(x):
         return spans(x[1]) + spans(x[2]) if x[0] == "I" else [(x[1], x[2], x[3])]
@@ -91,13 +88,15 @@ def plan(r):
     def act(o, i, f=None, **kw):
         op("s", ("activation", (o, i, f if f is not None else (F.Identity if kw else F.Copy)), kw))
 
-    def mov(key, o, i, bias=None):
-        if key in PAR["onv"]:
+    def mov(o, i, bias=None):
+        k = nm[0]; nm[0] += 1
+        if ONV[k] == "1":
             cp(o, i) if bias is None else ts(o, i, bias, None, A.add)
         elif bias is None:
             act(o, i)
         else:
             act(o, i, bias=bias)
+        ops[-1] = ops[-1][:5] + (k + 1,) + ops[-1][6:]
 
     def iota(o, pat, base, cm):
         op("gp", ("iota", (o, pat, base, cm), {} if SB[o[1]][1] == I32 else {"allow_small_or_imprecise_dtypes": True}))
@@ -114,10 +113,11 @@ def plan(r):
         rd = spans(items[0][3]) + spans(after) if after else []
         ops.append(("sy", "d", (load, items, split), rd if load else sp, sp if load else [], ns, mark[0]))
 
-    def remote(kind, t, n, w, src=None):
+    def remote(kind, t, n, w, src=None, after=None):
         sl = lambda b, x: V(b, w * x, w * x + w)
         srcs = [sl(src, x) for x in others] if src else [sl(n, r)]
-        ops.append(("gp", "r", (kind, t, srcs, sl(n, r)), [s for x in srcs for s in spans(x)], [s for x in others for s in spans(sl(n, x))], 0.0, mark[0]))
+        ops.append(("gp", "r", (kind, t, srcs, sl(n, r)), [s for x in srcs + ([after] if after else []) for s in spans(x)],
+                    [s for x in others for s in spans(sl(n, x))], 0.0, mark[0]))
 
     col = lambda n, j: V(n, j, j + 1)
     blk = lambda n, a: V(n, 128 * a, 128 * a + 128)
@@ -128,13 +128,27 @@ def plan(r):
     def loads(b):
         n = "zt_%d" % b; z = lambda lo, hi, hf, c0: (V(n, lo, hi), 64 * hf, 64, "z", 64 * b, 64, c0, hi - lo)
         t0 = 3400 + 2900 * b
-        dma([z(2048, 4096, 0, 0), z(2048, 4096, 1, 2048)], True, t0, True)
+        if b == 0:
+            dma([z(3056, 4096, 0, 1008), z(3056, 4096, 1, 3056)], True, t0 - 700, True)
+            dma([z(2048, 3056, 0, 0), z(2048, 3056, 1, 2048)], True, t0, True)
+        else:
+            dma([z(2048, 4096, 0, 0), z(2048, 4096, 1, 2048)], True, t0, True)
         dma([(V("qi_%d" % b), 64 * hf, 64, "q", 64 * b, 64, 128 * hf, 128) for hf in range(2)], True, t0 + 100, True)
         dma([z(4096, 6144, 0, 2048), z(0, 2048, 1, 0)], True, t0 + 1500, True)
-        h = lambda c, hf: V(n, c, c + 1) + (64 * hf,)
-        cp(h(2047, 0), h(6143, 0)); cp(h(6144, 0), h(2048, 0)); cp(h(4096, 1), h(0, 1))
 
+    def zero(n, ns, after):
+        dma([(V(n, 2048 * c, 2048 * c + 2048), 0, 128, V("zb"), 0, 128, 0, 0) for c in range(2)], True, ns, False, after)
+
+    ms(V("zb"), 0.0)
     mark[0] = 1; loads(0); mark[0] = 0; loads(1)
+    zero("WG", 8800, V("zb"))
+    for b in range(2):
+        dma([(V(x + "_%d" % b), 0, 128, V("zb", 0, PER[x][0]), 0, 128, 0, 0) for x in ("TP", "TM", "TQ")], True, 9100 + 100 * b, False, V("zb"))
+    for b in range(2):
+        h = lambda c, hf: V("zt_%d" % b, c, c + 1) + (64 * hf,)
+        mark[0] = 1 - b
+        for o, i in ((h(2047, 0), h(6143, 0)), (h(6144, 0), h(2048, 0)), (h(4096, 1), h(0, 1))):
+            mov(o, i)
 
     iota(V("X"), [[1, 272]], -64, 0)
     X = lambda lo, hi, st=1: V("X", 64 + lo, 64 + hi, st)
@@ -148,7 +162,7 @@ def plan(r):
         ts(col("pi", j + 1), col("pi", 0), sh, an, SHR, AND)
     cp(V("pf", 0, 9), V("pi", 0, 9))
     pf = lambda j: col("pf", j)
-    lin = lambda o, a, c, b: ts(pf(o), pf(a), float(c), b, MUL, ADD)
+    lin = lambda o, a, c, b: act(pf(o), pf(a), scale=float(c), bias=b)
     ms(V("grp"), 1.0)
     sel = lambda o, pat, f, base, cm: op("gp", ("affine_select", (o, V("grp"), pat, f, 0.0, base, cm), {}))
     for k in range(4):
@@ -160,19 +174,23 @@ def plan(r):
     act(V("nidb"), V("idh"), scale=-1.0)
     ts(V("pm", 0, 8), V("Y"), pf(2), None, EQ)
     ts(V("pm", 8, 16), V("Y"), pf(2), -1.0, EQ, MUL)
+    iota(V("Y4"), [[1, 4], [4, 4]], 0, 0); iota(V("cb"), [[0, 4], [3200, 2], [0, 16]], -1600, 0)
+    ts(V("pm", 16, 32), V("Y4"), pf(2), None, EQ)
+    ts(V("pm", 32, 48), V("Y4"), pf(2), -1.0, EQ, MUL)
     act(V("nidh"), V("idh"), scale=-1.0)
     sel(V("LT"), [[1, 128]], A.is_gt, 0, -1)
     sel(V("GE"), [[-1, 128]], A.is_ge, 0, 1)
     ts(V("blkf"), X(0, 8), pf(2), None, EQ)
     ts(V("blkh"), X(0, 8), pf(2), None, EQ)
     ts(V("Mi"), X(0, 16), pf(1), None, EQ)
-    for y in range(3):
-        iota(V("Y2", y, 6, 3), [[2, 2]], (0, 4, 1)[y], 0)
-    iota(V("Y2", 6, 8), [[2, 2]], 5, 0); iota(V("Y2", 8, 10), [[1, 2]], 0, 0)
+    iota(V("Y3", 0, 32), [[1, 16], [-100, 2]], 100, 0); iota(V("Y3", 32, 64), [[1, 16], [100, 2]], 0, 0)
+    ts(V("Mp"), V("Y3"), pf(1), None, EQ)
+    ts(V("pen"), X(0, 8), pf(2), -30000.0, EQ, MUL)
+    iota(V("Y2"), [[2, 2], [1, 2], [4, 2]], 0, 0)
     ts(V("sel"), V("Y2"), pf(7), None, EQ)
     ts(V("Mr"), V("X2"), pf(1), None, EQ)
     for a in range(8):
-        ts(blk("Rh", a), V("Mr"), col("blkf", a), None, MUL)
+        act(blk("Rh", a), V("Mr"), scale=col("blkf", a))
     ms(V("RS"), 0.0)
     for v in range(6):
         sel(V("RS", 176 * v + 48, 176 * v + 176), [[-64 if v < 4 else 64, 2], [1000, 4], [-1, 16]], EQ, -16 * v if v < 4 else 128 - 48 * v, 1)
@@ -191,6 +209,7 @@ def plan(r):
     ts(V("cl", 0, 3), V("cf", 3, 6), pf(14), None, ADD)
     lin(16, 2, 8, pf(5)); lin(17, 6, 64, pf(16)); lin(18, 2, 32, pf(1))
     ts(V("cl", 4, 6), X(0, 129, 128), pf(17), None, ADD)
+    ts(V("cl", 6, 8), X(0, 129, 128), pf(17), 256.0, ADD, ADD)
     lin(19, 2, 8, pf(7)); lin(20, 8, 256, pf(19))
     ts(V("cl", 16, 20), X(0, 193, 64), pf(19), None, ADD)
     ts(V("cl", 20, 24), X(0, 193, 64), pf(20), None, ADD)
@@ -198,15 +217,9 @@ def plan(r):
     ts(V("cl", 12, 14), X(0, 17, 16), pf(18), None, ADD)
     cS, cP, cP2, cP0, cQ0, cF = V("cl", 0, 3), V("cl", 16, 20), V("cl", 20, 24), V("cl", 4, 6), V("cl", 10, 12), V("cl", 12, 14)
     ms(V("two"), 2.0)
-    iota(V("TI"), [[0, 544]], 0, 0)
+    ms(V("TI"), 0.0)
     act(V("TI", 16, 528, 16), V("vI"))
     tt(V("TI", 17, 529, 16), V("vI"), V("TI", 16, 528, 16), SUB)
-    ms(V("zb", 0, 128), 0.0)
-    for c in range(4):
-        iota(V("zb", max(128, 512 * c), 512 * c + 512), [[0, 512 - 128 * (c == 0)]], 0, 0)
-    for k, n in enumerate(("WG", "W2_0", "W2_1")):
-        dma([(V(n, 2048 * c, 2048 * c + 2048), 0, 128, V("zb"), 0, 128, 0, 0) for c in range(2)], True, 4500 + 2700 * k, False, V("zt_%d" % min(k, 1)))
-    PLUS, MINUS = V("pm", 0, 8), V("pm", 8, 16)
     Rh = lambda a: blk("Rh", a)
 
     def batch(b):
@@ -227,36 +240,54 @@ def plan(r):
             d = {}
             for v, s in items:
                 d[v] = d.get(v, 0) + s
-            return [(out, v, PLUS if s > 0 else MINUS) for v, s in d.items() for _ in range(abs(s))]
+            sg = (V("pm", 0, 8), V("pm", 8, 16)) if nel(out) == 8 else (V("pm", 16, 30), V("pm", 32, 46))
+            return [(out, v, sg[s < 0]) for v, s in d.items() for _ in range(abs(s))]
 
         def rep(k, lo, rhs):
             n = nel(rhs)
             return [[(P(k, lo + a, lo + 8 * n, 8), Rh(a), rhs)] for a in range(8)]
 
-        def split(v, row):
-            st = 512 // nel(v); hi = W("TP", row, 512, st)
-            mov("hi", hi, v)
-            tt(W("TP", row + 1, 512, st), v, hi, SUB)
+        def split(v, row, tile="TP"):
+            st = 512 // nel(v); hi = W(tile, row, 512, st)
+            mov(hi, v)
+            tt(W(tile, row + 1, 512, st), v, hi, SUB)
 
-        def fields(q, w, ints, offs):
-            ts(W(ints, 0, w), q, 5, 255, SHR, AND)
-            ts(W(ints, w, 2 * w), q, 1, 15, SHR, AND)
-            cp(W(offs), W(ints))
+        def urgent(t):
+            p = t % 2
+            ts(W("qd", 128, 144), P(3, 0, 16), 2047.0, None, ADD); ts(W("qd", 144, 160), P(3, 48, 64), 2047.0, None, ADD)
+            ts(W("qd", 0, 32), W("qd", 128, 160), 5, None, SHR)
+            ts(W("qd", 32, 64), W("qd", 128, 160), 31, None, AND)
+            cp(W("uP", 0, 64), W("qd", 0, 64))
+            mov(W("maskE"), IND(V("Mp", 32 * p, 32 * p + 32), W("uP", 32, 48)))
+            mov(W("maskO"), IND(V("Mp", 32 - 32 * p, 64 - 32 * p), W("uP", 48, 64)))
 
-        def prep(t, q, c):
-            e = ("V", q[1], q[2], q[2] + 16, 1)
-            ts(W("qc"), e, c, 4097.0, ADD, MUL)
-            ts(W("uq"), e, c, None, ADD)
-            mov("VPq", W("VP", 64, 96), q, c + 8192.0)
-            fields(W("qc"), 16, "qd", "uP")
-            mov("maskE", W("maskE"), IND(V("Mi"), W("uP", 16, 32)))
+        def prep(t, c):
+            if t == 0:
+                ts(W("qd", 128, 144), P(3, 0, 16), c, None, ADD)
+            if t < 2:
+                mov(W("VP", 64, 128, 2), P(3, 0, 32), c + 8192.0)
+            else:
+                ts(W("qa", 0, 32), P(3, 0, 32), c, 4097.0, ADD, MUL)
+                ts(W("qb", 0, 32), W("qa", 0, 32), 5, 255, SHR, AND)
+                ts(W("qb", 32, 64), W("qa", 0, 32), 1, 15, SHR, AND)
+            if t == 1:
+                mov(W("VP", 65, 128, 2), P(3, 32, 64), c + 8192.0)
             if t:
                 rows(t)
+            else:
+                ts(W("qd", 0, 16), W("qd", 128, 144), 5, None, SHR)
+                ts(W("qd", 16, 32), W("qd", 128, 144), 31, None, AND)
+                cp(W("uP", 0, 32), W("qd", 0, 32)); cp(W("uq"), W("qd", 128, 144))
+                mov(W("maskE"), IND(V("Mp", 0, 32), W("uP", 16, 32)))
 
         def rows(t):
-            split(W("VP", 64, 96), 4 * t + 2 if t < 2 else 14)
-            mm([[(P(3, 128 * k, 128 * k + 128), blk(N("TP"), k), V("idb"))] for k in range(4)])
-            mov("rows", W("rows"), P(3))
+            if t < 2:
+                split(W("VP", 64, 128), 4 * t + 2)
+            else:
+                for k in range(2):
+                    cp(W("TQ", 12 + 2 * b + k, 512, 16), W("qb", 32 * k, 32 * k + 32))
+            mm([[(P(3, 128 * k, 128 * k + 128), blk(N("TP" if t < 2 else "TQ"), k), V("idb"))] for k in range(4)])
+            mov(W("rows"), P(3))
 
         def start():
             ts(W("qh"), W("qi"), -2048.0, None, ADD)
@@ -266,26 +297,26 @@ def plan(r):
             ts(W("LE", 0, 64), o, zc1, None, ADD)
 
         def prep0():
-            for n in ("TP", "TM", "wN"):
-                iota(W(n), [[0, AL[N(n)][2]]], 0, 0)
             ms(W("cum", 0, 8), 0.0)
-            iota(W("wI", 128, 256), [[0, 128]], 100000, 0); iota(W("wI", 256, 384), [[0, 128]], 0, 0)
+            for c in range(4 - 4 * b):
+                iota(V("wD", 1024 * c, 1024 * c + 1024), [[0, 1024]], 0, 0)
             mm([[(P(3, 128 * hf, 128 * hf + 128), Rh(4 * hf + r), W("qh"))] for hf in range(2)])
-            act(W("wL", 0, 256), P(3, 0, 256))
-            act(W("q0h"), IND(W("wL", 0, 256), cQ0))
+            mov(W("wL", 0, 256), P(3, 0, 256))
+            mov(W("q0h"), IND(W("wL", 0, 256), cQ0))
             ts(W("uq0"), W("q0h"), 2048.0, None, ADD)
             mm([[(P(3, 16 * pp, 16 * pp + 16), blk("sq", 2 * pp + e), W("q0h", e, 32, 2)) for e in range(2)] for pp in range(2)])
-            prep(0, P(3, 0, 32), 2048.0)
+            prep(0, 2048.0)
             mm([[(P(3, 128 * k, 128 * k + 128), V("TI", 16 - 2 * b + 128 * k, 144 - 2 * b + 128 * k), V("idb"))] for k in range(4)])
-            act(W("rowsI"), P(3))
+            mov(W("rowsI"), P(3))
             for k in range(2):
                 cp(IND(V("WG"), W("uq0", 16 * k, 16 * k + 16)), W("rowsI", 256 * k, 256 * k + 256))
-            mm([[(P(3, 16 * pp + cc, 16 * pp + cc + 1), V("WG", 256 * cc + pp, 256 * cc + 256, 2), col("sel", 8 + b))] for pp in range(2) for cc in range(16)])
-            act(W("l1", 32, 64), P(3, 0, 32), bias=-10240.0)
+            mm([[(P(3, 16 * pp + cc, 16 * pp + cc + 1), V("WG", 256 * cc + pp, 256 * cc + 256, 2), col("sel", 2 * b))] for pp in range(2) for cc in range(16)])
+            mov(W("l1", 32, 64), P(3, 0, 32), -10240.0)
             mm(rep(3, 256, W("l1", 32, 64)))
-            act(W("wL", 256, 512), P(3, 256, 512))
-            act(W("VP", 0, 64), IND(W("wL", 256, 512), cP), bias=10240.0)
-            act(W("VP", 0, 64, 2), V("idc"), bias=pf(13))
+            mov(W("wL", 256, 512), P(3, 256, 512))
+            mov(W("VP", 0, 64), IND(W("wL", 256, 512), cP), 10240.0)
+            mov(W("VP", 0, 64, 2), V("idc"), pf(13))
+            mov(W("VP", 65, 128, 2), W("VP", 1, 64, 2))
             split(W("VP", 0, 64), 0)
             rows(0)
 
@@ -306,103 +337,110 @@ def plan(r):
                 mm([gr], c == 1, False)
             for c in range(2):
                 s = 512 * c; S = PAR["S0"][c]
-                act(t_("Xt", s, 512), IND(ZW, W("LX", 32 * c, 32 * c + 32)))
+                mov(t_("Xt", s, 512), IND(ZW, W("LX", 32 * c, 32 * c + 32)))
                 term(t_("tD", s, 512), t_("Xt", s, 512), ze(s, 512), "D" in S)
-                i1 = IND(ZW, W("LE", 32 * c, 32 * c + 32))
-                e = ze(s, 512)
-                if PAR["X0"][c] == "s":
-                    act(t_("Et", s, 512), i1); i1 = t_("Et", s, 512)
-                else:
-                    e = t_("Et", s, 512); mov("E0", e, ze(s, 512))
-                tt(t_("tF", s, 512), i1, e, A.max)
-                tt(t_("tG", s, 512), i1, t_("Xt", s, 512), A.max)
+                mov(t_("Et", s, 512), IND(ZW, W("LE", 32 * c, 32 * c + 32)))
+                tt(t_("tF", s, 512), t_("Et", s, 512), ze(s, 512), A.max)
+                tt(t_("tG", s, 512), t_("Et", s, 512), t_("Xt", s, 512), A.max)
                 for n, sg in (("tD", -1), ("tF", -1), ("tG", 1)):
                     gr = []
                     for x in range(4 * c, 4 * c + 4):
                         k = 128 * x
                         gr += reduce(P(2, 256 + x, 320, 8), [(t_(n, k, 128), sg)] + [(ze(k, 128), -1)] * ("D" in S and n == "tD"))
                     mm([gr], False, c == 1 and n == "tG")
-            mov("sP", W("sP0"), P(2, 256, 320))
-            remote("rs", b, N("rP0"), 16, N("sP0"))
+            mov(W("sP0"), P(2, 256, 320))
+            remote("rs", b, N("rP0"), 16, N("sP0"), None if b else V("TQ_1"))
+            zero(N("W2"), 4500, W("rP0"))
 
         def coords(t):
             es = 1 - t % 2; E = N("rE%d" % (t - 1))
             rng = [(v, 0, 48, 3 + 48 * v) for v in range(4)] + [(4, 0, 2, 195)] + [(5, 46, 47, 1)] * es
-            mm([[(P(2, o, o + hi - lo), RS(v, x), V(E, 48 * x + lo, 48 * x + hi)) for x in [r] + others] for v, lo, hi, o in rng])
+            sh = lambda xs: [(P(2, o, o + hi - lo), RS(v, x), V(E, 48 * x + lo, 48 * x + hi)) for x in xs for v, lo, hi, o in rng]
+            mm([[(P(2, 0, 200), V("idb"), V("zb", 0, 200))] + sh([r])], last=False)
+            mm([sh(others)], first=False)
             ts(W("LO", 0, 65), P(2, 4 - 3 * es, 197 - 3 * es, 3), zc, None, ADD)
             ts(W("LE", 0, 64 + es), P(2, 3, 193 + 3 * es, 3), zc, None, ADD)
             ts(W("LX"), P(2, 5, 195, 3), zc, None, ADD)
             t_ = lambda n, s, w: W(n, s, s + w)
             left = lambda k, n: t_("Ot", k + 15 * es, n)
             right = lambda k, n: t_("Ot", k + 15 * es + 1, n)
-            SS = PAR["S"][2 * t - 2:2 * t]
+            SS = PAR["S"][4 * t - 4 + 2 * b:4 * t - 2 + 2 * b]
             for c in range(2):
                 s = 512 * c; S = SS[c]
                 for L, G, hi in (("LO", "Ot", 65), ("LE", "Et", 64 + es)):
                     lo, hi = (0, 34) if c == 0 else (34, hi)
-                    act(W(G, 16 * lo, 16 * hi), IND(ZW, W(L, lo, hi)))
+                    mov(W(G, 16 * lo, 16 * hi), IND(ZW, W(L, lo, hi)))
                 term(t_("tC", s, 512), left(s, 512), right(s, 512), "C" in S)
                 term(t_("tB", s, 512), t_("Et", s, 512), right(s, 512), "B" in S)
                 lo, n = (0, 512 + es) if c == 0 else (512 + es, 512)
-                term(t_("tA", lo, n), t_("Et", lo, n), left(lo, n), False)
+                term(t_("tA", lo, n), t_("Et", lo, n), left(lo, n), "A" in S)
             for c in range(2):
-                S = SS[c]; gr = [(P(2, 256, 384), V("idb"), V("zb", 0, 128))] if c == 0 else []
+                S = SS[c]; gr = [(P(2, 256, 384), V("idb"), V("cb"))] if c == 0 else []
                 for x in range(4 * c, 4 * c + 4):
                     k = 128 * x
-                    it = [(t_("tA", k, 128), 1), (t_("tB", k, 128), 1), (t_("tC", k, 128), -1)]
-                    it += [(right(k, 128), 1)] * ("B" in S) + [(right(k, 128), -1)] * ("C" in S)
-                    gr += reduce(P(2, 257 + 2 * x, 384, 16), it)
-                    gr += reduce(P(2, 256 + 2 * x, 384, 16), [(t_("tA", k + es, 128), -1)])
+                    it = [(t_("tA", k, 128), -1), (t_("tB", k, 128), -1), (t_("tC", k, 128), 1)]
+                    it += [(right(k, 128), -1)] * ("B" in S) + [(right(k, 128), 1)] * ("C" in S) + [(left(k, 128), -1)] * ("A" in S)
+                    gr += reduce(P(2, 272 + x, 377 + x, 8), it)
+                    gr += reduce(P(2, 256 + x, 361 + x, 8), [(t_("tA", k + es, 128), -1)] + [(left(k, 128), -1)] * ("A" in S))
                 mm([gr], c == 0, False)
             for c in range(2):
-                s = 512 * c; S = SS[c]
-                ix = IND(ZW, W("LX", 32 * c, 32 * c + 32))
-                if PAR["X"][2 * t - 2 + c] == "s":
-                    act(t_("Xt", s, 512), ix); ix = t_("Xt", s, 512)
+                s = 512 * c
+                ix = IND(ZW, W("LX", 32 * c, 32 * c + 32)); S = SS[c]
+                if "X" in S:
+                    mov(t_("Xt", s, 512), ix); ix = t_("Xt", s, 512)
                 for n, o in (("D", lambda k, w: left(k + es, w)), ("F", lambda k, w: t_("Et", k + es, w))):
                     term(t_("t" + n, s, 512), ix, o(s, 512), n in S)
                     gr = []
                     for x in range(4 * c, 4 * c + 4):
-                        gr += reduce(P(2, 256 + 2 * x, 384, 16), [(t_("t" + n, 128 * x, 128), 1)] + [(o(128 * x, 128), 1)] * (n in S))
+                        gr += reduce(P(2, 256 + x, 361 + x, 8), [(t_("t" + n, 128 * x, 128), 1)] + [(o(128 * x, 128), 1)] * (n in S))
                     mm([gr], False, c == 1 and n == "F")
-            mov("sP", W("sP%d" % t), P(2, 256, 384), -1600.0)
+            mov(W("sP%d" % t), P(2, 256, 384))
             remote("rs", 2 * t + b, N("rP%d" % t), 32, N("sP%d" % t))
 
         def index(t):
-            p = t % 2; row = 4 + 3 * b + t
-            w = 32 if t else 16; st = 2 if t else 1
-            part = lambda x, k: W(("sP%d" if x == r else "rP%d") % t, w * x + k, w * x + w, st)
-            L = P(1, 0, 16)
+            p = t % 2; row = 8 + b
+            w = 32 if t else 16
+            part = lambda x: W(("sP%d" if x == r else "rP%d") % t, w * x, w * x + w)
+            pen = lambda o, n: [(P(1, o + 8 * R, o + 8 * R + 8), blk(N(n), R), V("pen")) for R in range(2)]
+            PO = P(2, 0, 16) if t else P(1, 16, 32)
             if t:
-                o = 256 * (1 - p)
-                mm([[(P(0, 0, 128), V("idb"), V("zb", 0, 128))] + [(P(0, a, 128, 8), Rh(a), part(r, 0)) for a in range(8)]], last=False)
-                mm([[(P(0, a, 128, 8), Rh(a), part(x, 0)) for x in others for a in range(8)]], first=False)
-                mov("wI", W("wI", o, o + 128), P(0, 0, 128))
-            tt(W("gI"), IND(W("wI", 128 * (1 - p), 128 * (1 - p) + 256), W("uP", 0, 16)), W("maskE"), MUL)
-            if t:
-                mm([[(L, V("nidh"), part(x, 1)) for x in [r] + others]], last=False)
-                mm([[(P(1, 8 * R, 8 * R + 8), blk(N("gI"), R), V("blkf")) for R in range(2)]], first=False)
+                L = P(1, 0, 32)
+                mm([[(P(0, 0, 256), V("idb"), V("zb", 0, 256))] + [(P(0, a, 256, 8), Rh(a), part(r)) for a in range(8)]], last=False)
+                mm([[(P(0, a, 256, 8), Rh(a), part(x)) for x in others for a in range(8)]], first=False)
+                mov(W("wI"), P(0, 0, 256))
+                mm([[(L, V("idh"), part(r))] + pen(0, "maskO") + pen(16, "maskE")], last=False)
+                mm([[(L, V("idh"), part(x)) for x in others]], first=False, last=False)
+                tt(W("gI", 256, 512), IND(W("wI", 0, 128), W("uP", 0, 16)), W("maskE"), MUL)
+                mm([[(P(1, 8 * R, 8 * R + 8), blk(N("gI"), R), V("blkf")) for R in (2, 3)]], first=False, last=False)
+                tt(W("gI", 0, 256), IND(W("wI", 128, 256), W("uP", 16, 32)), W("maskO"), MUL)
+                mm([[(P(1, 8 * R, 8 * R + 8), blk(N("gI"), R), V("blkf")) for R in (0, 1)]], first=False)
+                ts(W("fl"), L, -30000.0, None, A.is_lt)
+                guest, mv = W("fl", 0, 16), W("fl", 16, 32)
+                mm([[(PO, V("idh"), V("c2", 16 * p, 16 * p + 16))]], last=False)
             else:
-                mm([[(L, V("nidh"), part(r, 0))] + [(P(1, 8 * R, 8 * R + 8), blk(N("gI"), R), V("blkf")) for R in range(2)]], last=False)
-                mm([[(L, V("nidh"), part(x, 0)) for x in others]], first=False)
-            mv = W("TM", row, 256, 16)
-            ts(mv, L, 0.0, None, A.is_lt)
-            mm([[(P(0, 128 + 128 * R, 256 + 128 * R), blk(N("TM"), R), V("idb"))] for R in range(2)])
-            mov("rowsM", W("rowsM"), P(0, 128, 384))
-            cp(IND(V("WG"), W("uq")), W("rowsM"))
-            PO = P(1, 16, 32)
-            mm([[(PO, V("idh"), V("c2", 16 * p, 16 * p + 16))] + ([(PO, V("nidb"), mv)] if p == 0 else [])], last=False)
-            mm([[(P(2, cc, cc + 1), V("WG", 256 * cc + 1 - p, 256 * cc + 256, 2), col("Mi", row))] for cc in range(16)])
+                L = P(1, 0, 16)
+                mm([[(L, V("nidh"), part(r))] + pen(0, "maskE")], last=False)
+                mm([[(L, V("nidh"), part(x)) for x in others]], first=False)
+                mv = W("TM", row, 256, 16); guest = P(2, 0, 16)
+                ts(mv, L, -30000.0, None, A.is_lt)
+                mm([[(P(0, 128 + 128 * R, 256 + 128 * R), blk(N("TM"), R), V("idb"))] for R in range(2)])
+                mov(W("rowsM"), P(0, 128, 384))
+                cp(IND(V("WG"), W("uq")), W("rowsM"))
+                mm([[(PO, V("idh"), V("c2", 0, 16)), (PO, V("nidb"), mv)]], last=False)
+                mm([[(P(2, cc, cc + 1), V("WG", 256 * cc + 1, 256 * cc + 256, 2), col("Mi", row))] for cc in range(16)])
             c1, cb = W("cum", 8, 24), W("cum", 7, 23)
-            op("v", ("tensor_tensor_scan", (c1, P(2, 0, 16), mv, 0.0, ADD, SUB), {}))
+            if t == 2:
+                mm([[(PO, V("nidh"), mv)]], first=False, last=False)
+            op("v", ("tensor_tensor_scan", (c1, guest, mv, 0.0, ADD, SUB), {}))
+            WW = W("W2") if t < 2 else V("WG")
             mm([[(PO, V("LT"), c1), (PO, V("GE"), cb)]], first=False)
             nE, nO = W("nt", 0, 16), W("nt", 16, 32)
-            mov("nO", nO, PO)
+            mov(nO, PO)
             ts(W("uO"), nO, 2047.0, None, ADD)
-            cp(IND(W("W2"), W("uO")), W("rows", 256, 512))
+            cp(IND(WW, W("uO")), W("rows", 256, 512))
             mm(rep(0, 0, nO))
-            mov("wNo", W("wN", 128 * (1 - p), 128 * (1 - p) + 128), P(0, 0, 128))
-            tt(W("gP"), IND(W("wN"), W("uP", 0, 16)), W("maskE"), MUL)
+            mov(W("wN", 128 * (1 - p), 128 * (1 - p) + 128), P(0, 0, 128))
+            tt(W("gP"), IND(W("wN", 128 * (1 - p), 128 * (1 - p) + 128), W("uP", 0, 16)), W("maskE"), MUL)
             stay = lambda o, u, d: [(o, u, nO)] + ([(o, u, c1), (o, d, cb)] if p else [(o, d, V("two"))])
             mm([stay(P(1, 48, 64), V("idh"), V("nidh"))])
             mm([stay(P(1, 32, 48), V("nidh"), V("idh"))], last=False)
@@ -410,60 +448,72 @@ def plan(r):
             tt(W("s1"), P(1, 32, 48), mv, MUL)
             tt(nE, P(1, 48, 64), W("s1"), ADD)
             ts(W("uE"), nE, 2048.0, None, ADD)
-            cp(IND(W("W2"), W("uE")), W("rows", 0, 256))
+            cp(IND(WW, W("uE")), W("rows", 0, 256))
             mm(rep(3, 0, nE))
-            mov("wNe", W("wN", 128 * p, 128 * p + 128), P(3, 0, 128), 1.0)
+            mov(W("wN", 128 * p, 128 * p + 128), P(3, 0, 128), 1.0)
             E = N("rE%d" % t)
             if t < 2:
                 pn = 1 - p
-                mm([[(P(2, 32 + 16 * k + cc, 128, 32), W("W2", 256 * cc + pp, 256 * cc + 256, 2), V("sel", 3 * t, 3 * t + 3))]
+                mm([[(P(2, 32 + 16 * k + cc, 160, 32), W("W2", 256 * cc + pp, 256 * cc + 256, 2), V("sel", 4 * t, 4 * t + 4))]
                     for k, pp in ((0, pn), (1, 1 - pn)) for cc in range(16)])
-                mov("l1", W("l1"), P(2, 32, 128), -10240.0)
+                mov(W("l1"), P(2, 32, 160), -10240.0)
                 mm(rep(1, 256, W("l1", 48 - 16 * (1 - t), 64)))
                 mm(rep(0, 0, W("l1", 0, 32)))
-                mov("wL2", W("wL", 256 + 128 * t, 512), P(1, 256, 512 - 128 * t))
-                mov("wL1", W("wL", 0, 256), P(0, 0, 256))
-                mov("rE", V(E, 48 * r, 48 * r + 48), IND(W("wL"), cS))
+                mov(W("wL", 256 + 128 * t, 512), P(1, 256, 512 - 128 * t))
+                mov(W("wL", 0, 256), P(0, 0, 256))
+                mov(V(E, 48 * r, 48 * r + 48), IND(W("wL"), cS))
                 remote("ag", 2 * t + b, E, 48)
                 if t == 0:
-                    mov("VP", W("VP", 0, 64), IND(W("wL"), cP2), 10240.0)
+                    mov(W("VP", 0, 64), IND(W("wL"), cP2), 10240.0)
                     split(W("VP", 0, 64), 4)
                 else:
-                    mov("VP", W("VP", 0, 32), IND(W("wL", 0, 256), cP0), 10240.0)
-                    split(W("VP", 0, 32), 10)
-                ts(W("qa"), W("l1", 64, 96), 2048.0, 4097.0, ADD, MUL)
+                    mov(W("VP", 0, 32), IND(W("wL", 0, 256), cP0), 10240.0)
+                    split(W("VP", 0, 32), 4 + 2 * b, "TQ")
+                ts(W("qa"), W("l1", 64, 128), 2048.0, 4097.0, ADD, MUL)
+                dma([(V("wD", 256 * i, 256 * i + 256), i, -16, W("wN"), 0, 0, 0, 0) for i in range(16)], True, 2000 + 270 * 15, False, W("wN"))
+                ts(W("qb", 0, 64), W("qa"), 5, 4095, SHR, AND)
+                cp(W("uN", 0, 64), W("qb", 0, 64))
+                for lo, hi in ((0, 16), (48, 64), (16, 48 - 16 * t)):
+                    mov(W("gQ", 16 * lo, 16 * hi), IND(V("wD"), W("uN", lo, hi)))
             else:
-                mm([[(P(2, 32 + cc, 33 + cc), blk(N("W2"), cc), col("sel", 6))] for cc in range(32)])
-                mov("l1", W("l1", 0, 32), P(2, 32, 64), -10240.0)
+                mm([[(P(2, 32 + cc, 33 + cc), blk("WG", cc), col("sel", 4 + 2 * b))] for cc in range(32)])
+                mov(W("l1", 0, 32), P(2, 32, 64), -10240.0)
                 mm(rep(0, 0, W("l1", 0, 32)))
-                mov("wL1", W("wL", 0, 256), P(0, 0, 256))
-                mov("rE", V(E, 32 * r, 32 * r + 32), IND(W("wL", 0, 256), cF))
+                mov(W("wL", 0, 256), P(0, 0, 256))
+                mov(V(E, 32 * r, 32 * r + 32), IND(W("wL", 0, 256), cF))
                 remote("ag" if b else "hx", 6 - b, E, 32)
-                mm([[(P(1, 64 + y, 65 + y), W("W2", y, 4096, 32), col("sel", 7))] for y in range(32)])
-                mov("l1q", W("l1", 32, 64), P(1, 64, 96), -10240.0)
-                mm(rep(3, 256, W("l1", 32, 64)))
-                mov("wL2", W("wL", 256, 512), P(3, 256, 512))
-                ts(W("qa"), IND(W("wL", 256, 512), cP0), 2048.0, 4097.0, ADD, MUL)
-            fields(W("qa"), 32, "qb", "uN")
-            mov("mask1", W("mask1"), IND(V("Mi"), W("uN", 32, 64)))
-            tt(W("gQ"), IND(W("wN"), W("uN", 0, 32)), W("mask1"), MUL)
-            mm([[(P(3, 8 * k, 8 * k + 8), blk(N("gQ"), k), V("blkh"))] for k in range(4)])
+                mm([[(P(1, 64 + y, 128, 32), V("WG", y, 4096, 32), V("Mi", 12 + 2 * b, 14 + 2 * b))] for y in range(32)])
+                mov(W("l1", 32, 96), P(1, 64, 128))
+                mm(rep(3, 0, W("l1", 32, 96)))
+                mov(W("gI"), P(3))
+                cp(W("uN", 0, 64), IND(W("gI"), V("cl", 4, 8)))
+                for lo, hi in ((0, 16), (16, 32)) if b else ((0, 32),):
+                    mov(W("mask1", 16 * lo, 16 * hi), IND(V("Mi"), W("uN", 32 + lo, 32 + hi)))
+                    tt(W("gQ", 16 * lo, 16 * hi), IND(W("wN"), W("uN", lo, hi)), W("mask1", 16 * lo, 16 * hi), MUL)
+            red = lambda ks: mm([[(P(3, 8 * k, 8 * k + 8), blk(N("gQ"), k), V("blkh"))] for k in ks])
             if t < 2:
-                prep(t + 1, P(3, 0, 32), 2047.0)
+                red((0, 1, 6, 7))
+                urgent(t + 1)
+            red(range(8 if t < 2 else 4))
+            if t < 2:
+                prep(t + 1, 2047.0)
             else:
-                mov("rX", W("rX2", 32 * r, 32 * r + 32), P(3, 0, 32))
+                mov(W("rX2", 32 * r, 32 * r + 32), P(3, 0, 32))
                 remote("hx", 4 + b, N("rX2"), 32)
-                mov("qf", W("qf"), W("rX2"), 2047.0)
+                mov(W("qf"), W("rX2"), 2047.0)
                 dma([(W("qf", 32 * x, 32 * x + 32), 0, 128, "yq", 4 * b + x, 1, 0, 4096) for x in range(4)], False, 2500, b == 1)
 
         def final():
             E = N("rE2")
-            mm([[(P(2, 32 * v, 32 * v + 32), RS(v, x), V(E, 32 * x, 32 * x + 32)) for x in [r] + others] for v in range(4)])
+            sh = lambda xs: [(P(2, 32 * v, 32 * v + 32), RS(v, x), V(E, 32 * x, 32 * x + 32)) for x in xs for v in range(4)]
+            mm([[(P(2, 0, 128), V("idb"), V("zb", 0, 128))] + sh([r])], last=False)
+            mm([sh(others)], first=False)
             ts(W("LY"), P(2, 0, 128), zc, None, ADD)
             for c in range(4):
-                (cp if PAR["fin"][c] == "v" else act)(W("yt", 512 * c, 512 * c + 512), IND(ZW, W("LY", 32 * c, 32 * c + 32)))
+                mov(W("yt", 512 * c, 512 * c + 512), IND(ZW, W("LY", 32 * c, 32 * c + 32)))
                 if c % 2:
-                    dma([(W("yt", 512 * c - 512, 512 * c + 512), 64 * hf, 64, "yz", 64 * b, 64, 2048 * hf + 512 * c - 512, 1024) for hf in range(2)], False, 3000, b + c == 4)
+                    lo = 512 * c - 512
+                    dma([(W("yt", lo, lo + 1024), 64 * hf, 64, "yz", 64 * b, 64, 2048 * hf + lo, 1024) for hf in range(2)], False, 3000, b == 1)
 
         return [start, coords0, prep0, lambda: index(0), lambda: coords(1), lambda: index(1), lambda: coords(2), lambda: index(2), final]
 
@@ -495,9 +545,7 @@ def depend(ops):
 
 def common_order(ops):
     al = "0123456789abcdefghijklmnopqrstuvwxyzABCDEFGHIJKLMNOPQRSTUVWXYZ"
-    o = [62 * al.index(ORDER[k]) + al.index(ORDER[k + 1]) for k in range(0, len(ORDER), 2)]
-    first = [j for j in range(len(ops)) if ops[j][1] == "d" and ops[j][2][0] and not ops[j][3]]
-    return first + [j for j in o if j not in first]
+    return [62 * al.index(ORDER[k]) + al.index(ORDER[k + 1]) for k in range(0, len(ORDER), 2)]
 
 
 def helper_of(T, topo, c):
@@ -607,7 +655,10 @@ def rank_program(g, core, T, topo):
                 ins.then_inc(S[eng], 1)
         elif kind == "d":
             for k, (v, p0, pn, tn, r0, rn, c0, cn) in enumerate(pay[1]):
-                sb, hb = T[v[1]][p0:p0 + pn, v[2]:v[3]], (ap(tn) if isv(tn) else T[tn][r0:r0 + rn, c0:c0 + cn])
+                if pn < 0:
+                    sb, hb = T[v[1]][p0:128:-pn, v[2]:v[3]], T[tn[1]][p0:128:-pn, tn[2]:tn[3]]
+                else:
+                    sb, hb = T[v[1]][p0:p0 + pn, v[2]:v[3]], (ap(tn) if isv(tn) else T[tn][r0:r0 + rn, c0:c0 + cn])
                 q = g.scalar if pay[2] and k % 2 else g.sync
                 (q.dma_start(sb, hb) if pay[0] else q.dma_start(hb, sb)).then_inc(S[sig[j][0]], 16)
         else:

@@ -1,41 +1,66 @@
 from concourse.mybir import AluOpType as A, ActivationFunctionType as F
 from concourse.bass import DstId, RemoteDMATransfer
 
-PAR = {"S": ("BCX",) * 8, "S0": ("BCD", "BC")}
-ONV = "10101100100000001100100001011110000001111001000101100000101000111100101010101111010101111000011001110011001010001111011100010000100010001100100101100011110101100001101000110"
-ORDER = "000102030405060708090a0i0j0l0k0x0s0o0E0t0q0r0p0v0u1D2R0h0w0G3p0Z0F1E0C0D0I0H0B1F0Q181Q140X161S0A1P1012110y1B0Y151G0W0S1R1j0z1H0R1k171l0U131I1m0T1J1T1n2W2S1K1W1o2X0c0V1p1X2Y302Z1U310b320d3334212a381Y1V242U22392c2b2m251Z2o26232T202e0N272d2n28292f1L2p2g2l3q1M2h2s3r2i1x351N3s0e0g370f0P3u1O3t2u1z3v3a3w0n3T2x0O3C2q0m2r1a2A3b1c3D2j2B2t3c2C2G2y193E3d1b2I3e2V363y3F1h2v2k3U3f2K3G1i3g2H2z3V2J1d3h3W1f2w3X3i0J2D3x3A3j0K2E3Y3H2F2L1q2M1y2N1g3Z3I2O3J2P3k403z1s1r3l3B1A0L3m410M3K423n1t434P1u3L461e443o494a473N48452Q4Q4b4c4R3M4d4S3O4g4e4T3P4V4f4h4u4U4i3Q4j4W1v1C1w4t4k4X4v4l4m4Y3R4n4Z4w52503S4o55564q4p5L534r545157584s595a5M5c5N5b5Q5O5X5d5S5R5e5T5P5Y5U665Z6b5V5f60695h5g5j67615i634x5k4y5W5l6i626c4A644z4B5p654C6e686a6d4D4E5m6f5r5q4I4F6g4H4J6h6j4G4K6P5s6k4L5n6S6u6n6Z6l4M6p6v6m6o4N6Q6I5o6A6T6r6R6q6W4O6w6U6D6L6V6X6t6x6Y706J6s716G72756E6y766B736z777879747a6C5v6F6H6K6M7b7c6N5t7d6O7P7e7f7Z5u7h7g7t5w7i5x7k7s5y7j7u5A7m5z7Q7v7l5B7n5C5E7o7R8P5F7p5D7U5G7S7W7T7V5H7q7X5I7r7Y5J805K8Q818R828U8S918588898692838W8T87848V8a8b9a8Y8c8d8f8e8X9f908h978Z938i9i8j948k9b958m988l968g8n9d8o9m7w999g7x9c9e7y9h9j7z9k8t7A8s9la37B8u7H7C7D8v7E7I9n7F7G9T9o7J7K9W9r9p7L9q7M9H7N9s9U8p9I9t9M9V9X9v8qa09y9Y9x9Z9ua19z9w9Aa28r9Ba4a59Ka69Ca79E9Daa9F9N7O9G9P9Jab9L9Oa8adac9Qae9R8xa99SafaE8waO8yag8z8Aah8Bakai8C8HajaF8D8I8E8J8K8G8FasaG8LaJamataLaH8MalanaIaKaMaoaN8NaQaPap8OaRauaSaqaVaTaraYaZbraUaWavaXawb0axb1b2b5b3b4b6bdaybeazaAbfaBb7bgbsbhb8bib9btbabkbbbxbjbcbAblbybmbnbvbobubzaCbBbwbCbHbGaDbEbDbFbIbpbq"
+PAR = {"m": ("- DF DF DF s s s s s s s s".split(),) * 2, "help": ("ag5", "ag8", "ag9", "yq0", "yq1", "yq2"), "pace": 4, "nch": 1, "late": 0,
+       "exact": 1, "seq": ("Vx123ybc", "V1x23ybc")}
+ONV = ["1" * 400, "1" * 400]
+ORDER = (
+    "0xdO19cGcFcT0zc9000LcLcH011GcUd0c802ca0HAu1b0304cK0Idh0S0G1F05cEcbcO0E0D0MccpXcddn0F0J1I0C0Kdkoo0609cR30cN0O0wcM1o1Jf7p924cP1K1acQ"
+    "dR07BhcSdS0A2ZdT1d2t1L18db1X1YcWdUcfci150Qd30a0ydmcge5eB0Ndi25cj0VdPdQcV2s1Mck1cdHf5cZ1z0P1Dda0Rf8f60W2Aqf161edzd4chcldcd22X1f1m21"
+    "48e60b0c2u2vdwdx201Bfe2Y0BdL360d262xdl33cm22230e27312BeIfbDpdrfdfjfa1scn34fi282w32291R2ado47eC0Ufc4935e7372b1V1W1N38cX2c4o1pfkec2C"
+    "djqA0f4c2de8eddYcYe90g4f4d4e3bdVff17qDfggwfnqz1S1hfofh2e2ofq2fqB39ee132m2g3add2h2p4a4bcJ4g2D3c4i4n4h4j4k0hea4p2idIefCTCregfpeE12qG"
+    "rt1g2y3g0i4ssBcoCZ10cpcqd84r3e3ffr0Xdeflfm3h3ieh4teF1TftqPei141jfs0jeGeKejdJgx3j3k1P4v4u113l3m4qeHgv2E2FfufvCA3oDMcI5AgM3ncr4y3pcs"
+    "CHeldfeL0kCJeme10lfxdu3qd5fz3r3sesgNgA4wenCL5Beogz3tCF5C1Aewe4F12Gd7ctgBeMcuqXgD1qgCgE3ucv4m3v4x4zeq0mgFeu3w3x1t4AqY3y2J1Q1r1idgex"
+    "fygyfAfBe35FgHfC4B0n3z5GgG5Id6gI5HgOgQ4EfD5EfE1OfFgPfG1u3C5Je0gR2PfHrQD3dpds0o2RfI2Q0pdA1U5L2KcwfJCO2LdNd9gJrT3F5DfKfMfLfR2M3EfSfN"
+    "3NfOgT4CgSfPdve2gUeOgVrXrWrYfQ0YgK4D4F5K2O2N1C5M5NgWsW3OfTfU0qfX3BfVeP4H4I4JeQeX3PfWu4gXgY4K2T2S2U2V0r4L3QcxeYez4M4N3R5R3J2r4OFf3S"
+    "eRdy4P3UrceTeSdD4R4Q4T4U4SdEfYeUeVdB3TeW5QDfeA4WdKdXdWdZcyh05P5Sf1fZ5Tf0hZ5V4Vg0h1Eh3Vh2gb5U4X5Z3Xg25Y0Z0sgcEkdC4Yg34Z5052515W5Xtj"
+    "55tm58dq3K5a57hYi0i1cz3W3Lg5g6f2g7i3h3Gif376i7i65g75Fkhagd7761h762tp5bh578h6i47aifh8h9hbi5hc60i8f441vp3Y7bg8hd5c6364vt7c676542hf7e"
+    "he437l7fi9ia7m403Z7n7o7p7giege44hh7qFyigihgfgihkiijt5hpDhj54ibicid663Mijin5iimhlhmghhghnhq7hgj68uphohphthu7i7uikil6hiqipgg6a6bvzio"
+    "jujvjwgl7k7t6chv6e7r6d6f6girhrgkhwgpFNjyGIhy7s4546HNgmithz6iiu5khAEG7wjCgn5jhs6jjJ6k6l6n6q8A6r6o7v7xiviwjAHRjK7yEH6m5d5mjzjF5ngohE"
+    "jDjEjG7z6pixiF8BiA0t5l8C5o6s8D8E6tiy5q5p8FiCjLizg96ujHjI6vjM7A7B5r5t8JhFga7C6w5sgsuNtu5u6ziB0u7D7EhGwY6ytL8H8GiDiEuQ5fgtiGiHEKiJiI"
+    "iLiKjOjNiM6BiNiOtM8K6C1k6EiP5xjQcA7FkZiQiR7GcBhI5yhHhLjSjPiSiTjRjUjTjViUuThMdtiXHehNhOjWIdj88MiVj01l7M7H6FhP7JiZ8L5z7IHi7K8N6KjY7L"
+    "6L7N6M6OhBx40v6GhJ8PhK6NHhj97O7P7Q7R7S7T7V7U6Q8RhRHjhSG9cC8Q6PjZkYl08S8T7WFS6RiWl16S7X7Y1v7Z1wk0hDGahQJj80k3dGhVk16T9Rl2k2jal5ka8U"
+    "xe6U8V8W6Xl7l68X81wi6Y8Z8485861y90lfk4878388wp91jb6Hk5k6j492k71xk8l4hW6ZlajchX7170k9kb8a9Ql9kckekdkgkjjdkkcD8bl8lbIx8flelgkilhlckf"
+    "kl6Vkm93knjejfxk9Skpj572wsjllimf6Iko6Wljme9Tlka7a6mgmhjmllyba8lnksIJ95dFjh8gkD9U6J9Wyea9kqkv9X9Z97lma173lplda0ku9698IMaakElojg999a"
+    "kxkyablqlr9b8hKy9cmj9elsjimDa2a3lv9d9fac9gyua49h9i8jj6kz9j9kad9l9r9m9odMjnjomCaf74beagj7ahbf9p9qbg9s9tltbhmka5luml9n8k8i8l9uaiaj9x"
+    "biyA8m9vKCzCmE9wmqjpjq8smFmnbjjkbnavlwjjly9A9ympmomrJNlAblbklzlCKIlBallD9Bjrbpbo1EkF8nmHmGmJ8tlEbq9CmImOlHmLmKmMmNlFlGlI9zbrzI8obt"
+    "lKkrkHmt8v9DxU9F8umumPlJlMjslLlPlQ8dkG8ekJammQawkKlNlO8pwG8xao8wkL9G8yyNaA8raCayxXazaBaDaEkIkMmR9ImvkQkRaH8zlRaFaGaIaKaJn1lSaLkNkO"
+    "kPaMlVaNlTlUkSmSaO9Jn2LjkTn69KkVaPaQaRaSn8y2aTlW9LlYlZn49Nn5kAn7m0nbanapn9KhIRKinaaUkCkUndaV9OaWaqasm49PKlncnenfaYbCmwb4mxaZmzlXb0"
+    "ngkWJdnKm6KnnimULzm3nlnTm8m9zlnkb6maaXnhzhnmmynnmTnombbvKsmdznaraub8b2nrnszpbunpmVnqmAbantmWbGmXnunAb3LebLLLnSKRnwnLn0zTbKbwbxLfzU"
+    "LRnCbFM3nMLNbyyJLTnybbzsbMbzbNA5bdbXnUzQnzzRnObSnVnEM5bWnFnQzXLWA4nHzZLYM7A6nJbYo4nWbZMdA9AgnYc4Alo5bIo0bRAac1AbMho6o7MfMiAiMjMoo9"
+    "MrocodofoaMuc3c7c6")
 
 BF, HF, FP, I32, U16 = "bfloat16", "float16", "float32", "int32", "uint16"
-PER = {
-    "zt": (6160, BF), "yt": (2048, BF), "Et": (1056, BF), "Ot": (1056, BF), "Xt": (1024, BF),
-    "tA": (1040, BF), "tB": (1024, BF), "tC": (1024, BF), "tD": (1024, BF), "tF": (1024, BF), "tG": (1024, BF),
-    "LE": (66, U16), "LO": (66, U16), "LX": (64, U16), "LY": (128, U16), "W2": (4096, BF), "rows": (512, BF), "rowsM": (256, BF), "rowsI": (512, BF),
-    "TP": (512, BF), "TM": (256, BF), "VP": (128, FP), "TQ": (512, BF), "fl": (32, HF),
-    "sP0": (64, HF), "rP0": (64, HF), "sP1": (128, HF), "rP1": (128, HF), "sP2": (128, HF), "rP2": (128, HF),
-    "rE0": (192, HF), "rE1": (192, HF), "rE2": (128, HF), "rX2": (128, HF), "qf": (128, FP),
-    "wI": (256, FP), "wN": (256, FP), "wL": (512, FP), "gI": (512, FP), "gP": (256, HF), "gQ": (1024, HF), "maskE": (256, HF), "maskO": (256, HF),
-    "mask1": (512, HF), "cum": (32, HF), "s1": (16, FP), "nt": (32, HF), "uO": (16, U16), "uE": (16, U16), "uq": (16, U16),
-    "l1": (128, HF), "qa": (64, I32), "qb": (128, I32), "uN": (128, U16), "qd": (192, I32), "uP": (128, U16),
-    "qi": (128, I32), "qh": (128, HF), "q0h": (32, HF), "uq0": (32, U16),
-}
-BUF = {
-    "WG": (4096, BF), "zb": (2048, BF), "TI": (544, BF), "vI": (32, FP), "X": (272, FP), "pi": (16, I32), "pf": (32, FP), "X2": (128, FP),
-    "Y": (8, FP), "idb": (128, BF), "nidb": (128, BF), "idh": (128, HF), "nidh": (128, HF), "LT": (128, HF), "GE": (128, HF),
-    "Mr": (128, HF), "Rh": (1024, HF), "RS": (1056, HF), "sq": (512, HF), "grp": (128, HF), "pm": (48, BF), "Y4": (16, FP), "cb": (128, BF),
-    "blkf": (8, FP), "blkh": (8, HF), "Mi": (16, BF), "Mp": (64, BF), "Y3": (64, FP), "pen": (8, HF), "sel": (8, BF), "Y2": (8, FP), "c2": (32, HF),
-    "c2f": (16, FP), "wD": (4096, FP), "two": (16, HF), "idc": (32, FP), "ci": (8, I32), "cf": (16, FP),
-    "cl": (24, U16), "hX4": (32, HF), "hX5": (32, HF), "hX6": (32, HF),
-}
-for _k, _v in PER.items():
-    BUF[_k + "_0"] = _v; BUF[_k + "_1"] = _v
+STR = {"zt": (7184, BF), "S": (1136, BF), "P2": (1024, BF), "f": (1024, BF), "g": (1024, BF), "f2": (1024, BF), "g2": (1024, BF), "yt": (1024, BF),
+       "L": (100, U16), "LY": (64, U16), "sP0": (32, HF), "sP1": (64, HF), "sP2": (64, HF),
+       "rE0": (96, HF), "rE1": (96, HF), "rE2": (64, HF), "rX2": (64, HF), "qf": (64, FP)}
+CHN = {"rows": (512, BF), "rowsI": (512, BF), "TP": (512, BF), "TQ": (512, BF), "VP": (128, FP),
+       "fl": (64, HF), "rP0": (64, HF), "rP1": (128, HF), "rP2": (128, HF), "wI": (256, FP), "wN": (256, FP), "wL": (512, FP), "gI": (512, FP),
+       "gP": (256, HF), "gQ": (1024, HF), "maskE": (256, HF), "maskO": (256, HF), "cum": (32, HF), "nt": (48, HF),
+       "uO": (16, U16), "uE": (16, U16), "l1": (128, HF), "qa": (64, I32), "qb": (128, I32), "uN": (64, U16), "qd": (192, I32),
+       "uP": (64, U16), "q0h": (32, HF), "uq0": (32, U16)}
+BUF = {"W1": (4096, BF), "W2": (4096, BF), "W3": (4096, BF), "zb": (1024, BF), "TI": (544, BF), "vI": (32, FP), "X": (272, FP), "pi": (16, I32), "pf": (32, FP),
+       "X2": (128, FP), "Y": (8, FP), "idb": (128, BF), "nidb": (128, BF), "idh": (128, HF), "nidh": (128, HF), "LT": (128, HF), "GE": (128, HF),
+       "Mr": (128, HF), "Rh": (1024, HF), "RS": (576, HF), "sq": (800, HF), "grp": (128, HF), "pm": (48, BF), "Y4": (16, FP),
+       "blkf": (8, FP), "blkh": (8, HF), "Mp": (64, BF), "Y3": (64, FP), "pen": (8, HF), "sel": (8, BF), "Y2": (8, FP), "c2": (32, HF),
+       "c2f": (16, FP), "wD": (4096, FP), "two": (16, HF), "idc": (32, FP), "ci": (8, I32), "cf": (16, FP), "cl": (32, U16), "qi": (256, I32), "qh": (1024, HF)}
+for _k, _v in STR.items():
+    for _b in range(4):
+        BUF["%s_%d" % (_k, _b)] = _v
+for _b in range(2):
+    for _k, _v in CHN.items():
+        BUF["%s_%d" % (_k, _b)] = _v
+for _b in range(4):
+    BUF["hX%d" % _b] = (48, HF)
 AL, SB = {}, {}
 for _k, (_w, _d) in BUF.items():
     _o = SB.get("pool" + _d, (0, _d))[0]
     AL[_k] = ("pool" + _d, _o, _w); SB["pool" + _d] = (_o + (_w + 15) // 16 * 16, _d)
 SCRATCH = {k: ("sbuf", [128, w], d) for k, (w, d) in SB.items()}
 for _b in range(8):
-    SCRATCH["p%d" % _b] = ("psum", [128, 512], "float32")
-SEMAPHORES = ["v", "t", "s", "gp", "loc"] + ["d%d" % k for k in range(26)] + [k + str(t) for k in ("rs", "ag", "hx", "hi") for t in range(7)]
+    SCRATCH["p%d" % _b] = ("psum", [128, 512], "float32") if _b < 6 else ("psum", [128, 1024], "bfloat16")
+SEMAPHORES = (["v", "t", "s", "gp", "loc"] + ["d%d" % k for k in range(60)] + ["l%d" % k for k in range(20)]
+              + [k + str(t) for k in ("rs", "ag") for t in range(12)] + [k + str(t) for k in ("yq", "hi") for t in range(4)])
 
 
 def V(n, lo=0, hi=None, st=1):
@@ -55,11 +80,13 @@ def isv(a):
     return isinstance(a, tuple) and len(a) > 0 and a[0] in ("V", "I")
 
 
-def plan(r):
-    ops = []; mark = [0]; nm = [0]
+def plan(r, own):
+    ops = []; nm = [0]; ty = 0 if r in own[0] else 1; xr = own[ty].index(r); big = []
 
     def spans(x):
-        return spans(x[1]) + spans(x[2]) if x[0] == "I" else [(x[1], x[2], x[3])]
+        if x[0] != "V":
+            return spans(x[1]) + spans(x[2]) if x[0] == "I" else []
+        return [(x[1], x[2], x[3], x[4] if PAR["exact"] else 1) + ((x[5], x[5] + x[6] * x[7]) if len(x) > 5 else (0, 128))]
 
     def op(eng, *ins):
         rd, wr = [], []
@@ -71,7 +98,7 @@ def plan(r):
             for x in list(a[1:]) + list(kw.values()):
                 if isv(x):
                     rd += spans(x)
-        ops.append((eng, "c", ins, sorted(set(rd)), sorted(set(wr)), 0.0, mark[0]))
+        ops.append((eng, "c", ins, sorted(set(rd)), sorted(set(wr)), 0))
 
     def ts(o, i, s1, s2, o0, o1=None):
         op("v", ("tensor_scalar", (o, i, s1, s2, o0) if o1 is None else (o, i, s1, s2, o0, o1), {}))
@@ -85,18 +112,21 @@ def plan(r):
     def ms(o, c):
         op("v", ("memset", (o, c), {}))
 
+    def scan(o, a, b, f0, f1):
+        op("v", ("tensor_tensor_scan", (o, a, b, 0.0, f0, f1), {}))
+
     def act(o, i, f=None, **kw):
         op("s", ("activation", (o, i, f if f is not None else (F.Identity if kw else F.Copy)), kw))
 
     def mov(o, i, bias=None):
         k = nm[0]; nm[0] += 1
-        if ONV[k] == "1":
+        if ONV[ty][k] == "1":
             cp(o, i) if bias is None else ts(o, i, bias, None, A.add)
         elif bias is None:
             act(o, i)
         else:
             act(o, i, bias=bias)
-        ops[-1] = ops[-1][:5] + (k + 1,) + ops[-1][6:]
+        ops[-1] = ops[-1][:5] + (k + 1,)
 
     def iota(o, pat, base, cm):
         op("gp", ("iota", (o, pat, base, cm), {} if SB[o[1]][1] == I32 else {"allow_small_or_imprecise_dtypes": True}))
@@ -108,73 +138,93 @@ def plan(r):
                 ins.append(("matmul", (o, l, x, first and k == 0, last and k == len(gr) - 1), {}))
         op("t", *ins)
 
-    def dma(items, load, ns, split, after=None):
-        sp = sorted(set(s for x in items for s in spans(x[0])))
-        rd = spans(items[0][3]) + spans(after) if after else []
-        ops.append(("sy", "d", (load, items, split), rd if load else sp, sp if load else [], ns, mark[0]))
+    def dma(items, split=False, paced=False):
+        after = big[-PAR["pace"]:][:1] if paced and len(big) >= PAR["pace"] else []
+        for k, it in enumerate((items[::2], items[1::2]) if split else (items,)):
+            q = "s" if k else "sy"; num = 0
+            if split == 2:
+                q = "sy" if ONV[ty][nm[0]] == "1" else "s"; nm[0] += 1; num = nm[0]
+            ops.append((q, "d", (it, None, after), sorted(set(s for x in it for s in spans(x[1]))), sorted(set(s for x in it for s in spans(x[0]))), num))
+        if paced:
+            big.append(len(ops) - 1)
 
-    def remote(kind, t, n, w, src=None, after=None):
-        sl = lambda b, x: V(b, w * x, w * x + w)
-        srcs = [sl(src, x) for x in others] if src else [sl(n, r)]
-        ops.append(("gp", "r", (kind, t, srcs, sl(n, r)), [s for x in srcs + ([after] if after else []) for s in spans(x)],
-                    [s for x in others for s in spans(sl(n, x))], 0.0, mark[0]))
+    def send(name, pairs, one):
+        ops.append(("gp", "r", (name, pairs, one), sorted(set(s for x in pairs for s in spans(x[1]))), [], 0))
+
+    def recv(name, views):
+        ops.append(("rx", "x", (name,), [], [s for x in views for s in spans(x)], 0))
+
+    def scatter_sums(s, t, w):
+        name = "rs%d" % (4 * t + s); ow = own[s % 2]; dst = lambda y: V("rP%d_%d" % (t, s // 2), w * y, w * y + w)
+        send(name, [(y, V("sP%d_%d" % (t, s), w * x, w * x + w), dst(r)) for x, y in enumerate(ow) if y != r], False)
+        if r in ow:
+            recv(name, [dst(y) for y in others])
+
+    def spread(name, n, w):
+        a = V(n, w * xr, w * xr + w)
+        send(name, [(y, a, a) for y in others], True)
+
+    def take(name, s, n, w):
+        recv(name, [V(n, w * x, w * x + w) for x, y in enumerate(own[s % 2]) if y != r])
 
     col = lambda n, j: V(n, j, j + 1)
     blk = lambda n, a: V(n, 128 * a, 128 * a + 128)
     SHR, AND = A.arith_shift_right, A.bitwise_and
-    EQ, MUL, ADD, SUB = A.is_equal, A.mult, A.add, A.subtract
+    EQ, MUL, ADD, SUB, MAX, MIN = A.is_equal, A.mult, A.add, A.subtract, A.max, A.min
     others = [x for x in range(4) if x != r]
+    C0 = 3072
 
-    def loads(b):
-        n = "zt_%d" % b; z = lambda lo, hi, hf, c0: (V(n, lo, hi), 64 * hf, 64, "z", 64 * b, 64, c0, hi - lo)
-        t0 = 3400 + 2900 * b
-        if b == 0:
-            dma([z(3056, 4096, 0, 1008), z(3056, 4096, 1, 3056)], True, t0 - 700, True)
-            dma([z(2048, 3056, 0, 0), z(2048, 3056, 1, 2048)], True, t0, True)
-        else:
-            dma([z(2048, 4096, 0, 0), z(2048, 4096, 1, 2048)], True, t0, True)
-        dma([(V("qi_%d" % b), 64 * hf, 64, "q", 64 * b, 64, 128 * hf, 128) for hf in range(2)], True, t0 + 100, True)
-        dma([z(4096, 6144, 0, 2048), z(0, 2048, 1, 0)], True, t0 + 1500, True)
-
-    def zero(n, ns, after):
-        dma([(V(n, 2048 * c, 2048 * c + 2048), 0, 128, V("zb"), 0, 128, 0, 0) for c in range(2)], True, ns, False, after)
+    def zl(s, u, lo, hi, sh=0):
+        return (V("zt_%d" % s, lo + sh + C0 - 1024 * u, hi + sh + C0 - 1024 * u) + (32 * u, 32, 1), ("T", "z", 32 * s, 32, lo, hi - lo))
 
     ms(V("zb"), 0.0)
-    mark[0] = 1; loads(0); mark[0] = 0; loads(1)
-    zero("WG", 8800, V("zb"))
-    for b in range(2):
-        dma([(V(x + "_%d" % b), 0, 128, V("zb", 0, PER[x][0]), 0, 128, 0, 0) for x in ("TP", "TM", "TQ")], True, 9100 + 100 * b, False, V("zb"))
-    for b in range(2):
-        h = lambda c, hf: V("zt_%d" % b, c, c + 1) + (64 * hf,)
-        mark[0] = 1 - b
-        for o, i in ((h(2047, 0), h(6143, 0)), (h(6144, 0), h(2048, 0)), (h(4096, 1), h(0, 1))):
-            mov(o, i)
+    dma([zl(0, u, max(1024 * u - 16, 0), 1024 * u + 1024) for u in range(4)] + [zl(0, 0, 4080, 4096, -4096)], True, True)
+    dma([(V("qi"), ("T", "q", 0, 128, 0, 256))], False, True)
+    dma([zl(0, u, 0, 1024 * u - 16) for u in range(1, 4)] + [zl(0, u, 1024 * u + 1024, 4096) for u in range(3)], True, True)
+    for ch in PAR["seq"][ty]:
+        if ch in "123":
+            for u in range(4):
+                dma([zl(int(ch), u, 0, 4096)], paced=True)
+        elif ch in "abc":
+            for c in range(4):
+                dma([(V("W%d" % (1 + "abc".index(ch)), 1024 * c, 1024 * c + 1024), V("zb", 0, 1024))], paced=True)
+        elif ch in "VBXY":
+            a = AL[{"V": "W1", "B": "W2", "X": "TP_0", "Y": "TP_1"}[ch]]
+            for lo, n in ((0, 512), (512, 512)) if ch in "XY" else [(1024 * c, 1024) for c in range(4)]:
+                o = ("V", a[0], a[1] + lo, a[1] + lo + n, 1)
+                ms(o, 0.0) if ONV[ty][nm[0]] == "1" else act(o, V("zb", 0, n))
+                nm[0] += 1; ops[-1] = ops[-1][:5] + (nm[0],)
+        else:
+            o = AL["TP_%d" % (ch == "y")]
+            dma([(("V", o[0], o[1], o[1] + 1024, 1), V("zb"))])
 
     iota(V("X"), [[1, 272]], -64, 0)
     X = lambda lo, hi, st=1: V("X", 64 + lo, 64 + hi, st)
     iota(col("pi", 0), [[0, 1]], 0, 1)
-    iota(V("X2"), [[0, 8], [1, 16]], 0, 0)
-    iota(V("Y"), [[1, 4], [4, 2]], 0, 0)
+    iota(V("Y"), [[1, 2], [2, 4]], 0, 0)
     iota(V("vI"), [[2048, 2], [128, 2], [256, 8]], 8192, 1)
     iota(V("c2f"), [[256, 16]], -2047, 2)
     iota(V("idc"), [[1, 2], [2048, 2], [32, 8]], 8192, 0)
-    for j, (sh, an) in enumerate([(0, 15), (4, 7), (6, 1), (4, 3), (0, 7), (3, 1), (1, 7), (0, 1)]):
+    for j, (sh, an) in enumerate([(0, 15), (4, 7), (5, 3), (4, 1), (0, 7), (3, 1), (1, 7), (0, 1)]):
         ts(col("pi", j + 1), col("pi", 0), sh, an, SHR, AND)
     cp(V("pf", 0, 9), V("pi", 0, 9))
     pf = lambda j: col("pf", j)
-    lin = lambda o, a, c, b: act(pf(o), pf(a), scale=float(c), bias=b)
+    lin = lambda o, a, c, b: ts(pf(o), pf(a), float(c), b, MUL, ADD)
     ms(V("grp"), 1.0)
-    sel = lambda o, pat, f, base, cm: op("gp", ("affine_select", (o, V("grp"), pat, f, 0.0, base, cm), {}))
+    sel = lambda o, pat, f, base, cm: op("gp", ("affine_select", (o, V("grp", 0, nel(o)), pat, f, 0.0, base, cm), {}))
+    ms(V("sq", 0, 544), 0.0)
+    sqo = (96, 320, 544, 672)
+    SQ = lambda k: V("sq", sqo[k], sqo[k] + 128)
     for k in range(4):
-        sel(blk("sq", k), [[-16, 8], [1000, 2], [-2, 8]], EQ, -(k // 2) - 1000 * (k % 2), 1)
-    lin(9, 3, -2048, 4096.0); lin(10, 3, -2048, 4097.0)
-    zc, zc1 = pf(9), pf(10)
+        sel(SQ(k), [[-16, 8], [1000, 2], [-2, 8]], EQ, -(k // 2) - 1000 * (k % 2), 1)
+    lin(9, 3, -1024, 5120.0)
+    zc = pf(9)
     sel(V("idh"), [[-1, 128]], EQ, 0, 1)
-    act(V("idb"), V("idh"))
+    mov(V("idb"), V("idh"))
     act(V("nidb"), V("idh"), scale=-1.0)
     ts(V("pm", 0, 8), V("Y"), pf(2), None, EQ)
     ts(V("pm", 8, 16), V("Y"), pf(2), -1.0, EQ, MUL)
-    iota(V("Y4"), [[1, 4], [4, 4]], 0, 0); iota(V("cb"), [[0, 4], [3200, 2], [0, 16]], -1600, 0)
+    iota(V("Y4"), [[1, 2], [100, 2], [2, 4]], 0, 0)
     ts(V("pm", 16, 32), V("Y4"), pf(2), None, EQ)
     ts(V("pm", 32, 48), V("Y4"), pf(2), -1.0, EQ, MUL)
     act(V("nidh"), V("idh"), scale=-1.0)
@@ -182,66 +232,158 @@ def plan(r):
     sel(V("GE"), [[-1, 128]], A.is_ge, 0, 1)
     ts(V("blkf"), X(0, 8), pf(2), None, EQ)
     ts(V("blkh"), X(0, 8), pf(2), None, EQ)
-    ts(V("Mi"), X(0, 16), pf(1), None, EQ)
     iota(V("Y3", 0, 32), [[1, 16], [-100, 2]], 100, 0); iota(V("Y3", 32, 64), [[1, 16], [100, 2]], 0, 0)
     ts(V("Mp"), V("Y3"), pf(1), None, EQ)
     ts(V("pen"), X(0, 8), pf(2), -30000.0, EQ, MUL)
     iota(V("Y2"), [[2, 2], [1, 2], [4, 2]], 0, 0)
     ts(V("sel"), V("Y2"), pf(7), None, EQ)
-    ts(V("Mr"), V("X2"), pf(1), None, EQ)
-    for a in range(8):
-        act(blk("Rh", a), V("Mr"), scale=col("blkf", a))
+    for a in range(0, 8, 2):
+        op("gp", ("affine_select", (V("Rh", 128 * a, 128 * a + 256), V("zb", 0, 256), [[-16, 2], [0, 8], [-1, 16]], A.not_equal, 1.0, -16 * a, 1), {}))
     ms(V("RS"), 0.0)
-    for v in range(6):
-        sel(V("RS", 176 * v + 48, 176 * v + 176), [[-64 if v < 4 else 64, 2], [1000, 4], [-1, 16]], EQ, -16 * v if v < 4 else 128 - 48 * v, 1)
-    RS = lambda v, x: V("RS", 176 * v + 48 - 16 * x, 176 * v + 176 - 16 * x)
-    act(V("c2", 0, 16), V("c2f"), bias=1.0)
-    act(V("c2", 16, 32), V("c2f"))
+    for v in range(2):
+        sel(V("RS", 144 * v + 16, 144 * v + 144), [[-32, 4], [1000, 2], [-1, 16]], EQ, -16 * v, 1)
+    for lo, n, base in ((304, 3, -32), (400, 1, 0), (448, 1, -112), (480, 3, -16)):
+        sel(V("RS", lo, lo + 32 * n), [[-32, n], [1000, 2], [-1, 16]], EQ, base, 1)
+    RS = lambda v, x: V("RS", 144 * v + 16 - 16 * x, 144 * v + 144 - 16 * x)
+    mov(V("c2", 0, 16), V("c2f"), 1.0)
+    mov(V("c2", 16, 32), V("c2f"))
     lin(12, 2, 256, 0.0); lin(13, 1, 2, pf(12))
-    ts(V("cf", 0, 3), X(0, 33, 16), pf(1), None, ADD)
-    ts(V("ci", 0, 3), V("cf", 0, 3), 1.0 / 3, -0.3, MUL, ADD)
-    ts(V("cf", 3, 6), V("ci", 0, 3), -3.0, None, MUL)
-    tt(V("cf", 6, 9), V("cf", 0, 3), V("cf", 3, 6), ADD)
-    ts(V("cf", 9, 12), V("cf", 6, 9), 64.0, 64.0, MUL, ADD)
-    tt(V("cf", 0, 3), V("cf", 9, 12), V("cf", 6, 9), MUL)
-    tt(V("cf", 3, 6), V("cf", 0, 3), V("ci", 0, 3), ADD)
-    lin(14, 2, 16, 0.0)
-    ts(V("cl", 0, 3), V("cf", 3, 6), pf(14), None, ADD)
+    iota(V("cf", 0, 4), [[128, 2], [384, 2]], 0, 0); iota(V("cf", 4, 8), [[-128, 2], [256, 2]], 128, 0)
+    lin(11, 1, 2, pf(4)); lin(14, 3, 32, pf(11))
+    ts(V("cl", 24, 32), V("cf", 0, 8), pf(14), None, ADD)
     lin(16, 2, 8, pf(5)); lin(17, 6, 64, pf(16)); lin(18, 2, 32, pf(1))
     ts(V("cl", 4, 6), X(0, 129, 128), pf(17), None, ADD)
-    ts(V("cl", 6, 8), X(0, 129, 128), pf(17), 256.0, ADD, ADD)
     lin(19, 2, 8, pf(7)); lin(20, 8, 256, pf(19))
     ts(V("cl", 16, 20), X(0, 193, 64), pf(19), None, ADD)
     ts(V("cl", 20, 24), X(0, 193, 64), pf(20), None, ADD)
     ts(V("cl", 10, 12), X(0, 129, 128), pf(0), None, ADD)
     ts(V("cl", 12, 14), X(0, 17, 16), pf(18), None, ADD)
-    cS, cP, cP2, cP0, cQ0, cF = V("cl", 0, 3), V("cl", 16, 20), V("cl", 20, 24), V("cl", 4, 6), V("cl", 10, 12), V("cl", 12, 14)
+    cP, cP2, cP0, cQ0, cF = V("cl", 16, 20), V("cl", 20, 24), V("cl", 4, 6), V("cl", 10, 12), V("cl", 12, 14)
     ms(V("two"), 2.0)
     ms(V("TI"), 0.0)
-    act(V("TI", 16, 528, 16), V("vI"))
+    mov(V("TI", 16, 528, 16), V("vI"))
     tt(V("TI", 17, 529, 16), V("vI"), V("TI", 16, 528, 16), SUB)
     Rh = lambda a: blk("Rh", a)
+    ts(V("qh", 0, 256), V("qi"), -2048.0, None, ADD)
+    ts(V("qh", 512, 768), V("qh", 0, 256), 1.0, None, ADD)
+    ts(V("qh", 768, 1024), V("qh", 0, 256), 2047.0, -4096.0, EQ, MUL)
+    tt(V("qh", 256, 512), V("qh", 512, 768), V("qh", 768, 1024), ADD)
+    for c in range(8):
+        iota(V("wD", 512 * c, 512 * c + 512), [[0, 512]], 0, 0)
 
-    def batch(b):
-        N = lambda n: "%s_%d" % (n, b)
-        W = lambda n, lo=0, hi=None, st=1: V(N(n), lo, hi, st)
-        P = lambda k, lo=0, hi=512, st=1: ("V", "p%d" % (4 * b + k), lo, hi, st)
-        ZW = W("zt"); flip = [0]
+    def stream(s):
+        W = lambda n, lo=0, hi=None, st=1: V("%s_%d" % (n, s), lo, hi, st)
+        P = lambda lo=0, hi=512, st=1: ("V", "p%d" % (4 + s % 2), lo, hi, st)
+        ZW = W("zt"); mine = r in own[s % 2]
+        odd = lambda n, j: W(n, 256 * j + 1, 256 * j + 256, 2)
+        sub = lambda v, j: v[:2] + (v[2] + 128 * j * v[4], v[2] + (128 * j + 127) * v[4] + 1, v[4])
 
         def term(o, a, x, on_s):
             if on_s:
-                k = flip[0]; flip[0] = 1 - k; ps = P(k, 0, nel(o))
-                mm([[(ps, V("idb"), a), (ps, V("nidb"), x)]])
-                act(o, ps, F.Relu)
+                mm([[(P(), V("idb"), a), (P(), V("nidb"), x)]])
+                act(o, P(), F.Relu)
             else:
-                tt(o, a, x, A.max)
+                tt(o, a, x, MAX)
 
         def reduce(out, items):
             d = {}
-            for v, s in items:
-                d[v] = d.get(v, 0) + s
-            sg = (V("pm", 0, 8), V("pm", 8, 16)) if nel(out) == 8 else (V("pm", 16, 30), V("pm", 32, 46))
-            return [(out, v, sg[s < 0]) for v, s in d.items() for _ in range(abs(s))]
+            for v, sg in items:
+                d[v] = d.get(v, 0) + sg
+            pm = (V("pm", 0, 8), V("pm", 8, 16)) if nel(out) == 8 else (V("pm", 16, 28), V("pm", 32, 44))
+            return [(out, v, pm[sg < 0]) for v, sg in d.items() for _ in range(abs(sg))]
+
+        def between(f, g, a, b):
+            n = 1024 // PAR["nch"]
+            for c in range(PAR["nch"]):
+                for o, f0, f1 in ((f, MAX, MIN), (g, MIN, MAX)):
+                    scan(W(o, n * c, n * c + n), a(n * c, n), b(n * c, n), f0, f1)
+
+        def start():
+            h = lambda c, u: W("zt", c, c + 1) + (32 * u, 32, 1)
+            if s:
+                mov(h(C0 - 1, 0), h(7167, 0))
+            k32 = (32 * s, 32, 1)
+            mm([[(P(32 * d, 32 * d + 32), V("sq", 96 + 224 * k + 32 * (s - u), 224 + 224 * k + 32 * (s - u)) + k32, V("qh", 256 * d + 64 * u + k, 256 * d + 64 * u + 64, 2) + k32)
+                 for u in range(4) for k in range(2)] for d in range(2)])
+            ts(W("L", 0, 64), P(0, 64), zc, None, ADD)
+
+        def coords0():
+            S = PAR["m"][ty][s]
+            between("f", "g", lambda k, n: W("zt", C0 + k, C0 + k + n), lambda k, n: W("zt", C0 - 1 + k, C0 - 1 + k + n))
+            e, x0, x1 = W("zt", C0, C0 + 1023, 2), W("P2", 0, 512), W("P2", 512, 1024)
+            D, Ft, G = W("f2", 0, 512), W("f2", 512, 1024), W("g2", 0, 512)
+            mov(x0, IND(ZW, W("L", 0, 32))); term(D, x0, e, "D" in S)
+            mov(x1, IND(ZW, W("L", 32, 64))); term(Ft, x1, e, "F" in S); term(G, x1, x0, "G" in S)
+            gr = [(P(0, 32), V("idb"), V("zb", 0, 32))]
+            for j in range(4):
+                gr += reduce(P(j, 32, 4), [(odd("g", j), -1), (odd("f", j), 1)])
+            mm([gr], True, False); gr = []
+            for j in range(4):
+                gr += reduce(P(j, 32, 4), [(sub(D, j), 1), (sub(Ft, j), 1), (sub(G, j), -1), (sub(e, j), -1)]
+                             + [(sub(e, j), 1)] * (("D" in S) + ("F" in S)) + [(sub(x0, j), -1)] * ("G" in S))
+            mm([gr], False, True)
+            mov(W("sP0"), P(0, 32))
+            scatter_sums(s, 0, 16)
+
+        def lists(t, w, n, rng):
+            E = "rE%d_%d" % (t, s); take("ag%d" % (4 * t + s), s, E, w)
+            sh = lambda xs: [(P(o, o + st * (hi - lo - 1) + 1, st), RS(v, x), V(E, w * x + lo, w * x + hi)) for x in xs for v, lo, hi, o, st in rng]
+            mm([[(P(0, n), V("idb"), V("zb", 0, n))] + (sh([xr]) if mine else [])], last=False)
+            mm([sh([1 - xr] if mine else [0, 1])], first=False)
+
+        def coords(t):
+            es = 1 - t % 2; S = PAR["m"][ty][4 * t + s]
+            lists(t - 1, 48, 100, [(v, 0, 48, 2 * es + v, 2) for v in range(2)] + [(2, 32, 33, 96 + 2 * es, 1)] + [(3, 15, 16, 1, 1)] * es)
+            ts(W("L"), P(0, 100), zc, None, ADD)
+            LO, LX, LE = (W("L", 0, 34), W("L", 34, 66), W("L", 66, 99)) if es else (W("L", 64, 97), W("L", 32, 64), W("L", 0, 32))
+            o0, i0 = 62 * es, 64 * es
+            mov(W("S", 0, 32 * nel(LO) - 1, 2), IND(ZW, LO))
+            mov(W("S", o0 + 1, o0 + 32 * nel(LE), 2), IND(ZW, LE))
+            between("f", "g", lambda k, n: W("S", o0 + 1 + k, o0 + 1 + k + n), lambda k, n: W("S", o0 + k, o0 + k + n))
+            o, e = W("S", i0, i0 + 1023, 2), W("S", i0 + 1, i0 + 1024, 2)
+            if S == "s":
+                mov(W("P2", 0, 1023, 2), o)
+                mov(W("P2", 1, 1024, 2), IND(ZW, LX))
+                between("f2", "g2", lambda k, n: W("S", i0 + k, i0 + k + n), lambda k, n: W("P2", k, k + n))
+                it = lambda j: [(odd("g2", j), 1), (odd("f2", j), -1)]
+            else:
+                x = W("P2", 0, 512); At, D, Ft = W("g2", 0, 512), W("f2", 0, 512), W("f2", 512, 1024)
+                term(At, e, o, "A" in S)
+                mov(x, IND(ZW, LX)); term(D, o, x, "D" in S); term(Ft, e, x, "F" in S)
+                it = lambda j: ([(sub(D, j), 1), (sub(Ft, j), 1), (sub(At, j), -1), (sub(x, j), -1)]
+                                + [(sub(x, j), 1)] * (("D" in S) + ("F" in S)) + [(sub(o, j), -1)] * ("A" in S))
+            gr = [(P(0, 64), V("idb"), V("zb", 0, 64))]
+            for j in range(4):
+                gr += reduce(P(16 + j, 61 + j, 4), [(odd("g", j), -1), (odd("f", j), 1)])
+            mm([gr], True, False)
+            mm([[m for j in range(4) for m in reduce(P(j, 45 + j, 4), it(j))]], False, True)
+            mov(W("sP%d" % t), P(0, 64))
+            scatter_sums(s, t, 32)
+
+        def final():
+            lists(2, 32, 64, [(v, 0, 32, 32 * v, 1) for v in range(2)])
+            ts(W("LY"), P(0, 64), zc, None, ADD)
+            for c in range(2):
+                mov(W("yt", 512 * c, 512 * c + 512), IND(ZW, W("LY", 32 * c, 32 * c + 32)))
+            dma([(("T", "yz", 32 * s, 32, 1024 * u, 1024), W("yt") + (32 * u, 32, 1)) for u in range(4)], 2)
+
+        def targets():
+            take("yq%d" % s, s, "rX2_%d" % s, 32)
+            mov(W("qf"), W("rX2"), 2047.0)
+            dma([(("T", "yq", 2 * s + x, 1, 0, 4096), W("qf", 32 * x, 32 * x + 32)) for x in range(2)], 2)
+
+        return [start, coords0, lambda: coords(1), lambda: coords(2), final, targets]
+
+    def chain(b):
+        s = 2 * b + ty
+        N = lambda n: "%s_%d" % (n, b)
+        W = lambda n, lo=0, hi=None, st=1: V(N(n), lo, hi, st)
+        P = lambda k, lo=0, hi=512, st=1: ("V", "p%d" % (2 * b + min(k, 1)), lo, hi, st)
+
+        def turn(o, tiles):
+            n = 128 * len(tiles); ps = lambda lo, hi: ("V", "p%d" % (6 + b), lo, hi, 1)
+            op("t", *[("transpose", (ps(128 * k, 128 * k + 128), x, V("idb")), {}) for k, x in enumerate(tiles)])
+            mov(o, ps(0, n))
 
         def rep(k, lo, rhs):
             n = nel(rhs)
@@ -254,7 +396,10 @@ def plan(r):
 
         def urgent(t):
             p = t % 2
-            ts(W("qd", 128, 144), P(3, 0, 16), 2047.0, None, ADD); ts(W("qd", 144, 160), P(3, 48, 64), 2047.0, None, ADD)
+            if t:
+                ts(W("qd", 128, 160), P(2, 64, 96), 2047.0, None, ADD)
+            else:
+                ts(W("qd", 144, 160), W("VP", 33, 64, 2), -8192.0, None, ADD)
             ts(W("qd", 0, 32), W("qd", 128, 160), 5, None, SHR)
             ts(W("qd", 32, 64), W("qd", 128, 160), 31, None, AND)
             cp(W("uP", 0, 64), W("qd", 0, 64))
@@ -263,289 +408,199 @@ def plan(r):
 
         def prep(t, c):
             if t == 0:
-                ts(W("qd", 128, 144), P(3, 0, 16), c, None, ADD)
-            if t < 2:
-                mov(W("VP", 64, 128, 2), P(3, 0, 32), c + 8192.0)
+                ts(W("qd", 128, 144), P(2, 0, 16), c, None, ADD)
+                mov(W("VP", 64, 128, 2), P(2, 0, 32), c + 8192.0)
+            elif t == 1:
+                mov(W("VP", 64, 128), P(2, 0, 64), c + 8192.0)
             else:
-                ts(W("qa", 0, 32), P(3, 0, 32), c, 4097.0, ADD, MUL)
-                ts(W("qb", 0, 32), W("qa", 0, 32), 5, 255, SHR, AND)
-                ts(W("qb", 32, 64), W("qa", 0, 32), 1, 15, SHR, AND)
-            if t == 1:
-                mov(W("VP", 65, 128, 2), P(3, 32, 64), c + 8192.0)
+                ts(W("qa", 0, 32), P(2, 0, 32), c, 4097.0, ADD, MUL)
+                ts(W("qb", 0, 32), W("qa", 0, 32), 5, 4032, SHR, AND)
+                ts(W("qb", 32, 64), W("qa", 0, 32), 5, 63, SHR, AND)
             if t:
                 rows(t)
-            else:
-                ts(W("qd", 0, 16), W("qd", 128, 144), 5, None, SHR)
-                ts(W("qd", 16, 32), W("qd", 128, 144), 31, None, AND)
-                cp(W("uP", 0, 32), W("qd", 0, 32)); cp(W("uq"), W("qd", 128, 144))
-                mov(W("maskE"), IND(V("Mp", 0, 32), W("uP", 16, 32)))
 
         def rows(t):
             if t < 2:
-                split(W("VP", 64, 128), 4 * t + 2)
+                split(W("VP", 64, 128), 4 * t * (1 - b) + 2)
             else:
                 for k in range(2):
                     cp(W("TQ", 12 + 2 * b + k, 512, 16), W("qb", 32 * k, 32 * k + 32))
-            mm([[(P(3, 128 * k, 128 * k + 128), blk(N("TP" if t < 2 else "TQ"), k), V("idb"))] for k in range(4)])
-            mov(W("rows"), P(3))
-
-        def start():
-            ts(W("qh"), W("qi"), -2048.0, None, ADD)
-            o = P(2, 0, 64)
-            mm([[(o, blk("sq", 0), W("qh", 0, 128, 2)), (o, blk("sq", 1), W("qh", 1, 128, 2))]])
-            ts(W("LX"), o, zc, None, ADD)
-            ts(W("LE", 0, 64), o, zc1, None, ADD)
+            turn(W("rows"), [blk(N("TP" if t < 2 else "TQ"), k) for k in range(4)])
 
         def prep0():
-            ms(W("cum", 0, 8), 0.0)
-            for c in range(4 - 4 * b):
-                iota(V("wD", 1024 * c, 1024 * c + 1024), [[0, 1024]], 0, 0)
-            mm([[(P(3, 128 * hf, 128 * hf + 128), Rh(4 * hf + r), W("qh"))] for hf in range(2)])
-            mov(W("wL", 0, 256), P(3, 0, 256))
+            ms(W("cum", 0, 8), 0.0); ms(W("fl"), 0.0)
+            mm([[(P(2, 0, 256), Rh(2 * s + xr), V("qh", 0, 256))]])
+            mov(W("wL", 0, 256), P(2, 0, 256))
             mov(W("q0h"), IND(W("wL", 0, 256), cQ0))
             ts(W("uq0"), W("q0h"), 2048.0, None, ADD)
-            mm([[(P(3, 16 * pp, 16 * pp + 16), blk("sq", 2 * pp + e), W("q0h", e, 32, 2)) for e in range(2)] for pp in range(2)])
+            mm([[(P(2, 16 * pp, 16 * pp + 16), SQ(2 * pp + e), W("q0h", e, 32, 2)) for e in range(2)] for pp in range(2)])
             prep(0, 2048.0)
-            mm([[(P(3, 128 * k, 128 * k + 128), V("TI", 16 - 2 * b + 128 * k, 144 - 2 * b + 128 * k), V("idb"))] for k in range(4)])
-            mov(W("rowsI"), P(3))
+            turn(W("rowsI"), [V("TI", 12 - 2 * b + 128 * k, 140 - 2 * b + 128 * k) for k in range(4)])
             for k in range(2):
-                cp(IND(V("WG"), W("uq0", 16 * k, 16 * k + 16)), W("rowsI", 256 * k, 256 * k + 256))
-            mm([[(P(3, 16 * pp + cc, 16 * pp + cc + 1), V("WG", 256 * cc + pp, 256 * cc + 256, 2), col("sel", 2 * b))] for pp in range(2) for cc in range(16)])
-            mov(W("l1", 32, 64), P(3, 0, 32), -10240.0)
-            mm(rep(3, 256, W("l1", 32, 64)))
-            mov(W("wL", 256, 512), P(3, 256, 512))
+                cp(IND(V("W1"), W("uq0", 16 * k, 16 * k + 16)), W("rowsI", 256 * k, 256 * k + 256))
+            mm([[(P(2, 16 * pp + cc, 16 * pp + cc + 1), V("W1", 256 * cc + pp, 256 * cc + 256, 2), col("sel", 4 + 2 * b))] for pp in range(2) for cc in range(16)])
+            mov(W("l1", 32, 64), P(2, 0, 32), -10240.0)
+            mm(rep(2, 256, W("l1", 32, 64)))
+            mov(W("wL", 256, 512), P(2, 256, 512))
             mov(W("VP", 0, 64), IND(W("wL", 256, 512), cP), 10240.0)
+            urgent(0)
             mov(W("VP", 0, 64, 2), V("idc"), pf(13))
             mov(W("VP", 65, 128, 2), W("VP", 1, 64, 2))
             split(W("VP", 0, 64), 0)
             rows(0)
 
-        def coords0():
-            ze = lambda s, n, d=0: W("zt", 2048 + 2 * s + d, 2048 + 2 * s + d + 2 * n - 1, 2)
-            t_ = lambda n, s, w: W(n, s, s + w)
-            for c in (1, 0):
-                s = 512 * c; S = PAR["S0"][c]
-                term(t_("tA", s, 512), ze(s, 512), ze(s, 512, -1), "A" in S)
-                term(t_("tB", s, 512), ze(s, 512), ze(s, 512, 1), "B" in S)
-                term(t_("tC", s, 512), ze(s, 512, -1), ze(s, 512, 1), "C" in S)
-                gr = [(P(2, 256, 320), V("idb"), V("zb", 0, 64))] if c == 1 else []
-                for x in range(4 * c, 4 * c + 4):
-                    k = 128 * x
-                    it = [(t_("tA", k, 128), 1), (t_("tB", k, 128), 1), (t_("tC", k, 128), -1)]
-                    it += [(ze(k, 128, -1), 1)] * ("A" in S) + [(ze(k, 128, 1), 1)] * ("B" in S) + [(ze(k, 128, 1), -1)] * ("C" in S)
-                    gr += reduce(P(2, 256 + x, 320, 8), it)
-                mm([gr], c == 1, False)
-            for c in range(2):
-                s = 512 * c; S = PAR["S0"][c]
-                mov(t_("Xt", s, 512), IND(ZW, W("LX", 32 * c, 32 * c + 32)))
-                term(t_("tD", s, 512), t_("Xt", s, 512), ze(s, 512), "D" in S)
-                mov(t_("Et", s, 512), IND(ZW, W("LE", 32 * c, 32 * c + 32)))
-                tt(t_("tF", s, 512), t_("Et", s, 512), ze(s, 512), A.max)
-                tt(t_("tG", s, 512), t_("Et", s, 512), t_("Xt", s, 512), A.max)
-                for n, sg in (("tD", -1), ("tF", -1), ("tG", 1)):
-                    gr = []
-                    for x in range(4 * c, 4 * c + 4):
-                        k = 128 * x
-                        gr += reduce(P(2, 256 + x, 320, 8), [(t_(n, k, 128), sg)] + [(ze(k, 128), -1)] * ("D" in S and n == "tD"))
-                    mm([gr], False, c == 1 and n == "tG")
-            mov(W("sP0"), P(2, 256, 320))
-            remote("rs", b, N("rP0"), 16, N("sP0"), None if b else V("TQ_1"))
-            zero(N("W2"), 4500, W("rP0"))
-
-        def coords(t):
-            es = 1 - t % 2; E = N("rE%d" % (t - 1))
-            rng = [(v, 0, 48, 3 + 48 * v) for v in range(4)] + [(4, 0, 2, 195)] + [(5, 46, 47, 1)] * es
-            sh = lambda xs: [(P(2, o, o + hi - lo), RS(v, x), V(E, 48 * x + lo, 48 * x + hi)) for x in xs for v, lo, hi, o in rng]
-            mm([[(P(2, 0, 200), V("idb"), V("zb", 0, 200))] + sh([r])], last=False)
-            mm([sh(others)], first=False)
-            ts(W("LO", 0, 65), P(2, 4 - 3 * es, 197 - 3 * es, 3), zc, None, ADD)
-            ts(W("LE", 0, 64 + es), P(2, 3, 193 + 3 * es, 3), zc, None, ADD)
-            ts(W("LX"), P(2, 5, 195, 3), zc, None, ADD)
-            t_ = lambda n, s, w: W(n, s, s + w)
-            left = lambda k, n: t_("Ot", k + 15 * es, n)
-            right = lambda k, n: t_("Ot", k + 15 * es + 1, n)
-            SS = PAR["S"][4 * t - 4 + 2 * b:4 * t - 2 + 2 * b]
-            for c in range(2):
-                s = 512 * c; S = SS[c]
-                for L, G, hi in (("LO", "Ot", 65), ("LE", "Et", 64 + es)):
-                    lo, hi = (0, 34) if c == 0 else (34, hi)
-                    mov(W(G, 16 * lo, 16 * hi), IND(ZW, W(L, lo, hi)))
-                term(t_("tC", s, 512), left(s, 512), right(s, 512), "C" in S)
-                term(t_("tB", s, 512), t_("Et", s, 512), right(s, 512), "B" in S)
-                lo, n = (0, 512 + es) if c == 0 else (512 + es, 512)
-                term(t_("tA", lo, n), t_("Et", lo, n), left(lo, n), "A" in S)
-            for c in range(2):
-                S = SS[c]; gr = [(P(2, 256, 384), V("idb"), V("cb"))] if c == 0 else []
-                for x in range(4 * c, 4 * c + 4):
-                    k = 128 * x
-                    it = [(t_("tA", k, 128), -1), (t_("tB", k, 128), -1), (t_("tC", k, 128), 1)]
-                    it += [(right(k, 128), -1)] * ("B" in S) + [(right(k, 128), 1)] * ("C" in S) + [(left(k, 128), -1)] * ("A" in S)
-                    gr += reduce(P(2, 272 + x, 377 + x, 8), it)
-                    gr += reduce(P(2, 256 + x, 361 + x, 8), [(t_("tA", k + es, 128), -1)] + [(left(k, 128), -1)] * ("A" in S))
-                mm([gr], c == 0, False)
-            for c in range(2):
-                s = 512 * c
-                ix = IND(ZW, W("LX", 32 * c, 32 * c + 32)); S = SS[c]
-                if "X" in S:
-                    mov(t_("Xt", s, 512), ix); ix = t_("Xt", s, 512)
-                for n, o in (("D", lambda k, w: left(k + es, w)), ("F", lambda k, w: t_("Et", k + es, w))):
-                    term(t_("t" + n, s, 512), ix, o(s, 512), n in S)
-                    gr = []
-                    for x in range(4 * c, 4 * c + 4):
-                        gr += reduce(P(2, 256 + x, 361 + x, 8), [(t_("t" + n, 128 * x, 128), 1)] + [(o(128 * x, 128), 1)] * (n in S))
-                    mm([gr], False, c == 1 and n == "F")
-            mov(W("sP%d" % t), P(2, 256, 384))
-            remote("rs", 2 * t + b, N("rP%d" % t), 32, N("sP%d" % t))
-
         def index(t):
-            p = t % 2; row = 8 + b
+            p = t % 2; ro = 4 * t * (1 - b)
             w = 32 if t else 16
-            part = lambda x: W(("sP%d" if x == r else "rP%d") % t, w * x, w * x + w)
+            part = lambda y: V("sP%d_%d" % (t, s), w * xr, w * xr + w) if y == r else W("rP%d" % t, w * y, w * y + w)
             pen = lambda o, n: [(P(1, o + 8 * R, o + 8 * R + 8), blk(N(n), R), V("pen")) for R in range(2)]
-            PO = P(2, 0, 16) if t else P(1, 16, 32)
+            PO = P(0, 256, 272); L = P(1, 32 - w, 32); n = 8 * w
+            mm([[(P(0, 0, n), V("idb"), V("zb", 0, n))] + [(P(0, a, n, 8), Rh(a), part(r)) for a in range(8)]], last=False)
+            mm([[(P(0, a, n, 8), Rh(a), part(x)) for x in others for a in range(8)]], first=False)
+            mov(W("wI", 256 - n, 256), P(0, 0, n))
+            mm([[(P(1, 0, 32), V("idb"), V("zb", 0, 32))] * (t == 0) + [(L, V("idh"), part(r))] + pen(0, "maskO") + pen(16, "maskE")], last=False)
+            mm([[(L, V("idh"), part(x)) for x in others]], first=False, last=False)
             if t:
-                L = P(1, 0, 32)
-                mm([[(P(0, 0, 256), V("idb"), V("zb", 0, 256))] + [(P(0, a, 256, 8), Rh(a), part(r)) for a in range(8)]], last=False)
-                mm([[(P(0, a, 256, 8), Rh(a), part(x)) for x in others for a in range(8)]], first=False)
-                mov(W("wI"), P(0, 0, 256))
-                mm([[(L, V("idh"), part(r))] + pen(0, "maskO") + pen(16, "maskE")], last=False)
-                mm([[(L, V("idh"), part(x)) for x in others]], first=False, last=False)
                 tt(W("gI", 256, 512), IND(W("wI", 0, 128), W("uP", 0, 16)), W("maskE"), MUL)
                 mm([[(P(1, 8 * R, 8 * R + 8), blk(N("gI"), R), V("blkf")) for R in (2, 3)]], first=False, last=False)
-                tt(W("gI", 0, 256), IND(W("wI", 128, 256), W("uP", 16, 32)), W("maskO"), MUL)
-                mm([[(P(1, 8 * R, 8 * R + 8), blk(N("gI"), R), V("blkf")) for R in (0, 1)]], first=False)
-                ts(W("fl"), L, -30000.0, None, A.is_lt)
-                guest, mv = W("fl", 0, 16), W("fl", 16, 32)
-                mm([[(PO, V("idh"), V("c2", 16 * p, 16 * p + 16))]], last=False)
-            else:
-                L = P(1, 0, 16)
-                mm([[(L, V("nidh"), part(r))] + pen(0, "maskE")], last=False)
-                mm([[(L, V("nidh"), part(x)) for x in others]], first=False)
-                mv = W("TM", row, 256, 16); guest = P(2, 0, 16)
-                ts(mv, L, -30000.0, None, A.is_lt)
-                mm([[(P(0, 128 + 128 * R, 256 + 128 * R), blk(N("TM"), R), V("idb"))] for R in range(2)])
-                mov(W("rowsM"), P(0, 128, 384))
-                cp(IND(V("WG"), W("uq")), W("rowsM"))
-                mm([[(PO, V("idh"), V("c2", 0, 16)), (PO, V("nidb"), mv)]], last=False)
-                mm([[(P(2, cc, cc + 1), V("WG", 256 * cc + 1, 256 * cc + 256, 2), col("Mi", row))] for cc in range(16)])
+            tt(W("gI", 0, 256), IND(W("wI", 128, 256), W("uP", 16, 32)), W("maskO"), MUL)
+            mm([[(P(1, 8 * R, 8 * R + 8), blk(N("gI"), R), V("blkf")) for R in (0, 1)]], first=False)
+            ts(W("fl", 1, 64, 2), P(1, 0, 32), -30000.0, None, A.is_lt)
+            guest, mv = W("fl", 1, 32, 2), W("fl", 33, 64, 2)
+            mm([[(PO, V("idh"), V("c2", 16 * p, 16 * p + 16))]], last=False)
             c1, cb = W("cum", 8, 24), W("cum", 7, 23)
-            if t == 2:
+            if p == 0:
                 mm([[(PO, V("nidh"), mv)]], first=False, last=False)
-            op("v", ("tensor_tensor_scan", (c1, guest, mv, 0.0, ADD, SUB), {}))
-            WW = W("W2") if t < 2 else V("WG")
+            scan(c1, guest, mv, ADD, SUB)
+            wn = "W%d" % min(3, 1 + t + b); WW = V(wn)
             mm([[(PO, V("LT"), c1), (PO, V("GE"), cb)]], first=False)
-            nE, nO = W("nt", 0, 16), W("nt", 16, 32)
-            mov(nO, PO)
-            ts(W("uO"), nO, 2047.0, None, ADD)
+            nE, nO = W("nt", 1, 32, 2), W("nt", 32, 48)
+            cp(nO, PO)
+            ts(W("uO"), PO, 2047.0, None, ADD)
             cp(IND(WW, W("uO")), W("rows", 256, 512))
             mm(rep(0, 0, nO))
             mov(W("wN", 128 * (1 - p), 128 * (1 - p) + 128), P(0, 0, 128))
             tt(W("gP"), IND(W("wN", 128 * (1 - p), 128 * (1 - p) + 128), W("uP", 0, 16)), W("maskE"), MUL)
             stay = lambda o, u, d: [(o, u, nO)] + ([(o, u, c1), (o, d, cb)] if p else [(o, d, V("two"))])
-            mm([stay(P(1, 48, 64), V("idh"), V("nidh"))])
-            mm([stay(P(1, 32, 48), V("nidh"), V("idh"))], last=False)
-            mm([[(P(1, 32 + 8 * R, 40 + 8 * R), blk(N("gP"), R), V("blkh")) for R in range(2)]], first=False)
-            tt(W("s1"), P(1, 32, 48), mv, MUL)
-            tt(nE, P(1, 48, 64), W("s1"), ADD)
+            mm([stay(P(1, 33, 64, 2), V("idh"), V("nidh"))])
+            mm([stay(P(1, 32, 63, 2), V("nidh"), V("idh"))], last=False)
+            mm([[(P(1, 32 + 16 * R, 47 + 16 * R, 2), blk(N("gP"), R), V("blkh")) for R in range(2)]], first=False)
+            scan(W("nt", 0, 32), W("fl", 32, 64), P(1, 32, 64), MUL, ADD)
             ts(W("uE"), nE, 2048.0, None, ADD)
             cp(IND(WW, W("uE")), W("rows", 0, 256))
-            mm(rep(3, 0, nE))
-            mov(W("wN", 128 * p, 128 * p + 128), P(3, 0, 128), 1.0)
-            E = N("rE%d" % t)
+            mm(rep(0, 128, nE))
+            mov(W("wN", 128 * p, 128 * p + 128), P(0, 128, 256), 1.0)
+            dma([(V("wD") + (0, 8, 16), W("wN"))])
+            E = "rE%d_%d" % (t, s); name = "ag%d" % (4 * t + s)
             if t < 2:
                 pn = 1 - p
-                mm([[(P(2, 32 + 16 * k + cc, 160, 32), W("W2", 256 * cc + pp, 256 * cc + 256, 2), V("sel", 4 * t, 4 * t + 4))]
+                mm([[(P(1, 128 + 16 * k + cc, 256, 32), V(wn, 256 * cc + pp, 256 * cc + 256, 2), V("sel", ro, ro + 4))]
                     for k, pp in ((0, pn), (1, 1 - pn)) for cc in range(16)])
-                mov(W("l1"), P(2, 32, 160), -10240.0)
+                mov(W("l1"), P(1, 128, 256), -10240.0)
                 mm(rep(1, 256, W("l1", 48 - 16 * (1 - t), 64)))
                 mm(rep(0, 0, W("l1", 0, 32)))
                 mov(W("wL", 256 + 128 * t, 512), P(1, 256, 512 - 128 * t))
                 mov(W("wL", 0, 256), P(0, 0, 256))
-                mov(V(E, 48 * r, 48 * r + 48), IND(W("wL"), cS))
-                remote("ag", 2 * t + b, E, 48)
+                mov(V(E, 48 * xr, 48 * xr + 48), IND(W("wL"), V("cl", 24 + 4 * t, 27 + 4 * t)))
+                spread(name, E, 48)
                 if t == 0:
                     mov(W("VP", 0, 64), IND(W("wL"), cP2), 10240.0)
-                    split(W("VP", 0, 64), 4)
+                    split(W("VP", 0, 64), 4 - 4 * b)
                 else:
                     mov(W("VP", 0, 32), IND(W("wL", 0, 256), cP0), 10240.0)
                     split(W("VP", 0, 32), 4 + 2 * b, "TQ")
                 ts(W("qa"), W("l1", 64, 128), 2048.0, 4097.0, ADD, MUL)
-                dma([(V("wD", 256 * i, 256 * i + 256), i, -16, W("wN"), 0, 0, 0, 0) for i in range(16)], True, 2000 + 270 * 15, False, W("wN"))
                 ts(W("qb", 0, 64), W("qa"), 5, 4095, SHR, AND)
                 cp(W("uN", 0, 64), W("qb", 0, 64))
-                for lo, hi in ((0, 16), (48, 64), (16, 48 - 16 * t)):
-                    mov(W("gQ", 16 * lo, 16 * hi), IND(V("wD"), W("uN", lo, hi)))
+                cuts = ((0, 16), (48, 64), (16, 32)) + ((32, 48),) * (1 - t)
             else:
-                mm([[(P(2, 32 + cc, 33 + cc), blk("WG", cc), col("sel", 4 + 2 * b))] for cc in range(32)])
-                mov(W("l1", 0, 32), P(2, 32, 64), -10240.0)
+                mm([[(P(1, 128 + cc, 129 + cc), blk("W3", cc), col("sel", 4 + 2 * b))] for cc in range(32)])
+                mov(W("l1", 0, 32), P(1, 128, 160), -10240.0)
                 mm(rep(0, 0, W("l1", 0, 32)))
                 mov(W("wL", 0, 256), P(0, 0, 256))
-                mov(V(E, 32 * r, 32 * r + 32), IND(W("wL", 0, 256), cF))
-                remote("ag" if b else "hx", 6 - b, E, 32)
-                mm([[(P(1, 64 + y, 128, 32), V("WG", y, 4096, 32), V("Mi", 12 + 2 * b, 14 + 2 * b))] for y in range(32)])
-                mov(W("l1", 32, 96), P(1, 64, 128))
-                mm(rep(3, 0, W("l1", 32, 96)))
-                mov(W("gI"), P(3))
-                cp(W("uN", 0, 64), IND(W("gI"), V("cl", 4, 8)))
-                for lo, hi in ((0, 16), (16, 32)) if b else ((0, 32),):
-                    mov(W("mask1", 16 * lo, 16 * hi), IND(V("Mi"), W("uN", 32 + lo, 32 + hi)))
-                    tt(W("gQ", 16 * lo, 16 * hi), IND(W("wN"), W("uN", lo, hi)), W("mask1", 16 * lo, 16 * hi), MUL)
-            red = lambda ks: mm([[(P(3, 8 * k, 8 * k + 8), blk(N("gQ"), k), V("blkh"))] for k in ks])
+                mov(V(E, 32 * xr, 32 * xr + 32), IND(W("wL", 0, 256), cF))
+                spread(name, E, 32)
+                mm([[(("V", "p%d" % (4 + ty if b else 1), 192 + y, 193 + y, 1), V("W3", y, 4096, 32), col("sel", 5 + 2 * b))] for y in range(32)])
+                mov(W("l1", 32, 64), ("V", "p%d" % (4 + ty if b else 1), 192, 224, 1), -2048.0)
+                mm(rep(2, 256, W("l1", 32, 64)))
+                mov(W("gI", 0, 256), P(2, 256, 512))
+                ts(W("uN", 0, 32), IND(W("gI", 0, 256), cP0), 2048.0, None, ADD)
+                cuts = ((0, 16), (16, 32))
+            for lo, hi in cuts:
+                mov(W("gQ", 16 * lo, 16 * hi), IND(V("wD"), W("uN", lo, hi)))
+            red = lambda ks, lo=0, st=1: mm([[(P(2, lo + c, lo + c + 7 * st + 1, st), blk(N("gQ"), k), V("blkh"))] for k, c in ks])
             if t < 2:
-                red((0, 1, 6, 7))
+                red(((0, 0), (1, 8), (6, 16), (7, 24)), 64)
                 urgent(t + 1)
-            red(range(8 if t < 2 else 4))
-            if t < 2:
+                if t == 0:
+                    red([(k, 16 * (k % 4) + k // 4) for k in range(8)], 0, 2)
+                else:
+                    red([(k, 8 * k) for k in range(4)])
                 prep(t + 1, 2047.0)
             else:
-                mov(W("rX2", 32 * r, 32 * r + 32), P(3, 0, 32))
-                remote("hx", 4 + b, N("rX2"), 32)
-                mov(W("qf"), W("rX2"), 2047.0)
-                dma([(W("qf", 32 * x, 32 * x + 32), 0, 128, "yq", 4 * b + x, 1, 0, 4096) for x in range(4)], False, 2500, b == 1)
+                red([(k, 8 * k) for k in range(4)])
+                mov(V("rX2_%d" % s, 32 * xr, 32 * xr + 32), P(2, 0, 32))
+                spread("yq%d" % s, "rX2_%d" % s, 32)
 
-        def final():
-            E = N("rE2")
-            sh = lambda xs: [(P(2, 32 * v, 32 * v + 32), RS(v, x), V(E, 32 * x, 32 * x + 32)) for x in xs for v in range(4)]
-            mm([[(P(2, 0, 128), V("idb"), V("zb", 0, 128))] + sh([r])], last=False)
-            mm([sh(others)], first=False)
-            ts(W("LY"), P(2, 0, 128), zc, None, ADD)
-            for c in range(4):
-                mov(W("yt", 512 * c, 512 * c + 512), IND(ZW, W("LY", 32 * c, 32 * c + 32)))
-                if c % 2:
-                    lo = 512 * c - 512
-                    dma([(W("yt", lo, lo + 1024), 64 * hf, 64, "yz", 64 * b, 64, 2048 * hf + lo, 1024) for hf in range(2)], False, 3000, b == 1)
+        return [prep0, index]
 
-        return [start, coords0, prep0, lambda: index(0), lambda: coords(1), lambda: index(1), lambda: coords(2), lambda: index(2), final]
-
-    for steps in zip(batch(0), batch(1)):
-        for b in range(2):
-            mark[0] = 1 - b
-            steps[b]()
+    st = [stream(s) for s in range(4)]; ch = [chain(b) for b in range(2)]
+    late = PAR["late"]
+    for b in range(2 - late):
+        ch[b][0]()
+    for t in range(4):
+        for s in range(4):
+            if t == 0:
+                st[s][0]()
+            if t < 3 or s > 1:
+                st[s][t + 1]()
+            if t == 2 and s > 1:
+                st[s - 2][4]()
+            if t == 3:
+                st[s][5]()
+            elif s % 2 == ty:
+                if t == 0 and s > 1 and late:
+                    ch[1][0]()
+                ch[s // 2][1](t)
     return ops
 
 
 def depend(ops):
     n = len(ops); deps = [set() for _ in range(n)]; acc = {}; bank = {}
-    home = {(b, c): o for (b, o, w) in AL.values() for c in range(o // 16, (o + w + 15) // 16)}
-    for j, (eng, kind, _, rd, wr) in enumerate(o[:5] for o in ops):
+    for j, (eng, kind, pay, rd, wr) in enumerate(o[:5] for o in ops):
+        if kind == "d":
+            deps[j].update(pay[2])
         for nm in set(x[0] for x in rd + wr if x[0] not in SB):
             before, now = bank.get(nm, ([], []))
-            if now and ops[now[0]][0] == eng:
-                deps[j].update(before + (now[-1:] if eng == "t" else [])); bank[nm] = (before, now + [j])
+            if now and eng == "v" == ops[now[0]][0] and not ops[j][5] and not ops[now[0]][5]:
+                deps[j].update(before); bank[nm] = (before, now + [j])
             else:
                 deps[j].update(now); bank[nm] = (now, [j])
         for lst, isw in ((rd, False), (wr, True)):
-            for (nm, lo, hi) in lst:
+            for (nm, lo, hi, st, pa, pb) in lst:
                 if nm in SB:
-                    key = (nm, home[(nm, lo // 16)]); old = acc.get(key, [])
-                    deps[j].update(i for (i, l2, h2, w2) in old if (isw or w2) and lo < h2 and l2 < hi and i != j)
-                    acc[key] = [x for x in old if not (isw and lo <= x[1] and x[2] <= hi)] + [(j, lo, hi, isw)]
+                    old = acc.get(nm, [])
+                    meet = lambda x: lo < x[2] and x[1] < hi and (st != x[4] or (lo - x[1]) % st == 0) and pa < x[6] and x[5] < pb
+                    deps[j].update(x[0] for x in old if (isw or x[3]) and meet(x) and x[0] != j)
+                    acc[nm] = [x for x in old if not (isw and lo <= x[1] and x[2] <= hi and (st == 1 or st == x[4]) and pa <= x[5] and x[6] <= pb and meet(x))] + [(j, lo, hi, isw, st, pa, pb)]
     return deps
 
 
-def common_order(ops):
-    al = "0123456789abcdefghijklmnopqrstuvwxyzABCDEFGHIJKLMNOPQRSTUVWXYZ"
-    return [62 * al.index(ORDER[k]) + al.index(ORDER[k + 1]) for k in range(0, len(ORDER), 2)]
+def ordered(r, own):
+    al = "0123456789abcdefghijklmnopqrstuvwxyzABCDEFGHIJKLMNOPQRSTUVWXYZ"; N = len(ORDER) // 2; ty = 0 if r in own[0] else 1
+    ONV[ty] = "1" * 400; ops = plan(r, own); n = len(ops); on = ["1"] * 400; order = []
+    for k in range(N):
+        c, j = divmod(62 * al.index(ORDER[2 * k]) + al.index(ORDER[2 * k + 1]), N); j -= ty * (N - n)
+        if 0 <= j < n:
+            order.append(j); on[ops[j][5] - 1] = str(c)
+    ONV[ty] = "".join(on)
+    return plan(r, own), order
+
+
+def owners(T, topo):
+    ch = [topo.chip(c) for c in T.cores]
+    far = [y for y in range(1, 4) if not topo.mates(ch[0], ch[y]) and not topo.same_plane(ch[0], ch[y])][0]
+    return ((0, far), tuple(y for y in range(1, 4) if y != far))
 
 
 def helper_of(T, topo, c):
@@ -558,66 +613,60 @@ def dst_id(topo, c):
     return DstId(rid=rid, pnc=pid)
 
 
-def mask_to_others(T, topo, src, r):
-    m = -1
-    for x in range(4):
-        if x != r:
-            m &= topo.mask(src, T.cores[x])
-    return m
+def common(T, topo, src, ranks):
+    return [e for e in topo.engines(src, T.cores[ranks[0]]) if all(topo.mask(src, T.cores[y]) >> e & 1 for y in ranks)]
 
 
-def mask_to_helper(T, topo, r):
-    c = T.cores[r]
-    return topo.mask(c, helper_of(T, topo, c)) & ~mask_to_others(T, topo, c, r)
-
-
-def bits(m):
-    return bin(m).count("1")
-
-
-def rs_masks(T, topo, r):
-    c = T.cores[r]; oth = [x for x in range(4) if x != r]
-    m = mask_to_others(T, topo, c, r); e = [k for k in topo.engines(c, T.cores[oth[0]]) if m >> k & 1]
-    direct = lambda x: topo.mates(topo.chip(c), topo.chip(T.cores[x])) or topo.same_plane(topo.chip(c), topo.chip(T.cores[x]))
-    q = len(e) // 4
-    return {x: sum(1 << k for k in part) for x, part in zip(sorted(oth, key=direct), (e[:2 * q], e[2 * q:3 * q], e[3 * q:]))}
+def mask_of(engines):
+    return sum(1 << e for e in engines)
 
 
 def rank_program(g, core, T, topo):
-    S = T.sem
+    S = T.sem; own = owners(T, topo)
+    rest = lambda r: [y for y in range(4) if y != r]
 
     def ap(x):
+        if isinstance(x, tuple) and x[0] == "T":
+            return T[x[1]][x[2]:x[2] + x[3], x[4]:x[4] + x[5]]
         if not isv(x):
             return x
         if x[0] == "I":
             return ap(x[1]).indirect(ap(x[2]))
-        if len(x) > 5:
-            return T[x[1]][x[5]:x[5] + 64, x[2]:x[3]]
-        return T[x[1]][:, x[2]:x[3]] if x[4] == 1 else T[x[1]][:, x[2]:x[3]:x[4]]
+        p = slice(None) if len(x) == 5 else slice(x[5], x[5] + x[6] * x[7], x[7]) if x[7] > 1 else slice(x[5], x[5] + x[6])
+        return T[x[1]][p, x[2]:x[3]] if x[4] == 1 else T[x[1]][p, x[2]:x[3]:x[4]]
 
-    def spread(src, dst, r, m, sem):
-        oth = [x for x in range(4) if x != r]
-        g.remote_dma_fused([RemoteDMATransfer(dst_ids=[dst_id(topo, T.cores[x]) for x in oth], dma_engine_mask=m, remote_sem=sem,
-                                              srcs=[ap(src)], dsts=[ap(dst) for x in oth])], local_sem=S.loc)
+    def spread(src, pairs, sem, loc):
+        e = common(T, topo, core, [y for y, _, _ in pairs])
+        g.remote_dma_fused([RemoteDMATransfer(dst_ids=[dst_id(topo, T.cores[y]) for y, _, _ in pairs], dma_engine_mask=mask_of(e), remote_sem=sem,
+                                              srcs=[ap(src)], dsts=[ap(d) for _, _, d in pairs])], local_sem=loc)
+        return len(e)
 
-    hbuf = lambda t: V("hX%d" % t)
+    def to_helper(r):
+        c = T.cores[r]; off = common(T, topo, c, rest(r))
+        return [e for e in topo.engines(c, helper_of(T, topo, c)) if e not in off]
+
+    def arrivals(name, r):
+        ow = own[int(name[2:]) % 2]
+        if name[:2] == "rs":
+            return sum(len(common(T, topo, T.cores[y], rest(y))) // (1 if y in ow else 2) for y in rest(r))
+        return sum(len(common(T, topo, helper_of(T, topo, T.cores[y]) if name in PAR["help"] else T.cores[y], rest(y))) for y in ow if y != r)
+
     for r in range(4):
         if core == helper_of(T, topo, T.cores[r]):
-            m = mask_to_others(T, topo, core, r); ops = plan(r); n = 0
-            for j in common_order(ops):
-                if ops[j][1] == "r" and ops[j][2][0] == "hx":
-                    t = ops[j][2][1]
-                    g.wait_ge(S["hi%d" % t], bits(mask_to_helper(T, topo, r)))
-                    spread(hbuf(t), ops[j][2][3], r, m, S["hx%d" % t]); n += 1
-            g.wait_ge(S.loc, n * bits(m))
+            ops, order = ordered(r, own); n = 0; loc = 0
+            for j in order:
+                if ops[j][1] == "r" and ops[j][2][0] in PAR["help"]:
+                    name, pairs, _ = ops[j][2]
+                    g.wait_ge(S["hi%d" % n], len(to_helper(r)))
+                    loc += spread(V("hX%d" % n, 0, nel(pairs[0][1])), pairs, S[name], S.loc); n += 1
+            g.wait_ge(S.loc, loc)
             return
     r = T.rank_of(core)
     if r is None:
         return
-    ops = plan(r); deps = depend(ops); order = common_order(ops)
+    ops, order = ordered(r, own); deps = depend(ops)
     pos = {j: k for k, j in enumerate(order)}
     assert len(pos) == len(ops) and all(pos[i] < pos[j] for j in range(len(ops)) for i in deps[j])
-    oth = [x for x in range(4) if x != r]
     QU = {"v": g.vector, "t": g.tensor, "s": g.scalar, "gp": g, "sy": g.sync}
     needed = set(i for j in range(len(ops)) for i in deps[j] if not (ops[i][0] == "t" and ops[j][0] == "t"))
     sig = {}; cnt = {"v": 0, "t": 0, "s": 0, "gp": 0}; nd = 0
@@ -627,56 +676,55 @@ def rank_program(g, core, T, topo):
             if j in needed:
                 cnt[eng] += 1; sig[j] = (eng, cnt[eng])
         elif kind == "d":
-            sig[j] = ("d%d" % nd, 16 * len(pay[1])); nd += 1
-        else:
-            snd = lambda x: T.cores[x] if pay[0] == "ag" else helper_of(T, topo, T.cores[x])
-            sig[j] = ("%s%d" % pay[:2], sum(bits(rs_masks(T, topo, x)[r] if pay[0] == "rs" else mask_to_others(T, topo, snd(x), x)) for x in oth))
+            sig[j] = ("d%d" % nd, 16 * len(pay[0])); nd += 1
+        elif kind == "x":
+            sig[j] = (pay[0], arrivals(pay[0], r))
 
     def call(q, m, a, kw):
-        f = {"matmul": lambda: q.matmul, "tensor_scalar": lambda: q.tensor_scalar, "tensor_tensor": lambda: q.tensor_tensor,
+        f = {"matmul": lambda: q.matmul, "transpose": lambda: q.transpose, "tensor_scalar": lambda: q.tensor_scalar, "tensor_tensor": lambda: q.tensor_tensor,
              "tensor_copy": lambda: q.tensor_copy, "memset": lambda: q.memset, "activation": lambda: q.activation,
              "iota": lambda: q.iota, "affine_select": lambda: q.affine_select, "tensor_tensor_scan": lambda: q.tensor_tensor_scan}[m]()
         return f(*[ap(x) for x in a], **{k: ap(x) for k, x in kw.items()})
 
-    waited = {}; loc = 0
+    waited = {}; left = []; gate = None; nh = 0
     for j in order:
-        eng, kind, pay = ops[j][:3]; q = QU[eng]; want = {}
+        eng, kind, pay = ops[j][:3]
+        if kind == "x":
+            continue
+        q = QU[eng]; want = {}
         for i in deps[j]:
             if not (ops[i][0] == "t" and eng == "t"):
                 nm, c = sig[i]; want[nm] = max(want.get(nm, 0), c)
-        for e in [eng] + (["s"] if kind == "d" and pay[2] else []):
-            for nm, c in sorted(want.items()):
-                if waited.get((e, nm), 0) < c:
-                    QU[e].wait_ge(S[nm], c); waited[(e, nm)] = c
+        if kind == "d" and gate:
+            for nm, c in gate.items():
+                want[nm] = max(want.get(nm, 0), c)
+        for nm, c in sorted(want.items()):
+            if waited.get((eng, nm), 0) < c:
+                q.wait_ge(S[nm], c); waited[(eng, nm)] = c
         if kind == "c":
             for m, a, kw in pay:
                 ins = call(q, m, a, kw)
             if j in sig:
                 ins.then_inc(S[eng], 1)
         elif kind == "d":
-            for k, (v, p0, pn, tn, r0, rn, c0, cn) in enumerate(pay[1]):
-                if pn < 0:
-                    sb, hb = T[v[1]][p0:128:-pn, v[2]:v[3]], T[tn[1]][p0:128:-pn, tn[2]:tn[3]]
-                else:
-                    sb, hb = T[v[1]][p0:p0 + pn, v[2]:v[3]], (ap(tn) if isv(tn) else T[tn][r0:r0 + rn, c0:c0 + cn])
-                q = g.scalar if pay[2] and k % 2 else g.sync
-                (q.dma_start(sb, hb) if pay[0] else q.dma_start(hb, sb)).then_inc(S[sig[j][0]], 16)
+            for o, i in pay[0]:
+                q.dma_start(ap(o), ap(i)).then_inc(S[sig[j][0]], 16)
         else:
-            k, t, srcs, dst = pay; sem = S[sig[j][0]]
-            if k == "rs":
-                mk = rs_masks(T, topo, r)
-                g.remote_dma_fused([RemoteDMATransfer(dst_ids=[dst_id(topo, T.cores[x])], dma_engine_mask=mk[x], remote_sem=sem, src=ap(a), dst=ap(dst))
-                                    for x, a in zip(oth, srcs)], local_sem=S.loc)
-                loc += sum(bits(v) for v in mk.values())
-            elif k == "ag":
-                m = mask_to_others(T, topo, core, r); spread(srcs[0], dst, r, m, sem); loc += bits(m)
+            name, pairs, one = pay; ln = "l%d" % len(left)
+            if name in PAR["help"]:
+                rid, pid, _ = topo.addr(helper_of(T, topo, core)); e = to_helper(r)
+                g.remote_dma(ap(V("hX%d" % nh, 0, nel(pairs[0][1]))), ap(pairs[0][1]), S["hi%d" % nh], S[ln], pid, rid, mask_of(e))
+                nh += 1; left.append((ln, len(e)))
+                continue
+            if one:
+                n = spread(pairs[0][1], pairs, S[name], S[ln])
             else:
-                hc = helper_of(T, topo, core); rid, pid, _ = topo.addr(hc); m = mask_to_helper(T, topo, r)
-                g.remote_dma(ap(hbuf(t)), ap(srcs[0]), S["hi%d" % t], S.loc, pid, rid, m)
-                loc += bits(m)
-    done = {}
+                e = common(T, topo, core, rest(r)); n = len(e); k = n // len(pairs)
+                g.remote_dma_fused([RemoteDMATransfer(dst_ids=[dst_id(topo, T.cores[y])], dma_engine_mask=mask_of(e[k * i:k * i + k]), remote_sem=S[name], src=ap(a), dst=ap(d))
+                                    for i, (y, a, d) in enumerate(pairs)], local_sem=S[ln])
+            left.append((ln, n)); gate = want
+    done = dict(left)
     for nm, c in sig.values():
         done[nm] = max(done.get(nm, 0), c)
     for nm, c in sorted(done.items()):
         g.wait_ge(S[nm], c)
-    g.wait_ge(S.loc, loc)

@@ -1,71 +1,47 @@
 from concourse.mybir import AluOpType as A, ActivationFunctionType as F
 from concourse.bass import DstId, RemoteDMATransfer
 
-PAR = {"m": ("- DF DF DF s s s s s s s s".split(),) * 2, "help": ("ag5", "ag8", "ag9", "yq0", "yq1", "yq2"), "pace": 4, "nch": 1, "late": 0,
-       "exact": 1, "seq": ("Vx123ybc", "V1x23ybc")}
-ONV = ["1" * 400, "1" * 400]
+PAR = {"m": ("- DFp - DFp".split(),) * 2, "help": ("ag8", "yq0", "yq2", "ag9", "yq1", "ag1"), "pace": 4,
+       "seq": ("Vx123ybc", "V1x23ybc"), "gate": 1, "s16": 1, "cut": 0, "half": ()}
 ORDER = (
-    "0xdO19cGcFcT0zc9000LcLcH011GcUd0c802ca0HAu1b0304cK0Idh0S0G1F05cEcbcO0E0D0MccpXcddn0F0J1I0C0Kdkoo0609cR30cN0O0wcM1o1Jf7p924cP1K1acQ"
-    "dR07BhcSdS0A2ZdT1d2t1L18db1X1YcWdUcfci150Qd30a0ydmcge5eB0Ndi25cj0VdPdQcV2s1Mck1cdHf5cZ1z0P1Dda0Rf8f60W2Aqf161edzd4chcldcd22X1f1m21"
-    "48e60b0c2u2vdwdx201Bfe2Y0BdL360d262xdl33cm22230e27312BeIfbDpdrfdfjfa1scn34fi282w32291R2ado47eC0Ufc4935e7372b1V1W1N38cX2c4o1pfkec2C"
-    "djqA0f4c2de8eddYcYe90g4f4d4e3bdVff17qDfggwfnqz1S1hfofh2e2ofq2fqB39ee132m2g3add2h2p4a4bcJ4g2D3c4i4n4h4j4k0hea4p2idIefCTCregfpeE12qG"
-    "rt1g2y3g0i4ssBcoCZ10cpcqd84r3e3ffr0Xdeflfm3h3ieh4teF1TftqPei141jfs0jeGeKejdJgx3j3k1P4v4u113l3m4qeHgv2E2FfufvCA3oDMcI5AgM3ncr4y3pcs"
-    "CHeldfeL0kCJeme10lfxdu3qd5fz3r3sesgNgA4wenCL5Beogz3tCF5C1Aewe4F12Gd7ctgBeMcuqXgD1qgCgE3ucv4m3v4x4zeq0mgFeu3w3x1t4AqY3y2J1Q1r1idgex"
-    "fygyfAfBe35FgHfC4B0n3z5GgG5Id6gI5HgOgQ4EfD5EfE1OfFgPfG1u3C5Je0gR2PfHrQD3dpds0o2RfI2Q0pdA1U5L2KcwfJCO2LdNd9gJrT3F5DfKfMfLfR2M3EfSfN"
-    "3NfOgT4CgSfPdve2gUeOgVrXrWrYfQ0YgK4D4F5K2O2N1C5M5NgWsW3OfTfU0qfX3BfVeP4H4I4JeQeX3PfWu4gXgY4K2T2S2U2V0r4L3QcxeYez4M4N3R5R3J2r4OFf3S"
-    "eRdy4P3UrceTeSdD4R4Q4T4U4SdEfYeUeVdB3TeW5QDfeA4WdKdXdWdZcyh05P5Sf1fZ5Tf0hZ5V4Vg0h1Eh3Vh2gb5U4X5Z3Xg25Y0Z0sgcEkdC4Yg34Z5052515W5Xtj"
-    "55tm58dq3K5a57hYi0i1cz3W3Lg5g6f2g7i3h3Gif376i7i65g75Fkhagd7761h762tp5bh578h6i47aifh8h9hbi5hc60i8f441vp3Y7bg8hd5c6364vt7c676542hf7e"
-    "he437l7fi9ia7m403Z7n7o7p7giege44hh7qFyigihgfgihkiijt5hpDhj54ibicid663Mijin5iimhlhmghhghnhq7hgj68uphohphthu7i7uikil6hiqipgg6a6bvzio"
-    "jujvjwgl7k7t6chv6e7r6d6f6girhrgkhwgpFNjyGIhy7s4546HNgmithz6iiu5khAEG7wjCgn5jhs6jjJ6k6l6n6q8A6r6o7v7xiviwjAHRjK7yEH6m5d5mjzjF5ngohE"
-    "jDjEjG7z6pixiF8BiA0t5l8C5o6s8D8E6tiy5q5p8FiCjLizg96ujHjI6vjM7A7B5r5t8JhFga7C6w5sgsuNtu5u6ziB0u7D7EhGwY6ytL8H8GiDiEuQ5fgtiGiHEKiJiI"
-    "iLiKjOjNiM6BiNiOtM8K6C1k6EiP5xjQcA7FkZiQiR7GcBhI5yhHhLjSjPiSiTjRjUjTjViUuThMdtiXHehNhOjWIdj88MiVj01l7M7H6FhP7JiZ8L5z7IHi7K8N6KjY7L"
-    "6L7N6M6OhBx40v6GhJ8PhK6NHhj97O7P7Q7R7S7T7V7U6Q8RhRHjhSG9cC8Q6PjZkYl08S8T7WFS6RiWl16S7X7Y1v7Z1wk0hDGahQJj80k3dGhVk16T9Rl2k2jal5ka8U"
-    "xe6U8V8W6Xl7l68X81wi6Y8Z8485861y90lfk4878388wp91jb6Hk5k6j492k71xk8l4hW6ZlajchX7170k9kb8a9Ql9kckekdkgkjjdkkcD8bl8lbIx8flelgkilhlckf"
-    "kl6Vkm93knjejfxk9Skpj572wsjllimf6Iko6Wljme9Tlka7a6mgmhjmllyba8lnksIJ95dFjh8gkD9U6J9Wyea9kqkv9X9Z97lma173lplda0ku9698IMaakElojg999a"
-    "kxkyablqlr9b8hKy9cmj9elsjimDa2a3lv9d9fac9gyua49h9i8jj6kz9j9kad9l9r9m9odMjnjomCaf74beagj7ahbf9p9qbg9s9tltbhmka5luml9n8k8i8l9uaiaj9x"
-    "biyA8m9vKCzCmE9wmqjpjq8smFmnbjjkbnavlwjjly9A9ympmomrJNlAblbklzlCKIlBallD9Bjrbpbo1EkF8nmHmGmJ8tlEbq9CmImOlHmLmKmMmNlFlGlI9zbrzI8obt"
-    "lKkrkHmt8v9DxU9F8umumPlJlMjslLlPlQ8dkG8ekJammQawkKlNlO8pwG8xao8wkL9G8yyNaA8raCayxXazaBaDaEkIkMmR9ImvkQkRaH8zlRaFaGaIaKaJn1lSaLkNkO"
-    "kPaMlVaNlTlUkSmSaO9Jn2LjkTn69KkVaPaQaRaSn8y2aTlW9LlYlZn49Nn5kAn7m0nbanapn9KhIRKinaaUkCkUndaV9OaWaqasm49PKlncnenfaYbCmwb4mxaZmzlXb0"
-    "ngkWJdnKm6KnnimULzm3nlnTm8m9zlnkb6maaXnhzhnmmynnmTnombbvKsmdznaraub8b2nrnszpbunpmVnqmAbantmWbGmXnunAb3LebLLLnSKRnwnLn0zTbKbwbxLfzU"
-    "LRnCbFM3nMLNbyyJLTnybbzsbMbzbNA5bdbXnUzQnzzRnObSnVnEM5bWnFnQzXLWA4nHzZLYM7A6nJbYo4nWbZMdA9AgnYc4Alo5bIo0bRAac1AbMho6o7MfMiAiMjMoo9"
-    "MrocodofoaMuc3c7c6")
+    "01020y0X1c040c00030x060Q0A0J0Fcv0b0C07050d1z0I0H0G0D0a0Ecw0K1B0B0R1E0e1y0N0M0Ldf1J1F0Z1Ce010290Uga18di1G1Pe80O192Be91Kdged1N1HdD0f0g2Aeb2y1jey1T1ReW2aez1iej3Oes2HeZ1U0Pe53P1b1S110h1A14f10idI2D1Z0jgf2F0k2G2d1h0lgi431d242I170m3R1w1nen3T0nep3Yeq15eB4626f63U3W0p2K0o271k3Qeo2f441x5j3X2g2j1p45161m2h2Lgv5k2N2PcW3Z401V5lgx2i2O2Q2R2Sgo490r42fg2p0s0q1tel2W1ohO4c2M2U2X4b2VeN5seP2Y1X0veO1e30472Z31eRhL322k2m3533362t2v370w344d2lfv3a4e5t393b3c3d2wfBfCgC3geL5p0u4g3h0t1f1q3ieU3r4hfQ4i5q2n0Y5n3j5m3s4n3k5u3l1s133m4j4l4k1v4m4o5v4p0W4q5w4s4r5zhU4t5A5y3u4uev4w1u3n4v4xfS5B1r4yfL4B4C124zfM3w5CfU4DfVi14A1a4E4G4H4Fi04J4Ii44K4L3qi54M4X4N4Z6Q4OfW5KfX4P5F5G6P6S6Rhd6T5J3B4Rjhhf4Y5Lji3C3G3H5M6W3Iia77hg3J3D3K5Ojm6Yjn3L5P6X5R5Tg95S783E5U3F797250jx5V71jy5W7351525X5Q745453jz605Z5YjD6261js7djC63768o644U66657ehi678n8qhs684W6b6c697i7jix7h8pht6d8r6e6g6h7k8s6fjI6i6j57iH7miIkQ6m596n585c6ohAkVkR5e5a7t6p5bkU5f6x5g8v7o7n6q6s8z7p7r6r5h7q5i7s8w7u6v8AjS7w8FiQ8B7y7x8C6u6w7A7zl08G8E8H7B8I6y7Cl77E7D7F6z7G7J7K6A7Hl66B6C7L7I7M7O7Plalb7N7Q9O7Rkfkgj07U837V7W9N9Q9P9Rmf8Q7Xj18Mmg8P6H6F7Ymh8L7Zmla5806G858R816K6Imk8S846J6L8T8U8Wkp6M9V8X8Z6N8Va0jb8Ya69W90a7869Z91mv92mx8788a1938a8994a29695mwa39897a4mA99abmBbm9a9ckz9bac9dky9e9h9iaf9f9jblbo9g9k8d9m9l9n9okBbnlNbplO9p8fkF9sbq8j9tagnOah9B8k9u9z8lnPnTai9A8m9vnSbtbumG9Cbyakatm0avaxbxbzm19wm2m3bA9xawbB8gaybC8hazaAmYlVaDaEaualm4aCaGaF9IaH9JaI9KaKaJaLm8aMaP9MaNndaRaOamaUnfaVanaTaWmLaXnlnmmMb0b7b1b9bEb8b2babbbcaqb3nBnAbNnrobbDbGarb5b6bWbFocbHnCbgo5bho6bibjbKbkbLasbXbYbMc9omodonc1bRbSopoqc8cbogcaccoibUcdcfoBoDc4choscicjckotouoJoI",
+    "0001020x0306e504050E0b0y1g0Hcv0I0Q1B0a0C0G0X0F0R0J0Bcu0K1E1h1f0A0N0O0T1F1c0D0Zcw101G0V1b1H1y0e171z190P2y0U0LcW1JeW2a1jdZeZ0d2B290c0fdl0g2A0odff11d2L1i1L2H1D182b2c2D2M2ddI1P0i1M2e1K2N2Fed1N2j2Gebfg1A1R2I0k0h0j1Tf62Ufd2O2K1n1S1k0mej2R2V110M2k1m2leS1Z1a2P2S0l141U2m0n430per2W1wgE441pen2X13evep25451V1teq162Y47ekel1s260r2Zgx1r27461q2f1o4i0s0qeR2g15324bgG4d0t30gM1v1e2hdjgv1x4q1u0w120v4l31eo2i3335343649373a384c2pfwgJ3c4k4e4r3d4f2q4neL0u4g3e2s3g4s3b3f3h4o3i3l3m3j3n3k4t2tfL3q2weK3r3p3s4ufRfS3tg63wgS3H2x5A4w4y3xg53y3Kg85z5C3z3M2r4D5BfX5D4xgagbfZ5E3B5Fi34z4B4A4Ci64Ei74G4F3D4Igd5H4J4Hgc4K3E4M4L5R5I4N4O5L4P5N4R5Mhf4T4Q5S5O4Whh5Tg24Xg35P5U4Y4V5Q4Z78hnhoii523R53545dijin777a3Sim555X5YgjhB79gk567b6163573T58597c62jA7p3Y5a5f3U643VjB3Z4065416668jF6742jE7f7q5g7g7rhy5h7s5c696bhF7k6a6djQ6c5j5k7j6e7l6fjR7mjV6i6g6kjK6jjU7v6l7o6h7whI6m6o6n7z6p7BhJ6q6t6u7A6r6v6siT7C6y5n6x6z6A8G6BiZj0hL6EhP5phQ6F7D6N6G7E5u8F8I8HhS8JhT6H8K8Ll97L7F6Ilc5q7H7J6J5x8Nld8X7I6KhV6O5r7K6L6P8O7G7M6Q8Rka8Tj96R7Q7Ojf7S8Yjg6U8Z7R8Sln7Tlo7U8U7W7P7V7X7Y81ls8V827Z6W8W83lta684kn87ji86858889kx6ZkykK8clp6X8da5a88ea7a9mxjl94mz8f7293my8l8g98738h9799jrkJ8i709aad75lyjtaf9c9dmDax9f9h8o71ay8jaeaz9gmX8p8qaiaj8s8rmY9j9iah9k9lmZn39o9nak9e9m9q9pn2alaE9ram9skQ9u9t8kaI9v9wkR9z9AaD9x9BlV8vaHlZ8x9EkTaoaJ8A9D9F9GaKm58Bm6n8mg9HaM9R8C8y8D8zmf9KaV8Em8aW9M9UaXaZaYb0b19Vb29Wmk9Y9Nb3b6b8b4anaqb5b7ap9Oarb99PasmQbabcbb9Qbdbebhmnbi9ZbfbjmRbgaNbkbmbnblboava1nNbpnObNbOocbsbzbtbBoda2bRbAbubCmqa4aOaPndbDbEbvaSbFo3mTnebXbwbyaUbxaTo4bIbWbZbYcbc0oobJopbKbLc3bMbSogoibUc5cccdc4cecgoCc6c7c8oEciowcacjckcmcl")
 
 BF, HF, FP, I32, U16 = "bfloat16", "float16", "float32", "int32", "uint16"
-STR = {"zt": (7184, BF), "S": (1136, BF), "P2": (1024, BF), "f": (1024, BF), "g": (1024, BF), "f2": (1024, BF), "g2": (1024, BF), "yt": (1024, BF),
-       "L": (100, U16), "LY": (64, U16), "sP0": (32, HF), "sP1": (64, HF), "sP2": (64, HF),
-       "rE0": (96, HF), "rE1": (96, HF), "rE2": (64, HF), "rX2": (64, HF), "qf": (64, FP)}
-CHN = {"rows": (512, BF), "rowsI": (512, BF), "TP": (512, BF), "TQ": (512, BF), "VP": (128, FP),
-       "fl": (64, HF), "rP0": (64, HF), "rP1": (128, HF), "rP2": (128, HF), "wI": (256, FP), "wN": (256, FP), "wL": (512, FP), "gI": (512, FP),
-       "gP": (256, HF), "gQ": (1024, HF), "maskE": (256, HF), "maskO": (256, HF), "cum": (32, HF), "nt": (48, HF),
-       "uO": (16, U16), "uE": (16, U16), "l1": (128, HF), "qa": (64, I32), "qb": (128, I32), "uN": (64, U16), "qd": (192, I32),
-       "uP": (64, U16), "q0h": (32, HF), "uq0": (32, U16)}
-BUF = {"W1": (4096, BF), "W2": (4096, BF), "W3": (4096, BF), "zb": (1024, BF), "TI": (544, BF), "vI": (32, FP), "X": (272, FP), "pi": (16, I32), "pf": (32, FP),
-       "X2": (128, FP), "Y": (8, FP), "idb": (128, BF), "nidb": (128, BF), "idh": (128, HF), "nidh": (128, HF), "LT": (128, HF), "GE": (128, HF),
-       "Mr": (128, HF), "Rh": (1024, HF), "RS": (576, HF), "sq": (800, HF), "grp": (128, HF), "pm": (48, BF), "Y4": (16, FP),
-       "blkf": (8, FP), "blkh": (8, HF), "Mp": (64, BF), "Y3": (64, FP), "pen": (8, HF), "sel": (8, BF), "Y2": (8, FP), "c2": (32, HF),
-       "c2f": (16, FP), "wD": (4096, FP), "two": (16, HF), "idc": (32, FP), "ci": (8, I32), "cf": (16, FP), "cl": (32, U16), "qi": (256, I32), "qh": (1024, HF)}
+STR = {"zt": (7184, BF), "S": (1136, BF), "f": (1024, BF), "g": (1024, BF), "f2": (1024, BF), "g2": (1024, BF), "yt": (1024, BF),
+       "L": (128, U16), "LY": (64, U16), "sP0": (32, HF), "sP1": (64, HF), "sP2": (64, HF),
+       "rE0": (96, HF), "rE1": (96, HF), "rE2": (64, HF), "rX2": (64, HF), "qf": (64, FP), "hX": (48, HF)}
+CHN = {"rows": (512, BF), "TP": (512, BF), "TQ": (512, BF), "fl": (32, HF), "rP0": (64, HF), "rP1": (128, HF), "rP2": (128, HF),
+       "wI": (256, FP), "wN": (128, FP), "gI": (512, FP), "gP": (256, HF), "gQ": (1024, BF), "maskE": (256, HF), "maskO": (256, HF),
+       "cum": (32, HF), "tn": (32, HF), "m32": (32, HF), "gm": (32, HF), "nt": (64, BF), "wS": (256, BF),
+       "uO": (16, U16), "uE": (16, U16), "uN": (64, U16), "uP": (96, U16), "uq": (32, U16)}
+BUF = {"W1": (4096, BF), "W2": (4096, BF), "W3": (4096, BF), "zb": (1024, BF), "TI": (528, BF), "X": (32, FP), "pi": (8, I32), "pf": (16, FP),
+       "one": (144, HF), "oneb": (144, BF), "idh": (128, HF), "idb": (128, BF), "nidb": (128, BF), "nidh": (128, HF), "i7": (128, HF), "ia": (128, HF), "ib": (128, HF),
+       "LT": (128, HF), "GE": (128, HF), "Rh": (1024, HF), "RS": (576, HF), "Bq": (408, HF), "Zh": (144, BF), "Zl": (144, BF), "Zf": (144, BF),
+       "Bc": (128, BF), "pm": (64, BF), "Y": (32, FP), "blkn": (8, FP), "blkh": (8, HF), "pen": (8, HF), "Mp": (64, BF), "CR": (24, BF),
+       "cT": (256, HF), "kc": (48, HF), "vI": (96, FP), "qi": (256, I32), "qh": (1024, HF)}
 for _k, _v in STR.items():
     for _b in range(4):
         BUF["%s_%d" % (_k, _b)] = _v
 for _b in range(2):
     for _k, _v in CHN.items():
         BUF["%s_%d" % (_k, _b)] = _v
-for _b in range(4):
-    BUF["hX%d" % _b] = (48, HF)
 AL, SB = {}, {}
 for _k, (_w, _d) in BUF.items():
-    _o = SB.get("pool" + _d, (0, _d))[0]
-    AL[_k] = ("pool" + _d, _o, _w); SB["pool" + _d] = (_o + (_w + 15) // 16 * 16, _d)
-SCRATCH = {k: ("sbuf", [128, w], d) for k, (w, d) in SB.items()}
+    _o = SB.get("pool" + _d, 0)
+    AL[_k] = ("pool" + _d, _o); SB["pool" + _d] = _o + (_w + 15) // 16 * 16
+SCRATCH = {k: ("sbuf", [128, w], k[4:]) for k, w in SB.items()}
+ROW = {"p6": 16, "p7": 32}
 for _b in range(8):
-    SCRATCH["p%d" % _b] = ("psum", [128, 512], "float32") if _b < 6 else ("psum", [128, 1024], "bfloat16")
-SEMAPHORES = (["v", "t", "s", "gp", "loc"] + ["d%d" % k for k in range(60)] + ["l%d" % k for k in range(20)]
-              + [k + str(t) for k in ("rs", "ag") for t in range(12)] + [k + str(t) for k in ("yq", "hi") for t in range(4)])
+    BUF["p%d" % _b] = (1024, BF) if _b == 7 else (512, FP)
+    SCRATCH["p%d" % _b] = ("psum", {6: [128, 32, 16], 7: [128, 32, 32]}.get(_b, [128, 512]), BUF["p%d" % _b][1])
+PS = ["p%d" % _b for _b in range(8)]
+SEMAPHORES = (["v", "t", "s", "gp", "loc", "dz"] + ["d%d" % k for k in range(60)] + ["rs%d_%d" % (k, y) for k in range(6) for y in range(4)]
+              + ["ag%d_%d" % (k, x) for k in range(12) for x in range(2)] + ["yq%d_%d" % (k, x) for k in range(4) for x in range(2)] + ["hi%d" % k for k in range(4)])
 
 
-def V(n, lo=0, hi=None, st=1):
-    b, o, w = AL[n]
-    return ("V", b, o + lo, o + (w if hi is None else hi), st)
+def V(n, lo=0, hi=None, st=1, part=(0, 128, 1), out=(1, 0)):
+    return ("V", n, lo, BUF[n][0] if hi is None else hi, st, part, out)
 
 
 def IND(w, o):
@@ -73,32 +49,34 @@ def IND(w, o):
 
 
 def nel(v):
-    return 16 * nel(v[2]) if v[0] == "I" else len(range(v[2], v[3], v[4]))
+    return 16 * nel(v[2]) if v[0] == "I" else len(range(v[2], v[3], v[4])) * v[6][0]
 
 
 def isv(a):
     return isinstance(a, tuple) and len(a) > 0 and a[0] in ("V", "I")
 
 
+def on(v, lo, n, st=1):
+    return v[:5] + ((lo, n, st), v[6])
+
+
 def plan(r, own):
-    ops = []; nm = [0]; ty = 0 if r in own[0] else 1; xr = own[ty].index(r); big = []
+    ops = []; ty = 0 if r in own[0] else 1; xr = own[ty].index(r); big = []
 
-    def spans(x):
-        if x[0] != "V":
-            return spans(x[1]) + spans(x[2]) if x[0] == "I" else []
-        return [(x[1], x[2], x[3], x[4] if PAR["exact"] else 1) + ((x[5], x[5] + x[6] * x[7]) if len(x) > 5 else (0, 128))]
+    def views(x):
+        return [x] if x[0] == "V" else views(x[1]) + views(x[2]) if x[0] == "I" else []
 
-    def op(eng, *ins):
+    def op(eng, *ins, alt=None, on="s"):
         rd, wr = [], []
         for m, a, kw in ins:
             if a[0][0] == "I":
-                wr += spans(a[0][1]); rd += spans(a[0][2])
+                wr += views(a[0][1]); rd += views(a[0][2])
             else:
-                wr += spans(a[0])
+                wr += views(a[0])
             for x in list(a[1:]) + list(kw.values()):
                 if isv(x):
-                    rd += spans(x)
-        ops.append((eng, "c", ins, sorted(set(rd)), sorted(set(wr)), 0))
+                    rd += views(x)
+        ops.append(((eng,) if alt is None else (eng, on), "c", (ins,) if alt is None else (ins, (alt,)), sorted(set(rd)), sorted(set(wr))))
 
     def ts(o, i, s1, s2, o0, o1=None):
         op("v", ("tensor_scalar", (o, i, s1, s2, o0) if o1 is None else (o, i, s1, s2, o0, o1), {}))
@@ -110,76 +88,71 @@ def plan(r, own):
         op("v", ("tensor_copy", (o, i), {}))
 
     def ms(o, c):
-        op("v", ("memset", (o, c), {}))
+        op("v", ("memset", (o, c), {}), alt=("iota", (o, [[0, nel(o)]], int(c), 0), {"allow_small_or_imprecise_dtypes": True}), on="gp")
 
     def scan(o, a, b, f0, f1):
         op("v", ("tensor_tensor_scan", (o, a, b, 0.0, f0, f1), {}))
 
-    def act(o, i, f=None, **kw):
-        op("s", ("activation", (o, i, f if f is not None else (F.Identity if kw else F.Copy)), kw))
-
-    def mov(o, i, bias=None):
-        k = nm[0]; nm[0] += 1
-        if ONV[ty][k] == "1":
-            cp(o, i) if bias is None else ts(o, i, bias, None, A.add)
-        elif bias is None:
-            act(o, i)
+    def mov(o, i, bias=None, scale=None):
+        kw = {k: x for k, x in (("bias", bias), ("scale", scale)) if x is not None}
+        alt = ("activation", (o, i, F.Identity if bias is not None else F.Copy), kw)
+        if BUF[o[1]][1] == U16 and not PAR["s16"]:
+            alt = None
+        if not kw:
+            op("v", ("tensor_copy", (o, i), {}), alt=alt)
+        elif len(kw) == 2:
+            op("v", ("tensor_scalar", (o, i, scale, bias, A.mult, A.add), {}), alt=alt)
         else:
-            act(o, i, bias=bias)
-        ops[-1] = ops[-1][:5] + (k + 1,)
+            op("v", ("tensor_scalar", (o, i, bias if scale is None else scale, None, A.add if scale is None else A.mult), {}), alt=alt)
 
     def iota(o, pat, base, cm):
-        op("gp", ("iota", (o, pat, base, cm), {} if SB[o[1]][1] == I32 else {"allow_small_or_imprecise_dtypes": True}))
+        op("gp", ("iota", (o, pat, base, cm), {} if BUF[o[1]][1] == I32 else {"allow_small_or_imprecise_dtypes": True}))
+
+    def pe(ins, k):
+        for a in range(0, len(ins), k if PAR["cut"] else len(ins)):
+            op("t", *ins[a:a + (k if PAR["cut"] else len(ins))])
 
     def mm(groups, first=True, last=True):
         ins = []
         for gr in groups:
             for k, (o, l, x) in enumerate(gr):
                 ins.append(("matmul", (o, l, x, first and k == 0, last and k == len(gr) - 1), {}))
-        op("t", *ins)
+        pe(ins, PAR["cut"] if nel(ins[-1][1][2]) < 256 else 1)
 
     def dma(items, split=False, paced=False):
         after = big[-PAR["pace"]:][:1] if paced and len(big) >= PAR["pace"] else []
         for k, it in enumerate((items[::2], items[1::2]) if split else (items,)):
-            q = "s" if k else "sy"; num = 0
-            if split == 2:
-                q = "sy" if ONV[ty][nm[0]] == "1" else "s"; nm[0] += 1; num = nm[0]
-            ops.append((q, "d", (it, None, after), sorted(set(s for x in it for s in spans(x[1]))), sorted(set(s for x in it for s in spans(x[0]))), num))
+            ops.append((("sy", "s") if split == 2 else ("s",) if k else ("sy",), "d", (it, after),
+                        sorted(set(s for x in it for s in views(x[1]))), sorted(set(s for x in it for s in views(x[0])))))
         if paced:
             big.append(len(ops) - 1)
 
     def send(name, pairs, one):
-        ops.append(("gp", "r", (name, pairs, one), sorted(set(s for x in pairs for s in spans(x[1]))), [], 0))
+        ops.append((("gp",), "r", (name, pairs, one), sorted(set(x[1] for x in pairs)), []))
 
-    def recv(name, views):
-        ops.append(("rx", "x", (name,), [], [s for x in views for s in spans(x)], 0))
+    def recv(name, y, view):
+        ops.append((("rx",), "x", (name, y), [], [view]))
 
     def scatter_sums(s, t, w):
-        name = "rs%d" % (4 * t + s); ow = own[s % 2]; dst = lambda y: V("rP%d_%d" % (t, s // 2), w * y, w * y + w)
-        send(name, [(y, V("sP%d_%d" % (t, s), w * x, w * x + w), dst(r)) for x, y in enumerate(ow) if y != r], False)
-        if r in ow:
-            recv(name, [dst(y) for y in others])
+        send("rs%d" % (4 * t + s), [(y, V("sP%d_%d" % (t, s), w * x, w * x + w), V("rP%d_%d" % (t, s // 2), w * r, w * r + w)) for x, y in enumerate(own[s % 2]) if y != r], False)
 
     def spread(name, n, w):
         a = V(n, w * xr, w * xr + w)
         send(name, [(y, a, a) for y in others], True)
 
-    def take(name, s, n, w):
-        recv(name, [V(n, w * x, w * x + w) for x, y in enumerate(own[s % 2]) if y != r])
-
     col = lambda n, j: V(n, j, j + 1)
     blk = lambda n, a: V(n, 128 * a, 128 * a + 128)
     SHR, AND = A.arith_shift_right, A.bitwise_and
-    EQ, MUL, ADD, SUB, MAX, MIN = A.is_equal, A.mult, A.add, A.subtract, A.max, A.min
+    EQ, MUL, ADD, MAX, MIN = A.is_equal, A.mult, A.add, A.max, A.min
     others = [x for x in range(4) if x != r]
     C0 = 3072
 
     def zl(s, u, lo, hi, sh=0):
-        return (V("zt_%d" % s, lo + sh + C0 - 1024 * u, hi + sh + C0 - 1024 * u) + (32 * u, 32, 1), ("T", "z", 32 * s, 32, lo, hi - lo))
+        return (V("zt_%d" % s, lo + sh + C0 - 1024 * u, hi + sh + C0 - 1024 * u, 1, (32 * u, 32, 1)), ("T", "z", 32 * s, 32, lo, hi - lo))
 
     ms(V("zb"), 0.0)
+    dma([(V("qi", 64 * s, 64 * s + 64), ("T", "q", 32 * s, 32, 0, 256)) for s in range(4)], True)
     dma([zl(0, u, max(1024 * u - 16, 0), 1024 * u + 1024) for u in range(4)] + [zl(0, 0, 4080, 4096, -4096)], True, True)
-    dma([(V("qi"), ("T", "q", 0, 128, 0, 256))], False, True)
     dma([zl(0, u, 0, 1024 * u - 16) for u in range(1, 4)] + [zl(0, u, 1024 * u + 1024, 4096) for u in range(3)], True, True)
     for ch in PAR["seq"][ty]:
         if ch in "123":
@@ -187,189 +160,167 @@ def plan(r, own):
                 dma([zl(int(ch), u, 0, 4096)], paced=True)
         elif ch in "abc":
             for c in range(4):
-                dma([(V("W%d" % (1 + "abc".index(ch)), 1024 * c, 1024 * c + 1024), V("zb", 0, 1024))], paced=True)
-        elif ch in "VBXY":
-            a = AL[{"V": "W1", "B": "W2", "X": "TP_0", "Y": "TP_1"}[ch]]
-            for lo, n in ((0, 512), (512, 512)) if ch in "XY" else [(1024 * c, 1024) for c in range(4)]:
-                o = ("V", a[0], a[1] + lo, a[1] + lo + n, 1)
-                ms(o, 0.0) if ONV[ty][nm[0]] == "1" else act(o, V("zb", 0, n))
-                nm[0] += 1; ops[-1] = ops[-1][:5] + (nm[0],)
+                dma([(V("W%d" % (1 + "abc".index(ch)), 1024 * c, 1024 * c + 1024), V("zb"))], paced=True)
+        elif ch == "V":
+            for c in range(4):
+                o = V("W1", 1024 * c, 1024 * c + 1024)
+                op("v", ("memset", (o, 0.0), {}), alt=("activation", (o, V("zb"), F.Copy), {}))
+                ops[-1] = ops[-1][:3] + ([V("zb")], ops[-1][4])
         else:
-            o = AL["TP_%d" % (ch == "y")]
-            dma([(("V", o[0], o[1], o[1] + 1024, 1), V("zb"))])
+            dma([(V(n + "_%d" % (ch == "y")), V("zb", 0, 512)) for n in ("TP", "TQ")])
 
-    iota(V("X"), [[1, 272]], -64, 0)
-    X = lambda lo, hi, st=1: V("X", 64 + lo, 64 + hi, st)
     iota(col("pi", 0), [[0, 1]], 0, 1)
-    iota(V("Y"), [[1, 2], [2, 4]], 0, 0)
-    iota(V("vI"), [[2048, 2], [128, 2], [256, 8]], 8192, 1)
-    iota(V("c2f"), [[256, 16]], -2047, 2)
-    iota(V("idc"), [[1, 2], [2048, 2], [32, 8]], 8192, 0)
-    for j, (sh, an) in enumerate([(0, 15), (4, 7), (5, 3), (4, 1), (0, 7), (3, 1), (1, 7), (0, 1)]):
+    ms(V("one"), 1.0); ms(V("oneb"), 1.0); ms(V("Bq", 0, 24), 0.0)
+    sel = lambda o, pat, base, f=EQ, cm=1: op("gp", ("affine_select", (o, V("one" if BUF[o[1]][1] == HF else "oneb", 0, nel(o)), pat, f, 0.0, base, cm), {}))
+    for k, (x, par) in enumerate(((0, 0), (1, 0), (xr, 1))):
+        sel(V("Bq", 24 + 128 * k, 152 + 128 * k), [[-1, 4], [1000, 4], [-8, 8]], -64 * x - 4 * par)
+    Bq = lambda k, sh: V("Bq", 24 + 128 * k - sh, 152 + 128 * k - sh)
+    iota(V("X"), [[1, 32]], 0, 0)
+    for j, (sh, an) in enumerate([(0, 15), (4, 7), (5, 3), (1, 7), (0, 1)]):
         ts(col("pi", j + 1), col("pi", 0), sh, an, SHR, AND)
-    cp(V("pf", 0, 9), V("pi", 0, 9))
+    cp(V("pf", 0, 6), V("pi", 0, 6))
     pf = lambda j: col("pf", j)
-    lin = lambda o, a, c, b: ts(pf(o), pf(a), float(c), b, MUL, ADD)
-    ms(V("grp"), 1.0)
-    sel = lambda o, pat, f, base, cm: op("gp", ("affine_select", (o, V("grp", 0, nel(o)), pat, f, 0.0, base, cm), {}))
-    ms(V("sq", 0, 544), 0.0)
-    sqo = (96, 320, 544, 672)
-    SQ = lambda k: V("sq", sqo[k], sqo[k] + 128)
-    for k in range(4):
-        sel(SQ(k), [[-16, 8], [1000, 2], [-2, 8]], EQ, -(k // 2) - 1000 * (k % 2), 1)
-    lin(9, 3, -1024, 5120.0)
-    zc = pf(9)
-    sel(V("idh"), [[-1, 128]], EQ, 0, 1)
-    mov(V("idb"), V("idh"))
-    act(V("nidb"), V("idh"), scale=-1.0)
-    ts(V("pm", 0, 8), V("Y"), pf(2), None, EQ)
-    ts(V("pm", 8, 16), V("Y"), pf(2), -1.0, EQ, MUL)
-    iota(V("Y4"), [[1, 2], [100, 2], [2, 4]], 0, 0)
-    ts(V("pm", 16, 32), V("Y4"), pf(2), None, EQ)
-    ts(V("pm", 32, 48), V("Y4"), pf(2), -1.0, EQ, MUL)
-    act(V("nidh"), V("idh"), scale=-1.0)
-    sel(V("LT"), [[1, 128]], A.is_gt, 0, -1)
-    sel(V("GE"), [[-1, 128]], A.is_ge, 0, 1)
-    ts(V("blkf"), X(0, 8), pf(2), None, EQ)
-    ts(V("blkh"), X(0, 8), pf(2), None, EQ)
-    iota(V("Y3", 0, 32), [[1, 16], [-100, 2]], 100, 0); iota(V("Y3", 32, 64), [[1, 16], [100, 2]], 0, 0)
-    ts(V("Mp"), V("Y3"), pf(1), None, EQ)
-    ts(V("pen"), X(0, 8), pf(2), -30000.0, EQ, MUL)
-    iota(V("Y2"), [[2, 2], [1, 2], [4, 2]], 0, 0)
-    ts(V("sel"), V("Y2"), pf(7), None, EQ)
+    lin = lambda o, a, c, b: ts(pf(o), pf(a), float(c), float(b), MUL, ADD)
+    lin(7, 3, -1024, 2048 + C0); lin(8, 5, -31, 32); lin(9, 1, 2, 0); lin(10, 1, 2, 1); lin(11, 2, 16, 0)
+    zc = pf(7)
+    sel(V("idh"), [[-1, 128]], 0)
+    for n, c in (("idb", 1), ("nidb", -1), ("nidh", -1), ("i7", 7), ("ia", -4064), ("ib", -4080)):
+        op("v", ("tensor_scalar", (V(n), V("idh"), float(c), None, MUL), {}), alt=("affine_select", (V(n), V("zb", 0, 128), [[-1, 128]], A.not_equal, float(c), 0, 1), {}), on="gp")
+        ops[-1] = ops[-1][:3] + ([V("idh"), V("zb", 0, 128)], ops[-1][4])
+    iota(V("Y", 0, 8), [[1, 2], [2, 4]], 0, 0)
+    ms(V("Y", 8, 12), 99.0)
+    ts(V("pm", 0, 8), V("Y", 0, 8), pf(2), None, EQ)
+    ts(V("pm", 8, 16), V("Y", 0, 8), pf(2), -1.0, EQ, MUL)
+    iota(V("Y", 12, 28), [[1, 2], [100, 2], [2, 4]], 0, 0)
+    ts(V("pm", 16, 36), V("Y", 8, 28), pf(2), None, EQ)
+    ts(V("pm", 36, 56), V("Y", 8, 28), pf(2), -1.0, EQ, MUL)
+    sel(V("LT"), [[1, 128]], 0, A.is_gt, -1)
+    sel(V("GE"), [[-1, 128]], 0, A.is_ge)
+    ts(V("blkn"), V("X", 0, 8), pf(2), -1.0, EQ, MUL)
+    ts(V("blkh"), V("X", 0, 8), pf(2), None, EQ)
+    ts(V("pen"), V("X", 0, 8), pf(2), 8192.0, EQ, MUL)
+    for e in range(2):
+        ts(V("Mp", 32 * e, 32 * e + 32), V("X"), pf(9 + e), None, EQ)
+        ts(V("CR", 12 * e, 12 * e + 4), V("X", 4 * e, 4 * e + 4), pf(4), pf(8), EQ, MUL)
+        ts(V("CR", 12 * e + 4, 12 * e + 12), V("X", 8 * e, 8 * e + 8), pf(1), None, EQ)
+        ms(blk("cT", e), 16384.0 * e - 8192.0)
     for a in range(0, 8, 2):
         op("gp", ("affine_select", (V("Rh", 128 * a, 128 * a + 256), V("zb", 0, 256), [[-16, 2], [0, 8], [-1, 16]], A.not_equal, 1.0, -16 * a, 1), {}))
     ms(V("RS"), 0.0)
     for v in range(2):
-        sel(V("RS", 144 * v + 16, 144 * v + 144), [[-32, 4], [1000, 2], [-1, 16]], EQ, -16 * v, 1)
+        sel(V("RS", 144 * v + 16, 144 * v + 144), [[-32, 4], [1000, 2], [-1, 16]], -16 * v)
     for lo, n, base in ((304, 3, -32), (400, 1, 0), (448, 1, -112), (480, 3, -16)):
-        sel(V("RS", lo, lo + 32 * n), [[-32, n], [1000, 2], [-1, 16]], EQ, base, 1)
+        sel(V("RS", lo, lo + 32 * n), [[-32, n], [1000, 2], [-1, 16]], base)
     RS = lambda v, x: V("RS", 144 * v + 16 - 16 * x, 144 * v + 144 - 16 * x)
-    mov(V("c2", 0, 16), V("c2f"), 1.0)
-    mov(V("c2", 16, 32), V("c2f"))
-    lin(12, 2, 256, 0.0); lin(13, 1, 2, pf(12))
-    iota(V("cf", 0, 4), [[128, 2], [384, 2]], 0, 0); iota(V("cf", 4, 8), [[-128, 2], [256, 2]], 128, 0)
-    lin(11, 1, 2, pf(4)); lin(14, 3, 32, pf(11))
-    ts(V("cl", 24, 32), V("cf", 0, 8), pf(14), None, ADD)
-    lin(16, 2, 8, pf(5)); lin(17, 6, 64, pf(16)); lin(18, 2, 32, pf(1))
-    ts(V("cl", 4, 6), X(0, 129, 128), pf(17), None, ADD)
-    lin(19, 2, 8, pf(7)); lin(20, 8, 256, pf(19))
-    ts(V("cl", 16, 20), X(0, 193, 64), pf(19), None, ADD)
-    ts(V("cl", 20, 24), X(0, 193, 64), pf(20), None, ADD)
-    ts(V("cl", 10, 12), X(0, 129, 128), pf(0), None, ADD)
-    ts(V("cl", 12, 14), X(0, 17, 16), pf(18), None, ADD)
-    cP, cP2, cP0, cQ0, cF = V("cl", 16, 20), V("cl", 20, 24), V("cl", 4, 6), V("cl", 10, 12), V("cl", 12, 14)
-    ms(V("two"), 2.0)
+    sel(V("Zh"), [[-16, 9], [1000, 16]], 16); sel(V("Zl"), [[-16, 9], [1000, 16]], 8)
+    op("gp", ("affine_select", (V("Zf"), V("Zh"), [[-16, 9], [1000, 16]], A.not_equal, 1.0, 8, 1), {}))
+    sel(V("Bc"), [[-16, 8], [0, 16]], -8)
+    iota(V("kc", 0, 32), [[0, 2], [128, 16]], -2047, 1); iota(V("kc", 32, 48), [[128, 16]], -2048, 1)
+    iota(V("vI", 0, 32), [[0, 2], [8, 2], [16, 8]], 0, 0); iota(V("vI", 32, 64), [[-1, 2], [0, 16]], 1, 0); iota(V("vI", 64, 96), [[0, 2], [1, 16]], 0, 0)
     ms(V("TI"), 0.0)
-    mov(V("TI", 16, 528, 16), V("vI"))
-    tt(V("TI", 17, 529, 16), V("vI"), V("TI", 16, 528, 16), SUB)
-    Rh = lambda a: blk("Rh", a)
+    mov(V("TI", 16, 528, 16), V("vI", 0, 32), pf(2)); mov(V("TI", 17, 528, 16), V("vI", 32, 64), pf(9))
     ts(V("qh", 0, 256), V("qi"), -2048.0, None, ADD)
     ts(V("qh", 512, 768), V("qh", 0, 256), 1.0, None, ADD)
     ts(V("qh", 768, 1024), V("qh", 0, 256), 2047.0, -4096.0, EQ, MUL)
     tt(V("qh", 256, 512), V("qh", 512, 768), V("qh", 768, 1024), ADD)
-    for c in range(8):
-        iota(V("wD", 512 * c, 512 * c + 512), [[0, 512]], 0, 0)
 
     def stream(s):
-        W = lambda n, lo=0, hi=None, st=1: V("%s_%d" % (n, s), lo, hi, st)
-        P = lambda lo=0, hi=512, st=1: ("V", "p%d" % (4 + s % 2), lo, hi, st)
-        ZW = W("zt"); mine = r in own[s % 2]
+        W = lambda n, *a: V("%s_%d" % (n, s), *a)
+        P = lambda *a: V("p6", *a); Q = lambda *a: V("p%d" % (4 + s % 2), *a)
+        ZW = W("zt"); ow = own[s % 2]
         odd = lambda n, j: W(n, 256 * j + 1, 256 * j + 256, 2)
-        sub = lambda v, j: v[:2] + (v[2] + 128 * j * v[4], v[2] + (128 * j + 127) * v[4] + 1, v[4])
+        sub = lambda v, j: v[:2] + (v[2] + 128 * j * v[4], v[2] + (128 * j + 127) * v[4] + 1) + v[4:]
 
-        def term(o, a, x, on_s):
+        def term(o, a, x, on_s, P=Q):
             if on_s:
                 mm([[(P(), V("idb"), a), (P(), V("nidb"), x)]])
-                act(o, P(), F.Relu)
+                op("s", ("activation", (o, P(), F.Relu), {}))
             else:
                 tt(o, a, x, MAX)
 
-        def reduce(out, items):
-            d = {}
-            for v, sg in items:
-                d[v] = d.get(v, 0) + sg
-            pm = (V("pm", 0, 8), V("pm", 8, 16)) if nel(out) == 8 else (V("pm", 16, 28), V("pm", 32, 44))
-            return [(out, v, pm[sg < 0]) for v, sg in d.items() for _ in range(abs(sg))]
+        def between(f, g, a, b, n=1):
+            for c in range(0, 1024, 1024 // n):
+                e = c + 1024 // n
+                scan(W(f, c, e), a(c, e), b(c, e), MAX, MIN); scan(W(g, c, e), a(c, e), b(c, e), MIN, MAX)
 
-        def between(f, g, a, b):
-            n = 1024 // PAR["nch"]
-            for c in range(PAR["nch"]):
-                for o, f0, f1 in ((f, MAX, MIN), (g, MIN, MAX)):
-                    scan(W(o, n * c, n * c + n), a(n * c, n), b(n * c, n), f0, f1)
+        seq = lambda o, n="S": lambda c, e: W(n, o + c, o + e)
+        red2 = lambda g, f, o, js=range(4): [(Q(j, 64, 4), odd(v, j), V("pm", o + c, o + c + 16)) for j in js for v, c in ((g, 16), (f, 36))]
 
         def start():
-            h = lambda c, u: W("zt", c, c + 1) + (32 * u, 32, 1)
             if s:
-                mov(h(C0 - 1, 0), h(7167, 0))
-            k32 = (32 * s, 32, 1)
-            mm([[(P(32 * d, 32 * d + 32), V("sq", 96 + 224 * k + 32 * (s - u), 224 + 224 * k + 32 * (s - u)) + k32, V("qh", 256 * d + 64 * u + k, 256 * d + 64 * u + 64, 2) + k32)
-                 for u in range(4) for k in range(2)] for d in range(2)])
-            ts(W("L", 0, 64), P(0, 64), zc, None, ADD)
+                mov(W("zt", C0 - 1, C0, 1, (0, 32, 1)), W("zt", 7167, 7168, 1, (0, 32, 1)))
+            mm([[(P(32 * d, 32 * d + 32), Bq(x, 16 * x + 8 * k), V("qh", 256 * d + 64 * s + k, 256 * d + 64 * s + 64, 2)) for x in range(2) for k in range(2)] for d in range(2)])
+            mov(W("L", 0, 64), P(0, 64), zc)
 
         def coords0():
             S = PAR["m"][ty][s]
-            between("f", "g", lambda k, n: W("zt", C0 + k, C0 + k + n), lambda k, n: W("zt", C0 - 1 + k, C0 - 1 + k + n))
-            e, x0, x1 = W("zt", C0, C0 + 1023, 2), W("P2", 0, 512), W("P2", 512, 1024)
+            between("f", "g", seq(C0, "zt"), seq(C0 - 1, "zt"))
+            e, x0, x1 = W("zt", C0, C0 + 1023, 2), W("yt", 0, 512), W("yt", 512, 1024)
             D, Ft, G = W("f2", 0, 512), W("f2", 512, 1024), W("g2", 0, 512)
-            mov(x0, IND(ZW, W("L", 0, 32))); term(D, x0, e, "D" in S)
-            mov(x1, IND(ZW, W("L", 32, 64))); term(Ft, x1, e, "F" in S); term(G, x1, x0, "G" in S)
-            gr = [(P(0, 32), V("idb"), V("zb", 0, 32))]
-            for j in range(4):
-                gr += reduce(P(j, 32, 4), [(odd("g", j), -1), (odd("f", j), 1)])
-            mm([gr], True, False); gr = []
-            for j in range(4):
-                gr += reduce(P(j, 32, 4), [(sub(D, j), 1), (sub(Ft, j), 1), (sub(G, j), -1), (sub(e, j), -1)]
-                             + [(sub(e, j), 1)] * (("D" in S) + ("F" in S)) + [(sub(x0, j), -1)] * ("G" in S))
-            mm([gr], False, True)
-            mov(W("sP0"), P(0, 32))
+            pm = lambda sg: V("pm", 8 * (sg < 0), 8 * (sg < 0) + 8)
+            red = lambda items: [(Q(j, 32, 4), sub(v, j) if v[0] == "V" else odd(v, j), pm(sg)) for j in range(4) for v, sg in items]
+            mov(x0, IND(ZW, W("L", 0, 32))); term(D, x0, e, "D" in S, P if "p" in S else Q)
+            if "x" in S:
+                tt(Ft, IND(ZW, W("L", 32, 64)), e, MAX); tt(G, IND(ZW, W("L", 32, 64)), x0, MAX)
+            else:
+                mov(x1, IND(ZW, W("L", 32, 64))); term(Ft, x1, e, "F" in S); term(G, x1, x0, "G" in S)
+            ne = 1 - ("D" in S) - ("F" in S)
+            items = [(D, -1), (Ft, -1), (G, 1)] + [(e, ne)] * abs(ne) + [(x0, 1)] * ("G" in S)
+            mm([[(Q(0, 32), V("idb"), V("zb", 0, 32))] + red([("g", 1), ("f", -1)])], True, False)
+            mm([red(items)], False, True)
+            mov(W("sP0"), Q(0, 32))
             scatter_sums(s, 0, 16)
 
-        def lists(t, w, n, rng):
-            E = "rE%d_%d" % (t, s); take("ag%d" % (4 * t + s), s, E, w)
-            sh = lambda xs: [(P(o, o + st * (hi - lo - 1) + 1, st), RS(v, x), V(E, w * x + lo, w * x + hi)) for x in xs for v, lo, hi, o, st in rng]
-            mm([[(P(0, n), V("idb"), V("zb", 0, n))] + (sh([xr]) if mine else [])], last=False)
-            mm([sh([1 - xr] if mine else [0, 1])], first=False)
+        def lists(t, w, n, rng, P=P):
+            E = "rE%d_%d" % (t, s)
+            xs = sorted(range(2), key=lambda x: ow[x] != r)
+            for k, x in enumerate(xs):
+                if ow[x] != r:
+                    recv("ag%d" % (4 * t + s), ow[x], V(E, w * x, w * x + w))
+                sh = [(o, RS(v, x), V(E, w * x + lo, w * x + hi)) for v, lo, hi, o in rng]
+                if k == 0 and ow[x] != r:
+                    mm([[(P(0, n), V("idb"), V("zb", 0, n))]], last=False)
+                mm([[(P(0, n), V("idb"), V("zb", 0, n))] * (ow[x] == r) + sh], ow[x] == r, k == 1)
 
         def coords(t):
-            es = 1 - t % 2; S = PAR["m"][ty][4 * t + s]
-            lists(t - 1, 48, 100, [(v, 0, 48, 2 * es + v, 2) for v in range(2)] + [(2, 32, 33, 96 + 2 * es, 1)] + [(3, 15, 16, 1, 1)] * es)
-            ts(W("L"), P(0, 100), zc, None, ADD)
-            LO, LX, LE = (W("L", 0, 34), W("L", 34, 66), W("L", 66, 99)) if es else (W("L", 64, 97), W("L", 32, 64), W("L", 0, 32))
-            o0, i0 = 62 * es, 64 * es
-            mov(W("S", 0, 32 * nel(LO) - 1, 2), IND(ZW, LO))
-            mov(W("S", o0 + 1, o0 + 32 * nel(LE), 2), IND(ZW, LE))
-            between("f", "g", lambda k, n: W("S", o0 + 1 + k, o0 + 1 + k + n), lambda k, n: W("S", o0 + k, o0 + k + n))
-            o, e = W("S", i0, i0 + 1023, 2), W("S", i0 + 1, i0 + 1024, 2)
-            if S == "s":
-                mov(W("P2", 0, 1023, 2), o)
-                mov(W("P2", 1, 1024, 2), IND(ZW, LX))
-                between("f2", "g2", lambda k, n: W("S", i0 + k, i0 + k + n), lambda k, n: W("P2", k, k + n))
-                it = lambda j: [(odd("g2", j), 1), (odd("f2", j), -1)]
+            es = 1 - t % 2; h16 = lambda c, n, st: P(c, c + 16, 1, (0, 128, 1), (n, st))
+            if es:
+                lists(t - 1, 48, 128, [x for h in range(2) for x in ((h, 0, 32, h16(16 + 16 * h, 2, 64)), (h, 32, 48, h16(48 + 16 * h, 1, 0)))] + [(2, 16, 17, P(112, 113)), (3, 15, 16, P(15, 16))])
             else:
-                x = W("P2", 0, 512); At, D, Ft = W("g2", 0, 512), W("f2", 0, 512), W("f2", 512, 1024)
-                term(At, e, o, "A" in S)
-                mov(x, IND(ZW, LX)); term(D, o, x, "D" in S); term(Ft, e, x, "F" in S)
-                it = lambda j: ([(sub(D, j), 1), (sub(Ft, j), 1), (sub(At, j), -1), (sub(x, j), -1)]
-                                + [(sub(x, j), 1)] * (("D" in S) + ("F" in S)) + [(sub(o, j), -1)] * ("A" in S))
-            gr = [(P(0, 64), V("idb"), V("zb", 0, 64))]
-            for j in range(4):
-                gr += reduce(P(16 + j, 61 + j, 4), [(odd("g", j), -1), (odd("f", j), 1)])
-            mm([gr], True, False)
-            mm([[m for j in range(4) for m in reduce(P(j, 45 + j, 4), it(j))]], False, True)
-            mov(W("sP%d" % t), P(0, 64))
+                lists(t - 1, 48, 112, [x for h in range(2) for x in ((h, 16, 48, h16(16 * h, 2, 32)), (h, 0, 16, h16(64 + 16 * h, 1, 0)))] + [(2, 0, 1, P(96, 97))])
+            mov(W("L", 0, 112 + 16 * es), P(0, 112 + 16 * es), zc)
+            LO, LX, LE = ((14, 48), (48, 80), (80, 113)) if es else ((64, 97), (32, 64), (0, 32))
+            o0, i0 = 62 * es, 64 * es; n = 1 + (4 * t + s in PAR["half"])
+
+            def take(c, l, cut, o="S"):
+                for a, b in ((l[0], l[0] + cut), (l[0] + cut, l[1])) if n > 1 else (l,):
+                    mov(W(o, c + 32 * (a - l[0]), c + 32 * (b - l[0]) - 1, 2), IND(ZW, W("L", a, b)))
+
+            take(0, LO, 18); take(o0 + 1, LE, 16 + 2 * es)
+            between("f", "g", seq(o0 + 1), seq(o0), n)
+            take(1, LX, 16, "yt")
+            for c in range(0, 1024, 1024 // n):
+                o, i = W("yt", c, c + 1024 // n - 1, 2), W("S", i0 + c, i0 + c + 1024 // n - 1, 2)
+                op("v", ("tensor_copy", (o, i), {}), alt=("affine_select", (o, i, [[0, 512 // n]], A.is_ge, 0.0, 0, 0), {}), on="gp")
+            between("f2", "g2", seq(i0), seq(0, "yt"), n)
+            mm([[(Q(0, 64), V("idb"), V("zb", 0, 64))] + red2("g", "f", 0)], True, False)
+            for c in range(n):
+                mm([red2("g2", "f2", 4, range(4 // n * c, 4 // n * (c + 1)))], False, c == n - 1)
+            mov(W("sP%d" % t), Q(0, 64))
             scatter_sums(s, t, 32)
 
         def final():
-            lists(2, 32, 64, [(v, 0, 32, 32 * v, 1) for v in range(2)])
-            ts(W("LY"), P(0, 64), zc, None, ADD)
+            lists(2, 32, 64, [(v, 0, 32, Q(32 * v, 32 * v + 32)) for v in range(2)], Q)
+            mov(W("LY"), Q(0, 64), zc)
             for c in range(2):
                 mov(W("yt", 512 * c, 512 * c + 512), IND(ZW, W("LY", 32 * c, 32 * c + 32)))
-            dma([(("T", "yz", 32 * s, 32, 1024 * u, 1024), W("yt") + (32 * u, 32, 1)) for u in range(4)], 2)
+            dma([(("T", "yz", 32 * s, 32, 1024 * u, 1024), on(W("yt"), 32 * u, 32)) for u in range(4)], 2)
 
         def targets():
-            take("yq%d" % s, s, "rX2_%d" % s, 32)
-            mov(W("qf"), W("rX2"), 2047.0)
+            for x in range(2):
+                if ow[x] != r:
+                    recv("yq%d" % s, ow[x], W("rX2", 32 * x, 32 * x + 32))
+            mov(W("qf"), W("rX2"), 2048.0)
             dma([(("T", "yq", 2 * s + x, 1, 0, 4096), W("qf", 32 * x, 32 * x + 32)) for x in range(2)], 2)
 
         return [start, coords0, lambda: coords(1), lambda: coords(2), final, targets]
@@ -377,176 +328,138 @@ def plan(r, own):
     def chain(b):
         s = 2 * b + ty
         N = lambda n: "%s_%d" % (n, b)
-        W = lambda n, lo=0, hi=None, st=1: V(N(n), lo, hi, st)
-        P = lambda k, lo=0, hi=512, st=1: ("V", "p%d" % (2 * b + min(k, 1)), lo, hi, st)
+        W = lambda n, *a: V(N(n), *a)
+        P = lambda k, *a: V("p%d" % (2 * b + k), *a)
+        PT = lambda *a: V("p7", *a)
+        row = lambda n, k: W(n, k, 512, 16)
 
-        def turn(o, tiles):
-            n = 128 * len(tiles); ps = lambda lo, hi: ("V", "p%d" % (6 + b), lo, hi, 1)
-            op("t", *[("transpose", (ps(128 * k, 128 * k + 128), x, V("idb")), {}) for k, x in enumerate(tiles)])
-            mov(o, ps(0, n))
+        def turn(tiles, flat):
+            o = lambda k: PT(128 * k, 128 * k + 128) if flat else PT(256 * (k // 2) + 16 * (k % 2), 256 * (k // 2) + 16 * (k % 2) + 16, 1, (0, 128, 1), (8, 32))
+            op("t", *[("transpose", (o(k), x, V("idb")), {}) for k, x in enumerate(tiles)])
+            mov(W("rows"), PT(0, 512))
 
-        def rep(k, lo, rhs):
-            n = nel(rhs)
-            return [[(P(k, lo + a, lo + 8 * n, 8), Rh(a), rhs)] for a in range(8)]
+        def rep(k, rhs):
+            return [(P(k, a, 8 * nel(rhs), 8), blk("Rh", a), rhs) for a in range(8)]
 
-        def split(v, row, tile="TP"):
-            st = 512 // nel(v); hi = W(tile, row, 512, st)
-            mov(hi, v)
-            tt(W(tile, row + 1, 512, st), v, hi, SUB)
-
-        def urgent(t):
-            p = t % 2
-            if t:
-                ts(W("qd", 128, 160), P(2, 64, 96), 2047.0, None, ADD)
-            else:
-                ts(W("qd", 144, 160), W("VP", 33, 64, 2), -8192.0, None, ADD)
-            ts(W("qd", 0, 32), W("qd", 128, 160), 5, None, SHR)
-            ts(W("qd", 32, 64), W("qd", 128, 160), 31, None, AND)
-            cp(W("uP", 0, 64), W("qd", 0, 64))
-            mov(W("maskE"), IND(V("Mp", 32 * p, 32 * p + 32), W("uP", 32, 48)))
-            mov(W("maskO"), IND(V("Mp", 32 - 32 * p, 64 - 32 * p), W("uP", 48, 64)))
-
-        def prep(t, c):
-            if t == 0:
-                ts(W("qd", 128, 144), P(2, 0, 16), c, None, ADD)
-                mov(W("VP", 64, 128, 2), P(2, 0, 32), c + 8192.0)
-            elif t == 1:
-                mov(W("VP", 64, 128), P(2, 0, 64), c + 8192.0)
-            else:
-                ts(W("qa", 0, 32), P(2, 0, 32), c, 4097.0, ADD, MUL)
-                ts(W("qb", 0, 32), W("qa", 0, 32), 5, 4032, SHR, AND)
-                ts(W("qb", 32, 64), W("qa", 0, 32), 5, 63, SHR, AND)
-            if t:
-                rows(t)
-
-        def rows(t):
-            if t < 2:
-                split(W("VP", 64, 128), 4 * t * (1 - b) + 2)
-            else:
-                for k in range(2):
-                    cp(W("TQ", 12 + 2 * b + k, 512, 16), W("qb", 32 * k, 32 * k + 32))
-            turn(W("rows"), [blk(N("TP" if t < 2 else "TQ"), k) for k in range(4)])
+        def address(u, ps, c, m, gm, last, pa, again):
+            big = 24576 if last else 49152
+            mov(m, ps, c + big - (7.5 if last else 15.5))
+            mov(gm, ps, c / 512.0 + 1535.5 + 1 / 1024.0, 1 / 512.0)
+            mm([again + [(pa, V("i7"), m), (pa, V("ib" if last else "ia"), gm)]], first=bool(again))
+            mov(u, pa, float(c - 7 * big + 1536 * (4080 if last else 4064)))
 
         def prep0():
-            ms(W("cum", 0, 8), 0.0); ms(W("fl"), 0.0)
-            mm([[(P(2, 0, 256), Rh(2 * s + xr), V("qh", 0, 256))]])
-            mov(W("wL", 0, 256), P(2, 0, 256))
-            mov(W("q0h"), IND(W("wL", 0, 256), cQ0))
-            ts(W("uq0"), W("q0h"), 2048.0, None, ADD)
-            mm([[(P(2, 16 * pp, 16 * pp + 16), SQ(2 * pp + e), W("q0h", e, 32, 2)) for e in range(2)] for pp in range(2)])
-            prep(0, 2048.0)
-            turn(W("rowsI"), [V("TI", 12 - 2 * b + 128 * k, 140 - 2 * b + 128 * k) for k in range(4)])
+            ms(W("cum", 0, 8), 0.0)
+            qd = lambda k: [(P(k, 16 - 16 * par, 32 - 16 * par), Bq(2 if par else xr, 16 * h + 8 * j), V("qh", 64 * s + 32 * h + j, 64 * s + 32 * h + 32, 2))
+                            for par in range(2) for h in range(2) for j in range(2)]
+            mm([[(P(0, 0, 32), V("idb"), V("zb", 0, 32))] + qd(0)])
+            mm([[(P(1, 0, 32), V("idb"), V("zb", 0, 32))] + qd(1)], last=False)
+            address(W("uq"), P(0, 0, 32), 2048, W("m32"), W("gm"), False, P(1, 0, 32), [])
+            turn([V("TI", 16 - 2 * b + 128 * k, 144 - 2 * b + 128 * k) for k in range(4)], True)
             for k in range(2):
-                cp(IND(V("W1"), W("uq0", 16 * k, 16 * k + 16)), W("rowsI", 256 * k, 256 * k + 256))
-            mm([[(P(2, 16 * pp + cc, 16 * pp + cc + 1), V("W1", 256 * cc + pp, 256 * cc + 256, 2), col("sel", 4 + 2 * b))] for pp in range(2) for cc in range(16)])
-            mov(W("l1", 32, 64), P(2, 0, 32), -10240.0)
-            mm(rep(2, 256, W("l1", 32, 64)))
-            mov(W("wL", 256, 512), P(2, 256, 512))
-            mov(W("VP", 0, 64), IND(W("wL", 256, 512), cP), 10240.0)
-            urgent(0)
-            mov(W("VP", 0, 64, 2), V("idc"), pf(13))
-            mov(W("VP", 65, 128, 2), W("VP", 1, 64, 2))
-            split(W("VP", 0, 64), 0)
-            rows(0)
+                cp(IND(V("W1"), W("uq", 16 * k, 16 * k + 16)), W("rows", 256 * k, 256 * k + 256))
+            mm([[(P(1, 0, 32), V("nidh"), W("m32"))] + qd(1)])
+            mov(row("TP", 13), P(1, 0, 32), 51200.0)
+            mov(W("uP", 80, 96), P(1, 16, 32), 51200.0)
+            mov(row("TP", 12), W("m32"), -1536.0, 1 / 32.0)
+            mov(W("uP", 64, 80), W("m32", 16, 32), -1536.0, 1 / 32.0)
+            mov(W("maskE"), IND(V("Mp", 32, 64), W("uP", 80, 96)))
+            mm([[(P(0, j, 64, 32), V("W1", 256 * (j % 16) + 1 - j // 16, 256 * (j % 16) + 256, 2), V("CR", 4 + 2 * b, 6 + 2 * b))] for j in range(32)])
+            mov(W("uP", 0, 48), P(0, 0, 48))
+            mov(W("maskO"), IND(V("Mp", 0, 32), W("uP", 32, 48)))
+            for k in range(2):
+                mov(row("TP", 10 + k), P(0, 32 * k, 32 * k + 32))
+            mov(row("TP", 8), V("vI", 64, 96), pf(11)); mov(row("TP", 9), V("vI", 32, 64), pf(9))
+            turn([blk(N("TP"), k) for k in range(4)], False)
 
         def index(t):
-            p = t % 2; ro = 4 * t * (1 - b)
-            w = 32 if t else 16
+            p = t % 2; w = 32 if t else 16; n = 8 * w; last = t == 2
+            uT, uG = [W("uP", c, c + 16) for c in ((64, 0), (48, 0), (16, 32))[t]]
             part = lambda y: V("sP%d_%d" % (t, s), w * xr, w * xr + w) if y == r else W("rP%d" % t, w * y, w * y + w)
-            pen = lambda o, n: [(P(1, o + 8 * R, o + 8 * R + 8), blk(N(n), R), V("pen")) for R in range(2)]
-            PO = P(0, 256, 272); L = P(1, 32 - w, 32); n = 8 * w
-            mm([[(P(0, 0, n), V("idb"), V("zb", 0, n))] + [(P(0, a, n, 8), Rh(a), part(r)) for a in range(8)]], last=False)
-            mm([[(P(0, a, n, 8), Rh(a), part(x)) for x in others for a in range(8)]], first=False)
+            L = P(1, 32 - w, 32); red = lambda o, x, k, m: [(P(1, o + R, o + 16, 2), blk(N(x), k + R), V(m)) for R in range(2)]
+            mm([[(P(0, 0, n), V("idh"), V("cT", 256 - n, 256))] + rep(0, part(r))], last=False)
+            mm([[(P(1, 0, 32), V("nidh"), V("cT", 112, 144)), (P(1, 0, 16), V("idh"), V("one", 0, 16)), (L, V("idh"), part(r))] + (red(16, "maskE", 0, "pen") if t == 0 else [])], last=False)
+            far = sorted(others, key=lambda y: y in own[ty])
+            for y in far:
+                recv("rs%d" % (4 * t + s), y, part(y))
+                mm([rep(0, part(y))], False, y == far[2])
             mov(W("wI", 256 - n, 256), P(0, 0, n))
-            mm([[(P(1, 0, 32), V("idb"), V("zb", 0, 32))] * (t == 0) + [(L, V("idh"), part(r))] + pen(0, "maskO") + pen(16, "maskE")], last=False)
-            mm([[(L, V("idh"), part(x)) for x in others]], first=False, last=False)
+            mm([[(L, V("idh"), part(y)) for y in others]], False, False)
+            PA = P(0, 256, 288); A1, A2 = P(0, 256, 272), P(0, 272, 288)
+            mm([[(PA, V("idh"), V("kc", 16 - 16 * p, 48 - 16 * p))]], last=False)
             if t:
-                tt(W("gI", 256, 512), IND(W("wI", 0, 128), W("uP", 0, 16)), W("maskE"), MUL)
-                mm([[(P(1, 8 * R, 8 * R + 8), blk(N("gI"), R), V("blkf")) for R in (2, 3)]], first=False, last=False)
-            tt(W("gI", 0, 256), IND(W("wI", 128, 256), W("uP", 16, 32)), W("maskO"), MUL)
-            mm([[(P(1, 8 * R, 8 * R + 8), blk(N("gI"), R), V("blkf")) for R in (0, 1)]], first=False)
-            ts(W("fl", 1, 64, 2), P(1, 0, 32), -30000.0, None, A.is_lt)
-            guest, mv = W("fl", 1, 32, 2), W("fl", 33, 64, 2)
-            mm([[(PO, V("idh"), V("c2", 16 * p, 16 * p + 16))]], last=False)
+                tt(W("gI", 256, 512), IND(W("wI", 0, 128), uT), W("maskE"), MUL)
+                mm([red(16, "gI", 2, "blkn")], False, False)
+            tt(W("gI", 0, 256), IND(W("wI", 128, 256), uG), W("maskO"), MUL)
+            mm([red(0, "gI", 0, "blkn")], False)
+            ts(W("fl"), P(1, 0, 32), 0.5, None, A.is_lt)
+            guest, stays = W("fl", 0, 16), W("fl", 16, 32)
             c1, cb = W("cum", 8, 24), W("cum", 7, 23)
-            if p == 0:
-                mm([[(PO, V("nidh"), mv)]], first=False, last=False)
-            scan(c1, guest, mv, ADD, SUB)
+            mm([[(A2, V("idh"), guest) if p else (A1, V("idh"), stays)]], False, False)
+            scan(c1, guest, stays, ADD, ADD)
+            pre = lambda o: [(o, V("LT"), c1), (o, V("GE"), cb)]
+            mm([pre(A1) + pre(A2)], False)
+            tt(W("tn"), PA, W("fl"), MUL)
+            mm([[x] for x in rep(1, W("tn", 0, 16))])
+            mov(W("wN"), P(1, 0, 128))
             wn = "W%d" % min(3, 1 + t + b); WW = V(wn)
-            mm([[(PO, V("LT"), c1), (PO, V("GE"), cb)]], first=False)
-            nE, nO = W("nt", 1, 32, 2), W("nt", 32, 48)
-            cp(nO, PO)
-            ts(W("uO"), PO, 2047.0, None, ADD)
-            cp(IND(WW, W("uO")), W("rows", 256, 512))
-            mm(rep(0, 0, nO))
-            mov(W("wN", 128 * (1 - p), 128 * (1 - p) + 128), P(0, 0, 128))
-            tt(W("gP"), IND(W("wN", 128 * (1 - p), 128 * (1 - p) + 128), W("uP", 0, 16)), W("maskE"), MUL)
-            stay = lambda o, u, d: [(o, u, nO)] + ([(o, u, c1), (o, d, cb)] if p else [(o, d, V("two"))])
-            mm([stay(P(1, 33, 64, 2), V("idh"), V("nidh"))])
-            mm([stay(P(1, 32, 63, 2), V("nidh"), V("idh"))], last=False)
-            mm([[(P(1, 32 + 16 * R, 47 + 16 * R, 2), blk(N("gP"), R), V("blkh")) for R in range(2)]], first=False)
-            scan(W("nt", 0, 32), W("fl", 32, 64), P(1, 32, 64), MUL, ADD)
-            ts(W("uE"), nE, 2048.0, None, ADD)
-            cp(IND(WW, W("uE")), W("rows", 0, 256))
-            mm(rep(0, 128, nE))
-            mov(W("wN", 128 * p, 128 * p + 128), P(0, 128, 256), 1.0)
-            dma([(V("wD") + (0, 8, 16), W("wN"))])
-            E = "rE%d_%d" % (t, s); name = "ag%d" % (4 * t + s)
-            if t < 2:
-                pn = 1 - p
-                mm([[(P(1, 128 + 16 * k + cc, 256, 32), V(wn, 256 * cc + pp, 256 * cc + 256, 2), V("sel", ro, ro + 4))]
-                    for k, pp in ((0, pn), (1, 1 - pn)) for cc in range(16)])
-                mov(W("l1"), P(1, 128, 256), -10240.0)
-                mm(rep(1, 256, W("l1", 48 - 16 * (1 - t), 64)))
-                mm(rep(0, 0, W("l1", 0, 32)))
-                mov(W("wL", 256 + 128 * t, 512), P(1, 256, 512 - 128 * t))
-                mov(W("wL", 0, 256), P(0, 0, 256))
-                mov(V(E, 48 * xr, 48 * xr + 48), IND(W("wL"), V("cl", 24 + 4 * t, 27 + 4 * t)))
-                spread(name, E, 48)
-                if t == 0:
-                    mov(W("VP", 0, 64), IND(W("wL"), cP2), 10240.0)
-                    split(W("VP", 0, 64), 4 - 4 * b)
-                else:
-                    mov(W("VP", 0, 32), IND(W("wL", 0, 256), cP0), 10240.0)
-                    split(W("VP", 0, 32), 4 + 2 * b, "TQ")
-                ts(W("qa"), W("l1", 64, 128), 2048.0, 4097.0, ADD, MUL)
-                ts(W("qb", 0, 64), W("qa"), 5, 4095, SHR, AND)
-                cp(W("uN", 0, 64), W("qb", 0, 64))
-                cuts = ((0, 16), (48, 64), (16, 32)) + ((32, 48),) * (1 - t)
-            else:
-                mm([[(P(1, 128 + cc, 129 + cc), blk("W3", cc), col("sel", 4 + 2 * b))] for cc in range(32)])
-                mov(W("l1", 0, 32), P(1, 128, 160), -10240.0)
-                mm(rep(0, 0, W("l1", 0, 32)))
-                mov(W("wL", 0, 256), P(0, 0, 256))
-                mov(V(E, 32 * xr, 32 * xr + 32), IND(W("wL", 0, 256), cF))
-                spread(name, E, 32)
-                mm([[(("V", "p%d" % (4 + ty if b else 1), 192 + y, 193 + y, 1), V("W3", y, 4096, 32), col("sel", 5 + 2 * b))] for y in range(32)])
-                mov(W("l1", 32, 64), ("V", "p%d" % (4 + ty if b else 1), 192, 224, 1), -2048.0)
-                mm(rep(2, 256, W("l1", 32, 64)))
-                mov(W("gI", 0, 256), P(2, 256, 512))
-                ts(W("uN", 0, 32), IND(W("gI", 0, 256), cP0), 2048.0, None, ADD)
-                cuts = ((0, 16), (16, 32))
-            for lo, hi in cuts:
-                mov(W("gQ", 16 * lo, 16 * hi), IND(V("wD"), W("uN", lo, hi)))
-            red = lambda ks, lo=0, st=1: mm([[(P(2, lo + c, lo + c + 7 * st + 1, st), blk(N("gQ"), k), V("blkh"))] for k, c in ks])
-            if t < 2:
-                red(((0, 0), (1, 8), (6, 16), (7, 24)), 64)
-                urgent(t + 1)
-                if t == 0:
-                    red([(k, 16 * (k % 4) + k // 4) for k in range(8)], 0, 2)
-                else:
-                    red([(k, 8 * k) for k in range(4)])
-                prep(t + 1, 2047.0)
-            else:
-                red([(k, 8 * k) for k in range(4)])
-                mov(V("rX2_%d" % s, 32 * xr, 32 * xr + 32), P(2, 0, 32))
+            mO, mE = W("m32", 1 - p, 32, 2), W("m32", p, 32, 2)
+            address(W("uO"), A1, 2047, mO, W("gm", 0, 16), last, A1, [(A1, V("idh"), V("kc", 0, 16))] + pre(A1) + [(A1, V("idh"), stays)] * (1 - p))
+            cp(IND(WW, W("uO")), W("rows", 0, 256))
+            tt(W("gP"), IND(W("wN"), uT), W("maskE"), MUL)
+            nE = lambda o, st, k=0: [(P(k, o, o + 16 * st, st), V("idh"), W("tn", 16, 32))] + [(P(k, o + R * st, o + 16 * st, 2 * st), blk(N("gP"), R), V("blkh")) for R in range(2)]
+            mm([nE(0, 1)[:1]], last=False)
+            mm([nE(0, 1)[1:]], False)
+            mm([nE(0, 1, 1)], last=False)
+            address(W("uE"), P(0, 0, 16), 2048, mE, W("gm", 16, 32), last, P(1, 0, 16), [])
+            cp(IND(WW, W("uE")), W("rows", 256, 512))
+            E = "rE%d_%d" % (t, s); name = "ag%d" % (4 * t + s); pn = 1 - p
+            c0, nq = ((12, 8), (12 * b, 6), (2 * b, 2))[t]
+            mm([[(P(1, j, 32 * nq, 32), blk(wn, j) if last else V(wn, 256 * (j % 16) + (pn if j // 16 else p), 256 * (j % 16) + 256, 2), V("CR", c0, c0 + nq))] for j in range(32)])
+            we = 32 if last else 48
+            mov(V(E, we * xr, we * xr + we), P(1, 0, we), -2048.0)
+            spread(name, E, we)
+            lo, nl = ((32, 64), (64, 48), (32, 32))[t]
+            mov(W("uN", 0, nl), P(1, lo, lo + nl))
+            tile, r0 = ("TQ", 4 * b) if t else ("TP", 8 * b)
+            for k in range((4, 2, 0)[t]):
+                mov(row(tile, r0 + k), P(1, 128 + 32 * k, 160 + 32 * k))
+            PO = P(0, 64 + 1 - p, 96, 2)
+            mm([[(P(0, 64, 96), V("nidh"), W("m32"))] + nE(64 + p, 2) + pre(PO) + [(PO, V("idh"), V("kc", 32, 48))] + [(PO, V("idh"), stays)] * (1 - p)])
+            mov(W("nt", 32, 64), P(0, 64, 96), 26624.0 if last else 51200.0)
+            mov(W("nt", 0, 32), W("m32"), -24576.0) if last else mov(W("nt", 0, 32), W("m32"), -1536.0, 1 / 32.0)
+            pe([("transpose", (PT(128 * par, 128 * par + 128, 1, (32 * k, 32, 1)), W("nt", par, 64, 2), V("idb")), {}) for k in range(4) for par in range(2)], 4)
+            for par in range(2):
+                mov(W("wS", par, 256, 2), PT(128 * par, 128 * par + 128))
+            dma([(on(V("W1"), 64 * k, 8, 8), W("wS")) for k in range(2)], 2)
+            for a in range(0, nl, 16 if last else 32):
+                e = min(a + (16 if last else 32), nl)
+                mov(W("gQ", 16 * a, 16 * e), IND(V("W1"), W("uN", a, e)))
+            Z = lambda z, i: V(z, 16 - i, 144 - i)
+            if last:
+                for h in range(2):
+                    mm([[(P(0, 0, 32), Z("Zf", i), W("gQ", 32 * i, 32 * i + 32)) for i in range(8 * h, 8 * h + 8)]], h == 0, h == 1)
+                mov(V("rX2_%d" % s, 32 * xr, 32 * xr + 32), P(0, 0, 32), -2048.0)
                 spread("yq%d" % s, "rX2_%d" % s, 32)
+                return
+            mm([[(P(0, 0, nl), Z("Zh", i), W("gQ", i, 16 * nl, 16)) for i in range(16)]])
+            mov(W("uP", 0, nl), P(0, 0, nl))
+            cT, cG = (48, 0) if t == 0 else (16, 32)
+            mm([[(P(1, 256 * k, 256 * k + 256), V("Bc"), W("gQ", 16 * c, 16 * c + 256))] for k, c in enumerate((cT, cG))])
+            ts(W("maskE"), P(1, 0, 256), pf(9 + p), None, EQ)
+            ts(W("maskO"), P(1, 256, 512), pf(9 + pn), None, EQ)
+            nr = 64 - 32 * t; dst = ((6, 4), (2,))[t]
+            for k, d in enumerate(dst):
+                mov(row(tile, r0 + d), P(0, 32 * k, 32 * k + 32))
+            mm([[(P(0, 64, 64 + nr), Z("Zl", i), W("gQ", i, 16 * nr, 16)) for i in range(16)]])
+            for k, d in enumerate(dst):
+                mov(row(tile, r0 + d + 1), P(0, 64 + 32 * k, 96 + 32 * k))
+            turn([blk(N(tile), k) for k in range(4)], False)
 
         return [prep0, index]
 
     st = [stream(s) for s in range(4)]; ch = [chain(b) for b in range(2)]
-    late = PAR["late"]
-    for b in range(2 - late):
+    for b in range(2):
         ch[b][0]()
     for t in range(4):
         for s in range(4):
@@ -559,42 +472,46 @@ def plan(r, own):
             if t == 3:
                 st[s][5]()
             elif s % 2 == ty:
-                if t == 0 and s > 1 and late:
-                    ch[1][0]()
                 ch[s // 2][1](t)
     return ops
 
 
-def depend(ops):
-    n = len(ops); deps = [set() for _ in range(n)]; acc = {}; bank = {}
-    for j, (eng, kind, pay, rd, wr) in enumerate(o[:5] for o in ops):
+def bits(v, dma):
+    n = len(range(v[2], v[3], v[4])); m = ((1 << (v[4] * n)) - 1) // ((1 << v[4]) - 1) << v[2]
+    if v[6][0] > 1:
+        m *= ((1 << (v[6][1] * v[6][0])) - 1) // ((1 << v[6][1]) - 1)
+    if dma:
+        k = 4 if BUF[v[1]][1] in (FP, I32) else 8; lo = v[2] // k * k; hi = -(-v[3] // k) * k
+        m = ((1 << (hi - lo)) - 1) << lo
+    return m, ((1 << (v[5][2] * v[5][1])) - 1) // ((1 << v[5][2]) - 1) << v[5][0]
+
+
+def depend(ops, eng):
+    deps = [set() for _ in ops]; acc = {}; bank = {}
+    for j, (_, kind, pay, rd, wr) in enumerate(ops):
         if kind == "d":
-            deps[j].update(pay[2])
-        for nm in set(x[0] for x in rd + wr if x[0] not in SB):
+            deps[j].update(pay[1])
+        for nm in set(x[1] for x in rd + wr if x[1] in PS):
             before, now = bank.get(nm, ([], []))
-            if now and eng == "v" == ops[now[0]][0] and not ops[j][5] and not ops[now[0]][5]:
+            if now and eng[j] == eng[now[0]] != "t":
                 deps[j].update(before); bank[nm] = (before, now + [j])
             else:
                 deps[j].update(now); bank[nm] = (now, [j])
         for lst, isw in ((rd, False), (wr, True)):
-            for (nm, lo, hi, st, pa, pb) in lst:
-                if nm in SB:
-                    old = acc.get(nm, [])
-                    meet = lambda x: lo < x[2] and x[1] < hi and (st != x[4] or (lo - x[1]) % st == 0) and pa < x[6] and x[5] < pb
-                    deps[j].update(x[0] for x in old if (isw or x[3]) and meet(x) and x[0] != j)
-                    acc[nm] = [x for x in old if not (isw and lo <= x[1] and x[2] <= hi and (st == 1 or st == x[4]) and pa <= x[5] and x[6] <= pb and meet(x))] + [(j, lo, hi, isw, st, pa, pb)]
+            for v in lst:
+                if v[1] not in PS:
+                    c, p = bits(v, isw and kind != "c"); old = acc.get(v[1], [])
+                    deps[j].update(x[0] for x in old if (isw or x[3]) and x[1] & c and x[2] & p and x[0] != j)
+                    acc[v[1]] = [x for x in old if not (isw and x[1] & ~c == 0 and x[2] & ~p == 0)] + [(j, c, p, isw)]
     return deps
 
 
 def ordered(r, own):
-    al = "0123456789abcdefghijklmnopqrstuvwxyzABCDEFGHIJKLMNOPQRSTUVWXYZ"; N = len(ORDER) // 2; ty = 0 if r in own[0] else 1
-    ONV[ty] = "1" * 400; ops = plan(r, own); n = len(ops); on = ["1"] * 400; order = []
-    for k in range(N):
-        c, j = divmod(62 * al.index(ORDER[2 * k]) + al.index(ORDER[2 * k + 1]), N); j -= ty * (N - n)
-        if 0 <= j < n:
-            order.append(j); on[ops[j][5] - 1] = str(c)
-    ONV[ty] = "".join(on)
-    return plan(r, own), order
+    al = "0123456789abcdefghijklmnopqrstuvwxyzABCDEFGHIJKLMNOPQRSTUVWXYZ"; ops = plan(r, own); n = len(ops)
+    o = ORDER[0 if r in own[0] else 1]; order = list(range(n)); eng = [x[0][0] for x in ops]
+    for k in range(len(o) // 2):
+        c, j = divmod(62 * al.index(o[2 * k]) + al.index(o[2 * k + 1]), n); order[k] = j; eng[j] = ops[j][0][c]
+    return ops, order, eng
 
 
 def owners(T, topo):
@@ -621,6 +538,23 @@ def mask_of(engines):
     return sum(1 << e for e in engines)
 
 
+def index_of(x):
+    _, n, lo, hi, st, (pa, pn, ps), (k, ks) = x
+    p = slice(pa, pa + (pn - 1) * ps + 1, ps); hi = lo + (len(range(lo, hi, st)) - 1) * st + 1
+    if n not in ROW:
+        b, o = AL.get(n, (n, 0))
+        return b, (p, slice(o + lo, o + hi, st))
+    w = ROW[n]; a, c = divmod(lo, w)
+    if k > 1:
+        return n, (p, slice(a, a + (k - 1) * (ks // w) + 1, ks // w), slice(c, c + hi - lo, st))
+    if (hi - 1) // w == a:
+        return n, (p, a, slice(c, c + hi - lo, st))
+    if st % w == 0:
+        return n, (p, slice(a, (hi - 1) // w + 1, st // w), c)
+    assert w % st == 0 and c < st and (hi - 1) % w >= w - st, x
+    return n, (p, slice(a, (hi - 1) // w + 1), slice(c, w, st))
+
+
 def rank_program(g, core, T, topo):
     S = T.sem; own = owners(T, topo)
     rest = lambda r: [y for y in range(4) if y != r]
@@ -632,8 +566,12 @@ def rank_program(g, core, T, topo):
             return x
         if x[0] == "I":
             return ap(x[1]).indirect(ap(x[2]))
-        p = slice(None) if len(x) == 5 else slice(x[5], x[5] + x[6] * x[7], x[7]) if x[7] > 1 else slice(x[5], x[5] + x[6])
-        return T[x[1]][p, x[2]:x[3]] if x[4] == 1 else T[x[1]][p, x[2]:x[3]:x[4]]
+        n, ix = index_of(x)
+        return T[n][ix]
+
+    def sem_of(name, y):
+        k = int(name[2:])
+        return "rs%d_%d" % (k // 2, y) if name[:2] == "rs" else "%s_%d" % (name, own[k % 2].index(y))
 
     def spread(src, pairs, sem, loc):
         e = common(T, topo, core, [y for y, _, _ in pairs])
@@ -645,40 +583,40 @@ def rank_program(g, core, T, topo):
         c = T.cores[r]; off = common(T, topo, c, rest(r))
         return [e for e in topo.engines(c, helper_of(T, topo, c)) if e not in off]
 
-    def arrivals(name, r):
-        ow = own[int(name[2:]) % 2]
+    def arrivals(name, y):
         if name[:2] == "rs":
-            return sum(len(common(T, topo, T.cores[y], rest(y))) // (1 if y in ow else 2) for y in rest(r))
-        return sum(len(common(T, topo, helper_of(T, topo, T.cores[y]) if name in PAR["help"] else T.cores[y], rest(y))) for y in ow if y != r)
+            return len(common(T, topo, T.cores[y], rest(y))) // (1 if y in own[int(name[2:]) % 2] else 2)
+        return len(common(T, topo, helper_of(T, topo, T.cores[y]) if name in PAR["help"] else T.cores[y], rest(y)))
 
     for r in range(4):
         if core == helper_of(T, topo, T.cores[r]):
-            ops, order = ordered(r, own); n = 0; loc = 0
+            ops, order, _ = ordered(r, own); n = 0; loc = 0
             for j in order:
                 if ops[j][1] == "r" and ops[j][2][0] in PAR["help"]:
                     name, pairs, _ = ops[j][2]
                     g.wait_ge(S["hi%d" % n], len(to_helper(r)))
-                    loc += spread(V("hX%d" % n, 0, nel(pairs[0][1])), pairs, S[name], S.loc); n += 1
+                    loc += spread(V("hX_%d" % n, 0, nel(pairs[0][1])), pairs, S[sem_of(name, r)], S.loc); n += 1
             g.wait_ge(S.loc, loc)
             return
     r = T.rank_of(core)
     if r is None:
         return
-    ops, order = ordered(r, own); deps = depend(ops)
+    ops, order, eng = ordered(r, own); deps = depend(ops, eng)
     pos = {j: k for k, j in enumerate(order)}
     assert len(pos) == len(ops) and all(pos[i] < pos[j] for j in range(len(ops)) for i in deps[j])
     QU = {"v": g.vector, "t": g.tensor, "s": g.scalar, "gp": g, "sy": g.sync}
-    needed = set(i for j in range(len(ops)) for i in deps[j] if not (ops[i][0] == "t" and ops[j][0] == "t"))
-    sig = {}; cnt = {"v": 0, "t": 0, "s": 0, "gp": 0}; nd = 0
+    needed = set(i for j in range(len(ops)) for i in deps[j] if not eng[i] == eng[j] == "t")
+    sig = {}; cnt = {"v": 0, "t": 0, "s": 0, "gp": 0, "dz": 0}; nd = 0
     for j in order:
-        eng, kind, pay = ops[j][:3]
-        if kind == "c":
-            if j in needed:
-                cnt[eng] += 1; sig[j] = (eng, cnt[eng])
-        elif kind == "d":
+        kind, pay = ops[j][1:3]
+        if kind == "c" and j in needed:
+            cnt[eng[j]] += 1; sig[j] = (eng[j], cnt[eng[j]])
+        elif kind == "d" and j in needed:
             sig[j] = ("d%d" % nd, 16 * len(pay[0])); nd += 1
+        elif kind == "d":
+            cnt["dz"] += 16 * len(pay[0]); sig[j] = ("dz", cnt["dz"])
         elif kind == "x":
-            sig[j] = (pay[0], arrivals(pay[0], r))
+            sig[j] = (sem_of(*pay), arrivals(*pay))
 
     def call(q, m, a, kw):
         f = {"matmul": lambda: q.matmul, "transpose": lambda: q.transpose, "tensor_scalar": lambda: q.tensor_scalar, "tensor_tensor": lambda: q.tensor_tensor,
@@ -686,44 +624,44 @@ def rank_program(g, core, T, topo):
              "iota": lambda: q.iota, "affine_select": lambda: q.affine_select, "tensor_tensor_scan": lambda: q.tensor_tensor_scan}[m]()
         return f(*[ap(x) for x in a], **{k: ap(x) for k, x in kw.items()})
 
-    waited = {}; left = []; gate = None; nh = 0
+    waited = {}; loc = 0; gate = None; nh = 0
     for j in order:
-        eng, kind, pay = ops[j][:3]
+        kind, pay = ops[j][1:3]; e = eng[j]
         if kind == "x":
             continue
-        q = QU[eng]; want = {}
+        q = QU[e]; want = {}
         for i in deps[j]:
-            if not (ops[i][0] == "t" and eng == "t"):
+            if not eng[i] == e == "t":
                 nm, c = sig[i]; want[nm] = max(want.get(nm, 0), c)
-        if kind == "d" and gate:
+        if kind == "d" and gate and PAR["gate"]:
             for nm, c in gate.items():
                 want[nm] = max(want.get(nm, 0), c)
         for nm, c in sorted(want.items()):
-            if waited.get((eng, nm), 0) < c:
-                q.wait_ge(S[nm], c); waited[(eng, nm)] = c
+            if waited.get((e, nm), 0) < c:
+                q.wait_ge(S[nm], c); waited[(e, nm)] = c
         if kind == "c":
-            for m, a, kw in pay:
+            for m, a, kw in pay[ops[j][0].index(e)]:
                 ins = call(q, m, a, kw)
             if j in sig:
-                ins.then_inc(S[eng], 1)
+                ins.then_inc(S[e], 1)
         elif kind == "d":
             for o, i in pay[0]:
                 q.dma_start(ap(o), ap(i)).then_inc(S[sig[j][0]], 16)
         else:
-            name, pairs, one = pay; ln = "l%d" % len(left)
+            name, pairs, one = pay; sem = S[sem_of(name, r)]
             if name in PAR["help"]:
-                rid, pid, _ = topo.addr(helper_of(T, topo, core)); e = to_helper(r)
-                g.remote_dma(ap(V("hX%d" % nh, 0, nel(pairs[0][1]))), ap(pairs[0][1]), S["hi%d" % nh], S[ln], pid, rid, mask_of(e))
-                nh += 1; left.append((ln, len(e)))
+                rid, pid, _ = topo.addr(helper_of(T, topo, core)); h = to_helper(r)
+                g.remote_dma(ap(V("hX_%d" % nh, 0, nel(pairs[0][1]))), ap(pairs[0][1]), S["hi%d" % nh], S.loc, pid, rid, mask_of(h))
+                nh += 1; loc += len(h)
                 continue
             if one:
-                n = spread(pairs[0][1], pairs, S[name], S[ln])
+                loc += spread(pairs[0][1], pairs, sem, S.loc)
             else:
-                e = common(T, topo, core, rest(r)); n = len(e); k = n // len(pairs)
-                g.remote_dma_fused([RemoteDMATransfer(dst_ids=[dst_id(topo, T.cores[y])], dma_engine_mask=mask_of(e[k * i:k * i + k]), remote_sem=S[name], src=ap(a), dst=ap(d))
-                                    for i, (y, a, d) in enumerate(pairs)], local_sem=S[ln])
-            left.append((ln, n)); gate = want
-    done = dict(left)
+                h = common(T, topo, core, rest(r)); k = len(h) // len(pairs); loc += len(h)
+                g.remote_dma_fused([RemoteDMATransfer(dst_ids=[dst_id(topo, T.cores[y])], dma_engine_mask=mask_of(h[k * i:k * i + k]), remote_sem=sem, src=ap(a), dst=ap(d))
+                                    for i, (y, a, d) in enumerate(pairs)], local_sem=S.loc)
+            gate = want
+    done = {"loc": loc}
     for nm, c in sig.values():
         done[nm] = max(done.get(nm, 0), c)
     for nm, c in sorted(done.items()):

@@ -1,25 +1,26 @@
 from concourse.mybir import AluOpType as A, ActivationFunctionType as F
 from concourse.bass import DstId, RemoteDMATransfer
 
-PAR = {"m": ("- DFp - DFp".split(),) * 2, "help": ("ag8", "yq0", "yq2", "ag9", "yq1", "ag1"), "pace": 4,
-       "seq": ("Vx123ybc", "V1x23ybc"), "gate": 1, "s16": 1, "cut": 0, "half": ()}
+PAR = {"m": ("- Dp - Dp".split(),) * 2, "help": ("ag8", "yq0", "yq2", "ag9", "yq1", "ag1"), "pace": 4,
+       "seq": ("Vx123ybc", "V1x23ybc"), "gate": 1, "sw": 1}
 ORDER = (
-    "01020y0X1c040c00030x060Q0A0J0Fcv0b0C07050d1z0I0H0G0D0a0Ecw0K1B0B0R1E0e1y0N0M0Ldf1J1F0Z1Ce010290Uga18di1G1Pe80O192Be91Kdged1N1HdD0f0g2Aeb2y1jey1T1ReW2aez1iej3Oes2HeZ1U0Pe53P1b1S110h1A14f10idI2D1Z0jgf2F0k2G2d1h0lgi431d242I170m3R1w1nen3T0nep3Yeq15eB4626f63U3W0p2K0o271k3Qeo2f441x5j3X2g2j1p45161m2h2Lgv5k2N2PcW3Z401V5lgx2i2O2Q2R2Sgo490r42fg2p0s0q1tel2W1ohO4c2M2U2X4b2VeN5seP2Y1X0veO1e30472Z31eRhL322k2m3533362t2v370w344d2lfv3a4e5t393b3c3d2wfBfCgC3geL5p0u4g3h0t1f1q3ieU3r4hfQ4i5q2n0Y5n3j5m3s4n3k5u3l1s133m4j4l4k1v4m4o5v4p0W4q5w4s4r5zhU4t5A5y3u4uev4w1u3n4v4xfS5B1r4yfL4B4C124zfM3w5CfU4DfVi14A1a4E4G4H4Fi04J4Ii44K4L3qi54M4X4N4Z6Q4OfW5KfX4P5F5G6P6S6Rhd6T5J3B4Rjhhf4Y5Lji3C3G3H5M6W3Iia77hg3J3D3K5Ojm6Yjn3L5P6X5R5Tg95S783E5U3F797250jx5V71jy5W7351525X5Q745453jz605Z5YjD6261js7djC63768o644U66657ehi678n8qhs684W6b6c697i7jix7h8pht6d8r6e6g6h7k8s6fjI6i6j57iH7miIkQ6m596n585c6ohAkVkR5e5a7t6p5bkU5f6x5g8v7o7n6q6s8z7p7r6r5h7q5i7s8w7u6v8AjS7w8FiQ8B7y7x8C6u6w7A7zl08G8E8H7B8I6y7Cl77E7D7F6z7G7J7K6A7Hl66B6C7L7I7M7O7Plalb7N7Q9O7Rkfkgj07U837V7W9N9Q9P9Rmf8Q7Xj18Mmg8P6H6F7Ymh8L7Zmla5806G858R816K6Imk8S846J6L8T8U8Wkp6M9V8X8Z6N8Va0jb8Ya69W90a7869Z91mv92mx8788a1938a8994a29695mwa39897a4mA99abmBbm9a9ckz9bac9dky9e9h9iaf9f9jblbo9g9k8d9m9l9n9okBbnlNbplO9p8fkF9sbq8j9tagnOah9B8k9u9z8lnPnTai9A8m9vnSbtbumG9Cbyakatm0avaxbxbzm19wm2m3bA9xawbB8gaybC8hazaAmYlVaDaEaualm4aCaGaF9IaH9JaI9KaKaJaLm8aMaP9MaNndaRaOamaUnfaVanaTaWmLaXnlnmmMb0b7b1b9bEb8b2babbbcaqb3nBnAbNnrobbDbGarb5b6bWbFocbHnCbgo5bho6bibjbKbkbLasbXbYbMc9omodonc1bRbSopoqc8cbogcaccoibUcdcfoBoDc4choscicjckotouoJoI",
-    "0001020x0306e504050E0b0y1g0Hcv0I0Q1B0a0C0G0X0F0R0J0Bcu0K1E1h1f0A0N0O0T1F1c0D0Zcw101G0V1b1H1y0e171z190P2y0U0LcW1JeW2a1jdZeZ0d2B290c0fdl0g2A0odff11d2L1i1L2H1D182b2c2D2M2ddI1P0i1M2e1K2N2Fed1N2j2Gebfg1A1R2I0k0h0j1Tf62Ufd2O2K1n1S1k0mej2R2V110M2k1m2leS1Z1a2P2S0l141U2m0n430per2W1wgE441pen2X13evep25451V1teq162Y47ekel1s260r2Zgx1r27461q2f1o4i0s0qeR2g15324bgG4d0t30gM1v1e2hdjgv1x4q1u0w120v4l31eo2i3335343649373a384c2pfwgJ3c4k4e4r3d4f2q4neL0u4g3e2s3g4s3b3f3h4o3i3l3m3j3n3k4t2tfL3q2weK3r3p3s4ufRfS3tg63wgS3H2x5A4w4y3xg53y3Kg85z5C3z3M2r4D5BfX5D4xgagbfZ5E3B5Fi34z4B4A4Ci64Ei74G4F3D4Igd5H4J4Hgc4K3E4M4L5R5I4N4O5L4P5N4R5Mhf4T4Q5S5O4Whh5Tg24Xg35P5U4Y4V5Q4Z78hnhoii523R53545dijin777a3Sim555X5YgjhB79gk567b6163573T58597c62jA7p3Y5a5f3U643VjB3Z4065416668jF6742jE7f7q5g7g7rhy5h7s5c696bhF7k6a6djQ6c5j5k7j6e7l6fjR7mjV6i6g6kjK6jjU7v6l7o6h7whI6m6o6n7z6p7BhJ6q6t6u7A6r6v6siT7C6y5n6x6z6A8G6BiZj0hL6EhP5phQ6F7D6N6G7E5u8F8I8HhS8JhT6H8K8Ll97L7F6Ilc5q7H7J6J5x8Nld8X7I6KhV6O5r7K6L6P8O7G7M6Q8Rka8Tj96R7Q7Ojf7S8Yjg6U8Z7R8Sln7Tlo7U8U7W7P7V7X7Y81ls8V827Z6W8W83lta684kn87ji86858889kx6ZkykK8clp6X8da5a88ea7a9mxjl94mz8f7293my8l8g98738h9799jrkJ8i709aad75lyjtaf9c9dmDax9f9h8o71ay8jaeaz9gmX8p8qaiaj8s8rmY9j9iah9k9lmZn39o9nak9e9m9q9pn2alaE9ram9skQ9u9t8kaI9v9wkR9z9AaD9x9BlV8vaHlZ8x9EkTaoaJ8A9D9F9GaKm58Bm6n8mg9HaM9R8C8y8D8zmf9KaV8Em8aW9M9UaXaZaYb0b19Vb29Wmk9Y9Nb3b6b8b4anaqb5b7ap9Oarb99PasmQbabcbb9Qbdbebhmnbi9ZbfbjmRbgaNbkbmbnblboava1nNbpnObNbOocbsbzbtbBoda2bRbAbubCmqa4aOaPndbDbEbvaSbFo3mTnebXbwbyaUbxaTo4bIbWbZbYcbc0oobJopbKbLc3bMbSogoibUc5cccdc4cecgoCc6c7c8oEciowcacjckcmcl")
+    "0201000x040306cH0c0I0bch1109050d0R0F0C0G1S0e0A0B0Kcg0J0S0H0D1V0L1W1P230O0P1Q0M2S2te20E0g0fe3d4eE0a29d5ee1YeF0N1j1M24ef0Q131Le81X272a1n20gc0h141lehd31e2Tep0i1heydv2Z1f1cea2b0kd22uf30j2x1R2d1a0l0o2yen1o2cdAeof51OdC0n0mgidD2V2jdz452XgfdF2YdBet4430evgp47ew4aexfa4h2q48324cdE2rdy4bgu2z2A4d4i35372Dgn2BhB334f0s390p0q0rdGer4oeu364mgs38dr3a2C1G34fk3cdHhH3d4k2Jebd73ehE1b4n3feT3g4p5ueVeW3i5t3h3jeq5wgz1deP3k4r0t0u0v5zd9fw3lfx4s1Ffv5A3p1N5Bfz3s15db5x4u4wdN3r4y3t3u4vcIfF4xfG3v19eN3y4zeX1k1K3zeO3J2P3AgJ5CeR2QeU4C4t5D1C4B5E3Kf0dI3B1g4DdR1B2H4E3C163DfNdQ3L4F2sfO4H17fP1A18dM4GfV4I4JfW4M4K4N3H3I3P4O3O4L4RgY4S4Q4T5F5Gh44Uh54X5Hh758hR4ZfZhS5L506R6Ug05N6S6T6Vj5513S5K520whi5Mj83U3T7753715Pg5g6j63Y5O7879jj3Z5Q406Yhd7041jk8k5R425S72jm5a735b5cjo747c8j8m5d5e7e8l5Z5Tje3V8nkx765V5Xd85W7gkA5Yd6607h61hp7i5f5U6362ky645h6665kC5i675l5m8q5n68js6a8s69hx6b7khy6c8v8uioip6dhe7lhf6e6k6h8wir7rhg6j6l6nkG6m5qix8y7n7p5jiyhA6q6z6r6s7oiJ7q7s6BjC5k6tiL7wiM7yiO6E7m1JiD7u7xiF6v7z7v7AiP7C7B6x7D6y8z7E7H7F7IiQ7J7G7K7M7N7L8A7O7PjZ8B6Ik0kL7SkM9G817T6J7U9F9I9H9JiVkO6N8E9K7V8HkblW6O7W6P8G7XlU6Q8I83lY8J9M9Vk7848K9Oke9WkU869X9Q879Rm78M6Kma9Z9S8Nm26Lmc9U8T8P8Ra28O8Qki8S888Ub9bcbal4bbbda08ann8Yk88Wno8X90a58Za491nq92a68b94958ens809396bi8f97a7ljbga898lkbk8clikp9cbl9flmbm9eajalan9gnw9h8hlsbo9iahltkr8d9l9saklvlCam9naoaimy9uasaqlE9olFau9y9xatlyav9r9qarawazaxaylIaAaBaEaCaFaGaD9BaJmQlJaKaIaLaMmW9CmXaPaWmZlMaXaR9EaYaaa9n8abbqn9bpbsacaSaemmb1b2braTbtaVaUafnDagb3ndbvb5b6bzbInJb7nFb8bDbEbJbKbVnKbLbybCnVbNbUbXbWbYnGbZbPbFo9c1bHbGbOocobc4c5c6c8bQc7bRbTo1",
+    "0003041Q020106050x0c110y1Pci0K0I0B0F0H0J0G1S0R0a0d0Dcg0LcJ2S0E0C0e0b0f0S0O1T0Xd5ch141U1V29d40M231f1W0h1c1n2t1B0N1Aee0i1Y1Xd20Pef2T24e82adH2720eE1h130g0j1lf31k1Cd3282u1o2b2ZeBeady0l2deFdbf51R2x2VdD0k0m2cdr0nfceHdGfi2D1j2j2e2Yepff2X0Q3034etex37ey313532gpdB3aevewdC383b2qdE3c2rgsdF4h3ddz4i2zfn4o2AgB3f0p0q0odveo1e4kgudA2B1F3ggEdI1a3m4m1L3i3ker4w1G4n1b0u0seu3h3jd72C4x3leb3p1M3n4pfx4tgH2J4q3r4r0r0wd84ucI3seT1d5GeV3t3qdR2P3u3veN4A3weqd9eX3xeW3A153y3B4zeP3CfI2QfM3F4Bf03E3G3H4CfSfT3IgM3L3WfV4E0v0tdQ3N4Fg6dN3Y3Z3O17404L2F2I164H4J4I3P41gbeQ3R3Q1OeU4K1N4M19g14G4Ng24QdM4Pg34Ogc1K3V4R5F5I5H4S5J4U4T184V5K4W44h84Xh9hW515V4Y525455hU53565W5745hh5XhihY5a465l495b4a5c4bi7hvi85Q5dia5O78777a4c795e7b4d5fic5M4e605R625S4fi26564jl5U5nhpjo7n7d667o47ig5o7p5p68jz7e5r5q7gjq487jjA697i6fhB6b6d5t6c6e6gjC7k6h1g6k6a6i5uhq6m6lhE7u8Aju6nhH7m6j6ojE5i6p6q7s6r5z7x6s1Jhs6t7wiE5AiFiD6xht7y6AiHhK7z6B5w6zhL7A6C6DiN5DiO7BhN7D7F6G6P6H6I7E7HiZ7G6R7I6S6T5x6U6J6VjS7M7O7CiT7K7NiV6L7P6Nj57L7Q7S7R6O7T8z8C8B7Uj68D7X7V7Y8E7Z7WkO8082838P818Q846YkfkgkQ85888R8h6Z72898SkS8a9W73l28I8bl48G748K75l68L768M8i8U9V9Y9X8N9Z8c8j8Om98W8d708Yktkn8Zma8l90718m8nala3lame929493a2amana4mxkx959796a698999amya78pa89b9c8fmA8q9e9g9d9fmi8r9h8umCaaaq8v9i9k9las9j9mkp9nav9qaulA9o9sly8skF9vlCaw9u9wmG9x8xlIay9yaHlJkH9B8t9IlLaJaLaKlS9DaMaNaO9KmYaSaIlUaQ9ElVaUlXlWaT9F9H9GaVaRaWlYaYaXaZb0b1b4b2b5b6b39Rb9nglZacbab8bbbcnm9Snnm2bfbmabaenp9UadbhnwafaAmpbomrbJazaBbpbibqahbsbrmLmNbjblbkajbXaDnCbzbAnKbvbuaGbEnLnMakbIbLbKbMbwbNbFnXbxbPbyaFbYbZo9bRobc1bHbQbGc4occ5c6c8bSbTc7bUo4bW")
 
 BF, HF, FP, I32, U16 = "bfloat16", "float16", "float32", "int32", "uint16"
-STR = {"zt": (7184, BF), "S": (1136, BF), "f": (1024, BF), "g": (1024, BF), "f2": (1024, BF), "g2": (1024, BF), "yt": (1024, BF),
+STR = {"zt": (7184, BF), "S": (1584, BF), "f": (1536, BF), "r": (512, BF), "p": (512, BF), "h": (1024, BF), "yt": (1024, BF),
        "L": (128, U16), "LY": (64, U16), "sP0": (32, HF), "sP1": (64, HF), "sP2": (64, HF),
        "rE0": (96, HF), "rE1": (96, HF), "rE2": (64, HF), "rX2": (64, HF), "qf": (64, FP), "hX": (48, HF)}
-CHN = {"rows": (512, BF), "TP": (512, BF), "TQ": (512, BF), "fl": (32, HF), "rP0": (64, HF), "rP1": (128, HF), "rP2": (128, HF),
-       "wI": (256, FP), "wN": (128, FP), "gI": (512, FP), "gP": (256, HF), "gQ": (1024, BF), "maskE": (256, HF), "maskO": (256, HF),
+CHN = {"rows": (512, BF), "TP": (512, BF), "TQ": (512, BF), "fl": (32, BF), "wb": (16, BF), "rP0": (64, HF), "rP1": (128, HF), "rP2": (128, HF),
+       "wI": (256, FP), "wN": (128, FP), "gI": (512, FP), "gP": (256, HF), "gQ": (1024, BF), "mask": (512, HF),
        "cum": (32, HF), "tn": (32, HF), "m32": (32, HF), "gm": (32, HF), "nt": (64, BF), "wS": (256, BF),
        "uO": (16, U16), "uE": (16, U16), "uN": (64, U16), "uP": (96, U16), "uq": (32, U16)}
-BUF = {"W1": (4096, BF), "W2": (4096, BF), "W3": (4096, BF), "zb": (1024, BF), "TI": (528, BF), "X": (32, FP), "pi": (8, I32), "pf": (16, FP),
+BUF = {"W1": (4096, BF), "W2": (4096, BF), "W3": (4096, BF), "zb": (1024, BF), "TI": (528, BF), "X": (32, FP), "pi": (8, I32), "pf": (32, FP),
        "one": (144, HF), "oneb": (144, BF), "idh": (128, HF), "idb": (128, BF), "nidb": (128, BF), "nidh": (128, HF), "i7": (128, HF), "ia": (128, HF), "ib": (128, HF),
-       "LT": (128, HF), "GE": (128, HF), "Rh": (1024, HF), "RS": (576, HF), "Bq": (408, HF), "Zh": (144, BF), "Zl": (144, BF), "Zf": (144, BF),
-       "Bc": (128, BF), "pm": (64, BF), "Y": (32, FP), "blkn": (8, FP), "blkh": (8, HF), "pen": (8, HF), "Mp": (64, BF), "CR": (24, BF),
-       "cT": (256, HF), "kc": (48, HF), "vI": (96, FP), "qi": (256, I32), "qh": (1024, HF)}
+       "ic": (128, HF), "id": (128, HF), "ie": (128, HF),
+       "LT": (128, HF), "GE": (128, HF), "Rh": (1024, HF), "RS": (560, HF), "R1": (256, HF), "W0": (128, BF), "L0": (256, U16),
+       "Bq": (408, HF), "Zh": (288, BF), "Zf": (144, BF), "Bc": (128, BF), "pm": (80, BF), "Y": (32, FP), "blkn": (8, FP), "blkh": (8, HF), "pen": (8, HF),
+       "Mp": (64, BF), "CR": (24, BF), "cT": (256, HF), "kc": (64, HF), "vI": (96, FP), "qi": (256, I32), "qh": (512, HF)}
 for _k, _v in STR.items():
     for _b in range(4):
         BUF["%s_%d" % (_k, _b)] = _v
@@ -33,7 +34,7 @@ for _k, (_w, _d) in BUF.items():
 SCRATCH = {k: ("sbuf", [128, w], k[4:]) for k, w in SB.items()}
 ROW = {"p6": 16, "p7": 32}
 for _b in range(8):
-    BUF["p%d" % _b] = (1024, BF) if _b == 7 else (512, FP)
+    BUF["p%d" % _b] = (1024, BF) if _b == 7 else (512, FP); AL["p%d" % _b] = ("p%d" % _b, 0)
     SCRATCH["p%d" % _b] = ("psum", {6: [128, 32, 16], 7: [128, 32, 32]}.get(_b, [128, 512]), BUF["p%d" % _b][1])
 PS = ["p%d" % _b for _b in range(8)]
 SEMAPHORES = (["v", "t", "s", "gp", "loc", "dz"] + ["d%d" % k for k in range(60)] + ["rs%d_%d" % (k, y) for k in range(6) for y in range(4)]
@@ -58,6 +59,10 @@ def isv(a):
 
 def on(v, lo, n, st=1):
     return v[:5] + ((lo, n, st), v[6])
+
+
+def cut(v, a, b):
+    return v[:2] + (v[2] + a * v[4], v[2] + (b - 1) * v[4] + 1) + v[4:]
 
 
 def plan(r, own):
@@ -96,8 +101,6 @@ def plan(r, own):
     def mov(o, i, bias=None, scale=None):
         kw = {k: x for k, x in (("bias", bias), ("scale", scale)) if x is not None}
         alt = ("activation", (o, i, F.Identity if bias is not None else F.Copy), kw)
-        if BUF[o[1]][1] == U16 and not PAR["s16"]:
-            alt = None
         if not kw:
             op("v", ("tensor_copy", (o, i), {}), alt=alt)
         elif len(kw) == 2:
@@ -108,16 +111,8 @@ def plan(r, own):
     def iota(o, pat, base, cm):
         op("gp", ("iota", (o, pat, base, cm), {} if BUF[o[1]][1] == I32 else {"allow_small_or_imprecise_dtypes": True}))
 
-    def pe(ins, k):
-        for a in range(0, len(ins), k if PAR["cut"] else len(ins)):
-            op("t", *ins[a:a + (k if PAR["cut"] else len(ins))])
-
     def mm(groups, first=True, last=True):
-        ins = []
-        for gr in groups:
-            for k, (o, l, x) in enumerate(gr):
-                ins.append(("matmul", (o, l, x, first and k == 0, last and k == len(gr) - 1), {}))
-        pe(ins, PAR["cut"] if nel(ins[-1][1][2]) < 256 else 1)
+        op("t", *[("matmul", (o, l, x, first and k == 0, last and k == len(gr) - 1), {}) for gr in groups for k, (o, l, x) in enumerate(gr)])
 
     def dma(items, split=False, paced=False):
         after = big[-PAR["pace"]:][:1] if paced and len(big) >= PAR["pace"] else []
@@ -127,18 +122,18 @@ def plan(r, own):
         if paced:
             big.append(len(ops) - 1)
 
-    def send(name, pairs, one):
-        ops.append((("gp",), "r", (name, pairs, one), sorted(set(x[1] for x in pairs)), []))
+    def send(name, pairs):
+        ops.append((("gp",), "r", (name, pairs), sorted(set(x[1] for x in pairs)), []))
 
     def recv(name, y, view):
         ops.append((("rx",), "x", (name, y), [], [view]))
 
     def scatter_sums(s, t, w):
-        send("rs%d" % (4 * t + s), [(y, V("sP%d_%d" % (t, s), w * x, w * x + w), V("rP%d_%d" % (t, s // 2), w * r, w * r + w)) for x, y in enumerate(own[s % 2]) if y != r], False)
+        send("rs%d" % (4 * t + s), [(y, V("sP%d_%d" % (t, s), w * x, w * x + w), V("rP%d_%d" % (t, s // 2), w * r, w * r + w)) for x, y in enumerate(own[s % 2]) if y != r])
 
     def spread(name, n, w):
         a = V(n, w * xr, w * xr + w)
-        send(name, [(y, a, a) for y in others], True)
+        send(name, [(y, a, a) for y in others])
 
     col = lambda n, j: V(n, j, j + 1)
     blk = lambda n, a: V(n, 128 * a, 128 * a + 128)
@@ -176,15 +171,15 @@ def plan(r, own):
         sel(V("Bq", 24 + 128 * k, 152 + 128 * k), [[-1, 4], [1000, 4], [-8, 8]], -64 * x - 4 * par)
     Bq = lambda k, sh: V("Bq", 24 + 128 * k - sh, 152 + 128 * k - sh)
     iota(V("X"), [[1, 32]], 0, 0)
-    for j, (sh, an) in enumerate([(0, 15), (4, 7), (5, 3), (1, 7), (0, 1)]):
+    for j, (sh, an) in enumerate([(0, 15), (4, 7), (5, 3), (1, 7), (0, 1), (4, 1)]):
         ts(col("pi", j + 1), col("pi", 0), sh, an, SHR, AND)
-    cp(V("pf", 0, 6), V("pi", 0, 6))
+    cp(V("pf", 0, 7), V("pi", 0, 7))
     pf = lambda j: col("pf", j)
     lin = lambda o, a, c, b: ts(pf(o), pf(a), float(c), float(b), MUL, ADD)
     lin(7, 3, -1024, 2048 + C0); lin(8, 5, -31, 32); lin(9, 1, 2, 0); lin(10, 1, 2, 1); lin(11, 2, 16, 0)
     zc = pf(7)
     sel(V("idh"), [[-1, 128]], 0)
-    for n, c in (("idb", 1), ("nidb", -1), ("nidh", -1), ("i7", 7), ("ia", -4064), ("ib", -4080)):
+    for n, c in (("idb", 1), ("nidb", -1), ("nidh", -1), ("i7", 7), ("ia", -4064), ("ib", -4080), ("ic", -52736), ("id", -51200), ("ie", 1 / 32.0)):
         op("v", ("tensor_scalar", (V(n), V("idh"), float(c), None, MUL), {}), alt=("affine_select", (V(n), V("zb", 0, 128), [[-1, 128]], A.not_equal, float(c), 0, 1), {}), on="gp")
         ops[-1] = ops[-1][:3] + ([V("idh"), V("zb", 0, 128)], ops[-1][4])
     iota(V("Y", 0, 8), [[1, 2], [2, 4]], 0, 0)
@@ -194,6 +189,8 @@ def plan(r, own):
     iota(V("Y", 12, 28), [[1, 2], [100, 2], [2, 4]], 0, 0)
     ts(V("pm", 16, 36), V("Y", 8, 28), pf(2), None, EQ)
     ts(V("pm", 36, 56), V("Y", 8, 28), pf(2), -1.0, EQ, MUL)
+    tt(V("pm", 56, 72), V("pm", 20, 36), V("pm", 36, 52), ADD)
+    sel(V("W0"), [[0, 128]], -127)
     sel(V("LT"), [[1, 128]], 0, A.is_gt, -1)
     sel(V("GE"), [[-1, 128]], 0, A.is_ge)
     ts(V("blkn"), V("X", 0, 8), pf(2), -1.0, EQ, MUL)
@@ -204,72 +201,77 @@ def plan(r, own):
         ts(V("CR", 12 * e, 12 * e + 4), V("X", 4 * e, 4 * e + 4), pf(4), pf(8), EQ, MUL)
         ts(V("CR", 12 * e + 4, 12 * e + 12), V("X", 8 * e, 8 * e + 8), pf(1), None, EQ)
         ms(blk("cT", e), 16384.0 * e - 8192.0)
-    for a in range(0, 8, 2):
-        op("gp", ("affine_select", (V("Rh", 128 * a, 128 * a + 256), V("zb", 0, 256), [[-16, 2], [0, 8], [-1, 16]], A.not_equal, 1.0, -16 * a, 1), {}))
-    ms(V("RS"), 0.0)
-    for v in range(2):
-        sel(V("RS", 144 * v + 16, 144 * v + 144), [[-32, 4], [1000, 2], [-1, 16]], -16 * v)
-    for lo, n, base in ((304, 3, -32), (400, 1, 0), (448, 1, -112), (480, 3, -16)):
+
+    def pick(o, i, c, pat, base):
+        one = V("one" if BUF[o[1]][1] == HF else "oneb", 0, 128)
+        op("v", ("tensor_scalar", (o, i, c, None, MUL), {}), alt=("affine_select", (o, one, pat, EQ, 0.0, base, 1), {}), on="gp")
+        ops[-1] = ops[-1][:3] + (ops[-1][3] + [one], ops[-1][4])
+
+    iota(V("R1", 0, 128), [[0, 8], [1, 16]], 0, 0)
+    ts(V("R1", 128, 256), V("R1", 0, 128), pf(1), -1.0, EQ, MUL)
+    for a in range(8):
+        pick(blk("Rh", a), blk("R1", 1), col("blkn", a), [[0, 8], [-1, 16]], -16 * a)
+    ms(V("RS"), 0.0); ms(V("Zh"), 0.0); ms(V("Zf", 0, 16), 0.0)
+    lin(12, 6, -1, 1); ts(pf(13), pf(1), 0.0, None, EQ); ts(pf(14), pf(1), 8.0, None, EQ)
+    pick(V("RS", 112, 240), V("idh"), pf(12), [[-32, 4], [1000, 2], [-1, 16]], 0); pick(V("RS", 272, 400), V("idh"), pf(6), [[-32, 4], [-1016, 2], [-1, 16]], 1000)
+    for lo, n, base in ((432, 3, -32), (528, 1, 0)):
         sel(V("RS", lo, lo + 32 * n), [[-32, n], [1000, 2], [-1, 16]], base)
-    RS = lambda v, x: V("RS", 144 * v + 16 - 16 * x, 144 * v + 144 - 16 * x)
-    sel(V("Zh"), [[-16, 9], [1000, 16]], 16); sel(V("Zl"), [[-16, 9], [1000, 16]], 8)
-    op("gp", ("affine_select", (V("Zf"), V("Zh"), [[-16, 9], [1000, 16]], A.not_equal, 1.0, 8, 1), {}))
+    RS = lambda v, sh: V("RS", 112 + 160 * v - sh, 240 + 160 * v - sh)
+    pick(V("Zh", 16, 144), V("idh"), pf(13), [[-16, 8], [1000, 16]], 0); pick(V("Zh", 152, 280), V("idh"), pf(14), [[-16, 8], [-1008, 2], [1000, 8]], 1000)
+    tt(V("Zf", 16, 144), V("Zh", 16, 144), V("Zh", 160, 288), ADD)
     sel(V("Bc"), [[-16, 8], [0, 16]], -8)
-    iota(V("kc", 0, 32), [[0, 2], [128, 16]], -2047, 1); iota(V("kc", 32, 48), [[128, 16]], -2048, 1)
+    iota(V("kc", 0, 48), [[1, 3], [128, 16]], -2049, 1); iota(V("kc", 48, 64), [[128, 16]], -2047, 1)
+    for c, b, f in ((0, 0, 2047.0), (63, -127, -4096.0)):
+        op("gp", ("affine_select", (col("kc", c), col("kc", c), [[0, 1]], A.not_equal, f, b, 1), {}))
+    Kc = lambda k: V("kc", 16 * k, 16 * k + 16)
     iota(V("vI", 0, 32), [[0, 2], [8, 2], [16, 8]], 0, 0); iota(V("vI", 32, 64), [[-1, 2], [0, 16]], 1, 0); iota(V("vI", 64, 96), [[0, 2], [1, 16]], 0, 0)
     ms(V("TI"), 0.0)
     mov(V("TI", 16, 528, 16), V("vI", 0, 32), pf(2)); mov(V("TI", 17, 528, 16), V("vI", 32, 64), pf(9))
     ts(V("qh", 0, 256), V("qi"), -2048.0, None, ADD)
-    ts(V("qh", 512, 768), V("qh", 0, 256), 1.0, None, ADD)
-    ts(V("qh", 768, 1024), V("qh", 0, 256), 2047.0, -4096.0, EQ, MUL)
-    tt(V("qh", 256, 512), V("qh", 512, 768), V("qh", 768, 1024), ADD)
+    ts(V("qh", 256, 512), V("qh", 0, 256), 2047.0, -4096.0, EQ, MUL)
+    lin(15, 7, 1, 1)
+    for d in range(2):
+        o = V("p%d" % (4 + d), 0, 128)
+        mm([[(o, Bq(x, 16 * x + 8 * k), V("qh", 256 * e + k, 256 * e + 256, 2)) for e in range(d + 1) for x in range(2) for k in range(2)]])
+        mov(V("L0", 128 * d, 128 * d + 128), o, pf(15) if d else zc)
 
     def stream(s):
         W = lambda n, *a: V("%s_%d" % (n, s), *a)
         P = lambda *a: V("p6", *a); Q = lambda *a: V("p%d" % (4 + s % 2), *a)
         ZW = W("zt"); ow = own[s % 2]
-        odd = lambda n, j: W(n, 256 * j + 1, 256 * j + 256, 2)
-        sub = lambda v, j: v[:2] + (v[2] + 128 * j * v[4], v[2] + (128 * j + 127) * v[4] + 1) + v[4:]
 
-        def term(o, a, x, on_s, P=Q):
+        def least(o, a, e, on_s, P=Q):
             if on_s:
-                mm([[(P(), V("idb"), a), (P(), V("nidb"), x)]])
+                mm([[(P(), V("idb"), e), (P(), V("nidb"), a)]])
                 op("s", ("activation", (o, P(), F.Relu), {}))
             else:
-                tt(o, a, x, MAX)
+                tt(o, a, e, MIN)
+            return o, 8 * on_s
 
-        def between(f, g, a, b, n=1):
-            for c in range(0, 1024, 1024 // n):
-                e = c + 1024 // n
-                scan(W(f, c, e), a(c, e), b(c, e), MAX, MIN); scan(W(g, c, e), a(c, e), b(c, e), MIN, MAX)
+        def walk(o, a, b, k=1):
+            n = nel(o) // k
+            for c in range(0, nel(o), n):
+                scan(cut(o, c, c + n), cut(a, c, c + n), cut(b, c, c + n), MAX, MIN)
 
-        seq = lambda o, n="S": lambda c, e: W(n, o + c, o + e)
-        red2 = lambda g, f, o, js=range(4): [(Q(j, 64, 4), odd(v, j), V("pm", o + c, o + c + 16)) for j in js for v, c in ((g, 16), (f, 36))]
+        def sums(t, items, n):
+            red = lambda it: [(Q(j, n, 4), cut(v, 128 * j, 128 * j + 128), V("pm", c, c + n // 4)) for j in range(4) for v, c in it]
+            for k, it in enumerate(items):
+                mm([[(Q(0, n), V("idb"), V("zb", 0, n))] * (k == 0) + red(it)], k == 0, k == len(items) - 1)
+            mov(W("sP%d" % t), Q(0, n))
+            scatter_sums(s, t, n // 2)
 
         def start():
             if s:
                 mov(W("zt", C0 - 1, C0, 1, (0, 32, 1)), W("zt", 7167, 7168, 1, (0, 32, 1)))
-            mm([[(P(32 * d, 32 * d + 32), Bq(x, 16 * x + 8 * k), V("qh", 256 * d + 64 * s + k, 256 * d + 64 * s + 64, 2)) for x in range(2) for k in range(2)] for d in range(2)])
-            mov(W("L", 0, 64), P(0, 64), zc)
 
         def coords0():
-            S = PAR["m"][ty][s]
-            between("f", "g", seq(C0, "zt"), seq(C0 - 1, "zt"))
+            S = PAR["m"][ty][s]; ne = ("D" in S) + ("F" in S)
+            walk(W("f", 0, 1024), W("zt", C0 - 1, C0 + 1023), W("zt", C0, C0 + 1024))
+            walk(W("r"), W("zt", C0 - 1, C0 + 1022, 2), W("zt", C0 + 1, C0 + 1024, 2))
             e, x0, x1 = W("zt", C0, C0 + 1023, 2), W("yt", 0, 512), W("yt", 512, 1024)
-            D, Ft, G = W("f2", 0, 512), W("f2", 512, 1024), W("g2", 0, 512)
-            pm = lambda sg: V("pm", 8 * (sg < 0), 8 * (sg < 0) + 8)
-            red = lambda items: [(Q(j, 32, 4), sub(v, j) if v[0] == "V" else odd(v, j), pm(sg)) for j in range(4) for v, sg in items]
-            mov(x0, IND(ZW, W("L", 0, 32))); term(D, x0, e, "D" in S, P if "p" in S else Q)
-            if "x" in S:
-                tt(Ft, IND(ZW, W("L", 32, 64)), e, MAX); tt(G, IND(ZW, W("L", 32, 64)), x0, MAX)
-            else:
-                mov(x1, IND(ZW, W("L", 32, 64))); term(Ft, x1, e, "F" in S); term(G, x1, x0, "G" in S)
-            ne = 1 - ("D" in S) - ("F" in S)
-            items = [(D, -1), (Ft, -1), (G, 1)] + [(e, ne)] * abs(ne) + [(x0, 1)] * ("G" in S)
-            mm([[(Q(0, 32), V("idb"), V("zb", 0, 32))] + red([("g", 1), ("f", -1)])], True, False)
-            mm([red(items)], False, True)
-            mov(W("sP0"), Q(0, 32))
-            scatter_sums(s, 0, 16)
+            mov(x0, IND(ZW, V("L0", 32 * s, 32 * s + 32))); d = least(W("p"), x0, e, "D" in S, P if "p" in S else Q)
+            mov(x1, IND(ZW, V("L0", 128 + 32 * s, 160 + 32 * s))); f = least(W("h", 0, 512), x1, e, "F" in S); tt(W("h", 512, 1024), x1, x0, MIN)
+            sums(0, [[(W("f", 0, 1024, 2), 8), (W("f", 1, 1024, 2), 8), (W("r"), 0)] + [(e, 0)] * ne, [d, f, (W("h", 512, 1024), 8)]], 32)
 
         def lists(t, w, n, rng, P=P):
             E = "rE%d_%d" % (t, s)
@@ -277,37 +279,23 @@ def plan(r, own):
             for k, x in enumerate(xs):
                 if ow[x] != r:
                     recv("ag%d" % (4 * t + s), ow[x], V(E, w * x, w * x + w))
-                sh = [(o, RS(v, x), V(E, w * x + lo, w * x + hi)) for v, lo, hi, o in rng]
+                sh = [(o, RS(v, 16 * (x - v % 2)), V(E, w * x + lo, w * x + hi)) for v, lo, hi, o in rng]
                 if k == 0 and ow[x] != r:
                     mm([[(P(0, n), V("idb"), V("zb", 0, n))]], last=False)
                 mm([[(P(0, n), V("idb"), V("zb", 0, n))] * (ow[x] == r) + sh], ow[x] == r, k == 1)
 
         def coords(t):
-            es = 1 - t % 2; h16 = lambda c, n, st: P(c, c + 16, 1, (0, 128, 1), (n, st))
-            if es:
-                lists(t - 1, 48, 128, [x for h in range(2) for x in ((h, 0, 32, h16(16 + 16 * h, 2, 64)), (h, 32, 48, h16(48 + 16 * h, 1, 0)))] + [(2, 16, 17, P(112, 113)), (3, 15, 16, P(15, 16))])
-            else:
-                lists(t - 1, 48, 112, [x for h in range(2) for x in ((h, 16, 48, h16(16 * h, 2, 32)), (h, 0, 16, h16(64 + 16 * h, 1, 0)))] + [(2, 0, 1, P(96, 97))])
-            mov(W("L", 0, 112 + 16 * es), P(0, 112 + 16 * es), zc)
-            LO, LX, LE = ((14, 48), (48, 80), (80, 113)) if es else ((64, 97), (32, 64), (0, 32))
-            o0, i0 = 62 * es, 64 * es; n = 1 + (4 * t + s in PAR["half"])
-
-            def take(c, l, cut, o="S"):
-                for a, b in ((l[0], l[0] + cut), (l[0] + cut, l[1])) if n > 1 else (l,):
-                    mov(W(o, c + 32 * (a - l[0]), c + 32 * (b - l[0]) - 1, 2), IND(ZW, W("L", a, b)))
-
-            take(0, LO, 18); take(o0 + 1, LE, 16 + 2 * es)
-            between("f", "g", seq(o0 + 1), seq(o0), n)
-            take(1, LX, 16, "yt")
-            for c in range(0, 1024, 1024 // n):
-                o, i = W("yt", c, c + 1024 // n - 1, 2), W("S", i0 + c, i0 + c + 1024 // n - 1, 2)
-                op("v", ("tensor_copy", (o, i), {}), alt=("affine_select", (o, i, [[0, 512 // n]], A.is_ge, 0.0, 0, 0), {}), on="gp")
-            between("f2", "g2", seq(i0), seq(0, "yt"), n)
-            mm([[(Q(0, 64), V("idb"), V("zb", 0, 64))] + red2("g", "f", 0)], True, False)
-            for c in range(n):
-                mm([red2("g2", "f2", 4, range(4 // n * c, 4 // n * (c + 1)))], False, c == n - 1)
-            mov(W("sP%d" % t), Q(0, 64))
-            scatter_sums(s, t, 32)
+            h16 = lambda c, n, st: P(c, c + 16, 1, (0, 128, 1), (n, st))
+            lists(t - 1, 48, 128, [(h, 0, 48, h16(16 * h, 3, 48)) for h in range(2)] + [(2, 0, 1, P(32, 33))])
+            mov(W("L"), P(0, 128), zc)
+            for o, lo, n in ((0, 0, 528), (2, 48, 512), (1, 96, 512)):
+                mov(cut(W("S", o, 1584, 3), 0, n), IND(ZW, W("L", lo, lo + n // 16)))
+                if o == 0:
+                    walk(W("r"), W("S", 0, 1534, 3), W("S", 3, 1537, 3))
+                if o == 2:
+                    tt(W("p"), W("S", 0, 1534, 3), W("S", 2, 1536, 3), MIN)
+            walk(W("f"), W("S", 0, 1536), W("S", 1, 1537), PAR["sw"])
+            sums(t, [[(W("r"), 16), (W("p"), 56)], [(W("f", 0, 1536, 3), 40), (W("f", 1, 1536, 3), 40), (W("f", 2, 1536, 3), 36)]], 64)
 
         def final():
             lists(2, 32, 64, [(v, 0, 32, Q(32 * v, 32 * v + 32)) for v in range(2)], Q)
@@ -363,59 +351,63 @@ def plan(r, own):
             mov(W("uP", 80, 96), P(1, 16, 32), 51200.0)
             mov(row("TP", 12), W("m32"), -1536.0, 1 / 32.0)
             mov(W("uP", 64, 80), W("m32", 16, 32), -1536.0, 1 / 32.0)
-            mov(W("maskE"), IND(V("Mp", 32, 64), W("uP", 80, 96)))
+            mov(W("mask", 0, 256), IND(V("Mp", 32, 64), W("uP", 80, 96)))
             mm([[(P(0, j, 64, 32), V("W1", 256 * (j % 16) + 1 - j // 16, 256 * (j % 16) + 256, 2), V("CR", 4 + 2 * b, 6 + 2 * b))] for j in range(32)])
             mov(W("uP", 0, 48), P(0, 0, 48))
-            mov(W("maskO"), IND(V("Mp", 0, 32), W("uP", 32, 48)))
+            mov(W("mask", 256, 512), IND(V("Mp", 0, 32), W("uP", 32, 48)))
             for k in range(2):
                 mov(row("TP", 10 + k), P(0, 32 * k, 32 * k + 32))
             mov(row("TP", 8), V("vI", 64, 96), pf(11)); mov(row("TP", 9), V("vI", 32, 64), pf(9))
             turn([blk(N("TP"), k) for k in range(4)], False)
 
         def index(t):
-            p = t % 2; w = 32 if t else 16; n = 8 * w; last = t == 2
+            w = 32 if t else 16; n = 8 * w; last = t == 2
             uT, uG = [W("uP", c, c + 16) for c in ((64, 0), (48, 0), (16, 32))[t]]
             part = lambda y: V("sP%d_%d" % (t, s), w * xr, w * xr + w) if y == r else W("rP%d" % t, w * y, w * y + w)
             L = P(1, 32 - w, 32); red = lambda o, x, k, m: [(P(1, o + R, o + 16, 2), blk(N(x), k + R), V(m)) for R in range(2)]
             mm([[(P(0, 0, n), V("idh"), V("cT", 256 - n, 256))] + rep(0, part(r))], last=False)
-            mm([[(P(1, 0, 32), V("nidh"), V("cT", 112, 144)), (P(1, 0, 16), V("idh"), V("one", 0, 16)), (L, V("idh"), part(r))] + (red(16, "maskE", 0, "pen") if t == 0 else [])], last=False)
+            mm([[(P(1, 0, 32), V("nidh"), V("cT", 112, 144)), (P(1, 0, 16), V("idh"), V("one", 0, 16)), (L, V("idh"), part(r))] + (red(16, "mask", 0, "pen") if t == 0 else [])], last=False)
             far = sorted(others, key=lambda y: y in own[ty])
             for y in far:
                 recv("rs%d" % (4 * t + s), y, part(y))
                 mm([rep(0, part(y))], False, y == far[2])
             mov(W("wI", 256 - n, 256), P(0, 0, n))
             mm([[(L, V("idh"), part(y)) for y in others]], False, False)
-            PA = P(0, 256, 288); A1, A2 = P(0, 256, 272), P(0, 272, 288)
-            mm([[(PA, V("idh"), V("kc", 16 - 16 * p, 48 - 16 * p))]], last=False)
+            PA = P(0, 256, 288); A1, A2, AO = P(0, 256, 272), P(0, 272, 288), P(0, 288, 304)
+            k1, k2, kO = ((2, 1, 1), (1, 1, 0), (2, 3, 1))[t]; pO = 0 if t else 1
+            mm([[(P(0, 256, 304), V("idb"), V("zb", 0, 48)), (A1, V("idh"), Kc(k1)), (A2, V("idh"), Kc(k2)), (AO, V("idh"), Kc(kO))]], last=False)
             if t:
-                tt(W("gI", 256, 512), IND(W("wI", 0, 128), uT), W("maskE"), MUL)
+                tt(W("gI", 256, 512), IND(W("wI", 0, 128), uT), W("mask", 0, 256), MUL)
                 mm([red(16, "gI", 2, "blkn")], False, False)
-            tt(W("gI", 0, 256), IND(W("wI", 128, 256), uG), W("maskO"), MUL)
+            tt(W("gI", 0, 256), IND(W("wI", 128, 256), uG), W("mask", 256, 512), MUL)
             mm([red(0, "gI", 0, "blkn")], False)
             ts(W("fl"), P(1, 0, 32), 0.5, None, A.is_lt)
             guest, stays = W("fl", 0, 16), W("fl", 16, 32)
             c1, cb = W("cum", 8, 24), W("cum", 7, 23)
-            mm([[(A2, V("idh"), guest) if p else (A1, V("idh"), stays)]], False, False)
+            mm([[(A2, V("idb"), guest)] if t else [(A1, V("idb"), stays), (AO, V("idb"), stays)]], False, False)
             scan(c1, guest, stays, ADD, ADD)
-            pre = lambda o: [(o, V("LT"), c1), (o, V("GE"), cb)]
-            mm([pre(A1) + pre(A2)], False)
+            if last:
+                ts(W("wb"), V("zb", 0, 16), col(N("fl"), 31), None, ADD)
+            pre = lambda o: [(o, V("LT"), c1), (o, V("GE"), cb)] + [(o, V("W0"), W("wb"))] * last
+            nO = lambda o: [(o, V("idh"), Kc(kO))] + pre(o) + [(o, V("idb"), stays)] * pO
+            mm([pre(A1) + pre(A2) + pre(AO)], False)
             tt(W("tn"), PA, W("fl"), MUL)
             mm([[x] for x in rep(1, W("tn", 0, 16))])
             mov(W("wN"), P(1, 0, 128))
             wn = "W%d" % min(3, 1 + t + b); WW = V(wn)
-            mO, mE = W("m32", 1 - p, 32, 2), W("m32", p, 32, 2)
-            address(W("uO"), A1, 2047, mO, W("gm", 0, 16), last, A1, [(A1, V("idh"), V("kc", 0, 16))] + pre(A1) + [(A1, V("idh"), stays)] * (1 - p))
+            mO, mE = W("m32", pO, 32, 2), W("m32", 1 - pO, 32, 2)
+            address(W("uO"), AO, 2048, mO, W("gm", 0, 16), last, AO, nO(AO))
             cp(IND(WW, W("uO")), W("rows", 0, 256))
-            tt(W("gP"), IND(W("wN"), uT), W("maskE"), MUL)
+            tt(W("gP"), IND(W("wN"), uT), W("mask", 0, 256), MUL)
             nE = lambda o, st, k=0: [(P(k, o, o + 16 * st, st), V("idh"), W("tn", 16, 32))] + [(P(k, o + R * st, o + 16 * st, 2 * st), blk(N("gP"), R), V("blkh")) for R in range(2)]
             mm([nE(0, 1)[:1]], last=False)
             mm([nE(0, 1)[1:]], False)
             mm([nE(0, 1, 1)], last=False)
             address(W("uE"), P(0, 0, 16), 2048, mE, W("gm", 16, 32), last, P(1, 0, 16), [])
             cp(IND(WW, W("uE")), W("rows", 256, 512))
-            E = "rE%d_%d" % (t, s); name = "ag%d" % (4 * t + s); pn = 1 - p
+            E = "rE%d_%d" % (t, s); name = "ag%d" % (4 * t + s)
             c0, nq = ((12, 8), (12 * b, 6), (2 * b, 2))[t]
-            mm([[(P(1, j, 32 * nq, 32), blk(wn, j) if last else V(wn, 256 * (j % 16) + (pn if j // 16 else p), 256 * (j % 16) + 256, 2), V("CR", c0, c0 + nq))] for j in range(32)])
+            mm([[(P(1, j, 32 * nq, 32), blk(wn, j) if last else V(wn, 256 * (j % 16) + j // 16, 256 * (j % 16) + 256, 2), V("CR", c0, c0 + nq))] for j in range(32)])
             we = 32 if last else 48
             mov(V(E, we * xr, we * xr + we), P(1, 0, we), -2048.0)
             spread(name, E, we)
@@ -424,18 +416,17 @@ def plan(r, own):
             tile, r0 = ("TQ", 4 * b) if t else ("TP", 8 * b)
             for k in range((4, 2, 0)[t]):
                 mov(row(tile, r0 + k), P(1, 128 + 32 * k, 160 + 32 * k))
-            PO = P(0, 64 + 1 - p, 96, 2)
-            mm([[(P(0, 64, 96), V("nidh"), W("m32"))] + nE(64 + p, 2) + pre(PO) + [(PO, V("idh"), V("kc", 32, 48))] + [(PO, V("idh"), stays)] * (1 - p)])
-            mov(W("nt", 32, 64), P(0, 64, 96), 26624.0 if last else 51200.0)
-            mov(W("nt", 0, 32), W("m32"), -24576.0) if last else mov(W("nt", 0, 32), W("m32"), -1536.0, 1 / 32.0)
-            pe([("transpose", (PT(128 * par, 128 * par + 128, 1, (32 * k, 32, 1)), W("nt", par, 64, 2), V("idb")), {}) for k in range(4) for par in range(2)], 4)
+            mm([[(P(0, 64, 96), V("nidh"), W("m32"))] + nE(65 - pO, 2) + nO(P(0, 64 + pO, 96, 2))
+                + [(P(0, 32, 64), V("idh" if last else "ie"), W("m32")), (P(0, 32, 64), V("id" if last else "ic"), V("one", 0, 32))]])
+            mov(W("nt"), P(0, 32, 96), 26624.0 if last else 51200.0)
+            op("t", *[("transpose", (PT(128 * par, 128 * par + 128, 1, (32 * k, 32, 1)), W("nt", par, 64, 2), V("idb")), {}) for k in range(4) for par in range(2)])
             for par in range(2):
                 mov(W("wS", par, 256, 2), PT(128 * par, 128 * par + 128))
             dma([(on(V("W1"), 64 * k, 8, 8), W("wS")) for k in range(2)], 2)
             for a in range(0, nl, 16 if last else 32):
                 e = min(a + (16 if last else 32), nl)
                 mov(W("gQ", 16 * a, 16 * e), IND(V("W1"), W("uN", a, e)))
-            Z = lambda z, i: V(z, 16 - i, 144 - i)
+            Z = lambda z, i: V("Zh", 160 - i, 288 - i) if z == "Zl" else V(z, 16 - i, 144 - i)
             if last:
                 for h in range(2):
                     mm([[(P(0, 0, 32), Z("Zf", i), W("gQ", 32 * i, 32 * i + 32)) for i in range(8 * h, 8 * h + 8)]], h == 0, h == 1)
@@ -445,9 +436,9 @@ def plan(r, own):
             mm([[(P(0, 0, nl), Z("Zh", i), W("gQ", i, 16 * nl, 16)) for i in range(16)]])
             mov(W("uP", 0, nl), P(0, 0, nl))
             cT, cG = (48, 0) if t == 0 else (16, 32)
-            mm([[(P(1, 256 * k, 256 * k + 256), V("Bc"), W("gQ", 16 * c, 16 * c + 256))] for k, c in enumerate((cT, cG))])
-            ts(W("maskE"), P(1, 0, 256), pf(9 + p), None, EQ)
-            ts(W("maskO"), P(1, 256, 512), pf(9 + pn), None, EQ)
+            mm([[(P(1, 256 * k, 256 * k + 256), V("Bc"), W("gQ", 16 * c, 16 * c + 256)) for k, c in enumerate((cT, cG))]
+                + [(P(1, c, c + 128), V("nidh"), V("one", 0, 128)) for c in (256, 384)]])
+            ts(W("mask"), P(1), pf(9), None, EQ)
             nr = 64 - 32 * t; dst = ((6, 4), (2,))[t]
             for k, d in enumerate(dst):
                 mov(row(tile, r0 + d), P(0, 32 * k, 32 * k + 32))
@@ -506,7 +497,7 @@ def depend(ops, eng):
     return deps
 
 
-def ordered(r, own):
+def ordered(r, own=((0, 3), (1, 2))):
     al = "0123456789abcdefghijklmnopqrstuvwxyzABCDEFGHIJKLMNOPQRSTUVWXYZ"; ops = plan(r, own); n = len(ops)
     o = ORDER[0 if r in own[0] else 1]; order = list(range(n)); eng = [x[0][0] for x in ops]
     for k in range(len(o) // 2):
@@ -542,7 +533,7 @@ def index_of(x):
     _, n, lo, hi, st, (pa, pn, ps), (k, ks) = x
     p = slice(pa, pa + (pn - 1) * ps + 1, ps); hi = lo + (len(range(lo, hi, st)) - 1) * st + 1
     if n not in ROW:
-        b, o = AL.get(n, (n, 0))
+        b, o = AL[n]
         return b, (p, slice(o + lo, o + hi, st))
     w = ROW[n]; a, c = divmod(lo, w)
     if k > 1:
@@ -593,7 +584,7 @@ def rank_program(g, core, T, topo):
             ops, order, _ = ordered(r, own); n = 0; loc = 0
             for j in order:
                 if ops[j][1] == "r" and ops[j][2][0] in PAR["help"]:
-                    name, pairs, _ = ops[j][2]
+                    name, pairs = ops[j][2]
                     g.wait_ge(S["hi%d" % n], len(to_helper(r)))
                     loc += spread(V("hX_%d" % n, 0, nel(pairs[0][1])), pairs, S[sem_of(name, r)], S.loc); n += 1
             g.wait_ge(S.loc, loc)
@@ -648,13 +639,13 @@ def rank_program(g, core, T, topo):
             for o, i in pay[0]:
                 q.dma_start(ap(o), ap(i)).then_inc(S[sig[j][0]], 16)
         else:
-            name, pairs, one = pay; sem = S[sem_of(name, r)]
+            name, pairs = pay; sem = S[sem_of(name, r)]
             if name in PAR["help"]:
                 rid, pid, _ = topo.addr(helper_of(T, topo, core)); h = to_helper(r)
                 g.remote_dma(ap(V("hX_%d" % nh, 0, nel(pairs[0][1]))), ap(pairs[0][1]), S["hi%d" % nh], S.loc, pid, rid, mask_of(h))
                 nh += 1; loc += len(h)
                 continue
-            if one:
+            if name[:2] != "rs":
                 loc += spread(pairs[0][1], pairs, sem, S.loc)
             else:
                 h = common(T, topo, core, rest(r)); k = len(h) // len(pairs); loc += len(h)

from concourse.mybir import AluOpType as A, ActivationFunctionType as F
from concourse.bass import DstId, RemoteDMATransfer

PAR = {"m": ("- Dp - Dp".split(),) * 2, "help": ("ag8", "yq0", "yq2", "ag9", "yq1", "ag1"), "pace": 4,
       "seq": ("Vx123ybc", "V1x23ybc"), "gate": 1, "sw": 1}
ORDER = (
    "0201000x040306cH0c0I0bch1109050d0R0F0C0G1S0e0A0B0Kcg0J0S0H0D1V0L1W1P230O0P1Q0M2S2te20E0g0fe3d4eE0a29d5ee1YeF0N1j1M24ef0Q131Le81X272a1n20gc0h141lehd31e2Tep0i1heydv2Z1f1cea2b0kd22uf30j2x1R2d1a0l0o2yen1o2cdAeof51OdC0n0mgidD2V2jdz452XgfdF2YdBet4430evgp47ew4aexfa4h2q48324cdE2rdy4bgu2z2A4d4i35372Dgn2BhB334f0s390p0q0rdGer4oeu364mgs38dr3a2C1G34fk3cdHhH3d4k2Jebd73ehE1b4n3feT3g4p5ueVeW3i5t3h3jeq5wgz1deP3k4r0t0u0v5zd9fw3lfx4s1Ffv5A3p1N5Bfz3s15db5x4u4wdN3r4y3t3u4vcIfF4xfG3v19eN3y4zeX1k1K3zeO3J2P3AgJ5CeR2QeU4C4t5D1C4B5E3Kf0dI3B1g4DdR1B2H4E3C163DfNdQ3L4F2sfO4H17fP1A18dM4GfV4I4JfW4M4K4N3H3I3P4O3O4L4RgY4S4Q4T5F5Gh44Uh54X5Hh758hR4ZfZhS5L506R6Ug05N6S6T6Vj5513S5K520whi5Mj83U3T7753715Pg5g6j63Y5O7879jj3Z5Q406Yhd7041jk8k5R425S72jm5a735b5cjo747c8j8m5d5e7e8l5Z5Tje3V8nkx765V5Xd85W7gkA5Yd6607h61hp7i5f5U6362ky645h6665kC5i675l5m8q5n68js6a8s69hx6b7khy6c8v8uioip6dhe7lhf6e6k6h8wir7rhg6j6l6nkG6m5qix8y7n7p5jiyhA6q6z6r6s7oiJ7q7s6BjC5k6tiL7wiM7yiO6E7m1JiD7u7xiF6v7z7v7AiP7C7B6x7D6y8z7E7H7F7IiQ7J7G7K7M7N7L8A7O7PjZ8B6Ik0kL7SkM9G817T6J7U9F9I9H9JiVkO6N8E9K7V8HkblW6O7W6P8G7XlU6Q8I83lY8J9M9Vk7848K9Oke9WkU869X9Q879Rm78M6Kma9Z9S8Nm26Lmc9U8T8P8Ra28O8Qki8S888Ub9bcbal4bbbda08ann8Yk88Wno8X90a58Za491nq92a68b94958ens809396bi8f97a7ljbga898lkbk8clikp9cbl9flmbm9eajalan9gnw9h8hlsbo9iahltkr8d9l9saklvlCam9naoaimy9uasaqlE9olFau9y9xatlyav9r9qarawazaxaylIaAaBaEaCaFaGaD9BaJmQlJaKaIaLaMmW9CmXaPaWmZlMaXaR9EaYaaa9n8abbqn9bpbsacaSaemmb1b2braTbtaVaUafnDagb3ndbvb5b6bzbInJb7nFb8bDbEbJbKbVnKbLbybCnVbNbUbXbWbYnGbZbPbFo9c1bHbGbOocobc4c5c6c8bQc7bRbTo1",
    "0003041Q020106050x0c110y1Pci0K0I0B0F0H0J0G1S0R0a0d0Dcg0LcJ2S0E0C0e0b0f0S0O1T0Xd5ch141U1V29d40M231f1W0h1c1n2t1B0N1Aee0i1Y1Xd20Pef2T24e82adH2720eE1h130g0j1lf31k1Cd3282u1o2b2ZeBeady0l2deFdbf51R2x2VdD0k0m2cdr0nfceHdGfi2D1j2j2e2Yepff2X0Q3034etex37ey313532gpdB3aevewdC383b2qdE3c2rgsdF4h3ddz4i2zfn4o2AgB3f0p0q0odveo1e4kgudA2B1F3ggEdI1a3m4m1L3i3ker4w1G4n1b0u0seu3h3jd72C4x3leb3p1M3n4pfx4tgH2J4q3r4r0r0wd84ucI3seT1d5GeV3t3qdR2P3u3veN4A3weqd9eX3xeW3A153y3B4zeP3CfI2QfM3F4Bf03E3G3H4CfSfT3IgM3L3WfV4E0v0tdQ3N4Fg6dN3Y3Z3O17404L2F2I164H4J4I3P41gbeQ3R3Q1OeU4K1N4M19g14G4Ng24QdM4Pg34Ogc1K3V4R5F5I5H4S5J4U4T184V5K4W44h84Xh9hW515V4Y525455hU53565W5745hh5XhihY5a465l495b4a5c4bi7hvi85Q5dia5O78777a4c795e7b4d5fic5M4e605R625S4fi26564jl5U5nhpjo7n7d667o47ig5o7p5p68jz7e5r5q7gjq487jjA697i6fhB6b6d5t6c6e6gjC7k6h1g6k6a6i5uhq6m6lhE7u8Aju6nhH7m6j6ojE5i6p6q7s6r5z7x6s1Jhs6t7wiE5AiFiD6xht7y6AiHhK7z6B5w6zhL7A6C6DiN5DiO7BhN7D7F6G6P6H6I7E7HiZ7G6R7I6S6T5x6U6J6VjS7M7O7CiT7K7NiV6L7P6Nj57L7Q7S7R6O7T8z8C8B7Uj68D7X7V7Y8E7Z7WkO8082838P818Q846YkfkgkQ85888R8h6Z72898SkS8a9W73l28I8bl48G748K75l68L768M8i8U9V9Y9X8N9Z8c8j8Om98W8d708Yktkn8Zma8l90718m8nala3lame929493a2amana4mxkx959796a698999amya78pa89b9c8fmA8q9e9g9d9fmi8r9h8umCaaaq8v9i9k9las9j9mkp9nav9qaulA9o9sly8skF9vlCaw9u9wmG9x8xlIay9yaHlJkH9B8t9IlLaJaLaKlS9DaMaNaO9KmYaSaIlUaQ9ElVaUlXlWaT9F9H9GaVaRaWlYaYaXaZb0b1b4b2b5b6b39Rb9nglZacbab8bbbcnm9Snnm2bfbmabaenp9UadbhnwafaAmpbomrbJazaBbpbibqahbsbrmLmNbjblbkajbXaDnCbzbAnKbvbuaGbEnLnMakbIbLbKbMbwbNbFnXbxbPbyaFbYbZo9bRobc1bHbQbGc4occ5c6c8bSbTc7bUo4bW")

BF, HF, FP, I32, U16 = "bfloat16", "float16", "float32", "int32", "uint16"
STR = {"zt": (7184, BF), "S": (1584, BF), "f": (1536, BF), "r": (512, BF), "p": (512, BF), "h": (1024, BF), "yt": (1024, BF),
       "L": (128, U16), "LY": (64, U16), "sP0": (32, HF), "sP1": (64, HF), "sP2": (64, HF),
       "rE0": (96, HF), "rE1": (96, HF), "rE2": (64, HF), "rX2": (64, HF), "qf": (64, FP), "hX": (48, HF)}
CHN = {"rows": (512, BF), "TP": (512, BF), "TQ": (512, BF), "fl": (32, BF), "wb": (16, BF), "rP0": (64, HF), "rP1": (128, HF), "rP2": (128, HF),
       "wI": (256, FP), "wN": (128, FP), "gI": (512, FP), "gP": (256, HF), "gQ": (1024, BF), "mask": (512, HF),
       "cum": (32, HF), "tn": (32, HF), "m32": (32, HF), "gm": (32, HF), "nt": (64, BF), "wS": (256, BF),
       "uO": (16, U16), "uE": (16, U16), "uN": (64, U16), "uP": (96, U16), "uq": (32, U16)}
BUF = {"W1": (4096, BF), "W2": (4096, BF), "W3": (4096, BF), "zb": (1024, BF), "TI": (528, BF), "X": (32, FP), "pi": (8, I32), "pf": (32, FP),
       "one": (144, HF), "oneb": (144, BF), "idh": (128, HF), "idb": (128, BF), "nidb": (128, BF), "nidh": (128, HF), "i7": (128, HF), "ia": (128, HF), "ib": (128, HF),
       "ic": (128, HF), "id": (128, HF), "ie": (128, HF),
       "LT": (128, HF), "GE": (128, HF), "Rh": (1024, HF), "RS": (560, HF), "R1": (256, HF), "W0": (128, BF), "L0": (256, U16),
       "Bq": (408, HF), "Zh": (288, BF), "Zf": (144, BF), "Bc": (128, BF), "pm": (80, BF), "Y": (32, FP), "blkn": (8, FP), "blkh": (8, HF), "pen": (8, HF),
       "Mp": (64, BF), "CR": (24, BF), "cT": (256, HF), "kc": (64, HF), "vI": (96, FP), "qi": (256, I32), "qh": (512, HF)}
for _k, _v in STR.items():
    for _b in range(4):
        BUF["%s_%d" % (_k, _b)] = _v
for _b in range(2):
    for _k, _v in CHN.items():
        BUF["%s_%d" % (_k, _b)] = _v
AL, SB = {}, {}
for _k, (_w, _d) in BUF.items():
    _o = SB.get("pool" + _d, 0)
    AL[_k] = ("pool" + _d, _o); SB["pool" + _d] = _o + (_w + 15) // 16 * 16
SCRATCH = {k: ("sbuf", [128, w], k[4:]) for k, w in SB.items()}
ROW = {"p6": 16, "p7": 32}
for _b in range(8):
    BUF["p%d" % _b] = (1024, BF) if _b == 7 else (512, FP); AL["p%d" % _b] = ("p%d" % _b, 0)
    SCRATCH["p%d" % _b] = ("psum", {6: [128, 32, 16], 7: [128, 32, 32]}.get(_b, [128, 512]), BUF["p%d" % _b][1])
PS = ["p%d" % _b for _b in range(8)]
SEMAPHORES = (["v", "t", "s", "gp", "loc", "dz"] + ["d%d" % k for k in range(60)] + ["rs%d_%d" % (k, y) for k in range(6) for y in range(4)]
              + ["ag%d_%d" % (k, x) for k in range(12) for x in range(2)] + ["yq%d_%d" % (k, x) for k in range(4) for x in range(2)] + ["hi%d" % k for k in range(4)])


def V(n, lo=0, hi=None, st=1, part=(0, 128, 1), out=(1, 0)):
    return ("V", n, lo, BUF[n][0] if hi is None else hi, st, part, out)


def IND(w, o):
    return ("I", w, o)


def nel(v):
    return 16 * nel(v[2]) if v[0] == "I" else len(range(v[2], v[3], v[4])) * v[6][0]


def isv(a):
    return isinstance(a, tuple) and len(a) > 0 and a[0] in ("V", "I")


def on(v, lo, n, st=1):
    return v[:5] + ((lo, n, st), v[6])


def cut(v, a, b):
    return v[:2] + (v[2] + a * v[4], v[2] + (b - 1) * v[4] + 1) + v[4:]


def plan(r, own):
    ops = []; ty = 0 if r in own[0] else 1; xr = own[ty].index(r); big = []

    def views(x):
        return [x] if x[0] == "V" else views(x[1]) + views(x[2]) if x[0] == "I" else []

    def op(eng, *ins, alt=None, on="s"):
        rd, wr = [], []
        for m, a, kw in ins:
            if a[0][0] == "I":
                wr += views(a[0][1]); rd += views(a[0][2])
            else:
                wr += views(a[0])
            for x in list(a[1:]) + list(kw.values()):
                if isv(x):
                    rd += views(x)
        ops.append(((eng,) if alt is None else (eng, on), "c", (ins,) if alt is None else (ins, (alt,)), sorted(set(rd)), sorted(set(wr))))

    def ts(o, i, s1, s2, o0, o1=None):
        op("v", ("tensor_scalar", (o, i, s1, s2, o0) if o1 is None else (o, i, s1, s2, o0, o1), {}))

    def tt(o, a, b, f):
        op("v", ("tensor_tensor", (o, a, b, f), {}))

    def cp(o, i):
        op("v", ("tensor_copy", (o, i), {}))

    def ms(o, c):
        op("v", ("memset", (o, c), {}), alt=("iota", (o, [[0, nel(o)]], int(c), 0), {"allow_small_or_imprecise_dtypes": True}), on="gp")

    def scan(o, a, b, f0, f1):
        op("v", ("tensor_tensor_scan", (o, a, b, 0.0, f0, f1), {}))

    def mov(o, i, bias=None, scale=None):
        kw = {k: x for k, x in (("bias", bias), ("scale", scale)) if x is not None}
        alt = ("activation", (o, i, F.Identity if bias is not None else F.Copy), kw)
        if not kw:
            op("v", ("tensor_copy", (o, i), {}), alt=alt)
        elif len(kw) == 2:
            op("v", ("tensor_scalar", (o, i, scale, bias, A.mult, A.add), {}), alt=alt)
        else:
            op("v", ("tensor_scalar", (o, i, bias if scale is None else scale, None, A.add if scale is None else A.mult), {}), alt=alt)

    def iota(o, pat, base, cm):
        op("gp", ("iota", (o, pat, base, cm), {} if BUF[o[1]][1] == I32 else {"allow_small_or_imprecise_dtypes": True}))

    def mm(groups, first=True, last=True):
        op("t", *[("matmul", (o, l, x, first and k == 0, last and k == len(gr) - 1), {}) for gr in groups for k, (o, l, x) in enumerate(gr)])

    def dma(items, split=False, paced=False):
        after = big[-PAR["pace"]:][:1] if paced and len(big) >= PAR["pace"] else []
        for k, it in enumerate((items[::2], items[1::2]) if split else (items,)):
            ops.append((("sy", "s") if split == 2 else ("s",) if k else ("sy",), "d", (it, after),
                        sorted(set(s for x in it for s in views(x[1]))), sorted(set(s for x in it for s in views(x[0])))))
        if paced:
            big.append(len(ops) - 1)

    def send(name, pairs):
        ops.append((("gp",), "r", (name, pairs), sorted(set(x[1] for x in pairs)), []))

    def recv(name, y, view):
        ops.append((("rx",), "x", (name, y), [], [view]))

    def scatter_sums(s, t, w):
        send("rs%d" % (4 * t + s), [(y, V("sP%d_%d" % (t, s), w * x, w * x + w), V("rP%d_%d" % (t, s // 2), w * r, w * r + w)) for x, y in enumerate(own[s % 2]) if y != r])

    def spread(name, n, w):
        a = V(n, w * xr, w * xr + w)
        send(name, [(y, a, a) for y in others])

    col = lambda n, j: V(n, j, j + 1)
    blk = lambda n, a: V(n, 128 * a, 128 * a + 128)
    SHR, AND = A.arith_shift_right, A.bitwise_and
    EQ, MUL, ADD, MAX, MIN = A.is_equal, A.mult, A.add, A.max, A.min
    others = [x for x in range(4) if x != r]
    C0 = 3072

    def zl(s, u, lo, hi, sh=0):
        return (V("zt_%d" % s, lo + sh + C0 - 1024 * u, hi + sh + C0 - 1024 * u, 1, (32 * u, 32, 1)), ("T", "z", 32 * s, 32, lo, hi - lo))

    ms(V("zb"), 0.0)
    dma([(V("qi", 64 * s, 64 * s + 64), ("T", "q", 32 * s, 32, 0, 256)) for s in range(4)], True)
    dma([zl(0, u, max(1024 * u - 16, 0), 1024 * u + 1024) for u in range(4)] + [zl(0, 0, 4080, 4096, -4096)], True, True)
    dma([zl(0, u, 0, 1024 * u - 16) for u in range(1, 4)] + [zl(0, u, 1024 * u + 1024, 4096) for u in range(3)], True, True)
    for ch in PAR["seq"][ty]:
        if ch in "123":
            for u in range(4):
                dma([zl(int(ch), u, 0, 4096)], paced=True)
        elif ch in "abc":
            for c in range(4):
                dma([(V("W%d" % (1 + "abc".index(ch)), 1024 * c, 1024 * c + 1024), V("zb"))], paced=True)
        elif ch == "V":
            for c in range(4):
                o = V("W1", 1024 * c, 1024 * c + 1024)
                op("v", ("memset", (o, 0.0), {}), alt=("activation", (o, V("zb"), F.Copy), {}))
                ops[-1] = ops[-1][:3] + ([V("zb")], ops[-1][4])
        else:
            dma([(V(n + "_%d" % (ch == "y")), V("zb", 0, 512)) for n in ("TP", "TQ")])

    iota(col("pi", 0), [[0, 1]], 0, 1)
    ms(V("one"), 1.0); ms(V("oneb"), 1.0); ms(V("Bq", 0, 24), 0.0)
    sel = lambda o, pat, base, f=EQ, cm=1: op("gp", ("affine_select", (o, V("one" if BUF[o[1]][1] == HF else "oneb", 0, nel(o)), pat, f, 0.0, base, cm), {}))
    for k, (x, par) in enumerate(((0, 0), (1, 0), (xr, 1))):
        sel(V("Bq", 24 + 128 * k, 152 + 128 * k), [[-1, 4], [1000, 4], [-8, 8]], -64 * x - 4 * par)
    Bq = lambda k, sh: V("Bq", 24 + 128 * k - sh, 152 + 128 * k - sh)
    iota(V("X"), [[1, 32]], 0, 0)
    for j, (sh, an) in enumerate([(0, 15), (4, 7), (5, 3), (1, 7), (0, 1), (4, 1)]):
        ts(col("pi", j + 1), col("pi", 0), sh, an, SHR, AND)
    cp(V("pf", 0, 7), V("pi", 0, 7))
    pf = lambda j: col("pf", j)
    lin = lambda o, a, c, b: ts(pf(o), pf(a), float(c), float(b), MUL, ADD)
    lin(7, 3, -1024, 2048 + C0); lin(8, 5, -31, 32); lin(9, 1, 2, 0); lin(10, 1, 2, 1); lin(11, 2, 16, 0)
    zc = pf(7)
    sel(V("idh"), [[-1, 128]], 0)
    for n, c in (("idb", 1), ("nidb", -1), ("nidh", -1), ("i7", 7), ("ia", -4064), ("ib", -4080), ("ic", -52736), ("id", -51200), ("ie", 1 / 32.0)):
        op("v", ("tensor_scalar", (V(n), V("idh"), float(c), None, MUL), {}), alt=("affine_select", (V(n), V("zb", 0, 128), [[-1, 128]], A.not_equal, float(c), 0, 1), {}), on="gp")
        ops[-1] = ops[-1][:3] + ([V("idh"), V("zb", 0, 128)], ops[-1][4])
    iota(V("Y", 0, 8), [[1, 2], [2, 4]], 0, 0)
    ms(V("Y", 8, 12), 99.0)
    ts(V("pm", 0, 8), V("Y", 0, 8), pf(2), None, EQ)
    ts(V("pm", 8, 16), V("Y", 0, 8), pf(2), -1.0, EQ, MUL)
    iota(V("Y", 12, 28), [[1, 2], [100, 2], [2, 4]], 0, 0)
    ts(V("pm", 16, 36), V("Y", 8, 28), pf(2), None, EQ)
    ts(V("pm", 36, 56), V("Y", 8, 28), pf(2), -1.0, EQ, MUL)
    tt(V("pm", 56, 72), V("pm", 20, 36), V("pm", 36, 52), ADD)
    sel(V("W0"), [[0, 128]], -127)
    sel(V("LT"), [[1, 128]], 0, A.is_gt, -1)
    sel(V("GE"), [[-1, 128]], 0, A.is_ge)
    ts(V("blkn"), V("X", 0, 8), pf(2), -1.0, EQ, MUL)
    ts(V("blkh"), V("X", 0, 8), pf(2), None, EQ)
    ts(V("pen"), V("X", 0, 8), pf(2), 8192.0, EQ, MUL)
    for e in range(2):
        ts(V("Mp", 32 * e, 32 * e + 32), V("X"), pf(9 + e), None, EQ)
        ts(V("CR", 12 * e, 12 * e + 4), V("X", 4 * e, 4 * e + 4), pf(4), pf(8), EQ, MUL)
        ts(V("CR", 12 * e + 4, 12 * e + 12), V("X", 8 * e, 8 * e + 8), pf(1), None, EQ)
        ms(blk("cT", e), 16384.0 * e - 8192.0)

    def pick(o, i, c, pat, base):
        one = V("one" if BUF[o[1]][1] == HF else "oneb", 0, 128)
        op("v", ("tensor_scalar", (o, i, c, None, MUL), {}), alt=("affine_select", (o, one, pat, EQ, 0.0, base, 1), {}), on="gp")
        ops[-1] = ops[-1][:3] + (ops[-1][3] + [one], ops[-1][4])

    iota(V("R1", 0, 128), [[0, 8], [1, 16]], 0, 0)
    ts(V("R1", 128, 256), V("R1", 0, 128), pf(1), -1.0, EQ, MUL)
    for a in range(8):
        pick(blk("Rh", a), blk("R1", 1), col("blkn", a), [[0, 8], [-1, 16]], -16 * a)
    ms(V("RS"), 0.0); ms(V("Zh"), 0.0); ms(V("Zf", 0, 16), 0.0)
    lin(12, 6, -1, 1); ts(pf(13), pf(1), 0.0, None, EQ); ts(pf(14), pf(1), 8.0, None, EQ)
    pick(V("RS", 112, 240), V("idh"), pf(12), [[-32, 4], [1000, 2], [-1, 16]], 0); pick(V("RS", 272, 400), V("idh"), pf(6), [[-32, 4], [-1016, 2], [-1, 16]], 1000)
    for lo, n, base in ((432, 3, -32), (528, 1, 0)):
        sel(V("RS", lo, lo + 32 * n), [[-32, n], [1000, 2], [-1, 16]], base)
    RS = lambda v, sh: V("RS", 112 + 160 * v - sh, 240 + 160 * v - sh)
    pick(V("Zh", 16, 144), V("idh"), pf(13), [[-16, 8], [1000, 16]], 0); pick(V("Zh", 152, 280), V("idh"), pf(14), [[-16, 8], [-1008, 2], [1000, 8]], 1000)
    tt(V("Zf", 16, 144), V("Zh", 16, 144), V("Zh", 160, 288), ADD)
    sel(V("Bc"), [[-16, 8], [0, 16]], -8)
    iota(V("kc", 0, 48), [[1, 3], [128, 16]], -2049, 1); iota(V("kc", 48, 64), [[128, 16]], -2047, 1)
    for c, b, f in ((0, 0, 2047.0), (63, -127, -4096.0)):
        op("gp", ("affine_select", (col("kc", c), col("kc", c), [[0, 1]], A.not_equal, f, b, 1), {}))
    Kc = lambda k: V("kc", 16 * k, 16 * k + 16)
    iota(V("vI", 0, 32), [[0, 2], [8, 2], [16, 8]], 0, 0); iota(V("vI", 32, 64), [[-1, 2], [0, 16]], 1, 0); iota(V("vI", 64, 96), [[0, 2], [1, 16]], 0, 0)
    ms(V("TI"), 0.0)
    mov(V("TI", 16, 528, 16), V("vI", 0, 32), pf(2)); mov(V("TI", 17, 528, 16), V("vI", 32, 64), pf(9))
    ts(V("qh", 0, 256), V("qi"), -2048.0, None, ADD)
    ts(V("qh", 256, 512), V("qh", 0, 256), 2047.0, -4096.0, EQ, MUL)
    lin(15, 7, 1, 1)
    for d in range(2):
        o = V("p%d" % (4 + d), 0, 128)
        mm([[(o, Bq(x, 16 * x + 8 * k), V("qh", 256 * e + k, 256 * e + 256, 2)) for e in range(d + 1) for x in range(2) for k in range(2)]])
        mov(V("L0", 128 * d, 128 * d + 128), o, pf(15) if d else zc)

    def stream(s):
        W = lambda n, *a: V("%s_%d" % (n, s), *a)
        P = lambda *a: V("p6", *a); Q = lambda *a: V("p%d" % (4 + s % 2), *a)
        ZW = W("zt"); ow = own[s % 2]

        def least(o, a, e, on_s, P=Q):
            if on_s:
                mm([[(P(), V("idb"), e), (P(), V("nidb"), a)]])
                op("s", ("activation", (o, P(), F.Relu), {}))
            else:
                tt(o, a, e, MIN)
            return o, 8 * on_s

        def walk(o, a, b, k=1):
            n = nel(o) // k
            for c in range(0, nel(o), n):
                scan(cut(o, c, c + n), cut(a, c, c + n), cut(b, c, c + n), MAX, MIN)

        def sums(t, items, n):
            red = lambda it: [(Q(j, n, 4), cut(v, 128 * j, 128 * j + 128), V("pm", c, c + n // 4)) for j in range(4) for v, c in it]
            for k, it in enumerate(items):
                mm([[(Q(0, n), V("idb"), V("zb", 0, n))] * (k == 0) + red(it)], k == 0, k == len(items) - 1)
            mov(W("sP%d" % t), Q(0, n))
            scatter_sums(s, t, n // 2)

        def start():
            if s:
                mov(W("zt", C0 - 1, C0, 1, (0, 32, 1)), W("zt", 7167, 7168, 1, (0, 32, 1)))

        def coords0():
            S = PAR["m"][ty][s]; ne = ("D" in S) + ("F" in S)
            walk(W("f", 0, 1024), W("zt", C0 - 1, C0 + 1023), W("zt", C0, C0 + 1024))
            walk(W("r"), W("zt", C0 - 1, C0 + 1022, 2), W("zt", C0 + 1, C0 + 1024, 2))
            e, x0, x1 = W("zt", C0, C0 + 1023, 2), W("yt", 0, 512), W("yt", 512, 1024)
            mov(x0, IND(ZW, V("L0", 32 * s, 32 * s + 32))); d = least(W("p"), x0, e, "D" in S, P if "p" in S else Q)
            mov(x1, IND(ZW, V("L0", 128 + 32 * s, 160 + 32 * s))); f = least(W("h", 0, 512), x1, e, "F" in S); tt(W("h", 512, 1024), x1, x0, MIN)
            sums(0, [[(W("f", 0, 1024, 2), 8), (W("f", 1, 1024, 2), 8), (W("r"), 0)] + [(e, 0)] * ne, [d, f, (W("h", 512, 1024), 8)]], 32)

        def lists(t, w, n, rng, P=P):
            E = "rE%d_%d" % (t, s)
            xs = sorted(range(2), key=lambda x: ow[x] != r)
            for k, x in enumerate(xs):
                if ow[x] != r:
                    recv("ag%d" % (4 * t + s), ow[x], V(E, w * x, w * x + w))
                sh = [(o, RS(v, 16 * (x - v % 2)), V(E, w * x + lo, w * x + hi)) for v, lo, hi, o in rng]
                if k == 0 and ow[x] != r:
                    mm([[(P(0, n), V("idb"), V("zb", 0, n))]], last=False)
                mm([[(P(0, n), V("idb"), V("zb", 0, n))] * (ow[x] == r) + sh], ow[x] == r, k == 1)

        def coords(t):
            h16 = lambda c, n, st: P(c, c + 16, 1, (0, 128, 1), (n, st))
            lists(t - 1, 48, 128, [(h, 0, 48, h16(16 * h, 3, 48)) for h in range(2)] + [(2, 0, 1, P(32, 33))])
            mov(W("L"), P(0, 128), zc)
            for o, lo, n in ((0, 0, 528), (2, 48, 512), (1, 96, 512)):
                mov(cut(W("S", o, 1584, 3), 0, n), IND(ZW, W("L", lo, lo + n // 16)))
                if o == 0:
                    walk(W("r"), W("S", 0, 1534, 3), W("S", 3, 1537, 3))
                if o == 2:
                    tt(W("p"), W("S", 0, 1534, 3), W("S", 2, 1536, 3), MIN)
            walk(W("f"), W("S", 0, 1536), W("S", 1, 1537), PAR["sw"])
            sums(t, [[(W("r"), 16), (W("p"), 56)], [(W("f", 0, 1536, 3), 40), (W("f", 1, 1536, 3), 40), (W("f", 2, 1536, 3), 36)]], 64)

        def final():
            lists(2, 32, 64, [(v, 0, 32, Q(32 * v, 32 * v + 32)) for v in range(2)], Q)
            mov(W("LY"), Q(0, 64), zc)
            for c in range(2):
                mov(W("yt", 512 * c, 512 * c + 512), IND(ZW, W("LY", 32 * c, 32 * c + 32)))
            dma([(("T", "yz", 32 * s, 32, 1024 * u, 1024), on(W("yt"), 32 * u, 32)) for u in range(4)], 2)

        def targets():
            for x in range(2):
                if ow[x] != r:
                    recv("yq%d" % s, ow[x], W("rX2", 32 * x, 32 * x + 32))
            mov(W("qf"), W("rX2"), 2048.0)
            dma([(("T", "yq", 2 * s + x, 1, 0, 4096), W("qf", 32 * x, 32 * x + 32)) for x in range(2)], 2)

        return [start, coords0, lambda: coords(1), lambda: coords(2), final, targets]

    def chain(b):
        s = 2 * b + ty
        N = lambda n: "%s_%d" % (n, b)
        W = lambda n, *a: V(N(n), *a)
        P = lambda k, *a: V("p%d" % (2 * b + k), *a)
        PT = lambda *a: V("p7", *a)
        row = lambda n, k: W(n, k, 512, 16)

        def turn(tiles, flat):
            o = lambda k: PT(128 * k, 128 * k + 128) if flat else PT(256 * (k // 2) + 16 * (k % 2), 256 * (k // 2) + 16 * (k % 2) + 16, 1, (0, 128, 1), (8, 32))
            op("t", *[("transpose", (o(k), x, V("idb")), {}) for k, x in enumerate(tiles)])
            mov(W("rows"), PT(0, 512))

        def rep(k, rhs):
            return [(P(k, a, 8 * nel(rhs), 8), blk("Rh", a), rhs) for a in range(8)]

        def address(u, ps, c, m, gm, last, pa, again):
            big = 24576 if last else 49152
            mov(m, ps, c + big - (7.5 if last else 15.5))
            mov(gm, ps, c / 512.0 + 1535.5 + 1 / 1024.0, 1 / 512.0)
            mm([again + [(pa, V("i7"), m), (pa, V("ib" if last else "ia"), gm)]], first=bool(again))
            mov(u, pa, float(c - 7 * big + 1536 * (4080 if last else 4064)))

        def prep0():
            ms(W("cum", 0, 8), 0.0)
            qd = lambda k: [(P(k, 16 - 16 * par, 32 - 16 * par), Bq(2 if par else xr, 16 * h + 8 * j), V("qh", 64 * s + 32 * h + j, 64 * s + 32 * h + 32, 2))
                            for par in range(2) for h in range(2) for j in range(2)]
            mm([[(P(0, 0, 32), V("idb"), V("zb", 0, 32))] + qd(0)])
            mm([[(P(1, 0, 32), V("idb"), V("zb", 0, 32))] + qd(1)], last=False)
            address(W("uq"), P(0, 0, 32), 2048, W("m32"), W("gm"), False, P(1, 0, 32), [])
            turn([V("TI", 16 - 2 * b + 128 * k, 144 - 2 * b + 128 * k) for k in range(4)], True)
            for k in range(2):
                cp(IND(V("W1"), W("uq", 16 * k, 16 * k + 16)), W("rows", 256 * k, 256 * k + 256))
            mm([[(P(1, 0, 32), V("nidh"), W("m32"))] + qd(1)])
            mov(row("TP", 13), P(1, 0, 32), 51200.0)
            mov(W("uP", 80, 96), P(1, 16, 32), 51200.0)
            mov(row("TP", 12), W("m32"), -1536.0, 1 / 32.0)
            mov(W("uP", 64, 80), W("m32", 16, 32), -1536.0, 1 / 32.0)
            mov(W("mask", 0, 256), IND(V("Mp", 32, 64), W("uP", 80, 96)))
            mm([[(P(0, j, 64, 32), V("W1", 256 * (j % 16) + 1 - j // 16, 256 * (j % 16) + 256, 2), V("CR", 4 + 2 * b, 6 + 2 * b))] for j in range(32)])
            mov(W("uP", 0, 48), P(0, 0, 48))
            mov(W("mask", 256, 512), IND(V("Mp", 0, 32), W("uP", 32, 48)))
            for k in range(2):
                mov(row("TP", 10 + k), P(0, 32 * k, 32 * k + 32))
            mov(row("TP", 8), V("vI", 64, 96), pf(11)); mov(row("TP", 9), V("vI", 32, 64), pf(9))
            turn([blk(N("TP"), k) for k in range(4)], False)

        def index(t):
            w = 32 if t else 16; n = 8 * w; last = t == 2
            uT, uG = [W("uP", c, c + 16) for c in ((64, 0), (48, 0), (16, 32))[t]]
            part = lambda y: V("sP%d_%d" % (t, s), w * xr, w * xr + w) if y == r else W("rP%d" % t, w * y, w * y + w)
            L = P(1, 32 - w, 32); red = lambda o, x, k, m: [(P(1, o + R, o + 16, 2), blk(N(x), k + R), V(m)) for R in range(2)]
            mm([[(P(0, 0, n), V("idh"), V("cT", 256 - n, 256))] + rep(0, part(r))], last=False)
            mm([[(P(1, 0, 32), V("nidh"), V("cT", 112, 144)), (P(1, 0, 16), V("idh"), V("one", 0, 16)), (L, V("idh"), part(r))] + (red(16, "mask", 0, "pen") if t == 0 else [])], last=False)
            far = sorted(others, key=lambda y: y in own[ty])
            for y in far:
                recv("rs%d" % (4 * t + s), y, part(y))
                mm([rep(0, part(y))], False, y == far[2])
            mov(W("wI", 256 - n, 256), P(0, 0, n))
            mm([[(L, V("idh"), part(y)) for y in others]], False, False)
            PA = P(0, 256, 288); A1, A2, AO = P(0, 256, 272), P(0, 272, 288), P(0, 288, 304)
            k1, k2, kO = ((2, 1, 1), (1, 1, 0), (2, 3, 1))[t]; pO = 0 if t else 1
            mm([[(P(0, 256, 304), V("idb"), V("zb", 0, 48)), (A1, V("idh"), Kc(k1)), (A2, V("idh"), Kc(k2)), (AO, V("idh"), Kc(kO))]], last=False)
            if t:
                tt(W("gI", 256, 512), IND(W("wI", 0, 128), uT), W("mask", 0, 256), MUL)
                mm([red(16, "gI", 2, "blkn")], False, False)
            tt(W("gI", 0, 256), IND(W("wI", 128, 256), uG), W("mask", 256, 512), MUL)
            mm([red(0, "gI", 0, "blkn")], False)
            ts(W("fl"), P(1, 0, 32), 0.5, None, A.is_lt)
            guest, stays = W("fl", 0, 16), W("fl", 16, 32)
            c1, cb = W("cum", 8, 24), W("cum", 7, 23)
            mm([[(A2, V("idb"), guest)] if t else [(A1, V("idb"), stays), (AO, V("idb"), stays)]], False, False)
            scan(c1, guest, stays, ADD, ADD)
            if last:
                ts(W("wb"), V("zb", 0, 16), col(N("fl"), 31), None, ADD)
            pre = lambda o: [(o, V("LT"), c1), (o, V("GE"), cb)] + [(o, V("W0"), W("wb"))] * last
            nO = lambda o: [(o, V("idh"), Kc(kO))] + pre(o) + [(o, V("idb"), stays)] * pO
            mm([pre(A1) + pre(A2) + pre(AO)], False)
            tt(W("tn"), PA, W("fl"), MUL)
            mm([[x] for x in rep(1, W("tn", 0, 16))])
            mov(W("wN"), P(1, 0, 128))
            wn = "W%d" % min(3, 1 + t + b); WW = V(wn)
            mO, mE = W("m32", pO, 32, 2), W("m32", 1 - pO, 32, 2)
            address(W("uO"), AO, 2048, mO, W("gm", 0, 16), last, AO, nO(AO))
            cp(IND(WW, W("uO")), W("rows", 0, 256))
            tt(W("gP"), IND(W("wN"), uT), W("mask", 0, 256), MUL)
            nE = lambda o, st, k=0: [(P(k, o, o + 16 * st, st), V("idh"), W("tn", 16, 32))] + [(P(k, o + R * st, o + 16 * st, 2 * st), blk(N("gP"), R), V("blkh")) for R in range(2)]
            mm([nE(0, 1)[:1]], last=False)
            mm([nE(0, 1)[1:]], False)
            mm([nE(0, 1, 1)], last=False)
            address(W("uE"), P(0, 0, 16), 2048, mE, W("gm", 16, 32), last, P(1, 0, 16), [])
            cp(IND(WW, W("uE")), W("rows", 256, 512))
            E = "rE%d_%d" % (t, s); name = "ag%d" % (4 * t + s)
            c0, nq = ((12, 8), (12 * b, 6), (2 * b, 2))[t]
            mm([[(P(1, j, 32 * nq, 32), blk(wn, j) if last else V(wn, 256 * (j % 16) + j // 16, 256 * (j % 16) + 256, 2), V("CR", c0, c0 + nq))] for j in range(32)])
            we = 32 if last else 48
            mov(V(E, we * xr, we * xr + we), P(1, 0, we), -2048.0)
            spread(name, E, we)
            lo, nl = ((32, 64), (64, 48), (32, 32))[t]
            mov(W("uN", 0, nl), P(1, lo, lo + nl))
            tile, r0 = ("TQ", 4 * b) if t else ("TP", 8 * b)
            for k in range((4, 2, 0)[t]):
                mov(row(tile, r0 + k), P(1, 128 + 32 * k, 160 + 32 * k))
            mm([[(P(0, 64, 96), V("nidh"), W("m32"))] + nE(65 - pO, 2) + nO(P(0, 64 + pO, 96, 2))
                + [(P(0, 32, 64), V("idh" if last else "ie"), W("m32")), (P(0, 32, 64), V("id" if last else "ic"), V("one", 0, 32))]])
            mov(W("nt"), P(0, 32, 96), 26624.0 if last else 51200.0)
            op("t", *[("transpose", (PT(128 * par, 128 * par + 128, 1, (32 * k, 32, 1)), W("nt", par, 64, 2), V("idb")), {}) for k in range(4) for par in range(2)])
            for par in range(2):
                mov(W("wS", par, 256, 2), PT(128 * par, 128 * par + 128))
            dma([(on(V("W1"), 64 * k, 8, 8), W("wS")) for k in range(2)], 2)
            for a in range(0, nl, 16 if last else 32):
                e = min(a + (16 if last else 32), nl)
                mov(W("gQ", 16 * a, 16 * e), IND(V("W1"), W("uN", a, e)))
            Z = lambda z, i: V("Zh", 160 - i, 288 - i) if z == "Zl" else V(z, 16 - i, 144 - i)
            if last:
                for h in range(2):
                    mm([[(P(0, 0, 32), Z("Zf", i), W("gQ", 32 * i, 32 * i + 32)) for i in range(8 * h, 8 * h + 8)]], h == 0, h == 1)
                mov(V("rX2_%d" % s, 32 * xr, 32 * xr + 32), P(0, 0, 32), -2048.0)
                spread("yq%d" % s, "rX2_%d" % s, 32)
                return
            mm([[(P(0, 0, nl), Z("Zh", i), W("gQ", i, 16 * nl, 16)) for i in range(16)]])
            mov(W("uP", 0, nl), P(0, 0, nl))
            cT, cG = (48, 0) if t == 0 else (16, 32)
            mm([[(P(1, 256 * k, 256 * k + 256), V("Bc"), W("gQ", 16 * c, 16 * c + 256)) for k, c in enumerate((cT, cG))]
                + [(P(1, c, c + 128), V("nidh"), V("one", 0, 128)) for c in (256, 384)]])
            ts(W("mask"), P(1), pf(9), None, EQ)
            nr = 64 - 32 * t; dst = ((6, 4), (2,))[t]
            for k, d in enumerate(dst):
                mov(row(tile, r0 + d), P(0, 32 * k, 32 * k + 32))
            mm([[(P(0, 64, 64 + nr), Z("Zl", i), W("gQ", i, 16 * nr, 16)) for i in range(16)]])
            for k, d in enumerate(dst):
                mov(row(tile, r0 + d + 1), P(0, 64 + 32 * k, 96 + 32 * k))
            turn([blk(N(tile), k) for k in range(4)], False)

        return [prep0, index]

    st = [stream(s) for s in range(4)]; ch = [chain(b) for b in range(2)]
    for b in range(2):
        ch[b][0]()
    for t in range(4):
        for s in range(4):
            if t == 0:
                st[s][0]()
            if t < 3 or s > 1:
                st[s][t + 1]()
            if t == 2 and s > 1:
                st[s - 2][4]()
            if t == 3:
                st[s][5]()
            elif s % 2 == ty:
                ch[s // 2][1](t)
    return ops


def bits(v, dma):
    n = len(range(v[2], v[3], v[4])); m = ((1 << (v[4] * n)) - 1) // ((1 << v[4]) - 1) << v[2]
    if v[6][0] > 1:
        m *= ((1 << (v[6][1] * v[6][0])) - 1) // ((1 << v[6][1]) - 1)
    if dma:
        k = 4 if BUF[v[1]][1] in (FP, I32) else 8; lo = v[2] // k * k; hi = -(-v[3] // k) * k
        m = ((1 << (hi - lo)) - 1) << lo
    return m, ((1 << (v[5][2] * v[5][1])) - 1) // ((1 << v[5][2]) - 1) << v[5][0]


def depend(ops, eng):
    deps = [set() for _ in ops]; acc = {}; bank = {}
    for j, (_, kind, pay, rd, wr) in enumerate(ops):
        if kind == "d":
            deps[j].update(pay[1])
        for nm in set(x[1] for x in rd + wr if x[1] in PS):
            before, now = bank.get(nm, ([], []))
            if now and eng[j] == eng[now[0]] != "t":
                deps[j].update(before); bank[nm] = (before, now + [j])
            else:
                deps[j].update(now); bank[nm] = (now, [j])
        for lst, isw in ((rd, False), (wr, True)):
            for v in lst:
                if v[1] not in PS:
                    c, p = bits(v, isw and kind != "c"); old = acc.get(v[1], [])
                    deps[j].update(x[0] for x in old if (isw or x[3]) and x[1] & c and x[2] & p and x[0] != j)
                    acc[v[1]] = [x for x in old if not (isw and x[1] & ~c == 0 and x[2] & ~p == 0)] + [(j, c, p, isw)]
    return deps


def ordered(r, own=((0, 3), (1, 2))):
    al = "0123456789abcdefghijklmnopqrstuvwxyzABCDEFGHIJKLMNOPQRSTUVWXYZ"; ops = plan(r, own); n = len(ops)
    o = ORDER[0 if r in own[0] else 1]; order = list(range(n)); eng = [x[0][0] for x in ops]
    for k in range(len(o) // 2):
        c, j = divmod(62 * al.index(o[2 * k]) + al.index(o[2 * k + 1]), n); order[k] = j; eng[j] = ops[j][0][c]
    return ops, order, eng


def owners(T, topo):
    ch = [topo.chip(c) for c in T.cores]
    far = [y for y in range(1, 4) if not topo.mates(ch[0], ch[y]) and not topo.same_plane(ch[0], ch[y])][0]
    return ((0, far), tuple(y for y in range(1, 4) if y != far))


def helper_of(T, topo, c):
    ok = [x for x in topo.cores_of(c) if T.rank_of(x) is None and all(topo.may_write(x, d) for d in T.cores if d != c)]
    return sorted(ok, key=lambda x: topo.die(x) != topo.die(c))[0]


def dst_id(topo, c):
    rid, pid, _ = topo.addr(c)
    return DstId(rid=rid, pnc=pid)


def common(T, topo, src, ranks):
    return [e for e in topo.engines(src, T.cores[ranks[0]]) if all(topo.mask(src, T.cores[y]) >> e & 1 for y in ranks)]


def mask_of(engines):
    return sum(1 << e for e in engines)


def index_of(x):
    _, n, lo, hi, st, (pa, pn, ps), (k, ks) = x
    p = slice(pa, pa + (pn - 1) * ps + 1, ps); hi = lo + (len(range(lo, hi, st)) - 1) * st + 1
    if n not in ROW:
        b, o = AL[n]
        return b, (p, slice(o + lo, o + hi, st))
    w = ROW[n]; a, c = divmod(lo, w)
    if k > 1:
        return n, (p, slice(a, a + (k - 1) * (ks // w) + 1, ks // w), slice(c, c + hi - lo, st))
    if (hi - 1) // w == a:
        return n, (p, a, slice(c, c + hi - lo, st))
    if st % w == 0:
        return n, (p, slice(a, (hi - 1) // w + 1, st // w), c)
    assert w % st == 0 and c < st and (hi - 1) % w >= w - st, x
    return n, (p, slice(a, (hi - 1) // w + 1), slice(c, w, st))


def rank_program(g, core, T, topo):
    S = T.sem; own = owners(T, topo)
    rest = lambda r: [y for y in range(4) if y != r]

    def ap(x):
        if isinstance(x, tuple) and x[0] == "T":
            return T[x[1]][x[2]:x[2] + x[3], x[4]:x[4] + x[5]]
        if not isv(x):
            return x
        if x[0] == "I":
            return ap(x[1]).indirect(ap(x[2]))
        n, ix = index_of(x)
        return T[n][ix]

    def sem_of(name, y):
        k = int(name[2:])
        return "rs%d_%d" % (k // 2, y) if name[:2] == "rs" else "%s_%d" % (name, own[k % 2].index(y))

    def spread(src, pairs, sem, loc):
        e = common(T, topo, core, [y for y, _, _ in pairs])
        g.remote_dma_fused([RemoteDMATransfer(dst_ids=[dst_id(topo, T.cores[y]) for y, _, _ in pairs], dma_engine_mask=mask_of(e), remote_sem=sem,
                                              srcs=[ap(src)], dsts=[ap(d) for _, _, d in pairs])], local_sem=loc)
        return len(e)

    def to_helper(r):
        c = T.cores[r]; off = common(T, topo, c, rest(r))
        return [e for e in topo.engines(c, helper_of(T, topo, c)) if e not in off]

    def arrivals(name, y):
        if name[:2] == "rs":
            return len(common(T, topo, T.cores[y], rest(y))) // (1 if y in own[int(name[2:]) % 2] else 2)
        return len(common(T, topo, helper_of(T, topo, T.cores[y]) if name in PAR["help"] else T.cores[y], rest(y)))

    for r in range(4):
        if core == helper_of(T, topo, T.cores[r]):
            ops, order, _ = ordered(r, own); n = 0; loc = 0
            for j in order:
                if ops[j][1] == "r" and ops[j][2][0] in PAR["help"]:
                    name, pairs = ops[j][2]
                    g.wait_ge(S["hi%d" % n], len(to_helper(r)))
                    loc += spread(V("hX_%d" % n, 0, nel(pairs[0][1])), pairs, S[sem_of(name, r)], S.loc); n += 1
            g.wait_ge(S.loc, loc)
            return
    r = T.rank_of(core)
    if r is None:
        return
    ops, order, eng = ordered(r, own); deps = depend(ops, eng)
    pos = {j: k for k, j in enumerate(order)}
    assert len(pos) == len(ops) and all(pos[i] < pos[j] for j in range(len(ops)) for i in deps[j])
    QU = {"v": g.vector, "t": g.tensor, "s": g.scalar, "gp": g, "sy": g.sync}
    needed = set(i for j in range(len(ops)) for i in deps[j] if not eng[i] == eng[j] == "t")
    sig = {}; cnt = {"v": 0, "t": 0, "s": 0, "gp": 0, "dz": 0}; nd = 0
    for j in order:
        kind, pay = ops[j][1:3]
        if kind == "c" and j in needed:
            cnt[eng[j]] += 1; sig[j] = (eng[j], cnt[eng[j]])
        elif kind == "d" and j in needed:
            sig[j] = ("d%d" % nd, 16 * len(pay[0])); nd += 1
        elif kind == "d":
            cnt["dz"] += 16 * len(pay[0]); sig[j] = ("dz", cnt["dz"])
        elif kind == "x":
            sig[j] = (sem_of(*pay), arrivals(*pay))

    def call(q, m, a, kw):
        f = {"matmul": lambda: q.matmul, "transpose": lambda: q.transpose, "tensor_scalar": lambda: q.tensor_scalar, "tensor_tensor": lambda: q.tensor_tensor,
             "tensor_copy": lambda: q.tensor_copy, "memset": lambda: q.memset, "activation": lambda: q.activation,
             "iota": lambda: q.iota, "affine_select": lambda: q.affine_select, "tensor_tensor_scan": lambda: q.tensor_tensor_scan}[m]()
        return f(*[ap(x) for x in a], **{k: ap(x) for k, x in kw.items()})

    waited = {}; loc = 0; gate = None; nh = 0
    for j in order:
        kind, pay = ops[j][1:3]; e = eng[j]
        if kind == "x":
            continue
        q = QU[e]; want = {}
        for i in deps[j]:
            if not eng[i] == e == "t":
                nm, c = sig[i]; want[nm] = max(want.get(nm, 0), c)
        if kind == "d" and gate and PAR["gate"]:
            for nm, c in gate.items():
                want[nm] = max(want.get(nm, 0), c)
        for nm, c in sorted(want.items()):
            if waited.get((e, nm), 0) < c:
                q.wait_ge(S[nm], c); waited[(e, nm)] = c
        if kind == "c":
            for m, a, kw in pay[ops[j][0].index(e)]:
                ins = call(q, m, a, kw)
            if j in sig:
                ins.then_inc(S[e], 1)
        elif kind == "d":
            for o, i in pay[0]:
                q.dma_start(ap(o), ap(i)).then_inc(S[sig[j][0]], 16)
        else:
            name, pairs = pay; sem = S[sem_of(name, r)]
            if name in PAR["help"]:
                rid, pid, _ = topo.addr(helper_of(T, topo, core)); h = to_helper(r)
                g.remote_dma(ap(V("hX_%d" % nh, 0, nel(pairs[0][1]))), ap(pairs[0][1]), S["hi%d" % nh], S.loc, pid, rid, mask_of(h))
                nh += 1; loc += len(h)
                continue
            if name[:2] != "rs":
                loc += spread(pairs[0][1], pairs, sem, S.loc)
            else:
                h = common(T, topo, core, rest(r)); k = len(h) // len(pairs); loc += len(h)
                g.remote_dma_fused([RemoteDMATransfer(dst_ids=[dst_id(topo, T.cores[y])], dma_engine_mask=mask_of(h[k * i:k * i + k]), remote_sem=sem, src=ap(a), dst=ap(d))
                                    for i, (y, a, d) in enumerate(pairs)], local_sem=S.loc)
            gate = want
    done = {"loc": loc}
    for nm, c in sig.values():
        done[nm] = max(done.get(nm, 0), c)
    for nm, c in sorted(done.items()):
        g.wait_ge(S[nm], c)
